import numpy as np
import ml_dtypes


def mxq(x, axis, fmt="e4m3"):
    dtype, down = {"e4m3": (ml_dtypes.float8_e4m3fn, 7), "e5m2": (ml_dtypes.float8_e5m2, 14)}[fmt]
    v = np.moveaxis(np.asarray(x, np.float32).astype(ml_dtypes.bfloat16).astype(np.float64), axis, -1)
    blocks = v.reshape(v.shape[:-1] + (-1, 32))
    amax = np.abs(blocks).max(-1, keepdims=True)
    byte = np.maximum(np.where(amax > 0, np.frexp(amax)[1] - 1 + 127, 0) - down, 1)
    scale = np.exp2(byte - 127.0)
    codes = (blocks / scale).astype(np.float32).astype(dtype).astype(np.float64)
    return np.moveaxis((codes * scale).reshape(v.shape), -1, axis)


WIDE = False


def mx_kscale(k):
    if not WIDE:
        return np.ones(k)
    levels = np.array([10, -10, 5, -5, 0])
    if k % 512:
        return np.exp2(np.random.permutation(np.resize(levels, k // 32))).repeat(32)
    a = np.empty((k // 512, 16))
    for p in range(k // 512):
        a[p, :8] = np.random.permutation(np.resize(levels, 8))
        for g in range(8):
            far = levels[np.abs(levels - a[p, g]) >= 10]
            a[p, g + 8] = far[np.random.randint(len(far))]
    return np.exp2(a.ravel()).repeat(32)


def f64(x):
    return np.asarray(x).astype(np.float64)


def striped(idx):
    return np.tile(idx.reshape(-1, 16).T, (8, 1)).astype(np.uint16)


def unstriped(offs):
    return offs[:16].T.reshape(-1).astype(np.int64)


E2M1 = np.array([0.0, 0.5, 1.0, 1.5, 2.0, 3.0, 4.0, 6.0, -0.0, -0.5, -1.0, -1.5, -2.0, -3.0, -4.0, -6.0])


def pack_weight(w, fmt):
    k, n = w.shape
    w = f64(np.asarray(w, np.float32).astype(ml_dtypes.bfloat16)).reshape(k // 32, 32, n)
    amax = np.abs(w).max(1)
    if fmt == "e4m3":
        byte = np.frexp(amax)[1] - 1 + 127 - 7
    else:
        mant, ex = np.frexp(amax / 6.0)
        byte = np.where(mant > 0.5, ex, ex - 1) + 127
    byte = np.clip(np.where(amax > 0, byte, 1), 1, 254)
    scaled = (w * np.exp2(127.0 - byte)[:, None, :]).reshape(k, n).astype(np.float32)
    by_word = np.ascontiguousarray(scaled.reshape(k // 512, 128, 4, n).transpose(0, 1, 3, 2))
    if fmt == "e4m3":
        words = by_word.astype(ml_dtypes.float8_e4m3fn).view(np.uint8)
    else:
        c = by_word.astype(ml_dtypes.float4_e2m1fn).view(np.uint8) & 0xF
        words = (c[..., 0::2] | (c[..., 1::2] << 4)).reshape(k // 512, 128, 2 * n)
    return np.ascontiguousarray(words), np.ascontiguousarray(byte.astype(np.uint8).reshape(k // 512, 16, n))


def unpack_weight(words, scales, fmt):
    g, _, n = scales.shape
    words = np.ascontiguousarray(words).reshape(g, 128, n, -1)
    if fmt == "e4m3":
        vals = words.view(ml_dtypes.float8_e4m3fn).astype(np.float64)
    else:
        nib = np.empty((g, 128, n, 4), np.uint8)
        nib[..., 0::2] = words & 0xF
        nib[..., 1::2] = words >> 4
        vals = E2M1[nib]
    vals = vals * np.repeat(np.exp2(scales.astype(np.float64) - 127.0), 8, axis=1)[..., None]
    return vals.transpose(0, 1, 3, 2).reshape(g * 512, n)


def gelu(v):
    return 0.5 * v * (1.0 + np.tanh(np.sqrt(2.0 / np.pi) * (v + 0.044715 * v**3)))


K, H, N, T, S, T2, P = 1024, 1024, 512, 2048, 1024, 2048, 1024

def setup_inputs():
    n = np.random.standard_normal
    s = mx_kscale(K)[:, None]
    u = mx_kscale(H)[:, None]
    tab_words, tab_scales = pack_weight(n((K, T)) * s, "e4m3")
    w4_words, w4_scales = pack_weight(0.9 * n((K, H)) / np.sqrt(K) / s, "e2m1")
    return {
        "tab_words": tab_words, "tab_scales": tab_scales,
        "offs": striped(np.random.permutation(T)[:S]),
        "w4_words": w4_words, "w4_scales": w4_scales,
        "wgs": np.exp(0.3 * n((128, S))).astype(np.float32),
        "offs2": striped(np.random.permutation(T2)[:S]),
        "offs3": striped(np.random.permutation(T2)[:P]),
        "work": (n((H, P)) * u).astype(np.float32),
        "wo": (n((H, N)) / np.sqrt(H) / u).astype(np.float32),
    }

def reference(tab_words, tab_scales, offs, w4_words, w4_scales, wgs, offs2, offs3, work, wo):
    v = unpack_weight(tab_words, tab_scales, "e4m3")[:, unstriped(offs)]
    w4 = unpack_weight(w4_words, w4_scales, "e2m1")
    d = w4.T @ v
    h = d * (1.0 + 0.5 * d)
    page = np.zeros((H, T2))
    page[:, unstriped(offs2)] = np.tile(f64(wgs), (H // 128, 1)) * h
    x = page[:, unstriped(offs3)]
    z = f64(work) * np.cos(np.minimum(x, 2.5))
    return mxq(f64(wo), 0, "e4m3").T @ mxq(z, 0, "e4m3")

@@ -1,0 +1,297 @@
+import math
+from contextlib import ExitStack
+
+import concourse.mybir as mybir
+
+K, H, N, T, S, T2, M = 1024, 1024, 512, 2048, 1024, 2048, 1024
+FLOPS = 2 * K * H * S + 2 * H * N * M
+
+F32 = mybir.dt.float32
+BF16 = mybir.dt.bfloat16
+I32 = mybir.dt.int32
+U32 = mybir.dt.uint32
+U16 = mybir.dt.uint16
+U8 = mybir.dt.uint8
+E4M3 = mybir.dt.float8_e4m3fn_x4
+E2M1 = mybir.dt.float4_e2m1fn_x4
+ACT = mybir.ActivationFunctionType
+ALU = mybir.AluOpType
+
+P = 128
+TILES = H // P
+CAP = 2.5
+TURN = 2.0 * math.pi
+PHASE = math.pi / 2 - CAP
+CHUNK = 256
+
+
+def tile_list_buffer_pool_prefetch_kernel(
+    tc, tab_words, tab_scales, offs, w4_words, w4_scales, wgs, offs2, offs3, work, wo, out
+):
+    nc = tc.nc
+    with ExitStack() as ctx:
+        held = ctx.enter_context(tc.tile_pool(name="held", bufs=1))
+        heat_pool = ctx.enter_context(tc.tile_pool(name="heat", bufs=8))
+        psum = ctx.enter_context(tc.psum_pool(name="psum", bufs=1))
+
+        list1 = held.tile([P, S // 16], U16, name="list1")
+        list2 = held.tile([P, S // 16], U16, name="list2")
+        list3 = held.tile([P, M // 16], U16, name="list3")
+        nc.sync.dma_start(list1[:], offs)
+        tab_s = held.tile([P, T], U8, name="tab_s", tag="slot_a")
+        nc.sync.dma_start(tab_s[0:32, :].bitcast(I32), tab_scales.bitcast(I32).rearrange("a q t -> (a q) t"))
+        nc.sync.dma_start(list2[:], offs2)
+        nc.sync.dma_start(list3[:], offs3)
+        tab_w = [held.tile([P, T], I32, name="tab_w%d" % a, tag="slot_%s" % "bc"[a]) for a in range(2)]
+        w4_raw = held.tile([P, 1024], I32, name="w4_raw", tag="slot_d")
+        nc.sync.dma_start(tab_w[0][:], tab_words[0].rearrange("p t i -> p (t i)").bitcast(I32))
+        nc.sync.dma_start(
+            w4_raw[:].rearrange("p (a c) -> p a c", a=2),
+            w4_words.bitcast(I32).rearrange("a p c -> p a c"),
+        )
+        nc.sync.dma_start(tab_w[1][:], tab_words[1].rearrange("p t i -> p (t i)").bitcast(I32))
+        nc.vector.memset(tab_s[32:64, :].bitcast(I32), 0)
+        nc.vector.memset(tab_s[64:128, :].bitcast(I32), 0)
+
+        w4s_raw = held.tile([P, 512], I32, name="w4s_raw", tag="slot_e")
+        nc.gpsimd.memset(w4s_raw[:], 0)
+        for quad in range(4):
+            nc.gpsimd.dma_start(
+                w4s_raw[32 * quad : 32 * quad + 4, :].rearrange("p (a c) -> p a c", a=2),
+                w4_scales[:, 4 * quad : 4 * quad + 4, :].bitcast(I32).rearrange("a r c -> r a c"),
+            )
+
+        v_s = held.tile([P, 2 * S], U8, name="v_s", align_bytes=64)
+        nc.vector.memset(v_s[:].bitcast(I32), 0)
+        page = held.tile([P, T2], F32, name="page")
+        nc.vector.memset(page[:], 0.0)
+
+        picked_s = held.tile([P, S], U8, name="picked_s", tag="slot_f")
+        nc.vector.tensor_copy(picked_s[:], tab_s[:].indirect(list1[:]))
+        for group in range(8):
+            a, quad = divmod(group, 4)
+            queue = nc.scalar if group < 6 else nc.gpsimd
+            queue.dma_start(
+                v_s[32 * quad : 32 * quad + 4, S * a : S * a + S].bitcast(I32),
+                picked_s[4 * group : 4 * group + 4, :].bitcast(I32),
+            )
+
+        wgs_rows = wgs.rearrange("(q t e) j -> t q e j", t=4, e=4)
+
+        def load_weight(tile, t):
+            for quad in (0, 2, 1, 3):
+                nc.sync.dma_start(tile[32 * quad : 32 * quad + 32, :], wgs_rows[t])
+
+        weight0 = held.tile([P, S], F32, name="weight0", tag="slot_a")
+        load_weight(weight0, 0)
+
+        v_w = [held.tile([P, S], U32, name="v_w%d" % a, align_bytes=64) for a in range(2)]
+        nc.vector.tensor_copy(v_w[0][:], tab_w[0][:].bitcast(U32).indirect(list1[:]))
+
+        w4_w = held.tile([P, 4096], U8, name="w4_w", align_bytes=64)
+        w4_s = held.tile([P, 2048], U8, name="w4_s", align_bytes=64)
+        nc.vector.tensor_copy(
+            w4_s[:].bitcast(I32).rearrange("p (s t q) -> p s t q", s=4, t=4),
+            w4s_raw[:].rearrange("p (s q t) -> p s t q", s=4, t=4),
+        )
+        nc.vector.tensor_copy(
+            w4_w[:].bitcast(I32).rearrange("p (s t q e) -> p s t q e", s=4, t=4, e=2),
+            w4_raw[:].rearrange("p (s q t e) -> p s t q e", s=4, t=4, e=2),
+        )
+
+        first_cuts = [(0, 256), (256, 512), (512, 1024)]
+        halves = [(0, 512), (512, 1024)]
+        quarters = [(lo, lo + CHUNK) for lo in range(0, M, CHUNK)]
+        for lo, hi in first_cuts:
+            nc.vector.tensor_copy(
+                v_w[1][:, lo:hi], tab_w[1][:].bitcast(U32).indirect(list1[:, lo // 16 : hi // 16])
+            )
+
+        weight_rest = held.tile([P, 3, S], F32, name="weight_rest", tag="slot_d")
+        weight = [weight0[:]] + [weight_rest[:, t, :] for t in range(3)]
+        for t in range(1, 4):
+            load_weight(weight[t], t)
+
+        work_pairs = {}
+
+        def load_work(pair, slot):
+            work_pairs[pair] = held.tile([P, 2, M], F32, name="work%d" % pair, tag=slot)
+            for i in (2 * pair, 2 * pair + 1):
+                b, t = divmod(i, 4)
+                rows = work[512 * b : 512 * b + 512, :].rearrange("(q t e) m -> t q e m", t=4, e=4)
+                nc.sync.dma_start(work_pairs[pair][:, i % 2, :], rows[t])
+
+        load_work(0, "slot_b")
+        load_work(1, "slot_c")
+        wo_raw = [held.tile([P, 4, N], F32, name="wo_raw%d" % b, tag="slot_%s" % "ef"[b]) for b in range(2)]
+        for b in range(2):
+            rows = wo[512 * b : 512 * b + 512, :].rearrange("(q t e) n -> t q e n", t=4, e=4)
+            for t in range(4):
+                nc.sync.dma_start(wo_raw[b][:, t, :], rows[t])
+
+        banks_used = []
+
+        def next_bank(shape):
+            tag = "bank%d" % (len(banks_used) % 8)
+            bank = psum.tile(shape, F32, name=tag, tag=tag)
+            banks_used.append(bank)
+            return bank
+
+        heat = {}
+
+        def make_heat(i):
+            heat[i] = heat_pool.tile([P, S], F32, name="heat")
+            cuts = first_cuts if i == 0 else halves
+            for lo, hi in cuts:
+                bank = next_bank([P, hi - lo])
+                width = 512 if hi - lo == 512 else 128
+                for c in range(lo, hi, width):
+                    for a in range(2):
+                        col = 1024 * a + 128 * i
+                        nc.tensor.matmul_mx(
+                            out=bank[:, c - lo : c - lo + width],
+                            lhsT=w4_w[:, 2 * col : 2 * col + 256].bitcast(E2M1),
+                            lhsT_scale=w4_s[:, col : col + 128],
+                            rhs=v_w[a][:, c : c + width].bitcast(E4M3),
+                            rhs_scale=v_s[:, S * a + c : S * a + c + width],
+                            start=(a == 0),
+                            stop=(a == 1),
+                        )
+                nc.scalar.activation(heat[i][:, lo:hi], bank[:], ACT.Square, bias=1.0)
+                if i == 0:
+                    nc.scalar.activation(heat[i][:, lo:hi], heat[i][:, lo:hi], ACT.Identity, bias=-0.5, scale=0.5)
+                    nc.gpsimd.tensor_tensor(heat[i][:, lo:hi], heat[i][:, lo:hi], weight[i % 4][:, lo:hi], ALU.mult)
+            if i > 0:
+                nc.scalar.activation(heat[i][:], heat[i][:], ACT.Identity, bias=-0.5, scale=0.5)
+                for lo, hi in halves:
+                    nc.gpsimd.tensor_tensor(heat[i][:, lo:hi], heat[i][:, lo:hi], weight[i % 4][:, lo:hi], ALU.mult)
+
+        def put(i):
+            cuts = first_cuts if i == 0 else [(0, S)]
+            for lo, hi in cuts:
+                nc.vector.tensor_copy(page[:].indirect(list2[:, lo // 16 : hi // 16]), heat[i][:, lo:hi])
+
+        turns = held.tile([P, M], F32, name="turns")
+        whole = held.tile([P, M], U32, name="whole")
+
+        def to_turns(x, cols):
+            nc.scalar.activation(turns[:, cols], x, ACT.Relu, bias=CAP / TURN, scale=-1.0 / TURN)
+
+        def reduce_turns(cols, engine):
+            nc.scalar.activation(whole[:, cols], turns[:, cols], ACT.Copy, bias=PHASE / TURN)
+            nc.scalar.activation(whole[:, cols].bitcast(F32), whole[:, cols], ACT.Copy)
+            engine.tensor_tensor(turns[:, cols], turns[:, cols], whole[:, cols].bitcast(F32), ALU.subtract)
+
+        def cosine(cos_out, cols):
+            nc.scalar.activation(cos_out, turns[:, cols], ACT.Sin, bias=PHASE, scale=TURN)
+
+        z_pairs = [held.tile([P, 2, M, 2], BF16, name="z_pairs%d" % b) for b in range(2)]
+        z = [held.tile([P, M, 4], BF16, name="z%d" % b, tag="z%d" % b, align_bytes=64) for b in range(2)]
+        z_w = [held.tile([P, M], U32, name="z_w%d" % b, align_bytes=64) for b in range(2)]
+        z_s = [held.tile([P, M], U8, name="z_s%d" % b, align_bytes=64) for b in range(2)]
+
+        def modulate(i, cos, lo, hi, engine):
+            b, t = divmod(i, 4)
+            engine.tensor_tensor(
+                z_pairs[b][:, t // 2, lo:hi, t % 2], cos[:, lo:hi], work_pairs[i // 2][:, i % 2, lo:hi], ALU.mult
+            )
+
+        def weave(b, lo, hi, word, copy):
+            copy(
+                z[b][:, lo:hi, :].rearrange("p m t -> p (m t)").bitcast(word).rearrange("p (m h) -> p m h", h=2),
+                z_pairs[b][:].rearrange("p h m t -> p h (m t)").bitcast(word)[:, :, lo:hi].rearrange("p h m -> p m h"),
+            )
+
+        def quantise_z(b, lo, hi):
+            nc.vector.quantize_mx(
+                out=z_w[b][:, lo:hi].bitcast(E4M3),
+                scales=z_s[b][:, lo:hi],
+                in_=z[b][:, lo:hi, :].rearrange("p m t -> p (m t)"),
+            )
+
+        wo_bf = held.tile([P, 2, N, 4], BF16, name="wo_bf", tag="wo_bf", align_bytes=64)
+        wo_w = held.tile([P, 2 * N], U32, name="wo_w", align_bytes=64)
+        wo_s = held.tile([P, 2 * N], U8, name="wo_s", align_bytes=64)
+
+        def quantise_wo():
+            for b in range(2):
+                for lo in range(0, N, 256):
+                    nc.scalar.copy(
+                        wo_bf[:, b, lo : lo + 256, :], wo_raw[b][:, :, lo : lo + 256].rearrange("p t n -> p n t")
+                    )
+            nc.vector.quantize_mx(
+                out=wo_w[:].bitcast(E4M3), scales=wo_s[:], in_=wo_bf[:].rearrange("p b n t -> p (b n t)")
+            )
+
+        def score(bank, b, n0, lo):
+            for s in range(2):
+                col = N * b + P * (n0 + s)
+                nc.tensor.matmul_mx(
+                    out=bank[:, s, :],
+                    lhsT=wo_w[:, col : col + P].bitcast(E4M3),
+                    lhsT_scale=wo_s[:, col : col + P],
+                    rhs=z_w[b][:, lo : lo + CHUNK].bitcast(E4M3),
+                    rhs_scale=z_s[b][:, lo : lo + CHUNK],
+                    start=(b == 0 and s == 0),
+                    stop=(b == 1 and s == 1),
+                )
+
+        AHEAD = 4
+        for i in range(AHEAD):
+            make_heat(i)
+        for i in range(TILES - 1):
+            put(i)
+            if i == TILES - 2:
+                x = held.tile([P, M], F32, name="x6", tag="z0", align_bytes=64)
+            elif i == TILES - 3:
+                x = held.tile([P, M], F32, name="x5", tag="wo_bf", align_bytes=64)
+            else:
+                x = heat[i]
+            nc.vector.tensor_copy(x[:], page[:].indirect(list3[:]))
+            to_turns(x[:], slice(0, M))
+            for lo, hi in halves:
+                reduce_turns(slice(lo, hi), nc.gpsimd)
+            for lo, hi in halves:
+                cosine(x[:, lo:hi], slice(lo, hi))
+            for lo, hi in halves:
+                modulate(i, x, lo, hi, nc.gpsimd)
+            if i + AHEAD < TILES:
+                make_heat(i + AHEAD)
+            if i == 0:
+                quantise_wo()
+                load_work(2, "slot_e")
+                load_work(3, "slot_f")
+            if i == 3:
+                weave(0, 0, M, U32, nc.scalar.copy)
+                quantise_z(0, 0, M)
+
+        sums = {}
+        for lo, hi in quarters:
+            for n0 in (0, 2):
+                sums[lo, n0] = next_bank([P, 2, CHUNK])
+                score(sums[lo, n0], 0, n0, lo)
+
+        cos = x
+        i = TILES - 1
+        put(i)
+        x = heat[i]
+        for lo, hi in quarters:
+            nc.vector.tensor_copy(x[:, lo:hi], page[:].indirect(list3[:, lo // 16 : hi // 16]))
+        out_rows = out.rearrange("(s p) m -> p s m", p=P)
+        for lo, hi in quarters:
+            spare = 512 + lo % 512
+            cols = slice(spare, spare + CHUNK)
+            to_turns(x[:, lo:hi], cols)
+            reduce_turns(cols, nc.vector)
+            cosine(cos[:, lo:hi], cols)
+            modulate(i, cos, lo, hi, nc.vector)
+            weave(1, lo, hi, I32, nc.vector.tensor_copy)
+            quantise_z(1, lo, hi)
+            for n0 in (0, 2):
+                score(sums[lo, n0], 1, n0, lo)
+                staged = held.tile([P, 2, CHUNK], F32, name="staged%d_%d" % (lo, n0))
+                if n0 == 0:
+                    nc.scalar.copy(staged[:], sums[lo, n0][:])
+                else:
+                    nc.vector.tensor_copy(staged[:], sums[lo, n0][:])
+                nc.sync.dma_start(out_rows[:, n0 : n0 + 2, lo:hi], staged[:])

@@ -40,6 +40,8 @@ def tile_list_buffer_pool_prefetch_kernel(
         nc.sync.dma_start(list1[:], offs)
         tab_s = held.tile([P, T], U8, name="tab_s", tag="slot_a")
         nc.sync.dma_start(tab_s[0:32, :].bitcast(I32), tab_scales.bitcast(I32).rearrange("a q t -> (a q) t"))
+        w4s_raw = held.tile([32, 256], I32, name="w4s_raw")
+        nc.sync.dma_start(w4s_raw[:], w4_scales.bitcast(I32).rearrange("a q c -> (a q) c"))
         nc.sync.dma_start(list2[:], offs2)
         nc.sync.dma_start(list3[:], offs3)
         tab_w = [held.tile([P, T], I32, name="tab_w%d" % a, tag="slot_%s" % "bc"[a]) for a in range(2)]
@@ -50,30 +52,28 @@ def tile_list_buffer_pool_prefetch_kernel(
             w4_words.bitcast(I32).rearrange("a p c -> p a c"),
         )
         nc.sync.dma_start(tab_w[1][:], tab_words[1].rearrange("p t i -> p (t i)").bitcast(I32))
-        nc.vector.memset(tab_s[32:64, :].bitcast(I32), 0)
-        nc.vector.memset(tab_s[64:128, :].bitcast(I32), 0)
+        nc.gpsimd.memset(tab_s[32:64, :].bitcast(I32), 0)
+        nc.gpsimd.memset(tab_s[64:128, :].bitcast(I32), 0)
 
-        w4s_raw = held.tile([P, 512], I32, name="w4s_raw", tag="slot_e")
-        nc.gpsimd.memset(w4s_raw[:], 0)
-        for quad in range(4):
-            nc.gpsimd.dma_start(
-                w4s_raw[32 * quad : 32 * quad + 4, :].rearrange("p (a c) -> p a c", a=2),
-                w4_scales[:, 4 * quad : 4 * quad + 4, :].bitcast(I32).rearrange("a r c -> r a c"),
-            )
-
-        v_s = held.tile([P, 2 * S], U8, name="v_s", align_bytes=64)
-        nc.vector.memset(v_s[:].bitcast(I32), 0)
+        planes = held.tile([P, 4096], U8, name="planes", align_bytes=64)
+        nc.gpsimd.memset(planes[:].bitcast(I32), 0)
         page = held.tile([P, T2], F32, name="page")
-        nc.vector.memset(page[:], 0.0)
+        nc.gpsimd.memset(page[:], 0.0)
 
         picked_s = held.tile([P, S], U8, name="picked_s", tag="slot_f")
         nc.vector.tensor_copy(picked_s[:], tab_s[:].indirect(list1[:]))
+        scale_rows = held.tile([32, 512], I32, name="scale_rows", tag="slot_e")
+        nc.vector.tensor_copy(
+            scale_rows[:, 256:512].rearrange("p (b t q) -> p b t q", b=2, t=4),
+            w4s_raw[:].rearrange("p (b q t) -> p b t q", b=2, t=4),
+        )
+        nc.vector.tensor_copy(scale_rows[:, 0:256], picked_s[0:32, :].bitcast(I32))
         for group in range(8):
             a, quad = divmod(group, 4)
             queue = nc.scalar if group < 6 else nc.gpsimd
             queue.dma_start(
-                v_s[32 * quad : 32 * quad + 4, S * a : S * a + S].bitcast(I32),
-                picked_s[4 * group : 4 * group + 4, :].bitcast(I32),
+                planes[32 * quad : 32 * quad + 4, 2048 * a : 2048 * a + 2048].bitcast(I32),
+                scale_rows[4 * group : 4 * group + 4, :],
             )
 
         wgs_rows = wgs.rearrange("(q t e) j -> t q e j", t=4, e=4)
@@ -89,11 +89,6 @@ def tile_list_buffer_pool_prefetch_kernel(
         nc.vector.tensor_copy(v_w[0][:], tab_w[0][:].bitcast(U32).indirect(list1[:]))
 
         w4_w = held.tile([P, 4096], U8, name="w4_w", align_bytes=64)
-        w4_s = held.tile([P, 2048], U8, name="w4_s", align_bytes=64)
-        nc.vector.tensor_copy(
-            w4_s[:].bitcast(I32).rearrange("p (s t q) -> p s t q", s=4, t=4),
-            w4s_raw[:].rearrange("p (s q t) -> p s t q", s=4, t=4),
-        )
         nc.vector.tensor_copy(
             w4_w[:].bitcast(I32).rearrange("p (s t q e) -> p s t q e", s=4, t=4, e=2),
             w4_raw[:].rearrange("p (s q t e) -> p s t q e", s=4, t=4, e=2),
@@ -151,16 +146,17 @@ def tile_list_buffer_pool_prefetch_kernel(
                         nc.tensor.matmul_mx(
                             out=bank[:, c - lo : c - lo + width],
                             lhsT=w4_w[:, 2 * col : 2 * col + 256].bitcast(E2M1),
-                            lhsT_scale=w4_s[:, col : col + 128],
+                            lhsT_scale=planes[:, 2048 * a + 1024 + 128 * i : 2048 * a + 1024 + 128 * i + 128],
                             rhs=v_w[a][:, c : c + width].bitcast(E4M3),
-                            rhs_scale=v_s[:, S * a + c : S * a + c + width],
+                            rhs_scale=planes[:, 2048 * a + c : 2048 * a + c + width],
                             start=(a == 0),
                             stop=(a == 1),
                         )
                 nc.scalar.activation(heat[i][:, lo:hi], bank[:], ACT.Square, bias=1.0)
                 if i == 0:
                     nc.scalar.activation(heat[i][:, lo:hi], heat[i][:, lo:hi], ACT.Identity, bias=-0.5, scale=0.5)
-                    nc.gpsimd.tensor_tensor(heat[i][:, lo:hi], heat[i][:, lo:hi], weight[i % 4][:, lo:hi], ALU.mult)
+                    engine = nc.vector if lo == 0 else nc.gpsimd
+                    engine.tensor_tensor(heat[i][:, lo:hi], heat[i][:, lo:hi], weight[i % 4][:, lo:hi], ALU.mult)
             if i > 0:
                 nc.scalar.activation(heat[i][:], heat[i][:], ACT.Identity, bias=-0.5, scale=0.5)
                 for lo, hi in halves:
@@ -185,6 +181,7 @@ def tile_list_buffer_pool_prefetch_kernel(
         def cosine(cos_out, cols):
             nc.scalar.activation(cos_out, turns[:, cols], ACT.Sin, bias=PHASE, scale=TURN)
 
+        cos_pair = held.tile([P, 2, M], F32, name="cos_pair")
         z_pairs = [held.tile([P, 2, M, 2], BF16, name="z_pairs%d" % b) for b in range(2)]
         z = [held.tile([P, M, 4], BF16, name="z%d" % b, tag="z%d" % b, align_bytes=64) for b in range(2)]
         z_w = [held.tile([P, M], U32, name="z_w%d" % b, align_bytes=64) for b in range(2)]
@@ -236,28 +233,26 @@ def tile_list_buffer_pool_prefetch_kernel(
                     stop=(b == 1 and s == 1),
                 )
 
-        AHEAD = 4
+        AHEAD = 5
         for i in range(AHEAD):
             make_heat(i)
         for i in range(TILES - 1):
             put(i)
-            if i == TILES - 2:
-                x = held.tile([P, M], F32, name="x6", tag="z0", align_bytes=64)
-            elif i == TILES - 3:
-                x = held.tile([P, M], F32, name="x5", tag="wo_bf", align_bytes=64)
-            else:
-                x = heat[i]
+            x = heat[i]
             nc.vector.tensor_copy(x[:], page[:].indirect(list3[:]))
             to_turns(x[:], slice(0, M))
             for lo, hi in halves:
                 reduce_turns(slice(lo, hi), nc.gpsimd)
-            for lo, hi in halves:
-                cosine(x[:, lo:hi], slice(lo, hi))
-            for lo, hi in halves:
-                modulate(i, x, lo, hi, nc.gpsimd)
+            if i < TILES - 2:
+                for lo, hi in halves:
+                    cosine(x[:, lo:hi], slice(lo, hi))
+                for lo, hi in halves:
+                    modulate(i, x, lo, hi, nc.gpsimd)
+            else:
+                cosine(cos_pair[:, 0, :], slice(0, M))
             if i + AHEAD < TILES:
                 make_heat(i + AHEAD)
-            if i == 0:
+            if i == 1:
                 quantise_wo()
                 load_work(2, "slot_e")
                 load_work(3, "slot_f")
@@ -271,26 +266,31 @@ def tile_list_buffer_pool_prefetch_kernel(
                 sums[lo, n0] = next_bank([P, 2, CHUNK])
                 score(sums[lo, n0], 0, n0, lo)
 
-        cos = x
         i = TILES - 1
         put(i)
-        x = heat[i]
         for lo, hi in quarters:
-            nc.vector.tensor_copy(x[:, lo:hi], page[:].indirect(list3[:, lo // 16 : hi // 16]))
-        out_rows = out.rearrange("(s p) m -> p s m", p=P)
+            nc.vector.tensor_copy(turns[:, lo:hi], page[:].indirect(list3[:, lo // 16 : hi // 16]))
         for lo, hi in quarters:
-            spare = 512 + lo % 512
-            cols = slice(spare, spare + CHUNK)
-            to_turns(x[:, lo:hi], cols)
+            cols = slice(lo, hi)
+            to_turns(turns[:, cols], cols)
             reduce_turns(cols, nc.vector)
-            cosine(cos[:, lo:hi], cols)
-            modulate(i, cos, lo, hi, nc.vector)
+            cosine(cos_pair[:, 1, cols], cols)
+        for lo, hi in quarters:
+            nc.vector.tensor_tensor(
+                z_pairs[1][:, 1, lo:hi, :].rearrange("p (c i) t -> p c t i", i=4),
+                cos_pair[:, :, lo:hi].rearrange("p t (c i) -> p c t i", i=4),
+                work_pairs[3][:, :, lo:hi].rearrange("p t (c i) -> p c t i", i=4),
+                ALU.mult,
+            )
             weave(1, lo, hi, I32, nc.vector.tensor_copy)
             quantise_z(1, lo, hi)
             for n0 in (0, 2):
                 score(sums[lo, n0], 1, n0, lo)
+        out_rows = out.rearrange("(s p) m -> p s m", p=P)
+        for lo, hi in quarters:
+            for n0 in (0, 2):
                 staged = held.tile([P, 2, CHUNK], F32, name="staged%d_%d" % (lo, n0))
-                if n0 == 0:
+                if n0 == 0 or lo < M // 2:
                     nc.scalar.copy(staged[:], sums[lo, n0][:])
                 else:
                     nc.vector.tensor_copy(staged[:], sums[lo, n0][:])

@@ -2,6 +2,7 @@ import math
 from contextlib import ExitStack
 
 import concourse.mybir as mybir
+from concourse.masks import make_identity
 
 K, H, N, T, S, T2, M = 1024, 1024, 512, 2048, 1024, 2048, 1024
 FLOPS = 2 * K * H * S + 2 * H * N * M
@@ -60,6 +61,8 @@ def tile_list_buffer_pool_prefetch_kernel(
         page = held.tile([P, T2], F32, name="page")
         nc.gpsimd.memset(page[:], 0.0)
 
+        ident = held.tile([P, P], F32, name="ident")
+        make_identity(nc, ident[:])
         picked_s = held.tile([P, S], U8, name="picked_s", tag="slot_f")
         nc.vector.tensor_copy(picked_s[:], tab_s[:].indirect(list1[:]))
         scale_rows = held.tile([32, 512], I32, name="scale_rows", tag="slot_e")
@@ -107,17 +110,16 @@ def tile_list_buffer_pool_prefetch_kernel(
         for t in range(1, 4):
             load_weight(weight[t], t)
 
-        work_pairs = {}
-
-        def load_work(pair, slot):
-            work_pairs[pair] = held.tile([P, 2, M], F32, name="work%d" % pair, tag=slot)
-            for i in (2 * pair, 2 * pair + 1):
-                b, t = divmod(i, 4)
+        def load_work(first, count, slot):
+            tile = held.tile([P, count, M], F32, name="work%d" % first, tag=slot)
+            for j in range(count):
+                b, t = divmod(first + j, 4)
                 rows = work[512 * b : 512 * b + 512, :].rearrange("(q t e) m -> t q e m", t=4, e=4)
-                nc.sync.dma_start(work_pairs[pair][:, i % 2, :], rows[t])
+                nc.sync.dma_start(tile[:, j, :], rows[t])
+            return tile
 
-        load_work(0, "slot_b")
-        load_work(1, "slot_c")
+        work_03 = load_work(0, 4, "slot_b")
+        work_45 = load_work(4, 2, "slot_c")
         wo_raw = [held.tile([P, 4, N], F32, name="wo_raw%d" % b, tag="slot_%s" % "ef"[b]) for b in range(2)]
         for b in range(2):
             rows = wo[512 * b : 512 * b + 512, :].rearrange("(q t e) n -> t q e n", t=4, e=4)
@@ -127,7 +129,7 @@ def tile_list_buffer_pool_prefetch_kernel(
         banks_used = []
 
         def next_bank(shape):
-            tag = "bank%d" % (len(banks_used) % 8)
+            tag = "bank%d" % (len(banks_used) % 6)
             bank = psum.tile(shape, F32, name=tag, tag=tag)
             banks_used.append(bank)
             return bank
@@ -155,17 +157,18 @@ def tile_list_buffer_pool_prefetch_kernel(
                 nc.scalar.activation(heat[i][:, lo:hi], bank[:], ACT.Square, bias=1.0)
                 if i == 0:
                     nc.scalar.activation(heat[i][:, lo:hi], heat[i][:, lo:hi], ACT.Identity, bias=-0.5, scale=0.5)
-                    engine = nc.vector if lo == 0 else nc.gpsimd
-                    engine.tensor_tensor(heat[i][:, lo:hi], heat[i][:, lo:hi], weight[i % 4][:, lo:hi], ALU.mult)
             if i > 0:
                 nc.scalar.activation(heat[i][:], heat[i][:], ACT.Identity, bias=-0.5, scale=0.5)
-                for lo, hi in halves:
-                    nc.gpsimd.tensor_tensor(heat[i][:, lo:hi], heat[i][:, lo:hi], weight[i % 4][:, lo:hi], ALU.mult)
 
         def put(i):
             cuts = first_cuts if i == 0 else [(0, S)]
             for lo, hi in cuts:
-                nc.vector.tensor_copy(page[:].indirect(list2[:, lo // 16 : hi // 16]), heat[i][:, lo:hi])
+                nc.vector.tensor_tensor(
+                    page[:].indirect(list2[:, lo // 16 : hi // 16]),
+                    heat[i][:, lo:hi],
+                    weight[i % 4][:, lo:hi],
+                    ALU.mult,
+                )
 
         turns = held.tile([P, M], F32, name="turns")
         whole = held.tile([P, M], U32, name="whole")
@@ -181,22 +184,53 @@ def tile_list_buffer_pool_prefetch_kernel(
         def cosine(cos_out, cols):
             nc.scalar.activation(cos_out, turns[:, cols], ACT.Sin, bias=PHASE, scale=TURN)
 
-        cos_pair = held.tile([P, 2, M], F32, name="cos_pair")
-        z_pairs = [held.tile([P, 2, M, 2], BF16, name="z_pairs%d" % b) for b in range(2)]
-        z = [held.tile([P, M, 4], BF16, name="z%d" % b, tag="z%d" % b, align_bytes=64) for b in range(2)]
+        def cosine_by_transposes(x, cos_out):
+            banks = [psum.tile([P, 512], F32, name="flip%d" % h, tag="flip%d" % h) for h in range(2)]
+            blocks = range(0, 512, P)
+            for h, (lo, hi) in enumerate(halves):
+                for c in blocks:
+                    nc.tensor.transpose(banks[h][:, c : c + P], x[:, lo + c : lo + c + P], ident[:])
+            for h, (lo, hi) in enumerate(halves):
+                to_turns(banks[h][:], slice(lo, hi))
+            angles = [psum.tile([P, 512], F32, name="flip%d" % h, tag="flip%d" % h) for h in range(2)]
+            for h, (lo, hi) in enumerate(halves):
+                for c in blocks:
+                    nc.tensor.matmul(
+                        angles[h][:, c : c + P], turns[:, lo + c : lo + c + P], ident[:],
+                        start=(c == 0), stop=False, is_transpose=True,
+                    )
+            nc.scalar.activation(whole[:], turns[:], ACT.Copy, bias=PHASE / TURN)
+            nc.scalar.activation(whole[:].bitcast(F32), whole[:], ACT.Copy, scale=-1.0)
+            for h, (lo, hi) in enumerate(halves):
+                for c in blocks:
+                    nc.tensor.matmul(
+                        angles[h][:, c : c + P], whole[:, lo + c : lo + c + P].bitcast(F32), ident[:],
+                        start=False, stop=(c == 512 - P), is_transpose=True,
+                    )
+            for h, (lo, hi) in enumerate(halves):
+                nc.scalar.activation(cos_out[:, lo:hi], angles[h][:], ACT.Sin, bias=PHASE, scale=TURN)
+
+        cos_03 = held.tile([P, 4, M], F32, name="cos_03")
+        cos_45 = held.tile([P, 2, M], F32, name="cos_45")
+        cos_67 = held.tile([P, 2, M], F32, name="cos_67")
+        cos_of = [cos_03[:, t, :] for t in range(4)] + [pair[:, t, :] for pair in (cos_45, cos_67) for t in range(2)]
+        z_pairs = held.tile([P, 2, M, 2], BF16, name="z_pairs")
+        z = [held.tile([P, M, 4], BF16, name="z%d" % b, align_bytes=64) for b in range(2)]
         z_w = [held.tile([P, M], U32, name="z_w%d" % b, align_bytes=64) for b in range(2)]
         z_s = [held.tile([P, M], U8, name="z_s%d" % b, align_bytes=64) for b in range(2)]
 
-        def modulate(i, cos, lo, hi, engine):
-            b, t = divmod(i, 4)
-            engine.tensor_tensor(
-                z_pairs[b][:, t // 2, lo:hi, t % 2], cos[:, lo:hi], work_pairs[i // 2][:, i % 2, lo:hi], ALU.mult
+        def modulate(z_out, cos, load):
+            nc.vector.tensor_tensor(
+                z_out.rearrange("p (c i) t -> p c t i", i=4),
+                cos.rearrange("p t (c i) -> p c t i", i=4),
+                load.rearrange("p t (c i) -> p c t i", i=4),
+                ALU.mult,
             )
 
-        def weave(b, lo, hi, word, copy):
-            copy(
-                z[b][:, lo:hi, :].rearrange("p m t -> p (m t)").bitcast(word).rearrange("p (m h) -> p m h", h=2),
-                z_pairs[b][:].rearrange("p h m t -> p h (m t)").bitcast(word)[:, :, lo:hi].rearrange("p h m -> p m h"),
+        def weave(lo, hi):
+            nc.vector.tensor_copy(
+                z[1][:, lo:hi, :].rearrange("p m t -> p (m t)").bitcast(I32).rearrange("p (m h) -> p m h", h=2),
+                z_pairs[:].rearrange("p h m t -> p h (m t)").bitcast(I32)[:, :, lo:hi].rearrange("p h m -> p m h"),
             )
 
         def quantise_z(b, lo, hi):
@@ -233,56 +267,48 @@ def tile_list_buffer_pool_prefetch_kernel(
                     stop=(b == 1 and s == 1),
                 )
 
-        AHEAD = 5
+        fetched = held.tile([P, M], F32, name="fetched")
+        AHEAD = 4
         for i in range(AHEAD):
             make_heat(i)
         for i in range(TILES - 1):
             put(i)
-            x = heat[i]
-            nc.vector.tensor_copy(x[:], page[:].indirect(list3[:]))
-            to_turns(x[:], slice(0, M))
-            for lo, hi in halves:
-                reduce_turns(slice(lo, hi), nc.gpsimd)
-            if i < TILES - 2:
-                for lo, hi in halves:
-                    cosine(x[:, lo:hi], slice(lo, hi))
-                for lo, hi in halves:
-                    modulate(i, x, lo, hi, nc.gpsimd)
-            else:
-                cosine(cos_pair[:, 0, :], slice(0, M))
+            nc.vector.tensor_copy(fetched[:], page[:].indirect(list3[:]))
+            cosine_by_transposes(fetched, cos_of[i])
             if i + AHEAD < TILES:
                 make_heat(i + AHEAD)
             if i == 1:
                 quantise_wo()
-                load_work(2, "slot_e")
-                load_work(3, "slot_f")
+                work_67 = load_work(6, 2, "slot_e")
             if i == 3:
-                weave(0, 0, M, U32, nc.scalar.copy)
+                modulate(z[0][:], cos_03[:], work_03[:])
                 quantise_z(0, 0, M)
+            if i == 5:
+                modulate(z_pairs[:, 0, :, :], cos_45[:], work_45[:])
 
+        tags = ["bank%d" % j for j in range(6)] + ["flip0", "flip1"]
         sums = {}
         for lo, hi in quarters:
             for n0 in (0, 2):
-                sums[lo, n0] = next_bank([P, 2, CHUNK])
+                tag = tags[len(sums)]
+                sums[lo, n0] = psum.tile([P, 2, CHUNK], F32, name=tag, tag=tag)
                 score(sums[lo, n0], 0, n0, lo)
 
         i = TILES - 1
         put(i)
         for lo, hi in quarters:
-            nc.vector.tensor_copy(turns[:, lo:hi], page[:].indirect(list3[:, lo // 16 : hi // 16]))
+            nc.vector.tensor_copy(heat[i][:, lo:hi], page[:].indirect(list3[:, lo // 16 : hi // 16]))
         for lo, hi in quarters:
             cols = slice(lo, hi)
-            to_turns(turns[:, cols], cols)
-            reduce_turns(cols, nc.vector)
-            cosine(cos_pair[:, 1, cols], cols)
+            part, count = whole[:, cols].bitcast(F32), turns[:, cols]
+            nc.scalar.activation(part, heat[i][:, cols], ACT.Relu, bias=CAP / TURN, scale=-1.0 / TURN)
+            nc.scalar.activation(count.bitcast(U32), part, ACT.Copy, bias=PHASE / TURN)
+            nc.scalar.activation(count, count.bitcast(U32), ACT.Copy)
+            nc.vector.tensor_tensor(part, part, count, ALU.subtract)
+            nc.scalar.activation(cos_67[:, 1, cols], part, ACT.Sin, bias=PHASE, scale=TURN)
         for lo, hi in quarters:
-            nc.vector.tensor_tensor(
-                z_pairs[1][:, 1, lo:hi, :].rearrange("p (c i) t -> p c t i", i=4),
-                cos_pair[:, :, lo:hi].rearrange("p t (c i) -> p c t i", i=4),
-                work_pairs[3][:, :, lo:hi].rearrange("p t (c i) -> p c t i", i=4),
-                ALU.mult,
-            )
-            weave(1, lo, hi, I32, nc.vector.tensor_copy)
+            modulate(z_pairs[:, 1, lo:hi, :], cos_67[:, :, lo:hi], work_67[:, :, lo:hi])
+            weave(lo, hi)
             quantise_z(1, lo, hi)
             for n0 in (0, 2):
                 score(sums[lo, n0], 1, n0, lo)

@@ -53,15 +53,13 @@ def tile_list_buffer_pool_prefetch_kernel(
             w4_words.bitcast(I32).rearrange("a p c -> p a c"),
         )
         nc.sync.dma_start(tab_w[1][:], tab_words[1].rearrange("p t i -> p (t i)").bitcast(I32))
-        nc.gpsimd.memset(tab_s[32:64, :].bitcast(I32), 0)
-        nc.gpsimd.memset(tab_s[64:128, :].bitcast(I32), 0)
+        nc.vector.memset(tab_s[32:64, :].bitcast(I32), 0)
+        nc.vector.memset(tab_s[64:128, :].bitcast(I32), 0)
 
         planes = held.tile([P, 4096], U8, name="planes", align_bytes=64)
-        nc.gpsimd.memset(planes[:].bitcast(I32), 0)
-        page = held.tile([P, T2], F32, name="page")
-        nc.gpsimd.memset(page[:], 0.0)
+        nc.vector.memset(planes[:].bitcast(I32), 0)
 
-        ident = held.tile([P, P], F32, name="ident")
+        ident = held.tile([P, P], F32, name="ident", tag="slot_g", align_bytes=64)
         make_identity(nc, ident[:])
         picked_s = held.tile([P, S], U8, name="picked_s", tag="slot_f")
         nc.vector.tensor_copy(picked_s[:], tab_s[:].indirect(list1[:]))
@@ -71,10 +69,10 @@ def tile_list_buffer_pool_prefetch_kernel(
             w4s_raw[:].rearrange("p (b q t) -> p b t q", b=2, t=4),
         )
         nc.vector.tensor_copy(scale_rows[:, 0:256], picked_s[0:32, :].bitcast(I32))
-        for group in range(8):
+        nc.vector.tensor_copy(planes[0:4, 0:2048].bitcast(I32), scale_rows[0:4, :])
+        for group in range(1, 8):
             a, quad = divmod(group, 4)
-            queue = nc.scalar if group < 6 else nc.gpsimd
-            queue.dma_start(
+            nc.scalar.dma_start(
                 planes[32 * quad : 32 * quad + 4, 2048 * a : 2048 * a + 2048].bitcast(I32),
                 scale_rows[4 * group : 4 * group + 4, :],
             )
@@ -105,26 +103,28 @@ def tile_list_buffer_pool_prefetch_kernel(
                 v_w[1][:, lo:hi], tab_w[1][:].bitcast(U32).indirect(list1[:, lo // 16 : hi // 16])
             )
 
+        page = held.tile([P, T2], F32, name="page", tag="slot_c")
+        nc.vector.memset(page[:], 0.0)
+
         weight_rest = held.tile([P, 3, S], F32, name="weight_rest", tag="slot_d")
         weight = [weight0[:]] + [weight_rest[:, t, :] for t in range(3)]
         for t in range(1, 4):
             load_weight(weight[t], t)
 
-        def load_work(first, count, slot):
-            tile = held.tile([P, count, M], F32, name="work%d" % first, tag=slot)
-            for j in range(count):
-                b, t = divmod(first + j, 4)
-                rows = work[512 * b : 512 * b + 512, :].rearrange("(q t e) m -> t q e m", t=4, e=4)
-                nc.sync.dma_start(tile[:, j, :], rows[t])
-            return tile
+        def load_work(i, dest):
+            b, t = divmod(i, 4)
+            rows = work[512 * b : 512 * b + 512, :].rearrange("(q t e) m -> t q e m", t=4, e=4)
+            nc.sync.dma_start(dest, rows[t])
 
-        work_03 = load_work(0, 4, "slot_b")
-        work_45 = load_work(4, 2, "slot_c")
         wo_raw = [held.tile([P, 4, N], F32, name="wo_raw%d" % b, tag="slot_%s" % "ef"[b]) for b in range(2)]
         for b in range(2):
             rows = wo[512 * b : 512 * b + 512, :].rearrange("(q t e) n -> t q e n", t=4, e=4)
             for t in range(4):
                 nc.sync.dma_start(wo_raw[b][:, t, :], rows[t])
+
+        work_67 = held.tile([P, 2, M], F32, name="work_67", tag="slot_b")
+        for j in range(2):
+            load_work(6 + j, work_67[:, j, :])
 
         banks_used = []
 
@@ -160,13 +160,22 @@ def tile_list_buffer_pool_prefetch_kernel(
             if i > 0:
                 nc.scalar.activation(heat[i][:], heat[i][:], ACT.Identity, bias=-0.5, scale=0.5)
 
+        def ring(j):
+            return heat[(0, 2, 1)[j % 3]]
+
+        def weigh(i):
+            engine = nc.vector if i == 2 else nc.gpsimd
+            engine.tensor_tensor(ring(i - 2)[:], heat[i][:], weight[i % 4], ALU.mult)
+
         def put(i):
-            cuts = first_cuts if i == 0 else [(0, S)]
-            for lo, hi in cuts:
+            if i >= 2:
+                nc.vector.tensor_copy(page[:].indirect(list2[:]), ring(i - 2)[:])
+                return
+            for lo, hi in first_cuts if i == 0 else [(0, S)]:
                 nc.vector.tensor_tensor(
                     page[:].indirect(list2[:, lo // 16 : hi // 16]),
                     heat[i][:, lo:hi],
-                    weight[i % 4][:, lo:hi],
+                    weight[i][:, lo:hi],
                     ALU.mult,
                 )
 
@@ -184,12 +193,16 @@ def tile_list_buffer_pool_prefetch_kernel(
         def cosine(cos_out, cols):
             nc.scalar.activation(cos_out, turns[:, cols], ACT.Sin, bias=PHASE, scale=TURN)
 
-        def cosine_by_transposes(x, cos_out):
+        blocks = range(0, 512, P)
+
+        def flip(x):
             banks = [psum.tile([P, 512], F32, name="flip%d" % h, tag="flip%d" % h) for h in range(2)]
-            blocks = range(0, 512, P)
             for h, (lo, hi) in enumerate(halves):
                 for c in blocks:
                     nc.tensor.transpose(banks[h][:, c : c + P], x[:, lo + c : lo + c + P], ident[:])
+            return banks
+
+        def cosine_by_transposes(banks, cos_out):
             for h, (lo, hi) in enumerate(halves):
                 to_turns(banks[h][:], slice(lo, hi))
             angles = [psum.tile([P, 512], F32, name="flip%d" % h, tag="flip%d" % h) for h in range(2)]
@@ -210,49 +223,71 @@ def tile_list_buffer_pool_prefetch_kernel(
             for h, (lo, hi) in enumerate(halves):
                 nc.scalar.activation(cos_out[:, lo:hi], angles[h][:], ACT.Sin, bias=PHASE, scale=TURN)
 
-        cos_03 = held.tile([P, 4, M], F32, name="cos_03")
-        cos_45 = held.tile([P, 2, M], F32, name="cos_45")
+        cos_ring = [held.tile([P, M], F32, name="cos%d" % j) for j in range(2)]
         cos_67 = held.tile([P, 2, M], F32, name="cos_67")
-        cos_of = [cos_03[:, t, :] for t in range(4)] + [pair[:, t, :] for pair in (cos_45, cos_67) for t in range(2)]
-        z_pairs = held.tile([P, 2, M, 2], BF16, name="z_pairs")
+        z_pairs = [held.tile([P, 2, M, 2], BF16, name="z_pairs%d" % b) for b in range(2)]
         z = [held.tile([P, M, 4], BF16, name="z%d" % b, align_bytes=64) for b in range(2)]
         z_w = [held.tile([P, M], U32, name="z_w%d" % b, align_bytes=64) for b in range(2)]
-        z_s = [held.tile([P, M], U8, name="z_s%d" % b, align_bytes=64) for b in range(2)]
+        z1_s = held.tile([P, M], U8, name="z1_s", align_bytes=64)
 
-        def modulate(z_out, cos, load):
-            nc.vector.tensor_tensor(
-                z_out.rearrange("p (c i) t -> p c t i", i=4),
-                cos.rearrange("p t (c i) -> p c t i", i=4),
-                load.rearrange("p t (c i) -> p c t i", i=4),
-                ALU.mult,
+        def modulate(i):
+            b, t = divmod(i, 4)
+            nc.gpsimd.tensor_tensor(z_pairs[b][:, t // 2, :, t % 2], cos_ring[i % 2][:], ring(i - 1)[:], ALU.mult)
+
+        def weave(b, lo, hi, word, copy):
+            copy(
+                z[b][:, lo:hi, :].rearrange("p m t -> p (m t)").bitcast(word).rearrange("p (m h) -> p m h", h=2),
+                z_pairs[b][:].rearrange("p h m t -> p h (m t)").bitcast(word)[:, :, lo:hi].rearrange("p h m -> p m h"),
             )
 
-        def weave(lo, hi):
-            nc.vector.tensor_copy(
-                z[1][:, lo:hi, :].rearrange("p m t -> p (m t)").bitcast(I32).rearrange("p (m h) -> p m h", h=2),
-                z_pairs[:].rearrange("p h m t -> p h (m t)").bitcast(I32)[:, :, lo:hi].rearrange("p h m -> p m h"),
-            )
-
-        def quantise_z(b, lo, hi):
-            nc.vector.quantize_mx(
-                out=z_w[b][:, lo:hi].bitcast(E4M3),
-                scales=z_s[b][:, lo:hi],
-                in_=z[b][:, lo:hi, :].rearrange("p m t -> p (m t)"),
-            )
+        def quantise(codes, scales, values):
+            nc.vector.quantize_mx(out=codes.bitcast(E4M3), scales=scales, in_=values)
 
         wo_bf = held.tile([P, 2, N, 4], BF16, name="wo_bf", tag="wo_bf", align_bytes=64)
         wo_w = held.tile([P, 2 * N], U32, name="wo_w", align_bytes=64)
-        wo_s = held.tile([P, 2 * N], U8, name="wo_s", align_bytes=64)
 
-        def quantise_wo():
-            for b in range(2):
-                for lo in range(0, N, 256):
-                    nc.scalar.copy(
-                        wo_bf[:, b, lo : lo + 256, :], wo_raw[b][:, :, lo : lo + 256].rearrange("p t n -> p n t")
-                    )
-            nc.vector.quantize_mx(
-                out=wo_w[:].bitcast(E4M3), scales=wo_s[:], in_=wo_bf[:].rearrange("p b n t -> p (b n t)")
-            )
+        AHEAD = 5
+        for i in range(AHEAD):
+            make_heat(i)
+        for i in range(TILES - 1):
+            put(i)
+            if i >= 1:
+                load_work(i - 1, ring(i - 2)[:])
+            nc.vector.tensor_copy(ring(i)[:], page[:].indirect(list3[:]))
+            banks = flip(ring(i))
+            if i >= 1:
+                modulate(i - 1)
+            if i + 2 < TILES:
+                weigh(i + 2)
+            cosine_by_transposes(banks, cos_ring[i % 2] if i < TILES - 2 else cos_67[:, 0, :])
+            if i + AHEAD < TILES:
+                make_heat(i + AHEAD)
+            if i == 4:
+                weave(0, 0, M, U32, nc.scalar.copy)
+            if i == 5:
+                for b in range(2):
+                    for lo in range(0, N, 256):
+                        nc.scalar.copy(
+                            wo_bf[:, b, lo : lo + 256, :], wo_raw[b][:, :, lo : lo + 256].rearrange("p t n -> p n t")
+                        )
+
+        i = TILES - 1
+        put(i)
+        x = ring(i)
+        for lo, hi in quarters:
+            nc.vector.tensor_copy(x[:, lo:hi], page[:].indirect(list3[:, lo // 16 : hi // 16]))
+        late_s = held.tile([P, 2 * N + M], U8, name="late_s", tag="slot_g", align_bytes=64)
+        wo_s, z_s = late_s[:, 0 : 2 * N], [late_s[:, 2 * N : 2 * N + M], z1_s[:]]
+        quantise(wo_w[:], wo_s, wo_bf[:].rearrange("p b n t -> p (b n t)"))
+        quantise(z_w[0][:], z_s[0], z[0][:].rearrange("p m t -> p (m t)"))
+        for lo, hi in quarters:
+            cols = slice(lo, hi)
+            part, count = whole[:, cols].bitcast(F32), turns[:, cols]
+            nc.scalar.activation(part, x[:, cols], ACT.Relu, bias=CAP / TURN, scale=-1.0 / TURN)
+            nc.scalar.activation(count.bitcast(U32), part, ACT.Copy, bias=PHASE / TURN)
+            nc.scalar.activation(count, count.bitcast(U32), ACT.Copy)
+            nc.vector.tensor_tensor(part, part, count, ALU.subtract)
+            nc.scalar.activation(cos_67[:, 1, cols], part, ACT.Sin, bias=PHASE, scale=TURN)
 
         def score(bank, b, n0, lo):
             for s in range(2):
@@ -267,25 +302,6 @@ def tile_list_buffer_pool_prefetch_kernel(
                     stop=(b == 1 and s == 1),
                 )
 
-        fetched = held.tile([P, M], F32, name="fetched")
-        AHEAD = 4
-        for i in range(AHEAD):
-            make_heat(i)
-        for i in range(TILES - 1):
-            put(i)
-            nc.vector.tensor_copy(fetched[:], page[:].indirect(list3[:]))
-            cosine_by_transposes(fetched, cos_of[i])
-            if i + AHEAD < TILES:
-                make_heat(i + AHEAD)
-            if i == 1:
-                quantise_wo()
-                work_67 = load_work(6, 2, "slot_e")
-            if i == 3:
-                modulate(z[0][:], cos_03[:], work_03[:])
-                quantise_z(0, 0, M)
-            if i == 5:
-                modulate(z_pairs[:, 0, :, :], cos_45[:], work_45[:])
-
         tags = ["bank%d" % j for j in range(6)] + ["flip0", "flip1"]
         sums = {}
         for lo, hi in quarters:
@@ -293,23 +309,14 @@ def tile_list_buffer_pool_prefetch_kernel(
                 tag = tags[len(sums)]
                 sums[lo, n0] = psum.tile([P, 2, CHUNK], F32, name=tag, tag=tag)
                 score(sums[lo, n0], 0, n0, lo)
-
-        i = TILES - 1
-        put(i)
-        for lo, hi in quarters:
-            nc.vector.tensor_copy(heat[i][:, lo:hi], page[:].indirect(list3[:, lo // 16 : hi // 16]))
-        for lo, hi in quarters:
-            cols = slice(lo, hi)
-            part, count = whole[:, cols].bitcast(F32), turns[:, cols]
-            nc.scalar.activation(part, heat[i][:, cols], ACT.Relu, bias=CAP / TURN, scale=-1.0 / TURN)
-            nc.scalar.activation(count.bitcast(U32), part, ACT.Copy, bias=PHASE / TURN)
-            nc.scalar.activation(count, count.bitcast(U32), ACT.Copy)
-            nc.vector.tensor_tensor(part, part, count, ALU.subtract)
-            nc.scalar.activation(cos_67[:, 1, cols], part, ACT.Sin, bias=PHASE, scale=TURN)
-        for lo, hi in quarters:
-            modulate(z_pairs[:, 1, lo:hi, :], cos_67[:, :, lo:hi], work_67[:, :, lo:hi])
-            weave(lo, hi)
-            quantise_z(1, lo, hi)
+            nc.vector.tensor_tensor(
+                z_pairs[1][:, 1, lo:hi, :].rearrange("p (c i) t -> p c t i", i=4),
+                cos_67[:, :, lo:hi].rearrange("p t (c i) -> p c t i", i=4),
+                work_67[:, :, lo:hi].rearrange("p t (c i) -> p c t i", i=4),
+                ALU.mult,
+            )
+            weave(1, lo, hi, I32, nc.vector.tensor_copy)
+            quantise(z_w[1][:, lo:hi], z_s[1][:, lo:hi], z[1][:, lo:hi, :].rearrange("p m t -> p (m t)"))
             for n0 in (0, 2):
                 score(sums[lo, n0], 1, n0, lo)
         out_rows = out.rearrange("(s p) m -> p s m", p=P)

@@ -20,10 +20,19 @@ ALU = mybir.AluOpType
 
 P = 128
 TILES = H // P
+LAST = TILES - 1
+BANK = 512
 CAP = 2.5
 TURN = 2.0 * math.pi
 PHASE = math.pi / 2 - CAP
+FUSED = 2
+AHEAD = 5
+HEAT_BANKS = 6
 CHUNK = 256
+FIRST_CUTS = [(0, 256), (256, 512), (512, S)]
+HALVES = [(0, BANK), (BANK, 2 * BANK)]
+CHUNKS = [(lo, lo + CHUNK) for lo in range(0, M, CHUNK)]
+BLOCKS = range(0, BANK, P)
 
 
 def tile_list_buffer_pool_prefetch_kernel(
@@ -32,7 +41,7 @@ def tile_list_buffer_pool_prefetch_kernel(
     nc = tc.nc
     with ExitStack() as ctx:
         held = ctx.enter_context(tc.tile_pool(name="held", bufs=1))
-        heat_pool = ctx.enter_context(tc.tile_pool(name="heat", bufs=8))
+        heat_pool = ctx.enter_context(tc.tile_pool(name="heat", bufs=TILES))
         psum = ctx.enter_context(tc.psum_pool(name="psum", bufs=1))
 
         list1 = held.tile([P, S // 16], U16, name="list1")
@@ -40,48 +49,51 @@ def tile_list_buffer_pool_prefetch_kernel(
         list3 = held.tile([P, M // 16], U16, name="list3")
         nc.sync.dma_start(list1[:], offs)
         tab_s = held.tile([P, T], U8, name="tab_s", tag="slot_a")
-        nc.sync.dma_start(tab_s[0:32, :].bitcast(I32), tab_scales.bitcast(I32).rearrange("a q t -> (a q) t"))
-        w4s_raw = held.tile([32, 256], I32, name="w4s_raw")
-        nc.sync.dma_start(w4s_raw[:], w4_scales.bitcast(I32).rearrange("a q c -> (a q) c"))
+        nc.sync.dma_start(tab_s[0:32, :].bitcast(I32), tab_scales.bitcast(I32).rearrange("a g t -> (a g) t"))
+        w4_s_raw = held.tile([32, H // 4], I32, name="w4_s_raw")
+        nc.sync.dma_start(w4_s_raw[:], w4_scales.bitcast(I32).rearrange("a g c -> (a g) c"))
         nc.sync.dma_start(list2[:], offs2)
         nc.sync.dma_start(list3[:], offs3)
         tab_w = [held.tile([P, T], I32, name="tab_w%d" % a, tag="slot_%s" % "bc"[a]) for a in range(2)]
-        w4_raw = held.tile([P, 1024], I32, name="w4_raw", tag="slot_d")
+        w4_w_raw = held.tile([P, H], I32, name="w4_w_raw", tag="slot_d")
         nc.sync.dma_start(tab_w[0][:], tab_words[0].rearrange("p t i -> p (t i)").bitcast(I32))
         nc.sync.dma_start(
-            w4_raw[:].rearrange("p (a c) -> p a c", a=2),
+            w4_w_raw[:].rearrange("p (a c) -> p a c", a=2),
             w4_words.bitcast(I32).rearrange("a p c -> p a c"),
         )
         nc.sync.dma_start(tab_w[1][:], tab_words[1].rearrange("p t i -> p (t i)").bitcast(I32))
         nc.vector.memset(tab_s[32:64, :].bitcast(I32), 0)
         nc.vector.memset(tab_s[64:128, :].bitcast(I32), 0)
 
-        planes = held.tile([P, 4096], U8, name="planes", align_bytes=64)
+        planes = held.tile([P, 2 * (S + H)], U8, name="planes", align_bytes=64)
         nc.vector.memset(planes[:].bitcast(I32), 0)
+        page0 = held.tile([P, T2], F32, name="page0")
+        nc.vector.memset(page0[:], 0.0)
 
         ident = held.tile([P, P], F32, name="ident", tag="slot_g", align_bytes=64)
         make_identity(nc, ident[:])
+
         picked_s = held.tile([P, S], U8, name="picked_s", tag="slot_f")
         nc.vector.tensor_copy(picked_s[:], tab_s[:].indirect(list1[:]))
-        scale_rows = held.tile([32, 512], I32, name="scale_rows", tag="slot_e")
+        scale_rows = held.tile([32, (S + H) // 4], I32, name="scale_rows", tag="slot_e")
         nc.vector.tensor_copy(
-            scale_rows[:, 256:512].rearrange("p (b t q) -> p b t q", b=2, t=4),
-            w4s_raw[:].rearrange("p (b q t) -> p b t q", b=2, t=4),
+            scale_rows[:, S // 4 :].rearrange("p (b t q) -> p b t q", b=2, t=4),
+            w4_s_raw[:].rearrange("p (b q t) -> p b t q", b=2, t=4),
         )
-        nc.vector.tensor_copy(scale_rows[:, 0:256], picked_s[0:32, :].bitcast(I32))
-        nc.vector.tensor_copy(planes[0:4, 0:2048].bitcast(I32), scale_rows[0:4, :])
+        nc.vector.tensor_copy(scale_rows[:, 0 : S // 4], picked_s[0:32, :].bitcast(I32))
+        nc.vector.tensor_copy(planes[0:4, 0 : S + H].bitcast(I32), scale_rows[0:4, :])
         for group in range(1, 8):
             a, quad = divmod(group, 4)
             nc.scalar.dma_start(
-                planes[32 * quad : 32 * quad + 4, 2048 * a : 2048 * a + 2048].bitcast(I32),
+                planes[32 * quad : 32 * quad + 4, (S + H) * a : (S + H) * (a + 1)].bitcast(I32),
                 scale_rows[4 * group : 4 * group + 4, :],
             )
 
         wgs_rows = wgs.rearrange("(q t e) j -> t q e j", t=4, e=4)
 
-        def load_weight(tile, t):
+        def load_weight(dest, t):
             for quad in (0, 2, 1, 3):
-                nc.sync.dma_start(tile[32 * quad : 32 * quad + 32, :], wgs_rows[t])
+                nc.sync.dma_start(dest[32 * quad : 32 * quad + 32, :], wgs_rows[t])
 
         weight0 = held.tile([P, S], F32, name="weight0", tag="slot_a")
         load_weight(weight0, 0)
@@ -89,22 +101,20 @@ def tile_list_buffer_pool_prefetch_kernel(
         v_w = [held.tile([P, S], U32, name="v_w%d" % a, align_bytes=64) for a in range(2)]
         nc.vector.tensor_copy(v_w[0][:], tab_w[0][:].bitcast(U32).indirect(list1[:]))
 
-        w4_w = held.tile([P, 4096], U8, name="w4_w", align_bytes=64)
+        w4_w = held.tile([P, 4 * H], U8, name="w4_w", align_bytes=64)
         nc.vector.tensor_copy(
-            w4_w[:].bitcast(I32).rearrange("p (s t q e) -> p s t q e", s=4, t=4, e=2),
-            w4_raw[:].rearrange("p (s q t e) -> p s t q e", s=4, t=4, e=2),
+            w4_w[:].bitcast(I32).rearrange("p (s t q w) -> p s t q w", s=4, t=4, w=2),
+            w4_w_raw[:].rearrange("p (s q t w) -> p s t q w", s=4, t=4, w=2),
         )
 
-        first_cuts = [(0, 256), (256, 512), (512, 1024)]
-        halves = [(0, 512), (512, 1024)]
-        quarters = [(lo, lo + CHUNK) for lo in range(0, M, CHUNK)]
-        for lo, hi in first_cuts:
+        for lo, hi in FIRST_CUTS:
             nc.vector.tensor_copy(
                 v_w[1][:, lo:hi], tab_w[1][:].bitcast(U32).indirect(list1[:, lo // 16 : hi // 16])
             )
 
-        page = held.tile([P, T2], F32, name="page", tag="slot_c")
-        nc.vector.memset(page[:], 0.0)
+        page1 = held.tile([P, T2], F32, name="page1", tag="slot_c")
+        nc.gpsimd.memset(page1[:], 0.0)
+        pages = [(page0, page1)[(i if i < 3 else i + 1) % 2] for i in range(TILES)]
 
         weight_rest = held.tile([P, 3, S], F32, name="weight_rest", tag="slot_d")
         weight = [weight0[:]] + [weight_rest[:, t, :] for t in range(3)]
@@ -118,39 +128,32 @@ def tile_list_buffer_pool_prefetch_kernel(
 
         wo_raw = [held.tile([P, 4, N], F32, name="wo_raw%d" % b, tag="slot_%s" % "ef"[b]) for b in range(2)]
         for b in range(2):
-            rows = wo[512 * b : 512 * b + 512, :].rearrange("(q t e) n -> t q e n", t=4, e=4)
+            wo_rows = wo[512 * b : 512 * b + 512, :].rearrange("(q t e) n -> t q e n", t=4, e=4)
             for t in range(4):
-                nc.sync.dma_start(wo_raw[b][:, t, :], rows[t])
-
-        work_67 = held.tile([P, 2, M], F32, name="work_67", tag="slot_b")
+                nc.sync.dma_start(wo_raw[b][:, t, :], wo_rows[t])
+        work_last = held.tile([P, 2, M], F32, name="work_last", tag="slot_b")
         for j in range(2):
-            load_work(6 + j, work_67[:, j, :])
-
-        banks_used = []
-
-        def next_bank(shape):
-            tag = "bank%d" % (len(banks_used) % 6)
-            bank = psum.tile(shape, F32, name=tag, tag=tag)
-            banks_used.append(bank)
-            return bank
+            load_work(LAST - 1 + j, work_last[:, j, :])
 
         heat = {}
+        heat_banks = []
 
         def make_heat(i):
             heat[i] = heat_pool.tile([P, S], F32, name="heat")
-            cuts = first_cuts if i == 0 else halves
-            for lo, hi in cuts:
-                bank = next_bank([P, hi - lo])
-                width = 512 if hi - lo == 512 else 128
+            for lo, hi in FIRST_CUTS if i == 0 else HALVES:
+                tag = "bank%d" % (len(heat_banks) % HEAT_BANKS)
+                bank = psum.tile([P, hi - lo], F32, name=tag, tag=tag)
+                heat_banks.append(bank)
+                width = BANK if hi - lo == BANK else P
                 for c in range(lo, hi, width):
                     for a in range(2):
-                        col = 1024 * a + 128 * i
+                        col, plane = H * a + P * i, (S + H) * a
                         nc.tensor.matmul_mx(
                             out=bank[:, c - lo : c - lo + width],
-                            lhsT=w4_w[:, 2 * col : 2 * col + 256].bitcast(E2M1),
-                            lhsT_scale=planes[:, 2048 * a + 1024 + 128 * i : 2048 * a + 1024 + 128 * i + 128],
+                            lhsT=w4_w[:, 2 * col : 2 * (col + P)].bitcast(E2M1),
+                            lhsT_scale=planes[:, plane + S + P * i : plane + S + P * (i + 1)],
                             rhs=v_w[a][:, c : c + width].bitcast(E4M3),
-                            rhs_scale=planes[:, 2048 * a + c : 2048 * a + c + width],
+                            rhs_scale=planes[:, plane + c : plane + c + width],
                             start=(a == 0),
                             stop=(a == 1),
                         )
@@ -164,16 +167,16 @@ def tile_list_buffer_pool_prefetch_kernel(
             return heat[(0, 2, 1)[j % 3]]
 
         def weigh(i):
-            engine = nc.vector if i == 2 else nc.gpsimd
+            engine = nc.vector if i == FUSED else nc.gpsimd
             engine.tensor_tensor(ring(i - 2)[:], heat[i][:], weight[i % 4], ALU.mult)
 
         def put(i):
-            if i >= 2:
-                nc.vector.tensor_copy(page[:].indirect(list2[:]), ring(i - 2)[:])
+            if i >= FUSED:
+                nc.vector.tensor_copy(pages[i][:].indirect(list2[:]), ring(i - 2)[:])
                 return
-            for lo, hi in first_cuts if i == 0 else [(0, S)]:
+            for lo, hi in FIRST_CUTS if i == 0 else [(0, S)]:
                 nc.vector.tensor_tensor(
-                    page[:].indirect(list2[:, lo // 16 : hi // 16]),
+                    pages[i][:].indirect(list2[:, lo // 16 : hi // 16]),
                     heat[i][:, lo:hi],
                     weight[i][:, lo:hi],
                     ALU.mult,
@@ -182,49 +185,39 @@ def tile_list_buffer_pool_prefetch_kernel(
         turns = held.tile([P, M], F32, name="turns")
         whole = held.tile([P, M], U32, name="whole")
 
-        def to_turns(x, cols):
-            nc.scalar.activation(turns[:, cols], x, ACT.Relu, bias=CAP / TURN, scale=-1.0 / TURN)
-
-        def reduce_turns(cols, engine):
-            nc.scalar.activation(whole[:, cols], turns[:, cols], ACT.Copy, bias=PHASE / TURN)
-            nc.scalar.activation(whole[:, cols].bitcast(F32), whole[:, cols], ACT.Copy)
-            engine.tensor_tensor(turns[:, cols], turns[:, cols], whole[:, cols].bitcast(F32), ALU.subtract)
-
-        def cosine(cos_out, cols):
-            nc.scalar.activation(cos_out, turns[:, cols], ACT.Sin, bias=PHASE, scale=TURN)
-
-        blocks = range(0, 512, P)
+        def flip_banks():
+            return [psum.tile([P, BANK], F32, name="flip%d" % half, tag="flip%d" % half) for half in range(2)]
 
         def flip(x):
-            banks = [psum.tile([P, 512], F32, name="flip%d" % h, tag="flip%d" % h) for h in range(2)]
-            for h, (lo, hi) in enumerate(halves):
-                for c in blocks:
-                    nc.tensor.transpose(banks[h][:, c : c + P], x[:, lo + c : lo + c + P], ident[:])
-            return banks
+            flipped = flip_banks()
+            for half, (lo, hi) in enumerate(HALVES):
+                for c in BLOCKS:
+                    nc.tensor.transpose(flipped[half][:, c : c + P], x[:, lo + c : lo + c + P], ident[:])
+            return flipped
 
-        def cosine_by_transposes(banks, cos_out):
-            for h, (lo, hi) in enumerate(halves):
-                to_turns(banks[h][:], slice(lo, hi))
-            angles = [psum.tile([P, 512], F32, name="flip%d" % h, tag="flip%d" % h) for h in range(2)]
-            for h, (lo, hi) in enumerate(halves):
-                for c in blocks:
+        def cosine(flipped, cos_out):
+            for half, (lo, hi) in enumerate(HALVES):
+                nc.scalar.activation(turns[:, lo:hi], flipped[half][:], ACT.Relu, bias=CAP / TURN, scale=-1.0 / TURN)
+            rest = flip_banks()
+            for half, (lo, hi) in enumerate(HALVES):
+                for c in BLOCKS:
                     nc.tensor.matmul(
-                        angles[h][:, c : c + P], turns[:, lo + c : lo + c + P], ident[:],
+                        rest[half][:, c : c + P], turns[:, lo + c : lo + c + P], ident[:],
                         start=(c == 0), stop=False, is_transpose=True,
                     )
             nc.scalar.activation(whole[:], turns[:], ACT.Copy, bias=PHASE / TURN)
             nc.scalar.activation(whole[:].bitcast(F32), whole[:], ACT.Copy, scale=-1.0)
-            for h, (lo, hi) in enumerate(halves):
-                for c in blocks:
+            for half, (lo, hi) in enumerate(HALVES):
+                for c in BLOCKS:
                     nc.tensor.matmul(
-                        angles[h][:, c : c + P], whole[:, lo + c : lo + c + P].bitcast(F32), ident[:],
-                        start=False, stop=(c == 512 - P), is_transpose=True,
+                        rest[half][:, c : c + P], whole[:, lo + c : lo + c + P].bitcast(F32), ident[:],
+                        start=False, stop=(c == BANK - P), is_transpose=True,
                     )
-            for h, (lo, hi) in enumerate(halves):
-                nc.scalar.activation(cos_out[:, lo:hi], angles[h][:], ACT.Sin, bias=PHASE, scale=TURN)
+            for half, (lo, hi) in enumerate(HALVES):
+                nc.scalar.activation(cos_out[:, lo:hi], rest[half][:], ACT.Sin, bias=PHASE, scale=TURN)
 
-        cos_ring = [held.tile([P, M], F32, name="cos%d" % j) for j in range(2)]
-        cos_67 = held.tile([P, 2, M], F32, name="cos_67")
+        cos_early = [held.tile([P, M], F32, name="cos%d" % j) for j in range(2)]
+        cos_last = held.tile([P, 2, M], F32, name="cos_last")
         z_pairs = [held.tile([P, 2, M, 2], BF16, name="z_pairs%d" % b) for b in range(2)]
         z = [held.tile([P, M, 4], BF16, name="z%d" % b, align_bytes=64) for b in range(2)]
         z_w = [held.tile([P, M], U32, name="z_w%d" % b, align_bytes=64) for b in range(2)]
@@ -232,99 +225,99 @@ def tile_list_buffer_pool_prefetch_kernel(
 
         def modulate(i):
             b, t = divmod(i, 4)
-            nc.gpsimd.tensor_tensor(z_pairs[b][:, t // 2, :, t % 2], cos_ring[i % 2][:], ring(i - 1)[:], ALU.mult)
+            nc.gpsimd.tensor_tensor(z_pairs[b][:, t // 2, :, t % 2], cos_early[i % 2][:], ring(i - 1)[:], ALU.mult)
 
         def weave(b, lo, hi, word, copy):
             copy(
-                z[b][:, lo:hi, :].rearrange("p m t -> p (m t)").bitcast(word).rearrange("p (m h) -> p m h", h=2),
-                z_pairs[b][:].rearrange("p h m t -> p h (m t)").bitcast(word)[:, :, lo:hi].rearrange("p h m -> p m h"),
+                z[b][:, lo:hi, :].rearrange("p m t -> p (m t)").bitcast(word).rearrange("p (m w) -> p m w", w=2),
+                z_pairs[b][:].rearrange("p w m t -> p w (m t)").bitcast(word)[:, :, lo:hi].rearrange("p w m -> p m w"),
             )
 
         def quantise(codes, scales, values):
             nc.vector.quantize_mx(out=codes.bitcast(E4M3), scales=scales, in_=values)
 
-        wo_bf = held.tile([P, 2, N, 4], BF16, name="wo_bf", tag="wo_bf", align_bytes=64)
+        wo_bf = held.tile([P, 2, N, 4], BF16, name="wo_bf", align_bytes=64)
         wo_w = held.tile([P, 2 * N], U32, name="wo_w", align_bytes=64)
 
-        AHEAD = 5
         for i in range(AHEAD):
             make_heat(i)
-        for i in range(TILES - 1):
+        for i in range(LAST):
             put(i)
             if i >= 1:
                 load_work(i - 1, ring(i - 2)[:])
-            nc.vector.tensor_copy(ring(i)[:], page[:].indirect(list3[:]))
-            banks = flip(ring(i))
+            nc.vector.tensor_copy(ring(i)[:], pages[i][:].indirect(list3[:]))
+            flipped = flip(ring(i))
             if i >= 1:
                 modulate(i - 1)
             if i + 2 < TILES:
                 weigh(i + 2)
-            cosine_by_transposes(banks, cos_ring[i % 2] if i < TILES - 2 else cos_67[:, 0, :])
+            cosine(flipped, cos_early[i % 2] if i < LAST - 1 else cos_last[:, 0, :])
             if i + AHEAD < TILES:
                 make_heat(i + AHEAD)
-            if i == 4:
+            if i - 1 == 3:
                 weave(0, 0, M, U32, nc.scalar.copy)
-            if i == 5:
+            if i == LAST - 2:
                 for b in range(2):
-                    for lo in range(0, N, 256):
+                    for n_lo in range(0, N, N // 2):
                         nc.scalar.copy(
-                            wo_bf[:, b, lo : lo + 256, :], wo_raw[b][:, :, lo : lo + 256].rearrange("p t n -> p n t")
+                            wo_bf[:, b, n_lo : n_lo + N // 2, :],
+                            wo_raw[b][:, :, n_lo : n_lo + N // 2].rearrange("p t n -> p n t"),
                         )
 
-        i = TILES - 1
+        i = LAST
         put(i)
-        x = ring(i)
-        for lo, hi in quarters:
-            nc.vector.tensor_copy(x[:, lo:hi], page[:].indirect(list3[:, lo // 16 : hi // 16]))
+        x_last = ring(i)
+        for lo, hi in CHUNKS:
+            nc.vector.tensor_copy(x_last[:, lo:hi], pages[i][:].indirect(list3[:, lo // 16 : hi // 16]))
         late_s = held.tile([P, 2 * N + M], U8, name="late_s", tag="slot_g", align_bytes=64)
         wo_s, z_s = late_s[:, 0 : 2 * N], [late_s[:, 2 * N : 2 * N + M], z1_s[:]]
         quantise(wo_w[:], wo_s, wo_bf[:].rearrange("p b n t -> p (b n t)"))
         quantise(z_w[0][:], z_s[0], z[0][:].rearrange("p m t -> p (m t)"))
-        for lo, hi in quarters:
-            cols = slice(lo, hi)
-            part, count = whole[:, cols].bitcast(F32), turns[:, cols]
-            nc.scalar.activation(part, x[:, cols], ACT.Relu, bias=CAP / TURN, scale=-1.0 / TURN)
-            nc.scalar.activation(count.bitcast(U32), part, ACT.Copy, bias=PHASE / TURN)
-            nc.scalar.activation(count, count.bitcast(U32), ACT.Copy)
-            nc.vector.tensor_tensor(part, part, count, ALU.subtract)
-            nc.scalar.activation(cos_67[:, 1, cols], part, ACT.Sin, bias=PHASE, scale=TURN)
+        for lo, hi in CHUNKS:
+            u, n_turns = whole[:, lo:hi].bitcast(F32), turns[:, lo:hi]
+            nc.scalar.activation(u, x_last[:, lo:hi], ACT.Relu, bias=CAP / TURN, scale=-1.0 / TURN)
+            nc.scalar.activation(n_turns.bitcast(U32), u, ACT.Copy, bias=PHASE / TURN)
+            nc.scalar.activation(n_turns, n_turns.bitcast(U32), ACT.Copy)
+            nc.vector.tensor_tensor(u, u, n_turns, ALU.subtract)
+            nc.scalar.activation(cos_last[:, 1, lo:hi], u, ACT.Sin, bias=PHASE, scale=TURN)
 
-        def score(bank, b, n0, lo):
-            for s in range(2):
-                col = N * b + P * (n0 + s)
+        def score(bank, b, n_tile, lo):
+            for side in range(2):
+                col = N * b + P * (n_tile + side)
                 nc.tensor.matmul_mx(
-                    out=bank[:, s, :],
+                    out=bank[:, side, :],
                     lhsT=wo_w[:, col : col + P].bitcast(E4M3),
                     lhsT_scale=wo_s[:, col : col + P],
                     rhs=z_w[b][:, lo : lo + CHUNK].bitcast(E4M3),
                     rhs_scale=z_s[b][:, lo : lo + CHUNK],
-                    start=(b == 0 and s == 0),
-                    stop=(b == 1 and s == 1),
+                    start=(b == 0 and side == 0),
+                    stop=(b == 1 and side == 1),
                 )
 
-        tags = ["bank%d" % j for j in range(6)] + ["flip0", "flip1"]
+        score_tags = ["bank%d" % j for j in range(HEAT_BANKS)] + ["flip0", "flip1"]
         sums = {}
-        for lo, hi in quarters:
-            for n0 in (0, 2):
-                tag = tags[len(sums)]
-                sums[lo, n0] = psum.tile([P, 2, CHUNK], F32, name=tag, tag=tag)
-                score(sums[lo, n0], 0, n0, lo)
+        for lo, hi in CHUNKS:
+            for n_tile in (0, 2):
+                tag = score_tags[len(sums)]
+                sums[lo, n_tile] = psum.tile([P, 2, CHUNK], F32, name=tag, tag=tag)
+                score(sums[lo, n_tile], 0, n_tile, lo)
             nc.vector.tensor_tensor(
-                z_pairs[1][:, 1, lo:hi, :].rearrange("p (c i) t -> p c t i", i=4),
-                cos_67[:, :, lo:hi].rearrange("p t (c i) -> p c t i", i=4),
-                work_67[:, :, lo:hi].rearrange("p t (c i) -> p c t i", i=4),
+                z_pairs[1][:, 1, lo:hi, :].rearrange("p (c f) t -> p c t f", f=4),
+                cos_last[:, :, lo:hi].rearrange("p t (c f) -> p c t f", f=4),
+                work_last[:, :, lo:hi].rearrange("p t (c f) -> p c t f", f=4),
                 ALU.mult,
             )
             weave(1, lo, hi, I32, nc.vector.tensor_copy)
             quantise(z_w[1][:, lo:hi], z_s[1][:, lo:hi], z[1][:, lo:hi, :].rearrange("p m t -> p (m t)"))
-            for n0 in (0, 2):
-                score(sums[lo, n0], 1, n0, lo)
+            for n_tile in (0, 2):
+                score(sums[lo, n_tile], 1, n_tile, lo)
+
         out_rows = out.rearrange("(s p) m -> p s m", p=P)
-        for lo, hi in quarters:
-            for n0 in (0, 2):
-                staged = held.tile([P, 2, CHUNK], F32, name="staged%d_%d" % (lo, n0))
-                if n0 == 0 or lo < M // 2:
-                    nc.scalar.copy(staged[:], sums[lo, n0][:])
+        for lo, hi in CHUNKS:
+            for n_tile in (0, 2):
+                staged = held.tile([P, 2, CHUNK], F32, name="staged%d_%d" % (lo, n_tile))
+                if n_tile == 0 or lo < M // 2:
+                    nc.scalar.copy(staged[:], sums[lo, n_tile][:])
                 else:
-                    nc.vector.tensor_copy(staged[:], sums[lo, n0][:])
-                nc.sync.dma_start(out_rows[:, n0 : n0 + 2, lo:hi], staged[:])
+                    nc.vector.tensor_copy(staged[:], sums[lo, n_tile][:])
+                nc.sync.dma_start(out_rows[:, n_tile : n_tile + 2, lo:hi], staged[:])

@@ -26,13 +26,14 @@ CAP = 2.5
 TURN = 2.0 * math.pi
 PHASE = math.pi / 2 - CAP
 FUSED = 2
-AHEAD = 5
+SKEWED = 4
+KIB = 1024
+DIRECT = 2
 HEAT_BANKS = 6
 CHUNK = 256
 FIRST_CUTS = [(0, 256), (256, 512), (512, S)]
 HALVES = [(0, BANK), (BANK, 2 * BANK)]
 CHUNKS = [(lo, lo + CHUNK) for lo in range(0, M, CHUNK)]
-BLOCKS = range(0, BANK, P)
 
 
 def tile_list_buffer_pool_prefetch_kernel(
@@ -41,21 +42,21 @@ def tile_list_buffer_pool_prefetch_kernel(
     nc = tc.nc
     with ExitStack() as ctx:
         held = ctx.enter_context(tc.tile_pool(name="held", bufs=1))
-        heat_pool = ctx.enter_context(tc.tile_pool(name="heat", bufs=TILES))
+        shared = ctx.enter_context(tc.tile_pool(name="shared", bufs=1))
         psum = ctx.enter_context(tc.psum_pool(name="psum", bufs=1))
 
         list1 = held.tile([P, S // 16], U16, name="list1")
         list2 = held.tile([P, S // 16], U16, name="list2")
         list3 = held.tile([P, M // 16], U16, name="list3")
         nc.sync.dma_start(list1[:], offs)
-        tab_s = held.tile([P, T], U8, name="tab_s", tag="slot_a")
+        tab_s = shared.tile([P, T], U8, name="tab_s", offset=24 * KIB)
         nc.sync.dma_start(tab_s[0:32, :].bitcast(I32), tab_scales.bitcast(I32).rearrange("a g t -> (a g) t"))
         w4_s_raw = held.tile([32, H // 4], I32, name="w4_s_raw")
         nc.sync.dma_start(w4_s_raw[:], w4_scales.bitcast(I32).rearrange("a g c -> (a g) c"))
         nc.sync.dma_start(list2[:], offs2)
         nc.sync.dma_start(list3[:], offs3)
-        tab_w = [held.tile([P, T], I32, name="tab_w%d" % a, tag="slot_%s" % "bc"[a]) for a in range(2)]
-        w4_w_raw = held.tile([P, H], I32, name="w4_w_raw", tag="slot_d")
+        tab_w = [shared.tile([P, T], I32, name="tab_w%d" % a, offset=(64, 12)[a] * KIB) for a in range(2)]
+        w4_w_raw = shared.tile([P, H], I32, name="w4_w_raw", offset=28 * KIB)
         nc.sync.dma_start(tab_w[0][:], tab_words[0].rearrange("p t i -> p (t i)").bitcast(I32))
         nc.sync.dma_start(
             w4_w_raw[:].rearrange("p (a c) -> p a c", a=2),
@@ -65,17 +66,17 @@ def tile_list_buffer_pool_prefetch_kernel(
         nc.vector.memset(tab_s[32:64, :].bitcast(I32), 0)
         nc.vector.memset(tab_s[64:128, :].bitcast(I32), 0)
 
-        planes = held.tile([P, 2 * (S + H)], U8, name="planes", align_bytes=64)
+        planes = shared.tile([P, 2 * (S + H)], U8, name="planes", align_bytes=64, offset=44 * KIB)
         nc.vector.memset(planes[:].bitcast(I32), 0)
         page0 = held.tile([P, T2], F32, name="page0")
         nc.vector.memset(page0[:], 0.0)
 
-        ident = held.tile([P, P], F32, name="ident", tag="slot_g", align_bytes=64)
+        ident = held.tile([P, P], F32, name="ident")
         make_identity(nc, ident[:])
 
-        picked_s = held.tile([P, S], U8, name="picked_s", tag="slot_f")
+        picked_s = held.tile([P, S], U8, name="picked_s")
         nc.vector.tensor_copy(picked_s[:], tab_s[:].indirect(list1[:]))
-        scale_rows = held.tile([32, (S + H) // 4], I32, name="scale_rows", tag="slot_e")
+        scale_rows = shared.tile([32, (S + H) // 4], I32, name="scale_rows", offset=107 * KIB)
         nc.vector.tensor_copy(
             scale_rows[:, S // 4 :].rearrange("p (b t q) -> p b t q", b=2, t=4),
             w4_s_raw[:].rearrange("p (b q t) -> p b t q", b=2, t=4),
@@ -95,13 +96,17 @@ def tile_list_buffer_pool_prefetch_kernel(
             for quad in (0, 2, 1, 3):
                 nc.sync.dma_start(dest[32 * quad : 32 * quad + 32, :], wgs_rows[t])
 
-        weight0 = held.tile([P, S], F32, name="weight0", tag="slot_a")
-        load_weight(weight0, 0)
+        weight = [
+            shared.tile([P, S], F32, name="weight%d" % t, offset=at * KIB) for t, at in enumerate((24, 28, 68, 64))
+        ]
+        load_weight(weight[0], 0)
 
-        v_w = [held.tile([P, S], U32, name="v_w%d" % a, align_bytes=64) for a in range(2)]
+        v_w = [
+            shared.tile([P, S], U32, name="v_w%d" % a, align_bytes=64, offset=(32 + 4 * a) * KIB) for a in range(2)
+        ]
         nc.vector.tensor_copy(v_w[0][:], tab_w[0][:].bitcast(U32).indirect(list1[:]))
 
-        w4_w = held.tile([P, 4 * H], U8, name="w4_w", align_bytes=64)
+        w4_w = shared.tile([P, 4 * H], U8, name="w4_w", align_bytes=64, offset=40 * KIB)
         nc.vector.tensor_copy(
             w4_w[:].bitcast(I32).rearrange("p (s t q w) -> p s t q w", s=4, t=4, w=2),
             w4_w_raw[:].rearrange("p (s q t w) -> p s t q w", s=4, t=4, w=2),
@@ -112,12 +117,10 @@ def tile_list_buffer_pool_prefetch_kernel(
                 v_w[1][:, lo:hi], tab_w[1][:].bitcast(U32).indirect(list1[:, lo // 16 : hi // 16])
             )
 
-        page1 = held.tile([P, T2], F32, name="page1", tag="slot_c")
-        nc.gpsimd.memset(page1[:], 0.0)
-        pages = [(page0, page1)[(i if i < 3 else i + 1) % 2] for i in range(TILES)]
+        pages = [page0] + [shared.tile([P, T2], F32, name="page%d" % j, offset=8 * KIB * j) for j in (1, 2)]
+        for j in (1, 2):
+            nc.gpsimd.memset(pages[j][:], 0.0)
 
-        weight_rest = held.tile([P, 3, S], F32, name="weight_rest", tag="slot_d")
-        weight = [weight0[:]] + [weight_rest[:, t, :] for t in range(3)]
         for t in range(1, 4):
             load_weight(weight[t], t)
 
@@ -126,24 +129,26 @@ def tile_list_buffer_pool_prefetch_kernel(
             rows = work[512 * b : 512 * b + 512, :].rearrange("(q t e) m -> t q e m", t=4, e=4)
             nc.sync.dma_start(dest, rows[t])
 
-        wo_raw = [held.tile([P, 4, N], F32, name="wo_raw%d" % b, tag="slot_%s" % "ef"[b]) for b in range(2)]
-        for b in range(2):
-            wo_rows = wo[512 * b : 512 * b + 512, :].rearrange("(q t e) n -> t q e n", t=4, e=4)
-            for t in range(4):
-                nc.sync.dma_start(wo_raw[b][:, t, :], wo_rows[t])
-        work_last = held.tile([P, 2, M], F32, name="work_last", tag="slot_b")
-        for j in range(2):
-            load_work(LAST - 1 + j, work_last[:, j, :])
+        def bank_tile(j, shape):
+            return psum.tile(shape, F32, name="bank%d" % j, tag="bank%d" % j)
 
-        heat = {}
-        heat_banks = []
-
-        def make_heat(i):
-            heat[i] = heat_pool.tile([P, S], F32, name="heat")
+        mid = shared.tile([P, 2 * S], F32, name="mid", offset=56 * KIB)
+        heat_at = {0: 88, 2: 84, 3: 0}
+        heat = [
+            shared.tile([P, S], F32, name="heat%d" % i, offset=heat_at[i] * KIB)
+            if i in heat_at
+            else mid[:, S // 2 : S // 2 + S]
+            if i == SKEWED + 1
+            else held.tile([P, S], F32, name="heat%d" % i)
+            for i in range(TILES)
+        ]
+        spare = held.tile([P, S], F32, name="spare")
+        banks_used = 0
+        for i in range(TILES):
+            squares = spare if i == FUSED else heat[i]
             for lo, hi in FIRST_CUTS if i == 0 else HALVES:
-                tag = "bank%d" % (len(heat_banks) % HEAT_BANKS)
-                bank = psum.tile([P, hi - lo], F32, name=tag, tag=tag)
-                heat_banks.append(bank)
+                bank = bank_tile(banks_used % HEAT_BANKS, [P, hi - lo])
+                banks_used = banks_used + 1
                 width = BANK if hi - lo == BANK else P
                 for c in range(lo, hi, width):
                     for a in range(2):
@@ -157,22 +162,30 @@ def tile_list_buffer_pool_prefetch_kernel(
                             start=(a == 0),
                             stop=(a == 1),
                         )
-                nc.scalar.activation(heat[i][:, lo:hi], bank[:], ACT.Square, bias=1.0)
+                nc.scalar.activation(squares[:, lo:hi], bank[:], ACT.Square, bias=1.0)
                 if i == 0:
-                    nc.scalar.activation(heat[i][:, lo:hi], heat[i][:, lo:hi], ACT.Identity, bias=-0.5, scale=0.5)
+                    nc.scalar.activation(heat[i][:, lo:hi], squares[:, lo:hi], ACT.Identity, bias=-0.5, scale=0.5)
             if i > 0:
-                nc.scalar.activation(heat[i][:], heat[i][:], ACT.Identity, bias=-0.5, scale=0.5)
+                nc.scalar.activation(heat[i][:], squares[:], ACT.Identity, bias=-0.5, scale=0.5)
 
-        def ring(j):
-            return heat[(0, 2, 1)[j % 3]]
+        wo_raw = [shared.tile([P, 4, N], F32, name="wo_raw%d" % b, offset=(100 + 8 * b) * KIB) for b in range(2)]
+        for b in range(2):
+            wo_rows = wo[512 * b : 512 * b + 512, :].rearrange("(q t e) n -> t q e n", t=4, e=4)
+            for t in range(4):
+                nc.sync.dma_start(wo_raw[b][:, t, :], wo_rows[t])
+
+        pair = [mid[:, S * j : S * (j + 1)] for j in range(2)]
+        fetched = [spare, heat[3], heat[4], pair[0], pair[1], heat[6], heat[7]]
+        cos_early = [heat[1], heat[2], heat[0], heat[3], heat[4], heat[1]]
+        weighed = {2: heat[0], 3: fetched[0], 4: cos_early[0], 5: cos_early[1], 6: fetched[4], 7: fetched[5]}
 
         def weigh(i):
             engine = nc.vector if i == FUSED else nc.gpsimd
-            engine.tensor_tensor(ring(i - 2)[:], heat[i][:], weight[i % 4], ALU.mult)
+            engine.tensor_tensor(weighed[i][:], heat[i][:], weight[i % 4][:], ALU.mult)
 
         def put(i):
             if i >= FUSED:
-                nc.vector.tensor_copy(pages[i][:].indirect(list2[:]), ring(i - 2)[:])
+                nc.vector.tensor_copy(pages[i % 3][:].indirect(list2[:]), weighed[i][:])
                 return
             for lo, hi in FIRST_CUTS if i == 0 else [(0, S)]:
                 nc.vector.tensor_tensor(
@@ -183,49 +196,55 @@ def tile_list_buffer_pool_prefetch_kernel(
                 )
 
         turns = held.tile([P, M], F32, name="turns")
-        whole = held.tile([P, M], U32, name="whole")
+        whole = shared.tile([P, M], U32, name="whole", offset=49 * KIB)
 
-        def flip_banks():
-            return [psum.tile([P, BANK], F32, name="flip%d" % half, tag="flip%d" % half) for half in range(2)]
-
-        def flip(x):
-            flipped = flip_banks()
-            for half, (lo, hi) in enumerate(HALVES):
-                for c in BLOCKS:
-                    nc.tensor.transpose(flipped[half][:, c : c + P], x[:, lo + c : lo + c + P], ident[:])
+        def fetch(i, cuts, skip, first_bank):
+            flipped = []
+            for lo, hi in cuts if i == LAST else [(0, M)]:
+                nc.vector.tensor_copy(fetched[i][:, lo:hi], pages[i % 3][:].indirect(list3[:, lo // 16 : hi // 16]))
+            for j, (lo, hi) in list(enumerate(cuts))[skip:]:
+                bank = bank_tile(first_bank + j, [P, hi - lo])
+                for c in range(lo, hi, P):
+                    nc.tensor.transpose(bank[:, c - lo : c - lo + P], fetched[i][:, c : c + P], ident[:])
+                flipped.append(bank)
             return flipped
 
-        def cosine(flipped, cos_out):
-            for half, (lo, hi) in enumerate(HALVES):
-                nc.scalar.activation(turns[:, lo:hi], flipped[half][:], ACT.Relu, bias=CAP / TURN, scale=-1.0 / TURN)
-            rest = flip_banks()
-            for half, (lo, hi) in enumerate(HALVES):
-                for c in BLOCKS:
+        def cosine(flipped, flip_cuts, cuts, banks, whole, cos_out):
+            start, stop = cuts[0][0], cuts[-1][1]
+            for j, (lo, hi) in enumerate(flip_cuts):
+                nc.scalar.activation(turns[:, lo:hi], flipped[j][:], ACT.Relu, bias=CAP / TURN, scale=-1.0 / TURN)
+            rest = [bank_tile(banks[j], [P, hi - lo]) for j, (lo, hi) in enumerate(cuts)]
+            for j, (lo, hi) in enumerate(cuts):
+                for c in range(lo, hi, P):
                     nc.tensor.matmul(
-                        rest[half][:, c : c + P], turns[:, lo + c : lo + c + P], ident[:],
-                        start=(c == 0), stop=False, is_transpose=True,
+                        rest[j][:, c - lo : c - lo + P], turns[:, c : c + P], ident[:],
+                        start=(c == lo), stop=False, is_transpose=True,
                     )
-            nc.scalar.activation(whole[:], turns[:], ACT.Copy, bias=PHASE / TURN)
-            nc.scalar.activation(whole[:].bitcast(F32), whole[:], ACT.Copy, scale=-1.0)
-            for half, (lo, hi) in enumerate(HALVES):
-                for c in BLOCKS:
+            nc.scalar.activation(whole[:, start:stop], turns[:, start:stop], ACT.Copy, bias=PHASE / TURN)
+            nc.scalar.activation(whole[:, start:stop].bitcast(F32), whole[:, start:stop], ACT.Copy, scale=-1.0)
+            for j, (lo, hi) in enumerate(cuts):
+                for c in range(lo, hi, P):
                     nc.tensor.matmul(
-                        rest[half][:, c : c + P], whole[:, lo + c : lo + c + P].bitcast(F32), ident[:],
-                        start=False, stop=(c == BANK - P), is_transpose=True,
+                        rest[j][:, c - lo : c - lo + P], whole[:, c : c + P].bitcast(F32), ident[:],
+                        start=False, stop=(c == hi - P), is_transpose=True,
                     )
-            for half, (lo, hi) in enumerate(HALVES):
-                nc.scalar.activation(cos_out[:, lo:hi], rest[half][:], ACT.Sin, bias=PHASE, scale=TURN)
+            for j, (lo, hi) in enumerate(cuts):
+                nc.scalar.activation(cos_out[:, lo:hi], rest[j][:], ACT.Sin, bias=PHASE, scale=TURN)
 
-        cos_early = [held.tile([P, M], F32, name="cos%d" % j) for j in range(2)]
         cos_last = held.tile([P, 2, M], F32, name="cos_last")
         z_pairs = [held.tile([P, 2, M, 2], BF16, name="z_pairs%d" % b) for b in range(2)]
-        z = [held.tile([P, M, 4], BF16, name="z%d" % b, align_bytes=64) for b in range(2)]
+        whole5 = shared.tile([P, M], U32, name="whole5", offset=92 * KIB)
+        z = [
+            shared.tile([P, M, 4], BF16, name="z0", align_bytes=64, offset=92 * KIB),
+            held.tile([P, M, 4], BF16, name="z1", align_bytes=64),
+        ]
         z_w = [held.tile([P, M], U32, name="z_w%d" % b, align_bytes=64) for b in range(2)]
         z1_s = held.tile([P, M], U8, name="z1_s", align_bytes=64)
 
-        def modulate(i):
+        def modulate(i, work_tile):
             b, t = divmod(i, 4)
-            nc.gpsimd.tensor_tensor(z_pairs[b][:, t // 2, :, t % 2], cos_early[i % 2][:], ring(i - 1)[:], ALU.mult)
+            load_work(i, work_tile[:])
+            nc.gpsimd.tensor_tensor(z_pairs[b][:, t // 2, :, t % 2], cos_early[i][:], work_tile[:], ALU.mult)
 
         def weave(b, lo, hi, word, copy):
             copy(
@@ -236,70 +255,109 @@ def tile_list_buffer_pool_prefetch_kernel(
         def quantise(codes, scales, values):
             nc.vector.quantize_mx(out=codes.bitcast(E4M3), scales=scales, in_=values)
 
-        wo_bf = held.tile([P, 2, N, 4], BF16, name="wo_bf", align_bytes=64)
+        wo_bf = [
+            shared.tile([P, N, 4], BF16, name="wo_bf%d" % b, align_bytes=64, offset=(72, 4)[b] * KIB)
+            for b in range(2)
+        ]
         wo_w = held.tile([P, 2 * N], U32, name="wo_w", align_bytes=64)
 
-        for i in range(AHEAD):
-            make_heat(i)
-        for i in range(LAST):
-            put(i)
-            if i >= 1:
-                load_work(i - 1, ring(i - 2)[:])
-            nc.vector.tensor_copy(ring(i)[:], pages[i][:].indirect(list3[:]))
-            flipped = flip(ring(i))
-            if i >= 1:
-                modulate(i - 1)
-            if i + 2 < TILES:
-                weigh(i + 2)
-            cosine(flipped, cos_early[i % 2] if i < LAST - 1 else cos_last[:, 0, :])
-            if i + AHEAD < TILES:
-                make_heat(i + AHEAD)
-            if i - 1 == 3:
-                weave(0, 0, M, U32, nc.scalar.copy)
-            if i == LAST - 2:
-                for b in range(2):
-                    for n_lo in range(0, N, N // 2):
-                        nc.scalar.copy(
-                            wo_bf[:, b, n_lo : n_lo + N // 2, :],
-                            wo_raw[b][:, :, n_lo : n_lo + N // 2].rearrange("p t n -> p n t"),
-                        )
+        def round_wo():
+            for b in range(2):
+                for n_lo in range(0, N, N // 2):
+                    nc.scalar.copy(
+                        wo_bf[b][:, n_lo : n_lo + N // 2, :],
+                        wo_raw[b][:, :, n_lo : n_lo + N // 2].rearrange("p t n -> p n t"),
+                    )
 
-        i = LAST
-        put(i)
-        x_last = ring(i)
-        for lo, hi in CHUNKS:
-            nc.vector.tensor_copy(x_last[:, lo:hi], pages[i][:].indirect(list3[:, lo // 16 : hi // 16]))
-        late_s = held.tile([P, 2 * N + M], U8, name="late_s", tag="slot_g", align_bytes=64)
-        wo_s, z_s = late_s[:, 0 : 2 * N], [late_s[:, 2 * N : 2 * N + M], z1_s[:]]
-        quantise(wo_w[:], wo_s, wo_bf[:].rearrange("p b n t -> p (b n t)"))
-        quantise(z_w[0][:], z_s[0], z[0][:].rearrange("p m t -> p (m t)"))
-        for lo, hi in CHUNKS:
-            u, n_turns = whole[:, lo:hi].bitcast(F32), turns[:, lo:hi]
-            nc.scalar.activation(u, x_last[:, lo:hi], ACT.Relu, bias=CAP / TURN, scale=-1.0 / TURN)
-            nc.scalar.activation(n_turns.bitcast(U32), u, ACT.Copy, bias=PHASE / TURN)
-            nc.scalar.activation(n_turns, n_turns.bitcast(U32), ACT.Copy)
-            nc.vector.tensor_tensor(u, u, n_turns, ALU.subtract)
+        def fetch_and_cosine(i):
+            cos_out = cos_early[i] if i < LAST - 1 else cos_last[:, 0, :]
+            first_bank = 1 if i < SKEWED else HEAT_BANKS
+            flipped = fetch(i, HALVES, 0, first_bank)
+            if i == SKEWED - 2:
+                return lambda: cosine(flipped, HALVES, CHUNKS, (1, 2, HEAT_BANKS, HEAT_BANKS + 1), whole, cos_out)
+            if i == LAST - 1:
+                return lambda: cosine(flipped, HALVES, CHUNKS, (0, 4, 1, 5), whole, cos_out)
+            return lambda: cosine(flipped, HALVES, HALVES, (first_bank, first_bank + 1), whole5 if i == 5 else whole, cos_out)
+
+        put(0)
+        put(1)
+        weigh(2)
+        finish = fetch_and_cosine(0)
+        for i in range(2, SKEWED + 1):
+            if i >= 3:
+                modulate(i - 3, weighed[i - 1])
+            weigh(i + 1)
+            finish()
+            if i == 3:
+                round_wo()
+            put(i)
+            finish = fetch_and_cosine(i - 1)
+        wo_s = [shared.tile([P, N], U8, name="wo%d_s" % b, align_bytes=64, offset=(28, 71)[b] * KIB) for b in range(2)]
+
+        def quantise_wo(b):
+            quantise(wo_w[:, N * b : N * (b + 1)], wo_s[b][:], wo_bf[b][:].rearrange("p n t -> p (n t)"))
+
+        finish_early = finish
+        finish = fetch_and_cosine(4)
+        weigh(6)
+        modulate(2, fetched[3])
+        finish_early()
+        finish()
+        put(5)
+        quantise_wo(0)
+        finish = fetch_and_cosine(5)
+        weigh(7)
+        modulate(3, shared.tile([P, M], F32, name="work3", offset=86 * KIB))
+        finish()
+        weave(0, 0, M, U32, nc.scalar.copy)
+        put(6)
+        quantise_wo(1)
+        finish = fetch_and_cosine(6)
+        modulate(4, shared.tile([P, M], F32, name="work4", offset=62 * KIB))
+        modulate(5, shared.tile([P, M], F32, name="work5", offset=66 * KIB + BANK))
+        finish()
+        work_last = shared.tile([P, 2, M], F32, name="work_last", offset=100 * KIB)
+        for j in range(2):
+            load_work(LAST - 1 + j, work_last[:, j, :])
+
+        put(LAST)
+        z0_s = [shared.tile([P, BANK], U8, name="z0_s%d" % j, align_bytes=64, offset=(66, 52)[j] * KIB) for j in range(2)]
+        fetched.append(shared.tile([P, M], F32, name="x_last", offset=48 * KIB))
+
+        def quantise_z0(j):
+            lo, hi = HALVES[j]
+            quantise(z_w[0][:, lo:hi], z0_s[j][:], z[0][:, lo:hi, :].rearrange("p m t -> p (m t)"))
+
+        quantise_z0(0)
+        flipped = fetch(LAST, CHUNKS, DIRECT, 0)
+        whole_last = held.tile([P, M], U32, name="whole_last")
+        for lo, hi in CHUNKS[:DIRECT]:
+            u, count = turns[:, lo:hi], whole_last[:, lo:hi]
+            nc.scalar.activation(u, fetched[LAST][:, lo:hi], ACT.Relu, bias=CAP / TURN, scale=-1.0 / TURN)
+            nc.scalar.activation(count, u, ACT.Copy, bias=PHASE / TURN)
+            nc.vector.tensor_tensor(u, u, count.bitcast(I32), ALU.subtract)
             nc.scalar.activation(cos_last[:, 1, lo:hi], u, ACT.Sin, bias=PHASE, scale=TURN)
+        quantise_z0(1)
+        for j, cut in enumerate(CHUNKS[DIRECT:]):
+            cosine([flipped[j]], [cut], [cut], [len(CHUNKS) + DIRECT + j], whole_last, cos_last[:, 1, :])
 
         def score(bank, b, n_tile, lo):
             for side in range(2):
-                col = N * b + P * (n_tile + side)
+                col = P * (n_tile + side)
                 nc.tensor.matmul_mx(
                     out=bank[:, side, :],
-                    lhsT=wo_w[:, col : col + P].bitcast(E4M3),
-                    lhsT_scale=wo_s[:, col : col + P],
+                    lhsT=wo_w[:, N * b + col : N * b + col + P].bitcast(E4M3),
+                    lhsT_scale=wo_s[b][:, col : col + P],
                     rhs=z_w[b][:, lo : lo + CHUNK].bitcast(E4M3),
-                    rhs_scale=z_s[b][:, lo : lo + CHUNK],
+                    rhs_scale=z0_s[lo // BANK][:, lo % BANK : lo % BANK + CHUNK] if b == 0 else z1_s[:, lo : lo + CHUNK],
                     start=(b == 0 and side == 0),
                     stop=(b == 1 and side == 1),
                 )
 
-        score_tags = ["bank%d" % j for j in range(HEAT_BANKS)] + ["flip0", "flip1"]
         sums = {}
-        for lo, hi in CHUNKS:
+        for j, (lo, hi) in enumerate(CHUNKS):
             for n_tile in (0, 2):
-                tag = score_tags[len(sums)]
-                sums[lo, n_tile] = psum.tile([P, 2, CHUNK], F32, name=tag, tag=tag)
+                sums[lo, n_tile] = bank_tile(j + len(CHUNKS) * (n_tile // 2), [P, 2, CHUNK])
                 score(sums[lo, n_tile], 0, n_tile, lo)
             nc.vector.tensor_tensor(
                 z_pairs[1][:, 1, lo:hi, :].rearrange("p (c f) t -> p c t f", f=4),
@@ -308,7 +366,7 @@ def tile_list_buffer_pool_prefetch_kernel(
                 ALU.mult,
             )
             weave(1, lo, hi, I32, nc.vector.tensor_copy)
-            quantise(z_w[1][:, lo:hi], z_s[1][:, lo:hi], z[1][:, lo:hi, :].rearrange("p m t -> p (m t)"))
+            quantise(z_w[1][:, lo:hi], z1_s[:, lo:hi], z[1][:, lo:hi, :].rearrange("p m t -> p (m t)"))
             for n_tile in (0, 2):
                 score(sums[lo, n_tile], 1, n_tile, lo)
 

@@ -49,62 +49,59 @@ def tile_list_buffer_pool_prefetch_kernel(
         list2 = held.tile([P, S // 16], U16, name="list2")
         list3 = held.tile([P, M // 16], U16, name="list3")
         nc.sync.dma_start(list1[:], offs)
-        tab_s = shared.tile([P, T], U8, name="tab_s", offset=24 * KIB)
-        nc.sync.dma_start(tab_s[0:32, :].bitcast(I32), tab_scales.bitcast(I32).rearrange("a g t -> (a g) t"))
+        tab_s = shared.tile([P, T], U8, name="tab_s", offset=60 * KIB)
+        nc.sync.dma_start(tab_s[0:32, :].bitcast(I32), tab_scales.bitcast(I32).rearrange("a g t -> g a t"))
         w4_s_raw = held.tile([32, H // 4], I32, name="w4_s_raw")
-        nc.sync.dma_start(w4_s_raw[:], w4_scales.bitcast(I32).rearrange("a g c -> (a g) c"))
+        nc.sync.dma_start(w4_s_raw[:], w4_scales.bitcast(I32).rearrange("a g c -> g a c"))
         nc.sync.dma_start(list2[:], offs2)
         nc.sync.dma_start(list3[:], offs3)
         tab_w = [shared.tile([P, T], I32, name="tab_w%d" % a, offset=(64, 12)[a] * KIB) for a in range(2)]
-        w4_w_raw = shared.tile([P, H], I32, name="w4_w_raw", offset=28 * KIB)
+        w4_w_raw = shared.tile([P, H], I32, name="w4_w_raw", offset=106 * KIB)
         nc.sync.dma_start(tab_w[0][:], tab_words[0].rearrange("p t i -> p (t i)").bitcast(I32))
         nc.sync.dma_start(
             w4_w_raw[:].rearrange("p (a c) -> p a c", a=2),
             w4_words.bitcast(I32).rearrange("a p c -> p a c"),
         )
         nc.sync.dma_start(tab_w[1][:], tab_words[1].rearrange("p t i -> p (t i)").bitcast(I32))
-        nc.vector.memset(tab_s[32:64, :].bitcast(I32), 0)
-        nc.vector.memset(tab_s[64:128, :].bitcast(I32), 0)
+        nc.gpsimd.memset(tab_s[32:64, :].bitcast(I32), 0)
+        nc.gpsimd.memset(tab_s[64:128, :].bitcast(I32), 0)
 
         planes = shared.tile([P, 2 * (S + H)], U8, name="planes", align_bytes=64, offset=44 * KIB)
-        nc.vector.memset(planes[:].bitcast(I32), 0)
-        page0 = held.tile([P, T2], F32, name="page0")
-        nc.vector.memset(page0[:], 0.0)
+        nc.gpsimd.memset(planes[:].bitcast(I32), 0)
 
         ident = held.tile([P, P], F32, name="ident")
         make_identity(nc, ident[:])
 
-        picked_s = held.tile([P, S], U8, name="picked_s")
+        picked_s = shared.tile([P, S], U8, name="picked_s", offset=0)
         nc.vector.tensor_copy(picked_s[:], tab_s[:].indirect(list1[:]))
-        scale_rows = shared.tile([32, (S + H) // 4], I32, name="scale_rows", offset=107 * KIB)
+        scale_rows = held.tile([32, (S + H) // 4], I32, name="scale_rows")
         nc.vector.tensor_copy(
             scale_rows[:, S // 4 :].rearrange("p (b t q) -> p b t q", b=2, t=4),
             w4_s_raw[:].rearrange("p (b q t) -> p b t q", b=2, t=4),
         )
         nc.vector.tensor_copy(scale_rows[:, 0 : S // 4], picked_s[0:32, :].bitcast(I32))
-        nc.vector.tensor_copy(planes[0:4, 0 : S + H].bitcast(I32), scale_rows[0:4, :])
-        for group in range(1, 8):
-            a, quad = divmod(group, 4)
+        for quad in range(4):
             nc.scalar.dma_start(
-                planes[32 * quad : 32 * quad + 4, (S + H) * a : (S + H) * (a + 1)].bitcast(I32),
-                scale_rows[4 * group : 4 * group + 4, :],
+                planes[32 * quad : 32 * quad + 4, :].bitcast(I32).rearrange("p (a c) -> p a c", a=2),
+                scale_rows[8 * quad : 8 * quad + 8, :],
             )
 
         wgs_rows = wgs.rearrange("(q t e) j -> t q e j", t=4, e=4)
 
-        def load_weight(dest, t):
+        def load_weight(dest, t, lo=0, hi=S):
             for quad in (0, 2, 1, 3):
-                nc.sync.dma_start(dest[32 * quad : 32 * quad + 32, :], wgs_rows[t])
+                nc.sync.dma_start(dest[32 * quad : 32 * quad + 32, lo:hi], wgs_rows[t][:, :, lo:hi])
 
-        weight = [
-            shared.tile([P, S], F32, name="weight%d" % t, offset=at * KIB) for t, at in enumerate((24, 28, 68, 64))
-        ]
-        load_weight(weight[0], 0)
+        weights = [shared.tile([P, 2, S], F32, name="weights%d" % j, offset=(64, 100)[j] * KIB) for j in range(2)]
+        weight = [weights[t // 2][:, t % 2, :] for t in range(4)]
 
         v_w = [
             shared.tile([P, S], U32, name="v_w%d" % a, align_bytes=64, offset=(32 + 4 * a) * KIB) for a in range(2)
         ]
         nc.vector.tensor_copy(v_w[0][:], tab_w[0][:].bitcast(U32).indirect(list1[:]))
+
+        for lo, hi in HALVES:
+            load_weight(weight[0], 0, lo, hi)
 
         w4_w = shared.tile([P, 4 * H], U8, name="w4_w", align_bytes=64, offset=40 * KIB)
         nc.vector.tensor_copy(
@@ -117,8 +114,8 @@ def tile_list_buffer_pool_prefetch_kernel(
                 v_w[1][:, lo:hi], tab_w[1][:].bitcast(U32).indirect(list1[:, lo // 16 : hi // 16])
             )
 
-        pages = [page0] + [shared.tile([P, T2], F32, name="page%d" % j, offset=8 * KIB * j) for j in (1, 2)]
-        for j in (1, 2):
+        pages = [shared.tile([P, T2], F32, name="page%d" % j, offset=8 * KIB * j) for j in range(3)]
+        for j in range(3):
             nc.gpsimd.memset(pages[j][:], 0.0)
 
         for t in range(1, 4):
@@ -132,19 +129,21 @@ def tile_list_buffer_pool_prefetch_kernel(
         def bank_tile(j, shape):
             return psum.tile(shape, F32, name="bank%d" % j, tag="bank%d" % j)
 
-        mid = shared.tile([P, 2 * S], F32, name="mid", offset=56 * KIB)
-        heat_at = {0: 88, 2: 84, 3: 0}
-        heat = [
-            shared.tile([P, S], F32, name="heat%d" % i, offset=heat_at[i] * KIB)
-            if i in heat_at
-            else mid[:, S // 2 : S // 2 + S]
-            if i == SKEWED + 1
-            else held.tile([P, S], F32, name="heat%d" % i)
-            for i in range(TILES)
+        lane = [
+            held.tile([P, 2 * S - P], F32, name="lane0"),
+            shared.tile([P, 3 * S - P], F32, name="lane1", offset=72 * KIB),
+            held.tile([P, 3 * S - P], F32, name="lane2"),
         ]
-        spare = held.tile([P, S], F32, name="spare")
+        heats = [lane[2][:, 0 : 2 * S], shared.tile([P, 2 * S], F32, name="heats1", offset=24 * KIB)]
+        heat = [
+            held.tile([P, S], F32, name="heat0"),
+            held.tile([P, S], F32, name="heat1"),
+            shared.tile([P, S], F32, name="heat2", offset=72 * KIB),
+            shared.tile([P, S], F32, name="heat3", offset=88 * KIB),
+        ] + [heats[i // 2][:, S * (i % 2) : S * (i % 2 + 1)] for i in range(4)]
+        spare = lane[0][:, S - P : 2 * S - P]
         banks_used = 0
-        for i in range(TILES):
+        for i in (0, 1, 3, 4, 2, 5, 6, 7):
             squares = spare if i == FUSED else heat[i]
             for lo, hi in FIRST_CUTS if i == 0 else HALVES:
                 bank = bank_tile(banks_used % HEAT_BANKS, [P, hi - lo])
@@ -168,20 +167,33 @@ def tile_list_buffer_pool_prefetch_kernel(
             if i > 0:
                 nc.scalar.activation(heat[i][:], squares[:], ACT.Identity, bias=-0.5, scale=0.5)
 
-        wo_raw = [shared.tile([P, 4, N], F32, name="wo_raw%d" % b, offset=(100 + 8 * b) * KIB) for b in range(2)]
+        wo_both = shared.tile([P, 2, 4, N], F32, name="wo_raw", offset=108 * KIB)
+        wo_raw = [wo_both[:, b, :, :] for b in range(2)]
         for b in range(2):
             wo_rows = wo[512 * b : 512 * b + 512, :].rearrange("(q t e) n -> t q e n", t=4, e=4)
             for t in range(4):
                 nc.sync.dma_start(wo_raw[b][:, t, :], wo_rows[t])
 
-        pair = [mid[:, S * j : S * (j + 1)] for j in range(2)]
-        fetched = [spare, heat[3], heat[4], pair[0], pair[1], heat[6], heat[7]]
-        cos_early = [heat[1], heat[2], heat[0], heat[3], heat[4], heat[1]]
-        weighed = {2: heat[0], 3: fetched[0], 4: cos_early[0], 5: cos_early[1], 6: fetched[4], 7: fetched[5]}
+        z_pairs = [
+            shared.tile([P, 3 * M - P], F32, name="z_pairs0", offset=88 * KIB),
+            held.tile([P, 2 * M], F32, name="z_pairs1"),
+        ]
+        fetched = [
+            spare,
+            lane[1][:, 2 * S - P : 3 * S - P],
+            z_pairs[0][:, M - P : 2 * M - P],
+            heat[4],
+            lane[2][:, 2 * S - P : 3 * S - P],
+            z_pairs[0][:, 2 * M - P : 3 * M - P],
+            z_pairs[1][:, M - P : 2 * M - P],
+        ]
+        weighed = {2: heat[0], 3: lane[0][:, 0:S]}
 
-        def weigh(i):
-            engine = nc.vector if i == FUSED else nc.gpsimd
-            engine.tensor_tensor(weighed[i][:], heat[i][:], weight[i % 4][:], ALU.mult)
+        def weigh_pair(j):
+            both = lane[j + 1][:, 0 : 2 * S]
+            nc.gpsimd.tensor_tensor(both, heats[j][:], weights[j][:].rearrange("p t j -> p (t j)"), ALU.mult)
+            for side in range(2):
+                weighed[4 + 2 * j + side] = both[:, S * side : S * (side + 1)]
 
         def put(i):
             if i >= FUSED:
@@ -231,32 +243,44 @@ def tile_list_buffer_pool_prefetch_kernel(
             for j, (lo, hi) in enumerate(cuts):
                 nc.scalar.activation(cos_out[:, lo:hi], rest[j][:], ACT.Sin, bias=PHASE, scale=TURN)
 
-        cos_last = held.tile([P, 2, M], F32, name="cos_last")
-        z_pairs = [held.tile([P, 2, M, 2], BF16, name="z_pairs%d" % b) for b in range(2)]
-        whole5 = shared.tile([P, M], U32, name="whole5", offset=92 * KIB)
+        cos = [held.tile([P, 2, M], F32, name="cos%d" % j) for j in range(2)]
+        works = [shared.tile([P, 2, M], F32, name="works%d" % j, offset=(32 + 8 * j) * KIB) for j in range(2)]
+        cos_last, work_last = cos[1], works[1]
+
+        def pairs(b, pair):
+            return z_pairs[b][:, M * pair : M * (pair + 1)].bitcast(BF16).rearrange("p (m t) -> p m t", t=2)
+
+        def load_works(pair):
+            for side in range(2):
+                load_work(2 * pair + side, works[pair % 2][:, side, :])
+
+        whole5 = shared.tile([P, M], U32, name="whole5", offset=108 * KIB)
         z = [
-            shared.tile([P, M, 4], BF16, name="z0", align_bytes=64, offset=92 * KIB),
+            shared.tile([P, M, 4], BF16, name="z0", align_bytes=64, offset=108 * KIB),
             held.tile([P, M, 4], BF16, name="z1", align_bytes=64),
         ]
         z_w = [held.tile([P, M], U32, name="z_w%d" % b, align_bytes=64) for b in range(2)]
         z1_s = held.tile([P, M], U8, name="z1_s", align_bytes=64)
 
-        def modulate(i, work_tile):
-            b, t = divmod(i, 4)
-            load_work(i, work_tile[:])
-            nc.gpsimd.tensor_tensor(z_pairs[b][:, t // 2, :, t % 2], cos_early[i][:], work_tile[:], ALU.mult)
+        def modulate(pair):
+            nc.gpsimd.tensor_tensor(
+                pairs(pair // 2, pair % 2),
+                cos[pair % 2][:].rearrange("p t m -> p m t"),
+                works[pair % 2][:].rearrange("p t m -> p m t"),
+                ALU.mult,
+            )
 
         def weave(b, lo, hi, word, copy):
             copy(
                 z[b][:, lo:hi, :].rearrange("p m t -> p (m t)").bitcast(word).rearrange("p (m w) -> p m w", w=2),
-                z_pairs[b][:].rearrange("p w m t -> p w (m t)").bitcast(word)[:, :, lo:hi].rearrange("p w m -> p m w"),
+                z_pairs[b][:, 0 : 2 * M].bitcast(word).rearrange("p (w m) -> p m w", w=2)[:, lo:hi, :],
             )
 
         def quantise(codes, scales, values):
             nc.vector.quantize_mx(out=codes.bitcast(E4M3), scales=scales, in_=values)
 
         wo_bf = [
-            shared.tile([P, N, 4], BF16, name="wo_bf%d" % b, align_bytes=64, offset=(72, 4)[b] * KIB)
+            shared.tile([P, N, 4], BF16, name="wo_bf%d" % b, align_bytes=64, offset=(56, 68)[b] * KIB)
             for b in range(2)
         ]
         wo_w = held.tile([P, 2 * N], U32, name="wo_w", align_bytes=64)
@@ -270,7 +294,7 @@ def tile_list_buffer_pool_prefetch_kernel(
                     )
 
         def fetch_and_cosine(i):
-            cos_out = cos_early[i] if i < LAST - 1 else cos_last[:, 0, :]
+            cos_out = cos[i // 2 % 2][:, i % 2, :]
             first_bank = 1 if i < SKEWED else HEAT_BANKS
             flipped = fetch(i, HALVES, 0, first_bank)
             if i == SKEWED - 2:
@@ -279,49 +303,50 @@ def tile_list_buffer_pool_prefetch_kernel(
                 return lambda: cosine(flipped, HALVES, CHUNKS, (0, 4, 1, 5), whole, cos_out)
             return lambda: cosine(flipped, HALVES, HALVES, (first_bank, first_bank + 1), whole5 if i == 5 else whole, cos_out)
 
-        put(0)
-        put(1)
-        weigh(2)
-        finish = fetch_and_cosine(0)
-        for i in range(2, SKEWED + 1):
-            if i >= 3:
-                modulate(i - 3, weighed[i - 1])
-            weigh(i + 1)
-            finish()
-            if i == 3:
-                round_wo()
-            put(i)
-            finish = fetch_and_cosine(i - 1)
-        wo_s = [shared.tile([P, N], U8, name="wo%d_s" % b, align_bytes=64, offset=(28, 71)[b] * KIB) for b in range(2)]
+        wo_s = [shared.tile([P, N], U8, name="wo%d_s" % b, align_bytes=64, offset=(64, 100)[b] * KIB) for b in range(2)]
 
         def quantise_wo(b):
             quantise(wo_w[:, N * b : N * (b + 1)], wo_s[b][:], wo_bf[b][:].rearrange("p n t -> p (n t)"))
 
-        finish_early = finish
+        load_works(0)
+        load_works(1)
+        put(0)
+        put(1)
+        nc.vector.tensor_tensor(weighed[2][:], heat[2][:], weight[2], ALU.mult)
+        finish = fetch_and_cosine(0)
+        nc.gpsimd.tensor_tensor(weighed[3][:], heat[3][:], weight[3], ALU.mult)
+        finish()
+        put(2)
+        finish = fetch_and_cosine(1)
+        weigh_pair(0)
+        finish()
+        round_wo()
+        put(3)
+        finish = fetch_and_cosine(2)
+        modulate(0)
+        load_works(2)
+        finish()
+        put(4)
+        finish_early = fetch_and_cosine(3)
         finish = fetch_and_cosine(4)
-        weigh(6)
-        modulate(2, fetched[3])
+        weigh_pair(1)
         finish_early()
         finish()
         put(5)
         quantise_wo(0)
         finish = fetch_and_cosine(5)
-        weigh(7)
-        modulate(3, shared.tile([P, M], F32, name="work3", offset=86 * KIB))
+        modulate(1)
+        load_works(3)
         finish()
         weave(0, 0, M, U32, nc.scalar.copy)
         put(6)
         quantise_wo(1)
         finish = fetch_and_cosine(6)
-        modulate(4, shared.tile([P, M], F32, name="work4", offset=62 * KIB))
-        modulate(5, shared.tile([P, M], F32, name="work5", offset=66 * KIB + BANK))
+        modulate(2)
         finish()
-        work_last = shared.tile([P, 2, M], F32, name="work_last", offset=100 * KIB)
-        for j in range(2):
-            load_work(LAST - 1 + j, work_last[:, j, :])
 
         put(LAST)
-        z0_s = [shared.tile([P, BANK], U8, name="z0_s%d" % j, align_bytes=64, offset=(66, 52)[j] * KIB) for j in range(2)]
+        z0_s = [shared.tile([P, BANK], U8, name="z0_s%d" % j, align_bytes=64, offset=(54, 52)[j] * KIB) for j in range(2)]
         fetched.append(shared.tile([P, M], F32, name="x_last", offset=48 * KIB))
 
         def quantise_z0(j):
@@ -360,7 +385,7 @@ def tile_list_buffer_pool_prefetch_kernel(
                 sums[lo, n_tile] = bank_tile(j + len(CHUNKS) * (n_tile // 2), [P, 2, CHUNK])
                 score(sums[lo, n_tile], 0, n_tile, lo)
             nc.vector.tensor_tensor(
-                z_pairs[1][:, 1, lo:hi, :].rearrange("p (c f) t -> p c t f", f=4),
+                pairs(1, 1)[:, lo:hi, :].rearrange("p (c f) t -> p c t f", f=4),
                 cos_last[:, :, lo:hi].rearrange("p t (c f) -> p c t f", f=4),
                 work_last[:, :, lo:hi].rearrange("p t (c f) -> p c t f", f=4),
                 ALU.mult,

@@ -28,6 +28,7 @@ PHASE = math.pi / 2 - CAP
 FUSED = 2
 SKEWED = 4
 KIB = 1024
+PAGE_OF = (0, 1, 2, 0, 1, 0, 1, 1)
 DIRECT = 2
 HEAT_BANKS = 6
 CHUNK = 256
@@ -49,7 +50,7 @@ def tile_list_buffer_pool_prefetch_kernel(
         list2 = held.tile([P, S // 16], U16, name="list2")
         list3 = held.tile([P, M // 16], U16, name="list3")
         nc.sync.dma_start(list1[:], offs)
-        tab_s = shared.tile([P, T], U8, name="tab_s", offset=60 * KIB)
+        tab_s = shared.tile([P, T], U8, name="tab_s", offset=61 * KIB)
         nc.sync.dma_start(tab_s[0:32, :].bitcast(I32), tab_scales.bitcast(I32).rearrange("a g t -> g a t"))
         w4_s_raw = held.tile([32, H // 4], I32, name="w4_s_raw")
         nc.sync.dma_start(w4_s_raw[:], w4_scales.bitcast(I32).rearrange("a g c -> g a c"))
@@ -66,7 +67,7 @@ def tile_list_buffer_pool_prefetch_kernel(
         nc.gpsimd.memset(tab_s[32:64, :].bitcast(I32), 0)
         nc.gpsimd.memset(tab_s[64:128, :].bitcast(I32), 0)
 
-        planes = shared.tile([P, 2 * (S + H)], U8, name="planes", align_bytes=64, offset=44 * KIB)
+        planes = shared.tile([P, 2 * (S + H)], U8, name="planes", align_bytes=64, offset=56 * KIB)
         nc.gpsimd.memset(planes[:].bitcast(I32), 0)
 
         ident = held.tile([P, P], F32, name="ident")
@@ -96,14 +97,14 @@ def tile_list_buffer_pool_prefetch_kernel(
         weight = [weights[t // 2][:, t % 2, :] for t in range(4)]
 
         v_w = [
-            shared.tile([P, S], U32, name="v_w%d" % a, align_bytes=64, offset=(32 + 4 * a) * KIB) for a in range(2)
+            shared.tile([P, S], U32, name="v_w%d" % a, align_bytes=64, offset=(44 + 4 * a) * KIB) for a in range(2)
         ]
         nc.vector.tensor_copy(v_w[0][:], tab_w[0][:].bitcast(U32).indirect(list1[:]))
 
         for lo, hi in HALVES:
             load_weight(weight[0], 0, lo, hi)
 
-        w4_w = shared.tile([P, 4 * H], U8, name="w4_w", align_bytes=64, offset=40 * KIB)
+        w4_w = shared.tile([P, 4 * H], U8, name="w4_w", align_bytes=64, offset=52 * KIB)
         nc.vector.tensor_copy(
             w4_w[:].bitcast(I32).rearrange("p (s t q w) -> p s t q w", s=4, t=4, w=2),
             w4_w_raw[:].rearrange("p (s q t w) -> p s t q w", s=4, t=4, w=2),
@@ -132,14 +133,18 @@ def tile_list_buffer_pool_prefetch_kernel(
         lane = [
             held.tile([P, 2 * S - P], F32, name="lane0"),
             shared.tile([P, 3 * S - P], F32, name="lane1", offset=72 * KIB),
-            held.tile([P, 3 * S - P], F32, name="lane2"),
+            shared.tile([P, 3 * S - P], F32, name="lane2", offset=40 * KIB + BANK),
         ]
-        heats = [lane[2][:, 0 : 2 * S], shared.tile([P, 2 * S], F32, name="heats1", offset=24 * KIB)]
+        z_pairs = [
+            shared.tile([P, 4 * S], F32, name="z_pairs0", offset=24 * KIB),
+            shared.tile([P, 2 * M], F32, name="z_pairs1", offset=52 * KIB),
+        ]
+        heats = [z_pairs[0][:, 2 * S * j : 2 * S * (j + 1)] for j in range(2)]
         heat = [
             held.tile([P, S], F32, name="heat0"),
             held.tile([P, S], F32, name="heat1"),
-            shared.tile([P, S], F32, name="heat2", offset=72 * KIB),
-            shared.tile([P, S], F32, name="heat3", offset=88 * KIB),
+            held.tile([P, S], F32, name="heat2"),
+            shared.tile([P, S], F32, name="heat3", offset=72 * KIB),
         ] + [heats[i // 2][:, S * (i % 2) : S * (i % 2 + 1)] for i in range(4)]
         spare = lane[0][:, S - P : 2 * S - P]
         banks_used = 0
@@ -174,15 +179,11 @@ def tile_list_buffer_pool_prefetch_kernel(
             for t in range(4):
                 nc.sync.dma_start(wo_raw[b][:, t, :], wo_rows[t])
 
-        z_pairs = [
-            shared.tile([P, 3 * M - P], F32, name="z_pairs0", offset=88 * KIB),
-            held.tile([P, 2 * M], F32, name="z_pairs1"),
-        ]
         fetched = [
             spare,
             lane[1][:, 2 * S - P : 3 * S - P],
             z_pairs[0][:, M - P : 2 * M - P],
-            heat[4],
+            lane[2][:, S - P : 2 * S - P],
             lane[2][:, 2 * S - P : 3 * S - P],
             z_pairs[0][:, 2 * M - P : 3 * M - P],
             z_pairs[1][:, M - P : 2 * M - P],
@@ -197,7 +198,7 @@ def tile_list_buffer_pool_prefetch_kernel(
 
         def put(i):
             if i >= FUSED:
-                nc.vector.tensor_copy(pages[i % 3][:].indirect(list2[:]), weighed[i][:])
+                nc.vector.tensor_copy(pages[PAGE_OF[i]][:].indirect(list2[:]), weighed[i][:])
                 return
             for lo, hi in FIRST_CUTS if i == 0 else [(0, S)]:
                 nc.vector.tensor_tensor(
@@ -208,12 +209,12 @@ def tile_list_buffer_pool_prefetch_kernel(
                 )
 
         turns = held.tile([P, M], F32, name="turns")
-        whole = shared.tile([P, M], U32, name="whole", offset=49 * KIB)
+        whole = shared.tile([P, M], U32, name="whole", offset=124 * KIB)
 
         def fetch(i, cuts, skip, first_bank):
             flipped = []
             for lo, hi in cuts if i == LAST else [(0, M)]:
-                nc.vector.tensor_copy(fetched[i][:, lo:hi], pages[i % 3][:].indirect(list3[:, lo // 16 : hi // 16]))
+                nc.vector.tensor_copy(fetched[i][:, lo:hi], pages[PAGE_OF[i]][:].indirect(list3[:, lo // 16 : hi // 16]))
             for j, (lo, hi) in list(enumerate(cuts))[skip:]:
                 bank = bank_tile(first_bank + j, [P, hi - lo])
                 for c in range(lo, hi, P):
@@ -243,16 +244,17 @@ def tile_list_buffer_pool_prefetch_kernel(
             for j, (lo, hi) in enumerate(cuts):
                 nc.scalar.activation(cos_out[:, lo:hi], rest[j][:], ACT.Sin, bias=PHASE, scale=TURN)
 
-        cos = [held.tile([P, 2, M], F32, name="cos%d" % j) for j in range(2)]
-        works = [shared.tile([P, 2, M], F32, name="works%d" % j, offset=(32 + 8 * j) * KIB) for j in range(2)]
-        cos_last, work_last = cos[1], works[1]
+        cos = [shared.tile([P, 2, M], F32, name="cos0", offset=88 * KIB), held.tile([P, 2, M], F32, name="cos1")]
+        works_at = (44 * KIB, 52 * KIB + BANK, 116 * KIB, 72 * KIB)
+        works = [shared.tile([P, 2, M], F32, name="works%d" % j, offset=works_at[j]) for j in range(4)]
+        cos_last, work_last = cos[1], works[3]
 
         def pairs(b, pair):
             return z_pairs[b][:, M * pair : M * (pair + 1)].bitcast(BF16).rearrange("p (m t) -> p m t", t=2)
 
         def load_works(pair):
             for side in range(2):
-                load_work(2 * pair + side, works[pair % 2][:, side, :])
+                load_work(2 * pair + side, works[pair][:, side, :])
 
         whole5 = shared.tile([P, M], U32, name="whole5", offset=108 * KIB)
         z = [
@@ -266,7 +268,7 @@ def tile_list_buffer_pool_prefetch_kernel(
             nc.gpsimd.tensor_tensor(
                 pairs(pair // 2, pair % 2),
                 cos[pair % 2][:].rearrange("p t m -> p m t"),
-                works[pair % 2][:].rearrange("p t m -> p m t"),
+                works[pair][:].rearrange("p t m -> p m t"),
                 ALU.mult,
             )
 
@@ -280,33 +282,35 @@ def tile_list_buffer_pool_prefetch_kernel(
             nc.vector.quantize_mx(out=codes.bitcast(E4M3), scales=scales, in_=values)
 
         wo_bf = [
-            shared.tile([P, N, 4], BF16, name="wo_bf%d" % b, align_bytes=64, offset=(56, 68)[b] * KIB)
+            shared.tile([P, N, 4], BF16, name="wo_bf%d" % b, align_bytes=64, offset=(84, 68)[b] * KIB)
             for b in range(2)
         ]
         wo_w = held.tile([P, 2 * N], U32, name="wo_w", align_bytes=64)
 
         def round_wo():
             for b in range(2):
-                for n_lo in range(0, N, N // 2):
+                for n_lo in range(0, N, P):
                     nc.scalar.copy(
-                        wo_bf[b][:, n_lo : n_lo + N // 2, :],
-                        wo_raw[b][:, :, n_lo : n_lo + N // 2].rearrange("p t n -> p n t"),
+                        wo_bf[b][:, n_lo : n_lo + P, :],
+                        wo_raw[b][:, :, n_lo : n_lo + P].rearrange("p t n -> p n t"),
                     )
 
         def fetch_and_cosine(i):
             cos_out = cos[i // 2 % 2][:, i % 2, :]
-            first_bank = 1 if i < SKEWED else HEAT_BANKS
+            first_bank = HEAT_BANKS if i == SKEWED else 3
             flipped = fetch(i, HALVES, 0, first_bank)
             if i == SKEWED - 2:
-                return lambda: cosine(flipped, HALVES, CHUNKS, (1, 2, HEAT_BANKS, HEAT_BANKS + 1), whole, cos_out)
+                return lambda: cosine(flipped, HALVES, CHUNKS, (3, 4, HEAT_BANKS, HEAT_BANKS + 1), whole, cos_out)
             if i == LAST - 1:
-                return lambda: cosine(flipped, HALVES, CHUNKS, (0, 4, 1, 5), whole, cos_out)
+                return lambda: cosine(flipped, HALVES, CHUNKS, (0, 1, 2, 5), whole, cos_out)
             return lambda: cosine(flipped, HALVES, HALVES, (first_bank, first_bank + 1), whole5 if i == 5 else whole, cos_out)
 
-        wo_s = [shared.tile([P, N], U8, name="wo%d_s" % b, align_bytes=64, offset=(64, 100)[b] * KIB) for b in range(2)]
+        wo_s = [shared.tile([P, N], U8, name="wo%d_s" % b, align_bytes=64, offset=(100, 60)[b] * KIB) for b in range(2)]
 
-        def quantise_wo(b):
-            quantise(wo_w[:, N * b : N * (b + 1)], wo_s[b][:], wo_bf[b][:].rearrange("p n t -> p (n t)"))
+        def quantise_wo(b, lo, hi):
+            quantise(
+                wo_w[:, N * b + lo : N * b + hi], wo_s[b][:, lo:hi], wo_bf[b][:, lo:hi, :].rearrange("p n t -> p (n t)")
+            )
 
         load_works(0)
         load_works(1)
@@ -324,8 +328,8 @@ def tile_list_buffer_pool_prefetch_kernel(
         put(3)
         finish = fetch_and_cosine(2)
         modulate(0)
-        load_works(2)
         finish()
+        load_works(2)
         put(4)
         finish_early = fetch_and_cosine(3)
         finish = fetch_and_cosine(4)
@@ -333,28 +337,31 @@ def tile_list_buffer_pool_prefetch_kernel(
         finish_early()
         finish()
         put(5)
-        quantise_wo(0)
+        quantise_wo(0, 0, N)
         finish = fetch_and_cosine(5)
-        modulate(1)
         load_works(3)
+        modulate(1)
         finish()
-        weave(0, 0, M, U32, nc.scalar.copy)
+        weave(0, 0, BANK, U32, nc.scalar.copy)
         put(6)
-        quantise_wo(1)
+        quantise_wo(1, 0, N // 2)
         finish = fetch_and_cosine(6)
+        quantise_wo(1, N // 2, N)
         modulate(2)
         finish()
+        for lo, hi in CHUNKS[2:]:
+            weave(0, lo, hi, U32, nc.scalar.copy)
 
         put(LAST)
-        z0_s = [shared.tile([P, BANK], U8, name="z0_s%d" % j, align_bytes=64, offset=(54, 52)[j] * KIB) for j in range(2)]
-        fetched.append(shared.tile([P, M], F32, name="x_last", offset=48 * KIB))
+        z0_s = [shared.tile([P, BANK], U8, name="z0_s%d" % j, align_bytes=64, offset=(116, 126)[j] * KIB) for j in range(2)]
+        fetched.append(shared.tile([P, M], F32, name="x_last", offset=122 * KIB))
 
         def quantise_z0(j):
             lo, hi = HALVES[j]
             quantise(z_w[0][:, lo:hi], z0_s[j][:], z[0][:, lo:hi, :].rearrange("p m t -> p (m t)"))
 
         quantise_z0(0)
-        flipped = fetch(LAST, CHUNKS, DIRECT, 0)
+        flipped = fetch(LAST, CHUNKS, DIRECT, 3 - DIRECT)
         whole_last = held.tile([P, M], U32, name="whole_last")
         for lo, hi in CHUNKS[:DIRECT]:
             u, count = turns[:, lo:hi], whole_last[:, lo:hi]
@@ -382,7 +389,7 @@ def tile_list_buffer_pool_prefetch_kernel(
         sums = {}
         for j, (lo, hi) in enumerate(CHUNKS):
             for n_tile in (0, 2):
-                sums[lo, n_tile] = bank_tile(j + len(CHUNKS) * (n_tile // 2), [P, 2, CHUNK])
+                sums[lo, n_tile] = bank_tile(((0, 1), (2, 5), (3, 6), (4, 7))[j][n_tile // 2], [P, 2, CHUNK])
                 score(sums[lo, n_tile], 0, n_tile, lo)
             nc.vector.tensor_tensor(
                 pairs(1, 1)[:, lo:hi, :].rearrange("p (c f) t -> p c t f", f=4),

@@ -28,12 +28,14 @@ PHASE = math.pi / 2 - CAP
 FUSED = 2
 SKEWED = 4
 KIB = 1024
+SIXTHS = [(0, 256), (256, 512), (512, 640), (640, 768), (768, 896), (896, 1024)]
 PAGE_OF = (0, 1, 2, 0, 1, 0, 1, 1)
 DIRECT = 2
 HEAT_BANKS = 6
 CHUNK = 256
 FIRST_CUTS = [(0, 256), (256, 512), (512, S)]
 HALVES = [(0, BANK), (BANK, 2 * BANK)]
+QUARTERS = FIRST_CUTS[:2]
 CHUNKS = [(lo, lo + CHUNK) for lo in range(0, M, CHUNK)]
 
 
@@ -101,8 +103,8 @@ def tile_list_buffer_pool_prefetch_kernel(
         ]
         nc.vector.tensor_copy(v_w[0][:], tab_w[0][:].bitcast(U32).indirect(list1[:]))
 
-        for lo, hi in HALVES:
-            load_weight(weight[0], 0, lo, hi)
+        for t in range(2):
+            load_weight(weight[t], t)
 
         w4_w = shared.tile([P, 4 * H], U8, name="w4_w", align_bytes=64, offset=52 * KIB)
         nc.vector.tensor_copy(
@@ -119,7 +121,7 @@ def tile_list_buffer_pool_prefetch_kernel(
         for j in range(3):
             nc.gpsimd.memset(pages[j][:], 0.0)
 
-        for t in range(1, 4):
+        for t in range(2, 4):
             load_weight(weight[t], t)
 
         def load_work(i, dest):
@@ -140,37 +142,46 @@ def tile_list_buffer_pool_prefetch_kernel(
             shared.tile([P, 2 * M], F32, name="z_pairs1", offset=52 * KIB),
         ]
         heats = [z_pairs[0][:, 2 * S * j : 2 * S * (j + 1)] for j in range(2)]
-        heat = [
-            held.tile([P, S], F32, name="heat0"),
-            held.tile([P, S], F32, name="heat1"),
-            held.tile([P, S], F32, name="heat2"),
-            shared.tile([P, S], F32, name="heat3", offset=72 * KIB),
-        ] + [heats[i // 2][:, S * (i % 2) : S * (i % 2 + 1)] for i in range(4)]
         spare = lane[0][:, S - P : 2 * S - P]
-        banks_used = 0
-        for i in (0, 1, 3, 4, 2, 5, 6, 7):
-            squares = spare if i == FUSED else heat[i]
-            for lo, hi in FIRST_CUTS if i == 0 else HALVES:
-                bank = bank_tile(banks_used % HEAT_BANKS, [P, hi - lo])
-                banks_used = banks_used + 1
-                width = BANK if hi - lo == BANK else P
-                for c in range(lo, hi, width):
-                    for a in range(2):
-                        col, plane = H * a + P * i, (S + H) * a
-                        nc.tensor.matmul_mx(
-                            out=bank[:, c - lo : c - lo + width],
-                            lhsT=w4_w[:, 2 * col : 2 * (col + P)].bitcast(E2M1),
-                            lhsT_scale=planes[:, plane + S + P * i : plane + S + P * (i + 1)],
-                            rhs=v_w[a][:, c : c + width].bitcast(E4M3),
-                            rhs_scale=planes[:, plane + c : plane + c + width],
-                            start=(a == 0),
-                            stop=(a == 1),
-                        )
-                nc.scalar.activation(squares[:, lo:hi], bank[:], ACT.Square, bias=1.0)
-                if i == 0:
-                    nc.scalar.activation(heat[i][:, lo:hi], squares[:, lo:hi], ACT.Identity, bias=-0.5, scale=0.5)
-            if i > 0:
-                nc.scalar.activation(heat[i][:], squares[:], ACT.Identity, bias=-0.5, scale=0.5)
+        early = held.tile([P, 2 * S], F32, name="early")
+        heat = [early[:, 0:S], None, spare, shared.tile([P, S], F32, name="heat3", offset=72 * KIB)]
+        heat = heat + [heats[i // 2][:, S * (i % 2) : S * (i % 2 + 1)] for i in range(4)]
+        heat1 = [early[:, 3 * BANK : 4 * BANK], early[:, 2 * BANK : 3 * BANK]]
+        banks_used = []
+
+        def square(i, lo, hi, dest):
+            bank = bank_tile(len(banks_used) % HEAT_BANKS, [P, hi - lo])
+            banks_used.append(bank)
+            width = BANK if hi - lo == BANK else P
+            for c in range(lo, hi, width):
+                for a in range(2):
+                    col, plane = H * a + P * i, (S + H) * a
+                    nc.tensor.matmul_mx(
+                        out=bank[:, c - lo : c - lo + width],
+                        lhsT=w4_w[:, 2 * col : 2 * (col + P)].bitcast(E2M1),
+                        lhsT_scale=planes[:, plane + S + P * i : plane + S + P * (i + 1)],
+                        rhs=v_w[a][:, c : c + width].bitcast(E4M3),
+                        rhs_scale=planes[:, plane + c : plane + c + width],
+                        start=(a == 0),
+                        stop=(a == 1),
+                    )
+            nc.scalar.activation(dest, bank[:], ACT.Square, bias=1.0)
+
+        def halve(values):
+            nc.scalar.activation(values, values, ACT.Identity, bias=-0.5, scale=0.5)
+
+        for lo, hi in QUARTERS:
+            square(0, lo, hi, heat[0][:, lo:hi])
+            halve(heat[0][:, lo:hi])
+        square(1, 0, BANK, heat1[0])
+        halve(heat1[0])
+        square(0, BANK, S, heat[0][:, BANK:S])
+        square(1, BANK, S, heat1[1])
+        halve(early[:, BANK : 3 * BANK])
+        for i in range(2, TILES):
+            for lo, hi in HALVES:
+                square(i, lo, hi, heat[i][:, lo:hi])
+            halve(heat[i][:])
 
         wo_both = shared.tile([P, 2, 4, N], F32, name="wo_raw", offset=108 * KIB)
         wo_raw = [wo_both[:, b, :, :] for b in range(2)]
@@ -197,35 +208,34 @@ def tile_list_buffer_pool_prefetch_kernel(
                 weighed[4 + 2 * j + side] = both[:, S * side : S * (side + 1)]
 
         def put(i):
-            if i >= FUSED:
-                nc.vector.tensor_copy(pages[PAGE_OF[i]][:].indirect(list2[:]), weighed[i][:])
-                return
-            for lo, hi in FIRST_CUTS if i == 0 else [(0, S)]:
-                nc.vector.tensor_tensor(
-                    pages[i][:].indirect(list2[:, lo // 16 : hi // 16]),
-                    heat[i][:, lo:hi],
-                    weight[i][:, lo:hi],
-                    ALU.mult,
-                )
+            nc.vector.tensor_copy(pages[PAGE_OF[i]][:].indirect(list2[:]), weighed[i][:])
+
+        def put_fused(i, lo, hi, values):
+            nc.vector.tensor_tensor(
+                pages[i][:].indirect(list2[:, lo // 16 : hi // 16]), values, weight[i][:, lo:hi], ALU.mult
+            )
 
         turns = held.tile([P, M], F32, name="turns")
-        whole = shared.tile([P, M], U32, name="whole", offset=124 * KIB)
+        whole = shared.tile([P, M], U32, name="whole", offset=128 * KIB)
 
-        def fetch(i, cuts, skip, first_bank):
+        def fetch(i, cuts, banks):
             flipped = []
-            for lo, hi in cuts if i == LAST else [(0, M)]:
-                nc.vector.tensor_copy(fetched[i][:, lo:hi], pages[PAGE_OF[i]][:].indirect(list3[:, lo // 16 : hi // 16]))
-            for j, (lo, hi) in list(enumerate(cuts))[skip:]:
-                bank = bank_tile(first_bank + j, [P, hi - lo])
+            nc.vector.tensor_copy(fetched[i][:], pages[PAGE_OF[i]][:].indirect(list3[:]))
+            for j, (lo, hi) in enumerate(cuts):
+                bank = bank_tile(banks[j], [P, hi - lo])
                 for c in range(lo, hi, P):
                     nc.tensor.transpose(bank[:, c - lo : c - lo + P], fetched[i][:, c : c + P], ident[:])
                 flipped.append(bank)
             return flipped
 
+        def split(u, count, x):
+            nc.scalar.activation(count, x, ACT.Relu, bias=0.25, scale=-1.0 / TURN)
+            nc.scalar.activation(u, x, ACT.Relu, bias=CAP / TURN, scale=-1.0 / TURN)
+
         def cosine(flipped, flip_cuts, cuts, banks, whole, cos_out):
             start, stop = cuts[0][0], cuts[-1][1]
             for j, (lo, hi) in enumerate(flip_cuts):
-                nc.scalar.activation(turns[:, lo:hi], flipped[j][:], ACT.Relu, bias=CAP / TURN, scale=-1.0 / TURN)
+                split(turns[:, lo:hi], whole[:, lo:hi], flipped[j][:])
             rest = [bank_tile(banks[j], [P, hi - lo]) for j, (lo, hi) in enumerate(cuts)]
             for j, (lo, hi) in enumerate(cuts):
                 for c in range(lo, hi, P):
@@ -233,7 +243,6 @@ def tile_list_buffer_pool_prefetch_kernel(
                         rest[j][:, c - lo : c - lo + P], turns[:, c : c + P], ident[:],
                         start=(c == lo), stop=False, is_transpose=True,
                     )
-            nc.scalar.activation(whole[:, start:stop], turns[:, start:stop], ACT.Copy, bias=PHASE / TURN)
             nc.scalar.activation(whole[:, start:stop].bitcast(F32), whole[:, start:stop], ACT.Copy, scale=-1.0)
             for j, (lo, hi) in enumerate(cuts):
                 for c in range(lo, hi, P):
@@ -266,9 +275,9 @@ def tile_list_buffer_pool_prefetch_kernel(
 
         def modulate(pair):
             nc.gpsimd.tensor_tensor(
-                pairs(pair // 2, pair % 2),
-                cos[pair % 2][:].rearrange("p t m -> p m t"),
-                works[pair][:].rearrange("p t m -> p m t"),
+                pairs(pair // 2, pair % 2).rearrange("p (c f) t -> p c t f", f=4),
+                cos[pair % 2][:].rearrange("p t (c f) -> p c t f", f=4),
+                works[pair][:].rearrange("p t (c f) -> p c t f", f=4),
                 ALU.mult,
             )
 
@@ -298,11 +307,11 @@ def tile_list_buffer_pool_prefetch_kernel(
         def fetch_and_cosine(i):
             cos_out = cos[i // 2 % 2][:, i % 2, :]
             first_bank = HEAT_BANKS if i == SKEWED else 3
-            flipped = fetch(i, HALVES, 0, first_bank)
+            flipped = fetch(i, HALVES, (first_bank, first_bank + 1))
             if i == SKEWED - 2:
                 return lambda: cosine(flipped, HALVES, CHUNKS, (3, 4, HEAT_BANKS, HEAT_BANKS + 1), whole, cos_out)
             if i == LAST - 1:
-                return lambda: cosine(flipped, HALVES, CHUNKS, (0, 1, 2, 5), whole, cos_out)
+                return lambda: cosine(flipped, HALVES, CHUNKS, (0, 1, 3, 4), whole, cos_out)
             return lambda: cosine(flipped, HALVES, HALVES, (first_bank, first_bank + 1), whole5 if i == 5 else whole, cos_out)
 
         wo_s = [shared.tile([P, N], U8, name="wo%d_s" % b, align_bytes=64, offset=(100, 60)[b] * KIB) for b in range(2)]
@@ -314,9 +323,13 @@ def tile_list_buffer_pool_prefetch_kernel(
 
         load_works(0)
         load_works(1)
-        put(0)
-        put(1)
-        nc.vector.tensor_tensor(weighed[2][:], heat[2][:], weight[2], ALU.mult)
+        for lo, hi in QUARTERS:
+            put_fused(0, lo, hi, heat[0][:, lo:hi])
+        put_fused(1, 0, BANK, heat1[0])
+        nc.vector.tensor_tensor(heat1[1], heat1[1], weight[1][:, BANK:S], ALU.mult)
+        put_fused(0, BANK, S, heat[0][:, BANK:S])
+        nc.vector.tensor_copy(pages[1][:].indirect(list2[:, BANK // 16 : S // 16]), heat1[1])
+        nc.gpsimd.tensor_tensor(weighed[2], heat[2], weight[2], ALU.mult)
         finish = fetch_and_cosine(0)
         nc.gpsimd.tensor_tensor(weighed[3][:], heat[3][:], weight[3], ALU.mult)
         finish()
@@ -342,36 +355,47 @@ def tile_list_buffer_pool_prefetch_kernel(
         load_works(3)
         modulate(1)
         finish()
-        weave(0, 0, BANK, U32, nc.scalar.copy)
+        weave(0, 0, M, U32, nc.scalar.copy)
         put(6)
         quantise_wo(1, 0, N // 2)
         finish = fetch_and_cosine(6)
         quantise_wo(1, N // 2, N)
         modulate(2)
         finish()
-        for lo, hi in CHUNKS[2:]:
-            weave(0, lo, hi, U32, nc.scalar.copy)
 
         put(LAST)
         z0_s = [shared.tile([P, BANK], U8, name="z0_s%d" % j, align_bytes=64, offset=(116, 126)[j] * KIB) for j in range(2)]
-        fetched.append(shared.tile([P, M], F32, name="x_last", offset=122 * KIB))
+        fetched.append(shared.tile([P, M], F32, name="x_last", offset=120 * KIB))
 
         def quantise_z0(j):
             lo, hi = HALVES[j]
             quantise(z_w[0][:, lo:hi], z0_s[j][:], z[0][:, lo:hi, :].rearrange("p m t -> p (m t)"))
 
         quantise_z0(0)
-        flipped = fetch(LAST, CHUNKS, DIRECT, 3 - DIRECT)
-        whole_last = held.tile([P, M], U32, name="whole_last")
-        for lo, hi in CHUNKS[:DIRECT]:
-            u, count = turns[:, lo:hi], whole_last[:, lo:hi]
-            nc.scalar.activation(u, fetched[LAST][:, lo:hi], ACT.Relu, bias=CAP / TURN, scale=-1.0 / TURN)
-            nc.scalar.activation(count, u, ACT.Copy, bias=PHASE / TURN)
+        x_last = fetched[LAST]
+        places = [0, CHUNK, 2 * CHUNK, 0]
+        parts = [shared.tile([P, M], F32, name="parts%d" % j, offset=(126 + 4 * j) * KIB) for j in range(2)]
+
+        def fetch_last(j):
+            lo, hi = CHUNKS[j]
+            x = x_last[:, places[j] : places[j] + CHUNK]
+            nc.vector.tensor_copy(x, pages[PAGE_OF[LAST]][:].indirect(list3[:, lo // 16 : hi // 16]))
+            return x
+
+        def cosine_direct(j, x):
+            lo, hi = CHUNKS[j]
+            at = lo % BANK
+            u, count = parts[j // 2][:, at : at + CHUNK], parts[j // 2][:, BANK + at : BANK + at + CHUNK]
+            split(u, count.bitcast(U32), x)
             nc.vector.tensor_tensor(u, u, count.bitcast(I32), ALU.subtract)
             nc.scalar.activation(cos_last[:, 1, lo:hi], u, ACT.Sin, bias=PHASE, scale=TURN)
-        quantise_z0(1)
-        for j, cut in enumerate(CHUNKS[DIRECT:]):
-            cosine([flipped[j]], [cut], [cut], [len(CHUNKS) + DIRECT + j], whole_last, cos_last[:, 1, :])
+
+        first = [fetch_last(j) for j in range(3)]
+        cosine_direct(0, first[0])
+        fourth = fetch_last(3)
+        cosine_direct(1, first[1])
+        cosine_direct(2, first[2])
+        cosine_direct(3, fourth)
 
         def score(bank, b, n_tile, lo):
             for side in range(2):
@@ -388,8 +412,10 @@ def tile_list_buffer_pool_prefetch_kernel(
 
         sums = {}
         for j, (lo, hi) in enumerate(CHUNKS):
+            if lo == BANK:
+                quantise_z0(1)
             for n_tile in (0, 2):
-                sums[lo, n_tile] = bank_tile(((0, 1), (2, 5), (3, 6), (4, 7))[j][n_tile // 2], [P, 2, CHUNK])
+                sums[lo, n_tile] = bank_tile(((0, 1), (3, 4), (2, 5), (6, 7))[j][n_tile // 2], [P, 2, CHUNK])
                 score(sums[lo, n_tile], 0, n_tile, lo)
             nc.vector.tensor_tensor(
                 pairs(1, 1)[:, lo:hi, :].rearrange("p (c f) t -> p c t f", f=4),

@@ -66,18 +66,20 @@ def tile_list_buffer_pool_prefetch_kernel(
             w4_words.bitcast(I32).rearrange("a p c -> p a c"),
         )
         nc.sync.dma_start(tab_w[1][:], tab_words[1].rearrange("p t i -> p (t i)").bitcast(I32))
-        nc.gpsimd.memset(tab_s[32:64, :].bitcast(I32), 0)
-        nc.gpsimd.memset(tab_s[64:128, :].bitcast(I32), 0)
+        nc.vector.memset(tab_s[32:64, :].bitcast(I32), 0)
+        nc.vector.memset(tab_s[64:128, :].bitcast(I32), 0)
 
         planes = shared.tile([P, 2 * (S + H)], U8, name="planes", align_bytes=64, offset=56 * KIB)
-        nc.gpsimd.memset(planes[:].bitcast(I32), 0)
+        nc.vector.memset(planes[:].bitcast(I32), 0)
 
         ident = held.tile([P, P], F32, name="ident")
         make_identity(nc, ident[:])
+        warm = held.tile([P, 1], F32, name="warm")
+        nc.scalar.activation(warm[:], ident[:, 0:1], ACT.Sin)
 
-        picked_s = shared.tile([P, S], U8, name="picked_s", offset=0)
+        picked_s = shared.tile([P, S], U8, name="picked_s", offset=126 * KIB - BANK)
         nc.vector.tensor_copy(picked_s[:], tab_s[:].indirect(list1[:]))
-        scale_rows = held.tile([32, (S + H) // 4], I32, name="scale_rows")
+        scale_rows = shared.tile([32, (S + H) // 4], I32, name="scale_rows", offset=99 * KIB)
         nc.vector.tensor_copy(
             scale_rows[:, S // 4 :].rearrange("p (b t q) -> p b t q", b=2, t=4),
             w4_s_raw[:].rearrange("p (b q t) -> p b t q", b=2, t=4),
@@ -91,11 +93,14 @@ def tile_list_buffer_pool_prefetch_kernel(
 
         wgs_rows = wgs.rearrange("(q t e) j -> t q e j", t=4, e=4)
 
-        def load_weight(dest, t, lo=0, hi=S):
+        def load_weight(dest, t, queue):
             for quad in (0, 2, 1, 3):
-                nc.sync.dma_start(dest[32 * quad : 32 * quad + 32, lo:hi], wgs_rows[t][:, :, lo:hi])
+                queue.dma_start(dest[32 * quad : 32 * quad + 32, :], wgs_rows[t])
 
-        weights = [shared.tile([P, 2, S], F32, name="weights%d" % j, offset=(64, 100)[j] * KIB) for j in range(2)]
+        first_weight = [shared.tile([P, S], F32, name="first_weight%d" % t, offset=(122, 96)[t] * KIB) for t in range(2)]
+        load_weight(first_weight[0], 0, nc.scalar)
+
+        weights = [shared.tile([P, 2, S], F32, name="weights%d" % j, offset=(90, 100)[j] * KIB) for j in range(2)]
         weight = [weights[t // 2][:, t % 2, :] for t in range(4)]
 
         v_w = [
@@ -103,8 +108,7 @@ def tile_list_buffer_pool_prefetch_kernel(
         ]
         nc.vector.tensor_copy(v_w[0][:], tab_w[0][:].bitcast(U32).indirect(list1[:]))
 
-        for t in range(2):
-            load_weight(weight[t], t)
+        load_weight(first_weight[1], 1, nc.sync)
 
         w4_w = shared.tile([P, 4 * H], U8, name="w4_w", align_bytes=64, offset=52 * KIB)
         nc.vector.tensor_copy(
@@ -117,12 +121,12 @@ def tile_list_buffer_pool_prefetch_kernel(
                 v_w[1][:, lo:hi], tab_w[1][:].bitcast(U32).indirect(list1[:, lo // 16 : hi // 16])
             )
 
-        pages = [shared.tile([P, T2], F32, name="page%d" % j, offset=8 * KIB * j) for j in range(3)]
+        pages = [shared.tile([P, T2], F32, name="page%d" % j, offset=(126, 8, 16)[j] * KIB) for j in range(3)]
         for j in range(3):
             nc.gpsimd.memset(pages[j][:], 0.0)
 
-        for t in range(2, 4):
-            load_weight(weight[t], t)
+        for t in (2, 3):
+            load_weight(weight[t], t, nc.sync)
 
         def load_work(i, dest):
             b, t = divmod(i, 4)
@@ -212,11 +216,11 @@ def tile_list_buffer_pool_prefetch_kernel(
 
         def put_fused(i, lo, hi, values):
             nc.vector.tensor_tensor(
-                pages[i][:].indirect(list2[:, lo // 16 : hi // 16]), values, weight[i][:, lo:hi], ALU.mult
+                pages[i][:].indirect(list2[:, lo // 16 : hi // 16]), values, first_weight[i][:, lo:hi], ALU.mult
             )
 
         turns = held.tile([P, M], F32, name="turns")
-        whole = shared.tile([P, M], U32, name="whole", offset=128 * KIB)
+        whole = shared.tile([P, M], U32, name="whole", offset=142 * KIB)
 
         def fetch(i, cuts, banks):
             flipped = []
@@ -253,7 +257,7 @@ def tile_list_buffer_pool_prefetch_kernel(
             for j, (lo, hi) in enumerate(cuts):
                 nc.scalar.activation(cos_out[:, lo:hi], rest[j][:], ACT.Sin, bias=PHASE, scale=TURN)
 
-        cos = [shared.tile([P, 2, M], F32, name="cos0", offset=88 * KIB), held.tile([P, 2, M], F32, name="cos1")]
+        cos = [shared.tile([P, 2, M], F32, name="cos0", offset=0), held.tile([P, 2, M], F32, name="cos1")]
         works_at = (44 * KIB, 52 * KIB + BANK, 116 * KIB, 72 * KIB)
         works = [shared.tile([P, 2, M], F32, name="works%d" % j, offset=works_at[j]) for j in range(4)]
         cos_last, work_last = cos[1], works[3]
@@ -291,7 +295,7 @@ def tile_list_buffer_pool_prefetch_kernel(
             nc.vector.quantize_mx(out=codes.bitcast(E4M3), scales=scales, in_=values)
 
         wo_bf = [
-            shared.tile([P, N, 4], BF16, name="wo_bf%d" % b, align_bytes=64, offset=(84, 68)[b] * KIB)
+            shared.tile([P, N, 4], BF16, name="wo_bf%d" % b, align_bytes=64, offset=(84, 90)[b] * KIB)
             for b in range(2)
         ]
         wo_w = held.tile([P, 2 * N], U32, name="wo_w", align_bytes=64)
@@ -321,12 +325,14 @@ def tile_list_buffer_pool_prefetch_kernel(
                 wo_w[:, N * b + lo : N * b + hi], wo_s[b][:, lo:hi], wo_bf[b][:, lo:hi, :].rearrange("p n t -> p (n t)")
             )
 
+        for t in range(2):
+            load_weight(weight[t], t, nc.sync)
         load_works(0)
         load_works(1)
         for lo, hi in QUARTERS:
             put_fused(0, lo, hi, heat[0][:, lo:hi])
         put_fused(1, 0, BANK, heat1[0])
-        nc.vector.tensor_tensor(heat1[1], heat1[1], weight[1][:, BANK:S], ALU.mult)
+        nc.vector.tensor_tensor(heat1[1], heat1[1], first_weight[1][:, BANK:S], ALU.mult)
         put_fused(0, BANK, S, heat[0][:, BANK:S])
         nc.vector.tensor_copy(pages[1][:].indirect(list2[:, BANK // 16 : S // 16]), heat1[1])
         nc.gpsimd.tensor_tensor(weighed[2], heat[2], weight[2], ALU.mult)
@@ -364,7 +370,7 @@ def tile_list_buffer_pool_prefetch_kernel(
         finish()
 
         put(LAST)
-        z0_s = [shared.tile([P, BANK], U8, name="z0_s%d" % j, align_bytes=64, offset=(116, 126)[j] * KIB) for j in range(2)]
+        z0_s = [shared.tile([P, BANK], U8, name="z0_s%d" % j, align_bytes=64, offset=(116, 140)[j] * KIB) for j in range(2)]
         fetched.append(shared.tile([P, M], F32, name="x_last", offset=120 * KIB))
 
         def quantise_z0(j):
@@ -374,7 +380,7 @@ def tile_list_buffer_pool_prefetch_kernel(
         quantise_z0(0)
         x_last = fetched[LAST]
         places = [0, CHUNK, 2 * CHUNK, 0]
-        parts = [shared.tile([P, M], F32, name="parts%d" % j, offset=(126 + 4 * j) * KIB) for j in range(2)]
+        parts = [shared.tile([P, M], F32, name="parts%d" % j, offset=(140 + 4 * j) * KIB) for j in range(2)]
 
         def fetch_last(j):
             lo, hi = CHUNKS[j]

@@ -25,18 +25,62 @@ BANK = 512
 CAP = 2.5
 TURN = 2.0 * math.pi
 PHASE = math.pi / 2 - CAP
-FUSED = 2
-SKEWED = 4
-KIB = 1024
-SIXTHS = [(0, 256), (256, 512), (512, 640), (640, 768), (768, 896), (896, 1024)]
-PAGE_OF = (0, 1, 2, 0, 1, 0, 1, 1)
-DIRECT = 2
-HEAT_BANKS = 6
 CHUNK = 256
-FIRST_CUTS = [(0, 256), (256, 512), (512, S)]
 HALVES = [(0, BANK), (BANK, 2 * BANK)]
-QUARTERS = FIRST_CUTS[:2]
 CHUNKS = [(lo, lo + CHUNK) for lo in range(0, M, CHUNK)]
+QUARTERS = CHUNKS[:2]
+
+PAGE_OF = (0, 1, 2, 0, 1, 0, 1, 1)
+
+HEAT_BANKS = 6
+FLIP_BANKS = (4, 5)
+SECOND_FLIP_BANKS = (6, 7)
+SCORE_BANKS = ((0, 1), FLIP_BANKS, (2, 3), SECOND_FLIP_BANKS)
+
+KIB = 1024
+AT = {
+    "cos0": 0,
+    "tab_w1": 12 * KIB,
+    "page1": 8 * KIB,
+    "page2": 16 * KIB,
+    "z_pairs0": 24 * KIB,
+    "v_w0": 44 * KIB,
+    "v_w1": 48 * KIB,
+    "w4_w": 52 * KIB,
+    "planes": 56 * KIB,
+    "works0": 44 * KIB,
+    "works1": 52 * KIB + 512,
+    "lane2": 40 * KIB + 512,
+    "z_pairs1": 52 * KIB,
+    "wo_s1": 60 * KIB,
+    "tab_s": 61 * KIB,
+    "tab_w0": 64 * KIB,
+    "heat3": 72 * KIB,
+    "lane1": 72 * KIB,
+    "works3": 72 * KIB,
+    "wo_bf0": 84 * KIB,
+    "scale_rows": 99 * KIB,
+    "first_weight1": 96 * KIB,
+    "weights1": 100 * KIB,
+    "weights0": 90 * KIB,
+    "wo_bf1": 90 * KIB,
+    "wo_s0": 100 * KIB,
+    "w4_w_raw": 106 * KIB,
+    "picked_s": 125 * KIB + 512,
+    "first_weight0": 122 * KIB,
+    "page0": 126 * KIB,
+    "wo_raw": 108 * KIB,
+    "whole5": 108 * KIB,
+    "z0": 108 * KIB,
+    "works2": 116 * KIB,
+    "z0_s0": 116 * KIB,
+    "x_last": 120 * KIB,
+    "whole": 142 * KIB,
+    "parts0": 140 * KIB,
+    "parts1": 144 * KIB,
+    "z0_s1": 140 * KIB,
+    "z0_s2": 144 * KIB,
+}
 
 
 def tile_list_buffer_pool_prefetch_kernel(
@@ -48,18 +92,27 @@ def tile_list_buffer_pool_prefetch_kernel(
         shared = ctx.enter_context(tc.tile_pool(name="shared", bufs=1))
         psum = ctx.enter_context(tc.psum_pool(name="psum", bufs=1))
 
+        def placed(name, shape, dtype):
+            return shared.tile(shape, dtype, name=name, offset=AT[name])
+
+        def placed_mx(name, shape, dtype):
+            return shared.tile(shape, dtype, name=name, align_bytes=64, offset=AT[name])
+
+        def bank_tile(j, shape):
+            return psum.tile(shape, F32, name="bank%d" % j, tag="bank%d" % j)
+
         list1 = held.tile([P, S // 16], U16, name="list1")
         list2 = held.tile([P, S // 16], U16, name="list2")
         list3 = held.tile([P, M // 16], U16, name="list3")
         nc.sync.dma_start(list1[:], offs)
-        tab_s = shared.tile([P, T], U8, name="tab_s", offset=61 * KIB)
+        tab_s = placed("tab_s", [P, T], U8)
         nc.sync.dma_start(tab_s[0:32, :].bitcast(I32), tab_scales.bitcast(I32).rearrange("a g t -> g a t"))
         w4_s_raw = held.tile([32, H // 4], I32, name="w4_s_raw")
         nc.sync.dma_start(w4_s_raw[:], w4_scales.bitcast(I32).rearrange("a g c -> g a c"))
         nc.sync.dma_start(list2[:], offs2)
         nc.sync.dma_start(list3[:], offs3)
-        tab_w = [shared.tile([P, T], I32, name="tab_w%d" % a, offset=(64, 12)[a] * KIB) for a in range(2)]
-        w4_w_raw = shared.tile([P, H], I32, name="w4_w_raw", offset=106 * KIB)
+        tab_w = [placed("tab_w%d" % a, [P, T], I32) for a in range(2)]
+        w4_w_raw = placed("w4_w_raw", [P, H], I32)
         nc.sync.dma_start(tab_w[0][:], tab_words[0].rearrange("p t i -> p (t i)").bitcast(I32))
         nc.sync.dma_start(
             w4_w_raw[:].rearrange("p (a c) -> p a c", a=2),
@@ -69,7 +122,7 @@ def tile_list_buffer_pool_prefetch_kernel(
         nc.vector.memset(tab_s[32:64, :].bitcast(I32), 0)
         nc.vector.memset(tab_s[64:128, :].bitcast(I32), 0)
 
-        planes = shared.tile([P, 2 * (S + H)], U8, name="planes", align_bytes=64, offset=56 * KIB)
+        planes = placed_mx("planes", [P, 2 * (S + H)], U8)
         nc.vector.memset(planes[:].bitcast(I32), 0)
 
         ident = held.tile([P, P], F32, name="ident")
@@ -77,9 +130,9 @@ def tile_list_buffer_pool_prefetch_kernel(
         warm = held.tile([P, 1], F32, name="warm")
         nc.scalar.activation(warm[:], ident[:, 0:1], ACT.Sin)
 
-        picked_s = shared.tile([P, S], U8, name="picked_s", offset=126 * KIB - BANK)
+        picked_s = placed("picked_s", [P, S], U8)
         nc.vector.tensor_copy(picked_s[:], tab_s[:].indirect(list1[:]))
-        scale_rows = shared.tile([32, (S + H) // 4], I32, name="scale_rows", offset=99 * KIB)
+        scale_rows = placed("scale_rows", [32, (S + H) // 4], I32)
         nc.vector.tensor_copy(
             scale_rows[:, S // 4 :].rearrange("p (b t q) -> p b t q", b=2, t=4),
             w4_s_raw[:].rearrange("p (b q t) -> p b t q", b=2, t=4),
@@ -97,65 +150,63 @@ def tile_list_buffer_pool_prefetch_kernel(
             for quad in (0, 2, 1, 3):
                 queue.dma_start(dest[32 * quad : 32 * quad + 32, :], wgs_rows[t])
 
-        first_weight = [shared.tile([P, S], F32, name="first_weight%d" % t, offset=(122, 96)[t] * KIB) for t in range(2)]
+        first_weight = [placed("first_weight%d" % t, [P, S], F32) for t in range(2)]
         load_weight(first_weight[0], 0, nc.scalar)
-
-        weights = [shared.tile([P, 2, S], F32, name="weights%d" % j, offset=(90, 100)[j] * KIB) for j in range(2)]
+        weights = [placed("weights%d" % j, [P, 2, S], F32) for j in range(2)]
         weight = [weights[t // 2][:, t % 2, :] for t in range(4)]
 
-        v_w = [
-            shared.tile([P, S], U32, name="v_w%d" % a, align_bytes=64, offset=(44 + 4 * a) * KIB) for a in range(2)
-        ]
+        v_w = [placed_mx("v_w%d" % a, [P, S], U32) for a in range(2)]
         nc.vector.tensor_copy(v_w[0][:], tab_w[0][:].bitcast(U32).indirect(list1[:]))
 
         load_weight(first_weight[1], 1, nc.sync)
 
-        w4_w = shared.tile([P, 4 * H], U8, name="w4_w", align_bytes=64, offset=52 * KIB)
+        w4_w = placed_mx("w4_w", [P, 4 * H], U8)
         nc.vector.tensor_copy(
             w4_w[:].bitcast(I32).rearrange("p (s t q w) -> p s t q w", s=4, t=4, w=2),
             w4_w_raw[:].rearrange("p (s q t w) -> p s t q w", s=4, t=4, w=2),
         )
 
-        for lo, hi in FIRST_CUTS:
+        for lo, hi in QUARTERS + HALVES[1:]:
             nc.vector.tensor_copy(
                 v_w[1][:, lo:hi], tab_w[1][:].bitcast(U32).indirect(list1[:, lo // 16 : hi // 16])
             )
 
-        pages = [shared.tile([P, T2], F32, name="page%d" % j, offset=(126, 8, 16)[j] * KIB) for j in range(3)]
+        pages = [placed("page%d" % j, [P, T2], F32) for j in range(3)]
         for j in range(3):
             nc.gpsimd.memset(pages[j][:], 0.0)
 
         for t in (2, 3):
             load_weight(weight[t], t, nc.sync)
 
-        def load_work(i, dest):
-            b, t = divmod(i, 4)
-            rows = work[512 * b : 512 * b + 512, :].rearrange("(q t e) m -> t q e m", t=4, e=4)
-            nc.sync.dma_start(dest, rows[t])
-
-        def bank_tile(j, shape):
-            return psum.tile(shape, F32, name="bank%d" % j, tag="bank%d" % j)
-
         lane = [
             held.tile([P, 2 * S - P], F32, name="lane0"),
-            shared.tile([P, 3 * S - P], F32, name="lane1", offset=72 * KIB),
-            shared.tile([P, 3 * S - P], F32, name="lane2", offset=40 * KIB + BANK),
+            placed("lane1", [P, 3 * S - P], F32),
+            placed("lane2", [P, 3 * S - P], F32),
         ]
-        z_pairs = [
-            shared.tile([P, 4 * S], F32, name="z_pairs0", offset=24 * KIB),
-            shared.tile([P, 2 * M], F32, name="z_pairs1", offset=52 * KIB),
+        z_pairs = [placed("z_pairs0", [P, 4 * S], F32), placed("z_pairs1", [P, 2 * M], F32)]
+        fetched = [
+            lane[0][:, S - P : 2 * S - P],
+            lane[1][:, 2 * S - P : 3 * S - P],
+            z_pairs[0][:, M - P : 2 * M - P],
+            lane[2][:, S - P : 2 * S - P],
+            lane[2][:, 2 * S - P : 3 * S - P],
+            z_pairs[0][:, 2 * M - P : 3 * M - P],
+            z_pairs[1][:, M - P : 2 * M - P],
         ]
-        heats = [z_pairs[0][:, 2 * S * j : 2 * S * (j + 1)] for j in range(2)]
-        spare = lane[0][:, S - P : 2 * S - P]
         early = held.tile([P, 2 * S], F32, name="early")
-        heat = [early[:, 0:S], None, spare, shared.tile([P, S], F32, name="heat3", offset=72 * KIB)]
-        heat = heat + [heats[i // 2][:, S * (i % 2) : S * (i % 2 + 1)] for i in range(4)]
-        heat1 = [early[:, 3 * BANK : 4 * BANK], early[:, 2 * BANK : 3 * BANK]]
-        banks_used = []
+        heat0, heat1_back, heat1_front = early[:, 0:S], early[:, S : S + BANK], early[:, S + BANK : 2 * S]
+        heat = {2: fetched[0], 3: placed("heat3", [P, S], F32)[:]}
+        for i in range(4, TILES):
+            heat[i] = z_pairs[0][:, S * (i - 4) : S * (i - 3)]
+        weighed = {2: heat0, 3: lane[0][:, 0:S]}
+        for i in range(4, TILES):
+            weighed[i] = lane[i // 2 - 1][:, S * (i % 2) : S * (i % 2 + 1)]
+
+        pieces_done = []
 
         def square(i, lo, hi, dest):
-            bank = bank_tile(len(banks_used) % HEAT_BANKS, [P, hi - lo])
-            banks_used.append(bank)
+            bank = bank_tile(len(pieces_done) % HEAT_BANKS, [P, hi - lo])
+            pieces_done.append((i, lo))
             width = BANK if hi - lo == BANK else P
             for c in range(lo, hi, width):
                 for a in range(2):
@@ -174,59 +225,61 @@ def tile_list_buffer_pool_prefetch_kernel(
         def halve(values):
             nc.scalar.activation(values, values, ACT.Identity, bias=-0.5, scale=0.5)
 
-        for lo, hi in QUARTERS:
-            square(0, lo, hi, heat[0][:, lo:hi])
-            halve(heat[0][:, lo:hi])
-        square(1, 0, BANK, heat1[0])
-        halve(heat1[0])
-        square(0, BANK, S, heat[0][:, BANK:S])
-        square(1, BANK, S, heat1[1])
-        halve(early[:, BANK : 3 * BANK])
+        for c in range(0, CHUNK, P):
+            square(0, c, c + P, heat0[:, c : c + P])
+        for c in range(0, CHUNK, P):
+            halve(heat0[:, c : c + P])
+        square(0, CHUNK, BANK, heat0[:, CHUNK:BANK])
+        halve(heat0[:, CHUNK:BANK])
+        square(1, 0, BANK, heat1_front)
+        halve(heat1_front)
+        square(0, BANK, S, heat0[:, BANK:S])
+        square(1, BANK, S, heat1_back)
+        halve(early[:, BANK : S + BANK])
         for i in range(2, TILES):
             for lo, hi in HALVES:
                 square(i, lo, hi, heat[i][:, lo:hi])
-            halve(heat[i][:])
+            halve(heat[i])
 
-        wo_both = shared.tile([P, 2, 4, N], F32, name="wo_raw", offset=108 * KIB)
-        wo_raw = [wo_both[:, b, :, :] for b in range(2)]
+        wo_raw = placed("wo_raw", [P, 2, 4, N], F32)
         for b in range(2):
             wo_rows = wo[512 * b : 512 * b + 512, :].rearrange("(q t e) n -> t q e n", t=4, e=4)
             for t in range(4):
-                nc.sync.dma_start(wo_raw[b][:, t, :], wo_rows[t])
-
-        fetched = [
-            spare,
-            lane[1][:, 2 * S - P : 3 * S - P],
-            z_pairs[0][:, M - P : 2 * M - P],
-            lane[2][:, S - P : 2 * S - P],
-            lane[2][:, 2 * S - P : 3 * S - P],
-            z_pairs[0][:, 2 * M - P : 3 * M - P],
-            z_pairs[1][:, M - P : 2 * M - P],
-        ]
-        weighed = {2: heat[0], 3: lane[0][:, 0:S]}
-
-        def weigh_pair(j):
-            both = lane[j + 1][:, 0 : 2 * S]
-            nc.gpsimd.tensor_tensor(both, heats[j][:], weights[j][:].rearrange("p t j -> p (t j)"), ALU.mult)
-            for side in range(2):
-                weighed[4 + 2 * j + side] = both[:, S * side : S * (side + 1)]
+                nc.sync.dma_start(wo_raw[:, b, t, :], wo_rows[t])
 
         def put(i):
-            nc.vector.tensor_copy(pages[PAGE_OF[i]][:].indirect(list2[:]), weighed[i][:])
+            nc.vector.tensor_copy(pages[PAGE_OF[i]][:].indirect(list2[:]), weighed[i])
 
         def put_fused(i, lo, hi, values):
             nc.vector.tensor_tensor(
-                pages[i][:].indirect(list2[:, lo // 16 : hi // 16]), values, first_weight[i][:, lo:hi], ALU.mult
+                pages[PAGE_OF[i]][:].indirect(list2[:, lo // 16 : hi // 16]), values, first_weight[i][:, lo:hi], ALU.mult
+            )
+
+        def weigh_pair(j):
+            nc.gpsimd.tensor_tensor(
+                lane[j + 1][:, 0 : 2 * S],
+                z_pairs[0][:, 2 * S * j : 2 * S * (j + 1)],
+                weights[j][:].rearrange("p t j -> p (t j)"),
+                ALU.mult,
             )
 
         turns = held.tile([P, M], F32, name="turns")
-        whole = shared.tile([P, M], U32, name="whole", offset=142 * KIB)
+        whole = placed("whole", [P, M], U32)
+        whole5 = placed("whole5", [P, M], U32)
+        cos = [placed("cos0", [P, 2, M], F32), held.tile([P, 2, M], F32, name="cos1")]
+        works = [placed("works%d" % j, [P, 2, M], F32) for j in range(4)]
 
-        def fetch(i, cuts, banks):
+        def load_works(pair):
+            for side in range(2):
+                b, t = divmod(2 * pair + side, 4)
+                rows = work[512 * b : 512 * b + 512, :].rearrange("(q t e) m -> t q e m", t=4, e=4)
+                nc.sync.dma_start(works[pair][:, side, :], rows[t])
+
+        def fetch(i, banks):
+            nc.vector.tensor_copy(fetched[i], pages[PAGE_OF[i]][:].indirect(list3[:]))
             flipped = []
-            nc.vector.tensor_copy(fetched[i][:], pages[PAGE_OF[i]][:].indirect(list3[:]))
-            for j, (lo, hi) in enumerate(cuts):
-                bank = bank_tile(banks[j], [P, hi - lo])
+            for (lo, hi), j in zip(HALVES, banks):
+                bank = bank_tile(j, [P, BANK])
                 for c in range(lo, hi, P):
                     nc.tensor.transpose(bank[:, c - lo : c - lo + P], fetched[i][:, c : c + P], ident[:])
                 flipped.append(bank)
@@ -236,54 +289,42 @@ def tile_list_buffer_pool_prefetch_kernel(
             nc.scalar.activation(count, x, ACT.Relu, bias=0.25, scale=-1.0 / TURN)
             nc.scalar.activation(u, x, ACT.Relu, bias=CAP / TURN, scale=-1.0 / TURN)
 
-        def cosine(flipped, flip_cuts, cuts, banks, whole, cos_out):
-            start, stop = cuts[0][0], cuts[-1][1]
-            for j, (lo, hi) in enumerate(flip_cuts):
-                split(turns[:, lo:hi], whole[:, lo:hi], flipped[j][:])
-            rest = [bank_tile(banks[j], [P, hi - lo]) for j, (lo, hi) in enumerate(cuts)]
-            for j, (lo, hi) in enumerate(cuts):
-                for c in range(lo, hi, P):
-                    nc.tensor.matmul(
-                        rest[j][:, c - lo : c - lo + P], turns[:, c : c + P], ident[:],
-                        start=(c == lo), stop=False, is_transpose=True,
-                    )
-            nc.scalar.activation(whole[:, start:stop].bitcast(F32), whole[:, start:stop], ACT.Copy, scale=-1.0)
-            for j, (lo, hi) in enumerate(cuts):
-                for c in range(lo, hi, P):
-                    nc.tensor.matmul(
-                        rest[j][:, c - lo : c - lo + P], whole[:, c : c + P].bitcast(F32), ident[:],
-                        start=False, stop=(c == hi - P), is_transpose=True,
-                    )
-            for j, (lo, hi) in enumerate(cuts):
-                nc.scalar.activation(cos_out[:, lo:hi], rest[j][:], ACT.Sin, bias=PHASE, scale=TURN)
+        def cosine(i, flipped, banks, counts):
+            for (lo, hi), bank in zip(HALVES, flipped):
+                split(turns[:, lo:hi], counts[:, lo:hi], bank[:])
+            width = M // len(banks)
+            rest = [bank_tile(j, [P, width]) for j in banks]
+            for c in range(0, M, P):
+                nc.tensor.matmul(
+                    rest[c // width][:, c % width : c % width + P], turns[:, c : c + P], ident[:],
+                    start=(c % width == 0), stop=False, is_transpose=True,
+                )
+            nc.scalar.activation(counts[:].bitcast(F32), counts[:], ACT.Copy, scale=-1.0)
+            for c in range(0, M, P):
+                nc.tensor.matmul(
+                    rest[c // width][:, c % width : c % width + P], counts[:, c : c + P].bitcast(F32), ident[:],
+                    start=False, stop=(c % width == width - P), is_transpose=True,
+                )
+            for j, bank in enumerate(rest):
+                nc.scalar.activation(
+                    cos[i // 2 % 2][:, i % 2, width * j : width * (j + 1)], bank[:], ACT.Sin, bias=PHASE, scale=TURN
+                )
 
-        cos = [shared.tile([P, 2, M], F32, name="cos0", offset=0), held.tile([P, 2, M], F32, name="cos1")]
-        works_at = (44 * KIB, 52 * KIB + BANK, 116 * KIB, 72 * KIB)
-        works = [shared.tile([P, 2, M], F32, name="works%d" % j, offset=works_at[j]) for j in range(4)]
-        cos_last, work_last = cos[1], works[3]
-
-        def pairs(b, pair):
-            return z_pairs[b][:, M * pair : M * (pair + 1)].bitcast(BF16).rearrange("p (m t) -> p m t", t=2)
-
-        def load_works(pair):
-            for side in range(2):
-                load_work(2 * pair + side, works[pair][:, side, :])
-
-        whole5 = shared.tile([P, M], U32, name="whole5", offset=108 * KIB)
-        z = [
-            shared.tile([P, M, 4], BF16, name="z0", align_bytes=64, offset=108 * KIB),
-            held.tile([P, M, 4], BF16, name="z1", align_bytes=64),
-        ]
-        z_w = [held.tile([P, M], U32, name="z_w%d" % b, align_bytes=64) for b in range(2)]
-        z1_s = held.tile([P, M], U8, name="z1_s", align_bytes=64)
-
-        def modulate(pair):
-            nc.gpsimd.tensor_tensor(
-                pairs(pair // 2, pair % 2).rearrange("p (c f) t -> p c t f", f=4),
-                cos[pair % 2][:].rearrange("p t (c f) -> p c t f", f=4),
-                works[pair][:].rearrange("p t (c f) -> p c t f", f=4),
+        def multiply(engine, pair, lo, hi):
+            both = z_pairs[pair // 2][:, M * (pair % 2) : M * (pair % 2 + 1)].bitcast(BF16)
+            engine.tensor_tensor(
+                both.rearrange("p (m t) -> p m t", t=2)[:, lo:hi, :].rearrange("p (c f) t -> p c t f", f=4),
+                cos[pair % 2][:, :, lo:hi].rearrange("p t (c f) -> p c t f", f=4),
+                works[pair][:, :, lo:hi].rearrange("p t (c f) -> p c t f", f=4),
                 ALU.mult,
             )
+
+        z = [placed_mx("z0", [P, M, 4], BF16), held.tile([P, M, 4], BF16, name="z1", align_bytes=64)]
+        z_w = [held.tile([P, M], U32, name="z_w%d" % b, align_bytes=64) for b in range(2)]
+        z1_s = held.tile([P, M], U8, name="z1_s", align_bytes=64)
+        wo_bf = [placed_mx("wo_bf%d" % b, [P, N, 4], BF16) for b in range(2)]
+        wo_w = held.tile([P, 2 * N], U32, name="wo_w", align_bytes=64)
+        wo_s = [placed_mx("wo_s%d" % b, [P, N], U8) for b in range(2)]
 
         def weave(b, lo, hi, word, copy):
             copy(
@@ -292,154 +333,142 @@ def tile_list_buffer_pool_prefetch_kernel(
             )
 
         def quantise(codes, scales, values):
-            nc.vector.quantize_mx(out=codes.bitcast(E4M3), scales=scales, in_=values)
-
-        wo_bf = [
-            shared.tile([P, N, 4], BF16, name="wo_bf%d" % b, align_bytes=64, offset=(84, 90)[b] * KIB)
-            for b in range(2)
-        ]
-        wo_w = held.tile([P, 2 * N], U32, name="wo_w", align_bytes=64)
-
-        def round_wo():
-            for b in range(2):
-                for n_lo in range(0, N, P):
-                    nc.scalar.copy(
-                        wo_bf[b][:, n_lo : n_lo + P, :],
-                        wo_raw[b][:, :, n_lo : n_lo + P].rearrange("p t n -> p n t"),
-                    )
-
-        def fetch_and_cosine(i):
-            cos_out = cos[i // 2 % 2][:, i % 2, :]
-            first_bank = HEAT_BANKS if i == SKEWED else 3
-            flipped = fetch(i, HALVES, (first_bank, first_bank + 1))
-            if i == SKEWED - 2:
-                return lambda: cosine(flipped, HALVES, CHUNKS, (3, 4, HEAT_BANKS, HEAT_BANKS + 1), whole, cos_out)
-            if i == LAST - 1:
-                return lambda: cosine(flipped, HALVES, CHUNKS, (0, 1, 3, 4), whole, cos_out)
-            return lambda: cosine(flipped, HALVES, HALVES, (first_bank, first_bank + 1), whole5 if i == 5 else whole, cos_out)
-
-        wo_s = [shared.tile([P, N], U8, name="wo%d_s" % b, align_bytes=64, offset=(100, 60)[b] * KIB) for b in range(2)]
+            nc.vector.quantize_mx(out=codes.bitcast(E4M3), scales=scales, in_=values.rearrange("p c t -> p (c t)"))
 
         def quantise_wo(b, lo, hi):
-            quantise(
-                wo_w[:, N * b + lo : N * b + hi], wo_s[b][:, lo:hi], wo_bf[b][:, lo:hi, :].rearrange("p n t -> p (n t)")
-            )
+            quantise(wo_w[:, N * b + lo : N * b + hi], wo_s[b][:, lo:hi], wo_bf[b][:, lo:hi, :])
 
         for t in range(2):
             load_weight(weight[t], t, nc.sync)
         load_works(0)
         load_works(1)
+
         for lo, hi in QUARTERS:
-            put_fused(0, lo, hi, heat[0][:, lo:hi])
-        put_fused(1, 0, BANK, heat1[0])
-        nc.vector.tensor_tensor(heat1[1], heat1[1], first_weight[1][:, BANK:S], ALU.mult)
-        put_fused(0, BANK, S, heat[0][:, BANK:S])
-        nc.vector.tensor_copy(pages[1][:].indirect(list2[:, BANK // 16 : S // 16]), heat1[1])
+            put_fused(0, lo, hi, heat0[:, lo:hi])
+        put_fused(1, 0, BANK, heat1_front)
+        nc.vector.tensor_tensor(heat1_back, heat1_back, first_weight[1][:, BANK:S], ALU.mult)
+        put_fused(0, BANK, S, heat0[:, BANK:S])
+        nc.vector.tensor_copy(pages[PAGE_OF[1]][:].indirect(list2[:, BANK // 16 : S // 16]), heat1_back)
         nc.gpsimd.tensor_tensor(weighed[2], heat[2], weight[2], ALU.mult)
-        finish = fetch_and_cosine(0)
-        nc.gpsimd.tensor_tensor(weighed[3][:], heat[3][:], weight[3], ALU.mult)
-        finish()
+
+        flipped = fetch(0, FLIP_BANKS)
+        nc.gpsimd.tensor_tensor(weighed[3], heat[3], weight[3], ALU.mult)
+        cosine(0, flipped, FLIP_BANKS, whole)
         put(2)
-        finish = fetch_and_cosine(1)
+
+        flipped = fetch(1, FLIP_BANKS)
         weigh_pair(0)
-        finish()
-        round_wo()
+        cosine(1, flipped, FLIP_BANKS, whole)
+        for b in range(2):
+            for lo in range(0, N, P):
+                nc.scalar.copy(wo_bf[b][:, lo : lo + P, :], wo_raw[:, b, :, lo : lo + P].rearrange("p t n -> p n t"))
         put(3)
-        finish = fetch_and_cosine(2)
-        modulate(0)
-        finish()
+
+        flipped = fetch(2, FLIP_BANKS)
+        multiply(nc.gpsimd, 0, 0, M)
+        cosine(2, flipped, FLIP_BANKS + SECOND_FLIP_BANKS, whole)
         load_works(2)
         put(4)
-        finish_early = fetch_and_cosine(3)
-        finish = fetch_and_cosine(4)
+
+        flipped = fetch(3, FLIP_BANKS)
+        flipped_next = fetch(4, SECOND_FLIP_BANKS)
         weigh_pair(1)
-        finish_early()
-        finish()
+        cosine(3, flipped, FLIP_BANKS, whole)
+        cosine(4, flipped_next, SECOND_FLIP_BANKS, whole)
         put(5)
         quantise_wo(0, 0, N)
-        finish = fetch_and_cosine(5)
+
+        flipped = fetch(5, FLIP_BANKS)
         load_works(3)
-        modulate(1)
-        finish()
+        multiply(nc.gpsimd, 1, 0, M)
+        cosine(5, flipped, FLIP_BANKS, whole5)
         weave(0, 0, M, U32, nc.scalar.copy)
         put(6)
-        quantise_wo(1, 0, N // 2)
-        finish = fetch_and_cosine(6)
-        quantise_wo(1, N // 2, N)
-        modulate(2)
-        finish()
 
+        quantise_wo(1, 0, N // 2)
+        flipped = fetch(6, FLIP_BANKS)
+        quantise_wo(1, N // 2, N)
+        multiply(nc.gpsimd, 2, 0, M)
+        cosine(6, flipped, SCORE_BANKS[0] + SCORE_BANKS[1], whole)
         put(LAST)
-        z0_s = [shared.tile([P, BANK], U8, name="z0_s%d" % j, align_bytes=64, offset=(116, 140)[j] * KIB) for j in range(2)]
-        fetched.append(shared.tile([P, M], F32, name="x_last", offset=120 * KIB))
+
+        z0_cuts = HALVES[:1] + CHUNKS[2:]
+        z0_s = [placed_mx("z0_s%d" % j, [P, hi - lo], U8) for j, (lo, hi) in enumerate(z0_cuts)]
+        z_planes = [
+            [z0_s[0][:, 0:CHUNK], z0_s[0][:, CHUNK:BANK], z0_s[1][:], z0_s[2][:]],
+            [z1_s[:, lo:hi] for lo, hi in CHUNKS],
+        ]
+        x_last = placed("x_last", [P, M], F32)
+        parts = [placed("parts%d" % j, [P, M], F32) for j in range(2)]
+        u_last = [parts[lo // BANK][:, lo % BANK : lo % BANK + CHUNK] for lo, hi in CHUNKS]
+        n_last = [parts[lo // BANK][:, BANK + lo % BANK : BANK + lo % BANK + CHUNK] for lo, hi in CHUNKS]
+        x_chunk = [x_last[:, lo % (3 * CHUNK) : lo % (3 * CHUNK) + CHUNK] for lo, hi in CHUNKS]
+        sums = {}
 
         def quantise_z0(j):
-            lo, hi = HALVES[j]
-            quantise(z_w[0][:, lo:hi], z0_s[j][:], z[0][:, lo:hi, :].rearrange("p m t -> p (m t)"))
-
-        quantise_z0(0)
-        x_last = fetched[LAST]
-        places = [0, CHUNK, 2 * CHUNK, 0]
-        parts = [shared.tile([P, M], F32, name="parts%d" % j, offset=(140 + 4 * j) * KIB) for j in range(2)]
+            lo, hi = z0_cuts[j]
+            quantise(z_w[0][:, lo:hi], z0_s[j][:], z[0][:, lo:hi, :])
 
         def fetch_last(j):
             lo, hi = CHUNKS[j]
-            x = x_last[:, places[j] : places[j] + CHUNK]
-            nc.vector.tensor_copy(x, pages[PAGE_OF[LAST]][:].indirect(list3[:, lo // 16 : hi // 16]))
-            return x
+            nc.vector.tensor_copy(x_chunk[j], pages[PAGE_OF[LAST]][:].indirect(list3[:, lo // 16 : hi // 16]))
 
-        def cosine_direct(j, x):
+        def subtract_turns(j):
+            split(u_last[j], n_last[j].bitcast(U32), x_chunk[j])
+            nc.vector.tensor_tensor(u_last[j], u_last[j], n_last[j].bitcast(I32), ALU.subtract)
+
+        def sine(j):
             lo, hi = CHUNKS[j]
-            at = lo % BANK
-            u, count = parts[j // 2][:, at : at + CHUNK], parts[j // 2][:, BANK + at : BANK + at + CHUNK]
-            split(u, count.bitcast(U32), x)
-            nc.vector.tensor_tensor(u, u, count.bitcast(I32), ALU.subtract)
-            nc.scalar.activation(cos_last[:, 1, lo:hi], u, ACT.Sin, bias=PHASE, scale=TURN)
+            nc.scalar.activation(cos[LAST // 2 % 2][:, LAST % 2, lo:hi], u_last[j], ACT.Sin, bias=PHASE, scale=TURN)
 
-        first = [fetch_last(j) for j in range(3)]
-        cosine_direct(0, first[0])
-        fourth = fetch_last(3)
-        cosine_direct(1, first[1])
-        cosine_direct(2, first[2])
-        cosine_direct(3, fourth)
-
-        def score(bank, b, n_tile, lo):
+        def score(j, n_tile, b):
+            lo, hi = CHUNKS[j]
             for side in range(2):
                 col = P * (n_tile + side)
                 nc.tensor.matmul_mx(
-                    out=bank[:, side, :],
+                    out=sums[j, n_tile][:, side, :],
                     lhsT=wo_w[:, N * b + col : N * b + col + P].bitcast(E4M3),
                     lhsT_scale=wo_s[b][:, col : col + P],
-                    rhs=z_w[b][:, lo : lo + CHUNK].bitcast(E4M3),
-                    rhs_scale=z0_s[lo // BANK][:, lo % BANK : lo % BANK + CHUNK] if b == 0 else z1_s[:, lo : lo + CHUNK],
+                    rhs=z_w[b][:, lo:hi].bitcast(E4M3),
+                    rhs_scale=z_planes[b][j],
                     start=(b == 0 and side == 0),
                     stop=(b == 1 and side == 1),
                 )
 
-        sums = {}
-        for j, (lo, hi) in enumerate(CHUNKS):
-            if lo == BANK:
-                quantise_z0(1)
+        def finish(j):
+            lo, hi = CHUNKS[j]
             for n_tile in (0, 2):
-                sums[lo, n_tile] = bank_tile(((0, 1), (3, 4), (2, 5), (6, 7))[j][n_tile // 2], [P, 2, CHUNK])
-                score(sums[lo, n_tile], 0, n_tile, lo)
-            nc.vector.tensor_tensor(
-                pairs(1, 1)[:, lo:hi, :].rearrange("p (c f) t -> p c t f", f=4),
-                cos_last[:, :, lo:hi].rearrange("p t (c f) -> p c t f", f=4),
-                work_last[:, :, lo:hi].rearrange("p t (c f) -> p c t f", f=4),
-                ALU.mult,
-            )
+                sums[j, n_tile] = bank_tile(SCORE_BANKS[j][n_tile // 2], [P, 2, CHUNK])
+                score(j, n_tile, 0)
+            multiply(nc.vector, LAST // 2, lo, hi)
             weave(1, lo, hi, I32, nc.vector.tensor_copy)
-            quantise(z_w[1][:, lo:hi], z1_s[:, lo:hi], z[1][:, lo:hi, :].rearrange("p m t -> p (m t)"))
+            quantise(z_w[1][:, lo:hi], z_planes[1][j], z[1][:, lo:hi, :])
             for n_tile in (0, 2):
-                score(sums[lo, n_tile], 1, n_tile, lo)
+                score(j, n_tile, 1)
+
+        quantise_z0(0)
+        for j in range(3):
+            fetch_last(j)
+        subtract_turns(0)
+        sine(0)
+        fetch_last(3)
+        subtract_turns(1)
+        subtract_turns(2)
+        finish(0)
+        sine(1)
+        subtract_turns(3)
+        finish(1)
+        for j in (2, 3):
+            sine(j)
+            quantise_z0(j - 1)
+            finish(j)
 
         out_rows = out.rearrange("(s p) m -> p s m", p=P)
-        for lo, hi in CHUNKS:
+        for j, (lo, hi) in enumerate(CHUNKS):
             for n_tile in (0, 2):
                 staged = held.tile([P, 2, CHUNK], F32, name="staged%d_%d" % (lo, n_tile))
                 if n_tile == 0 or lo < M // 2:
-                    nc.scalar.copy(staged[:], sums[lo, n_tile][:])
+                    nc.scalar.copy(staged[:], sums[j, n_tile][:])
                 else:
-                    nc.vector.tensor_copy(staged[:], sums[lo, n_tile][:])
+                    nc.vector.tensor_copy(staged[:], sums[j, n_tile][:])
                 nc.sync.dma_start(out_rows[:, n_tile : n_tile + 2, lo:hi], staged[:])

@@ -44,31 +44,33 @@ AT = {
     "page1": 8 * KIB,
     "page2": 16 * KIB,
     "z_pairs0": 24 * KIB,
+    "w4_s_raw": 44 * KIB,
     "v_w0": 44 * KIB,
     "v_w1": 48 * KIB,
     "w4_w": 52 * KIB,
-    "planes": 56 * KIB,
+    "tab_s": 56 * KIB,
+    "w4_w_raw": 58 * KIB,
+    "planes0": 56 * KIB,
+    "planes1": 58 * KIB,
     "works0": 44 * KIB,
     "works1": 52 * KIB + 512,
     "lane2": 40 * KIB + 512,
     "z_pairs1": 52 * KIB,
     "wo_s1": 60 * KIB,
-    "tab_s": 61 * KIB,
-    "tab_w0": 64 * KIB,
+    "page0": 64 * KIB,
     "heat3": 72 * KIB,
     "lane1": 72 * KIB,
     "works3": 72 * KIB,
     "wo_bf0": 84 * KIB,
-    "scale_rows": 99 * KIB,
-    "first_weight1": 96 * KIB,
+    "picked_s": 95 * KIB + 512,
+    "first_weight0": 96 * KIB,
+    "scale_rows": 100 * KIB,
     "weights1": 100 * KIB,
     "weights0": 90 * KIB,
     "wo_bf1": 90 * KIB,
     "wo_s0": 100 * KIB,
-    "w4_w_raw": 106 * KIB,
-    "picked_s": 125 * KIB + 512,
-    "first_weight0": 122 * KIB,
-    "page0": 126 * KIB,
+    "tab_w0": 125 * KIB,
+    "first_weight1": 122 * KIB,
     "wo_raw": 108 * KIB,
     "whole5": 108 * KIB,
     "z0": 108 * KIB,
@@ -105,9 +107,9 @@ def tile_list_buffer_pool_prefetch_kernel(
         list2 = held.tile([P, S // 16], U16, name="list2")
         list3 = held.tile([P, M // 16], U16, name="list3")
         nc.sync.dma_start(list1[:], offs)
-        tab_s = placed("tab_s", [P, T], U8)
+        tab_s = placed_mx("tab_s", [P, T], U8)
         nc.sync.dma_start(tab_s[0:32, :].bitcast(I32), tab_scales.bitcast(I32).rearrange("a g t -> g a t"))
-        w4_s_raw = held.tile([32, H // 4], I32, name="w4_s_raw")
+        w4_s_raw = placed("w4_s_raw", [32, H // 4], I32)
         nc.sync.dma_start(w4_s_raw[:], w4_scales.bitcast(I32).rearrange("a g c -> g a c"))
         nc.sync.dma_start(list2[:], offs2)
         nc.sync.dma_start(list3[:], offs3)
@@ -122,43 +124,52 @@ def tile_list_buffer_pool_prefetch_kernel(
         nc.vector.memset(tab_s[32:64, :].bitcast(I32), 0)
         nc.vector.memset(tab_s[64:128, :].bitcast(I32), 0)
 
-        planes = placed_mx("planes", [P, 2 * (S + H)], U8)
-        nc.vector.memset(planes[:].bitcast(I32), 0)
+        pages = [placed("page%d" % j, [P, T2], F32) for j in range(3)]
+        nc.vector.memset(pages[0][:], 0.0)
+        planes = [placed_mx("planes%d" % half, [P, S + H], U8) for half in range(2)]
 
         ident = held.tile([P, P], F32, name="ident")
         make_identity(nc, ident[:])
         warm = held.tile([P, 1], F32, name="warm")
-        nc.scalar.activation(warm[:], ident[:, 0:1], ACT.Sin)
+        nc.scalar.activation(warm[:], pages[0][:, 0:1], ACT.Sin)
 
         picked_s = placed("picked_s", [P, S], U8)
         nc.vector.tensor_copy(picked_s[:], tab_s[:].indirect(list1[:]))
         scale_rows = placed("scale_rows", [32, (S + H) // 4], I32)
         nc.vector.tensor_copy(
-            scale_rows[:, S // 4 :].rearrange("p (b t q) -> p b t q", b=2, t=4),
+            scale_rows[:].rearrange("p (b s t q) -> p b s t q", b=2, s=2, t=4)[:, :, 1],
             w4_s_raw[:].rearrange("p (b q t) -> p b t q", b=2, t=4),
         )
-        nc.vector.tensor_copy(scale_rows[:, 0 : S // 4], picked_s[0:32, :].bitcast(I32))
-        for quad in range(4):
-            nc.scalar.dma_start(
-                planes[32 * quad : 32 * quad + 4, :].bitcast(I32).rearrange("p (a c) -> p a c", a=2),
-                scale_rows[8 * quad : 8 * quad + 8, :],
-            )
+        nc.vector.tensor_copy(
+            scale_rows[:].rearrange("p (b s c) -> p b s c", b=2, s=2)[:, :, 0],
+            picked_s[0:32, :].bitcast(I32).rearrange("p (b c) -> p b c", b=2),
+        )
+
+        def move_scales(half):
+            for quad in (0, 2, 1, 3):
+                nc.sync.dma_start(
+                    planes[half][32 * quad : 32 * quad + 4, :].bitcast(I32).rearrange("p (a c) -> p a c", a=2),
+                    scale_rows[8 * quad : 8 * quad + 8, S // 4 * half : S // 4 * (half + 1)],
+                )
+
+        move_scales(0)
 
         wgs_rows = wgs.rearrange("(q t e) j -> t q e j", t=4, e=4)
 
-        def load_weight(dest, t, queue):
+        def load_weight(dest, t):
             for quad in (0, 2, 1, 3):
-                queue.dma_start(dest[32 * quad : 32 * quad + 32, :], wgs_rows[t])
+                nc.sync.dma_start(dest[32 * quad : 32 * quad + 32, :], wgs_rows[t])
 
         first_weight = [placed("first_weight%d" % t, [P, S], F32) for t in range(2)]
-        load_weight(first_weight[0], 0, nc.scalar)
+        load_weight(first_weight[0], 0)
         weights = [placed("weights%d" % j, [P, 2, S], F32) for j in range(2)]
         weight = [weights[t // 2][:, t % 2, :] for t in range(4)]
 
         v_w = [placed_mx("v_w%d" % a, [P, S], U32) for a in range(2)]
         nc.vector.tensor_copy(v_w[0][:], tab_w[0][:].bitcast(U32).indirect(list1[:]))
 
-        load_weight(first_weight[1], 1, nc.sync)
+        load_weight(first_weight[1], 1)
+        move_scales(1)
 
         w4_w = placed_mx("w4_w", [P, 4 * H], U8)
         nc.vector.tensor_copy(
@@ -171,12 +182,11 @@ def tile_list_buffer_pool_prefetch_kernel(
                 v_w[1][:, lo:hi], tab_w[1][:].bitcast(U32).indirect(list1[:, lo // 16 : hi // 16])
             )
 
-        pages = [placed("page%d" % j, [P, T2], F32) for j in range(3)]
-        for j in range(3):
+        for j in (1, 2):
             nc.gpsimd.memset(pages[j][:], 0.0)
 
         for t in (2, 3):
-            load_weight(weight[t], t, nc.sync)
+            load_weight(weight[t], t)
 
         lane = [
             held.tile([P, 2 * S - P], F32, name="lane0"),
@@ -204,42 +214,48 @@ def tile_list_buffer_pool_prefetch_kernel(
 
         pieces_done = []
 
-        def square(i, lo, hi, dest):
-            bank = bank_tile(len(pieces_done) % HEAT_BANKS, [P, hi - lo])
+        def square(i, lo, hi, dest, passes=(1, 0)):
+            bank = bank_tile(3 if (i, lo) == (2, 0) else len(pieces_done) % HEAT_BANKS, [P, hi - lo])
             pieces_done.append((i, lo))
             width = BANK if hi - lo == BANK else P
             for c in range(lo, hi, width):
-                for a in range(2):
-                    col, plane = H * a + P * i, (S + H) * a
+                for a in passes:
+                    col, plane = H * a + P * i, 2 * BANK * a
                     nc.tensor.matmul_mx(
                         out=bank[:, c - lo : c - lo + width],
                         lhsT=w4_w[:, 2 * col : 2 * (col + P)].bitcast(E2M1),
-                        lhsT_scale=planes[:, plane + S + P * i : plane + S + P * (i + 1)],
+                        lhsT_scale=planes[i // 4][:, plane + BANK + P * (i % 4) : plane + BANK + P * (i % 4 + 1)],
                         rhs=v_w[a][:, c : c + width].bitcast(E4M3),
-                        rhs_scale=planes[:, plane + c : plane + c + width],
-                        start=(a == 0),
-                        stop=(a == 1),
+                        rhs_scale=planes[lo // BANK][:, plane + c % BANK : plane + c % BANK + width],
+                        start=(a == passes[0]),
+                        stop=(a == passes[1]),
                     )
             nc.scalar.activation(dest, bank[:], ACT.Square, bias=1.0)
 
-        def halve(values):
-            nc.scalar.activation(values, values, ACT.Identity, bias=-0.5, scale=0.5)
+        def halve(dest, values):
+            nc.scalar.activation(dest, values, ACT.Identity, bias=-0.5, scale=0.5)
 
-        for c in range(0, CHUNK, P):
-            square(0, c, c + P, heat0[:, c : c + P])
-        for c in range(0, CHUNK, P):
-            halve(heat0[:, c : c + P])
-        square(0, CHUNK, BANK, heat0[:, CHUNK:BANK])
-        halve(heat0[:, CHUNK:BANK])
+        def put_fused(i, lo, hi, values):
+            nc.vector.tensor_tensor(
+                pages[PAGE_OF[i]][:].indirect(list2[:, lo // 16 : hi // 16]), values, first_weight[i][:, lo:hi], ALU.mult
+            )
+
+        squared = [heat1_front[:, 0:P], heat1_front[:, P:CHUNK]]
+        for j in range(2):
+            square(0, P * j, P * (j + 1), squared[j], passes=(0, 1))
+        for j in range(2):
+            halve(heat0[:, P * j : P * (j + 1)], squared[j])
+        square(0, CHUNK, BANK, heat1_front[:, 0:CHUNK])
+        halve(heat0[:, CHUNK:BANK], heat1_front[:, 0:CHUNK])
         square(1, 0, BANK, heat1_front)
-        halve(heat1_front)
+        halve(heat1_front, heat1_front)
         square(0, BANK, S, heat0[:, BANK:S])
         square(1, BANK, S, heat1_back)
-        halve(early[:, BANK : S + BANK])
+        halve(early[:, BANK : S + BANK], early[:, BANK : S + BANK])
         for i in range(2, TILES):
             for lo, hi in HALVES:
                 square(i, lo, hi, heat[i][:, lo:hi])
-            halve(heat[i])
+            halve(heat[i], heat[i])
 
         wo_raw = placed("wo_raw", [P, 2, 4, N], F32)
         for b in range(2):
@@ -249,11 +265,6 @@ def tile_list_buffer_pool_prefetch_kernel(
 
         def put(i):
             nc.vector.tensor_copy(pages[PAGE_OF[i]][:].indirect(list2[:]), weighed[i])
-
-        def put_fused(i, lo, hi, values):
-            nc.vector.tensor_tensor(
-                pages[PAGE_OF[i]][:].indirect(list2[:, lo // 16 : hi // 16]), values, first_weight[i][:, lo:hi], ALU.mult
-            )
 
         def weigh_pair(j):
             nc.gpsimd.tensor_tensor(
@@ -339,7 +350,7 @@ def tile_list_buffer_pool_prefetch_kernel(
             quantise(wo_w[:, N * b + lo : N * b + hi], wo_s[b][:, lo:hi], wo_bf[b][:, lo:hi, :])
 
         for t in range(2):
-            load_weight(weight[t], t, nc.sync)
+            load_weight(weight[t], t)
         load_works(0)
         load_works(1)
 

@@ -35,8 +35,9 @@ PAGE_OF = (0, 1, 2, 0, 1, 0, 1, 1)
 HEAT_BANKS = 6
 FLIP_BANKS = (4, 5)
 SECOND_FLIP_BANKS = (6, 7)
-SCORE_BANKS = ((0, 1), FLIP_BANKS, (2, 3), SECOND_FLIP_BANKS)
+SCORE_BANKS = ((0, 1) + FLIP_BANKS, SECOND_FLIP_BANKS, (2, 3), (0, 1) + FLIP_BANKS)
 
+SCALAR_WEAVES = (0,)
 KIB = 1024
 AT = {
     "cos0": 0,
@@ -78,10 +79,14 @@ AT = {
     "z0_s0": 116 * KIB,
     "x_last": 120 * KIB,
     "whole": 142 * KIB,
-    "parts0": 140 * KIB,
-    "parts1": 144 * KIB,
-    "z0_s1": 140 * KIB,
-    "z0_s2": 144 * KIB,
+    "parts0": 140 * KIB + 512,
+    "parts1": 142 * KIB + 512,
+    "parts2": 145 * KIB,
+    "parts3": 147 * KIB,
+    "x_end": 140 * KIB + 512,
+    "z0_s1": 144 * KIB + 512,
+    "z0_s2": 144 * KIB + 768,
+    "z0_s3": 145 * KIB,
 }
 
 
@@ -400,86 +405,121 @@ def tile_list_buffer_pool_prefetch_kernel(
         flipped = fetch(6, FLIP_BANKS)
         quantise_wo(1, N // 2, N)
         multiply(nc.gpsimd, 2, 0, M)
-        cosine(6, flipped, SCORE_BANKS[0] + SCORE_BANKS[1], whole)
+        cosine(6, flipped, SCORE_BANKS[0], whole)
         put(LAST)
 
-        z0_cuts = HALVES[:1] + CHUNKS[2:]
-        z0_s = [placed_mx("z0_s%d" % j, [P, hi - lo], U8) for j, (lo, hi) in enumerate(z0_cuts)]
         z_planes = [
-            [z0_s[0][:, 0:CHUNK], z0_s[0][:, CHUNK:BANK], z0_s[1][:], z0_s[2][:]],
+            [placed_mx("z0_s%d" % j, [P, CHUNK], U8)[:] for j in range(4)],
             [z1_s[:, lo:hi] for lo, hi in CHUNKS],
         ]
-        x_last = placed("x_last", [P, M], F32)
-        parts = [placed("parts%d" % j, [P, M], F32) for j in range(2)]
-        u_last = [parts[lo // BANK][:, lo % BANK : lo % BANK + CHUNK] for lo, hi in CHUNKS]
-        n_last = [parts[lo // BANK][:, BANK + lo % BANK : BANK + lo % BANK + CHUNK] for lo, hi in CHUNKS]
-        x_chunk = [x_last[:, lo % (3 * CHUNK) : lo % (3 * CHUNK) + CHUNK] for lo, hi in CHUNKS]
+        x_last = placed("x_last", [P, BANK], F32)
+        parts = [placed("parts%d" % j, [P, 2, CHUNK], F32) for j in range(4)]
+        u_last = [parts[j][:, 0, :] for j in range(4)]
+        n_last = [parts[j][:, 1, :] for j in range(4)]
+        x_chunk = [x_last[:, 0:CHUNK], x_last[:, CHUNK:BANK], x_last[:, 0:CHUNK], placed("x_end", [P, CHUNK], F32)[:]]
         sums = {}
 
         def quantise_z0(j):
-            lo, hi = z0_cuts[j]
-            quantise(z_w[0][:, lo:hi], z0_s[j][:], z[0][:, lo:hi, :])
+            lo, hi = CHUNKS[j]
+            quantise(z_w[0][:, lo:hi], z_planes[0][j], z[0][:, lo:hi, :])
+            if j < 3:
+                score_first(j)
+
+        def score_first(j):
+            sides = N // P // len(SCORE_BANKS[j])
+            sums[j] = [bank_tile(bank, [P, sides, CHUNK]) for bank in SCORE_BANKS[j]]
+            score(j, 0)
 
         def fetch_last(j):
             lo, hi = CHUNKS[j]
             nc.vector.tensor_copy(x_chunk[j], pages[PAGE_OF[LAST]][:].indirect(list3[:, lo // 16 : hi // 16]))
 
-        def subtract_turns(j):
+        def split_last(j):
             split(u_last[j], n_last[j].bitcast(U32), x_chunk[j])
+
+        def subtract_turns(j):
             nc.vector.tensor_tensor(u_last[j], u_last[j], n_last[j].bitcast(I32), ALU.subtract)
 
         def sine(j):
             lo, hi = CHUNKS[j]
             nc.scalar.activation(cos[LAST // 2 % 2][:, LAST % 2, lo:hi], u_last[j], ACT.Sin, bias=PHASE, scale=TURN)
 
-        def score(j, n_tile, b):
+        def score(j, b):
             lo, hi = CHUNKS[j]
-            for side in range(2):
-                col = P * (n_tile + side)
+            sides = N // P // len(sums[j])
+            for n_tile in range(N // P):
+                col, side = P * n_tile, n_tile % sides
                 nc.tensor.matmul_mx(
-                    out=sums[j, n_tile][:, side, :],
+                    out=sums[j][n_tile // sides][:, side, :],
                     lhsT=wo_w[:, N * b + col : N * b + col + P].bitcast(E4M3),
                     lhsT_scale=wo_s[b][:, col : col + P],
                     rhs=z_w[b][:, lo:hi].bitcast(E4M3),
                     rhs_scale=z_planes[b][j],
                     start=(b == 0 and side == 0),
-                    stop=(b == 1 and side == 1),
+                    stop=(b == 1 and side == sides - 1),
                 )
 
         def finish(j):
             lo, hi = CHUNKS[j]
-            for n_tile in (0, 2):
-                sums[j, n_tile] = bank_tile(SCORE_BANKS[j][n_tile // 2], [P, 2, CHUNK])
-                score(j, n_tile, 0)
-            multiply(nc.vector, LAST // 2, lo, hi)
-            weave(1, lo, hi, I32, nc.vector.tensor_copy)
             quantise(z_w[1][:, lo:hi], z_planes[1][j], z[1][:, lo:hi, :])
-            for n_tile in (0, 2):
-                score(j, n_tile, 1)
-
-        quantise_z0(0)
-        for j in range(3):
-            fetch_last(j)
-        subtract_turns(0)
-        sine(0)
-        fetch_last(3)
-        subtract_turns(1)
-        subtract_turns(2)
-        finish(0)
-        sine(1)
-        subtract_turns(3)
-        finish(1)
-        for j in (2, 3):
-            sine(j)
-            quantise_z0(j - 1)
-            finish(j)
+            score(j, 1)
 
         out_rows = out.rearrange("(s p) m -> p s m", p=P)
-        for j, (lo, hi) in enumerate(CHUNKS):
-            for n_tile in (0, 2):
-                staged = held.tile([P, 2, CHUNK], F32, name="staged%d_%d" % (lo, n_tile))
-                if n_tile == 0 or lo < M // 2:
-                    nc.scalar.copy(staged[:], sums[j, n_tile][:])
+
+        def store(j):
+            lo, hi = CHUNKS[j]
+            sides = N // P // len(sums[j])
+            for place, bank in enumerate(sums[j]):
+                staged = held.tile([P, sides, CHUNK], F32, name="staged%d_%d" % (lo, place))
+                if place % 2 == 0 or lo < M // 2:
+                    nc.scalar.copy(staged[:], bank[:])
                 else:
-                    nc.vector.tensor_copy(staged[:], sums[j, n_tile][:])
-                nc.sync.dma_start(out_rows[:, n_tile : n_tile + 2, lo:hi], staged[:])
+                    nc.vector.tensor_copy(staged[:], bank[:])
+                nc.sync.dma_start(out_rows[:, sides * place : sides * (place + 1), lo:hi], staged[:])
+
+        def product(j):
+            multiply(nc.vector, LAST // 2, *CHUNKS[j])
+
+        def weave_last(j):
+            if j in SCALAR_WEAVES:
+                weave(1, *CHUNKS[j], U32, nc.scalar.copy)
+            else:
+                weave(1, *CHUNKS[j], I32, nc.vector.tensor_copy)
+
+        quantise_z0(0)
+        fetch_last(0)
+        fetch_last(1)
+        quantise_z0(1)
+        quantise_z0(2)
+        split_last(0)
+        subtract_turns(0)
+        split_last(1)
+        sine(0)
+        fetch_last(2)
+        subtract_turns(1)
+        product(0)
+        weave_last(0)
+        fetch_last(3)
+        split_last(2)
+        sine(1)
+        subtract_turns(2)
+        product(1)
+        finish(0)
+        split_last(3)
+        sine(2)
+        subtract_turns(3)
+        weave_last(1)
+        product(2)
+        finish(1)
+        sine(3)
+        weave_last(2)
+        store(0)
+        product(3)
+        finish(2)
+        store(1)
+        weave_last(3)
+        quantise_z0(3)
+        score_first(3)
+        finish(3)
+        store(2)
+        store(3)

@@ -48,9 +48,9 @@ AT = {
     "w4_s_raw": 44 * KIB,
     "v_w0": 44 * KIB,
     "v_w1": 48 * KIB,
-    "w4_w": 52 * KIB,
+    "w4_w0": 52 * KIB,
     "tab_s": 56 * KIB,
-    "w4_w_raw": 58 * KIB,
+    "w4_w_raw0": 58 * KIB,
     "planes0": 56 * KIB,
     "planes1": 58 * KIB,
     "works0": 44 * KIB,
@@ -64,14 +64,17 @@ AT = {
     "works3": 72 * KIB,
     "wo_bf0": 84 * KIB,
     "picked_s": 95 * KIB + 512,
-    "first_weight0": 96 * KIB,
+    "first_weight0_front": 96 * KIB,
+    "w4_w1": 96 * KIB,
     "scale_rows": 100 * KIB,
     "weights1": 100 * KIB,
-    "weights0": 90 * KIB,
-    "wo_bf1": 90 * KIB,
+    "weights0": 128 * KIB,
+    "wo_bf1": 128 * KIB,
     "wo_s0": 100 * KIB,
-    "tab_w0": 125 * KIB,
-    "first_weight1": 122 * KIB,
+    "tab_w0": 124 * KIB,
+    "first_weight1": 126 * KIB,
+    "first_weight0_back": 123 * KIB,
+    "w4_w_raw1": 130 * KIB,
     "wo_raw": 108 * KIB,
     "whole5": 108 * KIB,
     "z0": 108 * KIB,
@@ -113,21 +116,18 @@ def tile_list_buffer_pool_prefetch_kernel(
         list3 = held.tile([P, M // 16], U16, name="list3")
         nc.sync.dma_start(list1[:], offs)
         tab_s = placed_mx("tab_s", [P, T], U8)
-        nc.sync.dma_start(tab_s[0:32, :].bitcast(I32), tab_scales.bitcast(I32).rearrange("a g t -> g a t"))
-        w4_s_raw = placed("w4_s_raw", [32, H // 4], I32)
-        nc.sync.dma_start(w4_s_raw[:], w4_scales.bitcast(I32).rearrange("a g c -> g a c"))
+        nc.sync.dma_start(tab_s[96:128, :].bitcast(I32), tab_scales.bitcast(I32).rearrange("a g t -> g a t"))
+        w4_s_raw = placed("w4_s_raw", [P, H // 4], I32)
+        nc.sync.dma_start(w4_s_raw[96:128, :], w4_scales.bitcast(I32).rearrange("a g c -> g a c"))
         nc.sync.dma_start(list2[:], offs2)
         nc.sync.dma_start(list3[:], offs3)
         tab_w = [placed("tab_w%d" % a, [P, T], I32) for a in range(2)]
-        w4_w_raw = placed("w4_w_raw", [P, H], I32)
+        w4_w_raw = [placed("w4_w_raw%d" % b, [P, 2, H // 4], I32) for b in range(2)]
+        w4_halves = w4_words.bitcast(I32).rearrange("a p (b c) -> b p a c", b=2)
         nc.sync.dma_start(tab_w[0][:], tab_words[0].rearrange("p t i -> p (t i)").bitcast(I32))
-        nc.sync.dma_start(
-            w4_w_raw[:].rearrange("p (a c) -> p a c", a=2),
-            w4_words.bitcast(I32).rearrange("a p c -> p a c"),
-        )
+        nc.sync.dma_start(w4_w_raw[0][:], w4_halves[0])
         nc.sync.dma_start(tab_w[1][:], tab_words[1].rearrange("p t i -> p (t i)").bitcast(I32))
-        nc.vector.memset(tab_s[32:64, :].bitcast(I32), 0)
-        nc.vector.memset(tab_s[64:128, :].bitcast(I32), 0)
+        nc.vector.memset(tab_s[0:96, :].bitcast(I32), 0)
 
         pages = [placed("page%d" % j, [P, T2], F32) for j in range(3)]
         nc.vector.memset(pages[0][:], 0.0)
@@ -140,47 +140,55 @@ def tile_list_buffer_pool_prefetch_kernel(
 
         picked_s = placed("picked_s", [P, S], U8)
         nc.vector.tensor_copy(picked_s[:], tab_s[:].indirect(list1[:]))
-        scale_rows = placed("scale_rows", [32, (S + H) // 4], I32)
+        scale_rows = placed("scale_rows", [P, (S + H) // 4], I32)
         nc.vector.tensor_copy(
-            scale_rows[:].rearrange("p (b s t q) -> p b s t q", b=2, s=2, t=4)[:, :, 1],
-            w4_s_raw[:].rearrange("p (b q t) -> p b t q", b=2, t=4),
+            scale_rows[96:128, :].rearrange("p (b s t q) -> p b s t q", b=2, s=2, t=4)[:, :, 1],
+            w4_s_raw[96:128, :].rearrange("p (b q t) -> p b t q", b=2, t=4),
         )
         nc.vector.tensor_copy(
-            scale_rows[:].rearrange("p (b s c) -> p b s c", b=2, s=2)[:, :, 0],
-            picked_s[0:32, :].bitcast(I32).rearrange("p (b c) -> p b c", b=2),
+            scale_rows[96:128, :].rearrange("p (b s c) -> p b s c", b=2, s=2)[:, :, 0],
+            picked_s[96:128, :].bitcast(I32).rearrange("p (b c) -> p b c", b=2),
         )
 
         def move_scales(half):
             for quad in (0, 2, 1, 3):
                 nc.sync.dma_start(
                     planes[half][32 * quad : 32 * quad + 4, :].bitcast(I32).rearrange("p (a c) -> p a c", a=2),
-                    scale_rows[8 * quad : 8 * quad + 8, S // 4 * half : S // 4 * (half + 1)],
+                    scale_rows[96 + 8 * quad : 96 + 8 * quad + 8, S // 4 * half : S // 4 * (half + 1)],
                 )
 
         move_scales(0)
 
         wgs_rows = wgs.rearrange("(q t e) j -> t q e j", t=4, e=4)
 
-        def load_weight(dest, t):
+        def load_weight(dest, t, lo=0, hi=S):
             for quad in (0, 2, 1, 3):
-                nc.sync.dma_start(dest[32 * quad : 32 * quad + 32, :], wgs_rows[t])
+                nc.sync.dma_start(dest[32 * quad : 32 * quad + 32, :], wgs_rows[t][:, :, lo:hi])
 
-        first_weight = [placed("first_weight%d" % t, [P, S], F32) for t in range(2)]
-        load_weight(first_weight[0], 0)
+        weight0_front = placed("first_weight0_front", [P, BANK], F32)
+        weight0_back = placed("first_weight0_back", [P, BANK], F32)
+        weight1 = placed("first_weight1", [P, S], F32)
+        load_weight(weight0_front, 0, 0, BANK)
         weights = [placed("weights%d" % j, [P, 2, S], F32) for j in range(2)]
         weight = [weights[t // 2][:, t % 2, :] for t in range(4)]
 
         v_w = [placed_mx("v_w%d" % a, [P, S], U32) for a in range(2)]
         nc.vector.tensor_copy(v_w[0][:], tab_w[0][:].bitcast(U32).indirect(list1[:]))
 
-        load_weight(first_weight[1], 1)
+        load_weight(weight1, 1)
+        load_weight(weight0_back, 0, BANK, S)
         move_scales(1)
+        nc.sync.dma_start(w4_w_raw[1][:], w4_halves[1])
 
-        w4_w = placed_mx("w4_w", [P, 4 * H], U8)
-        nc.vector.tensor_copy(
-            w4_w[:].bitcast(I32).rearrange("p (s t q w) -> p s t q w", s=4, t=4, w=2),
-            w4_w_raw[:].rearrange("p (s q t w) -> p s t q w", s=4, t=4, w=2),
-        )
+        w4_w = [placed_mx("w4_w%d" % b, [P, 2 * H], U8) for b in range(2)]
+
+        def sort_w4(b):
+            nc.vector.tensor_copy(
+                w4_w[b][:].bitcast(I32).rearrange("p (a t q w) -> p a t q w", a=2, t=4, w=2),
+                w4_w_raw[b][:].rearrange("p a (q t w) -> p a t q w", t=4, w=2),
+            )
+
+        sort_w4(0)
 
         for lo, hi in QUARTERS + HALVES[1:]:
             nc.vector.tensor_copy(
@@ -225,10 +233,10 @@ def tile_list_buffer_pool_prefetch_kernel(
             width = BANK if hi - lo == BANK else P
             for c in range(lo, hi, width):
                 for a in passes:
-                    col, plane = H * a + P * i, 2 * BANK * a
+                    col, plane = H // 2 * a + P * (i % 4), 2 * BANK * a
                     nc.tensor.matmul_mx(
                         out=bank[:, c - lo : c - lo + width],
-                        lhsT=w4_w[:, 2 * col : 2 * (col + P)].bitcast(E2M1),
+                        lhsT=w4_w[i // 4][:, 2 * col : 2 * (col + P)].bitcast(E2M1),
                         lhsT_scale=planes[i // 4][:, plane + BANK + P * (i % 4) : plane + BANK + P * (i % 4 + 1)],
                         rhs=v_w[a][:, c : c + width].bitcast(E4M3),
                         rhs_scale=planes[lo // BANK][:, plane + c % BANK : plane + c % BANK + width],
@@ -240,9 +248,9 @@ def tile_list_buffer_pool_prefetch_kernel(
         def halve(dest, values):
             nc.scalar.activation(dest, values, ACT.Identity, bias=-0.5, scale=0.5)
 
-        def put_fused(i, lo, hi, values):
+        def put_fused(i, lo, hi, values, factors):
             nc.vector.tensor_tensor(
-                pages[PAGE_OF[i]][:].indirect(list2[:, lo // 16 : hi // 16]), values, first_weight[i][:, lo:hi], ALU.mult
+                pages[PAGE_OF[i]][:].indirect(list2[:, lo // 16 : hi // 16]), values, factors, ALU.mult
             )
 
         squared = [heat1_front[:, 0:P], heat1_front[:, P:CHUNK]]
@@ -258,6 +266,11 @@ def tile_list_buffer_pool_prefetch_kernel(
         square(1, BANK, S, heat1_back)
         halve(early[:, BANK : S + BANK], early[:, BANK : S + BANK])
         for i in range(2, TILES):
+            if i == 4:
+                for lo, hi in QUARTERS:
+                    put_fused(0, lo, hi, heat0[:, lo:hi], weight0_front[:, lo:hi])
+                put_fused(1, 0, BANK, heat1_front, weight1[:, 0:BANK])
+                sort_w4(1)
             for lo, hi in HALVES:
                 square(i, lo, hi, heat[i][:, lo:hi])
             halve(heat[i], heat[i])
@@ -359,11 +372,8 @@ def tile_list_buffer_pool_prefetch_kernel(
         load_works(0)
         load_works(1)
 
-        for lo, hi in QUARTERS:
-            put_fused(0, lo, hi, heat0[:, lo:hi])
-        put_fused(1, 0, BANK, heat1_front)
-        nc.vector.tensor_tensor(heat1_back, heat1_back, first_weight[1][:, BANK:S], ALU.mult)
-        put_fused(0, BANK, S, heat0[:, BANK:S])
+        nc.vector.tensor_tensor(heat1_back, heat1_back, weight1[:, BANK:S], ALU.mult)
+        put_fused(0, BANK, S, heat0[:, BANK:S], weight0_back[:])
         nc.vector.tensor_copy(pages[PAGE_OF[1]][:].indirect(list2[:, BANK // 16 : S // 16]), heat1_back)
         nc.gpsimd.tensor_tensor(weighed[2], heat[2], weight[2], ALU.mult)
 

@@ -76,20 +76,19 @@ AT = {
     "first_weight0_back": 123 * KIB,
     "w4_w_raw1": 130 * KIB,
     "wo_raw": 108 * KIB,
-    "whole5": 108 * KIB,
+    "whole5": 136 * KIB,
     "z0": 108 * KIB,
     "works2": 116 * KIB,
     "z0_s0": 116 * KIB,
     "x_last": 120 * KIB,
-    "whole": 142 * KIB,
-    "parts0": 140 * KIB + 512,
-    "parts1": 142 * KIB + 512,
-    "parts2": 145 * KIB,
-    "parts3": 147 * KIB,
-    "x_end": 140 * KIB + 512,
-    "z0_s1": 144 * KIB + 512,
-    "z0_s2": 144 * KIB + 768,
-    "z0_s3": 145 * KIB,
+    "whole": 124 * KIB,
+    "parts0": 124 * KIB + 256,
+    "parts1": 126 * KIB + 256,
+    "parts2": 128 * KIB + 256,
+    "parts3": 130 * KIB + 256,
+    "x_end": 124 * KIB + 256,
+    "z0_s12": 123 * KIB + 768,
+    "z0_s3": 128 * KIB + 256,
 }
 
 
@@ -176,8 +175,8 @@ def tile_list_buffer_pool_prefetch_kernel(
         nc.vector.tensor_copy(v_w[0][:], tab_w[0][:].bitcast(U32).indirect(list1[:]))
 
         load_weight(weight1, 1)
-        load_weight(weight0_back, 0, BANK, S)
         move_scales(1)
+        load_weight(weight0_back, 0, BANK, S)
         nc.sync.dma_start(w4_w_raw[1][:], w4_halves[1])
 
         w4_w = [placed_mx("w4_w%d" % b, [P, 2 * H], U8) for b in range(2)]
@@ -321,19 +320,17 @@ def tile_list_buffer_pool_prefetch_kernel(
         def cosine(i, flipped, banks, counts):
             for (lo, hi), bank in zip(HALVES, flipped):
                 split(turns[:, lo:hi], counts[:, lo:hi], bank[:])
+                nc.scalar.activation(counts[:, lo:hi].bitcast(F32), counts[:, lo:hi], ACT.Copy, scale=-1.0)
             width = M // len(banks)
             rest = [bank_tile(j, [P, width]) for j in banks]
-            for c in range(0, M, P):
-                nc.tensor.matmul(
-                    rest[c // width][:, c % width : c % width + P], turns[:, c : c + P], ident[:],
-                    start=(c % width == 0), stop=False, is_transpose=True,
-                )
-            nc.scalar.activation(counts[:].bitcast(F32), counts[:], ACT.Copy, scale=-1.0)
-            for c in range(0, M, P):
-                nc.tensor.matmul(
-                    rest[c // width][:, c % width : c % width + P], counts[:, c : c + P].bitcast(F32), ident[:],
-                    start=False, stop=(c % width == width - P), is_transpose=True,
-                )
+            for lo, hi in HALVES:
+                for first, part in ((True, turns[:]), (False, counts[:].bitcast(F32))):
+                    for c in range(lo, hi, P):
+                        nc.tensor.matmul(
+                            rest[c // width][:, c % width : c % width + P], part[:, c : c + P], ident[:],
+                            start=(first and c % width == 0), stop=(not first and c % width == width - P),
+                            is_transpose=True,
+                        )
             for j, bank in enumerate(rest):
                 nc.scalar.activation(
                     cos[i // 2 % 2][:, i % 2, width * j : width * (j + 1)], bank[:], ACT.Sin, bias=PHASE, scale=TURN
@@ -400,26 +397,27 @@ def tile_list_buffer_pool_prefetch_kernel(
         flipped_next = fetch(4, SECOND_FLIP_BANKS)
         weigh_pair(1)
         cosine(3, flipped, FLIP_BANKS, whole)
-        cosine(4, flipped_next, SECOND_FLIP_BANKS, whole)
+        cosine(4, flipped_next, SECOND_FLIP_BANKS, whole5)
         put(5)
         quantise_wo(0, 0, N)
 
-        flipped = fetch(5, FLIP_BANKS)
+        flipped = fetch(5, SECOND_FLIP_BANKS)
         load_works(3)
         multiply(nc.gpsimd, 1, 0, M)
-        cosine(5, flipped, FLIP_BANKS, whole5)
+        cosine(5, flipped, SECOND_FLIP_BANKS, whole)
         weave(0, 0, M, U32, nc.scalar.copy)
         put(6)
 
         quantise_wo(1, 0, N // 2)
-        flipped = fetch(6, FLIP_BANKS)
+        flipped = fetch(6, SECOND_FLIP_BANKS)
         quantise_wo(1, N // 2, N)
         multiply(nc.gpsimd, 2, 0, M)
         cosine(6, flipped, SCORE_BANKS[0], whole)
         put(LAST)
 
+        middle = placed_mx("z0_s12", [P, BANK], U8)
         z_planes = [
-            [placed_mx("z0_s%d" % j, [P, CHUNK], U8)[:] for j in range(4)],
+            [placed_mx("z0_s0", [P, CHUNK], U8)[:], middle[:, 0:CHUNK], middle[:, CHUNK:BANK], placed_mx("z0_s3", [P, CHUNK], U8)[:]],
             [z1_s[:, lo:hi] for lo, hi in CHUNKS],
         ]
         x_last = placed("x_last", [P, BANK], F32)

@@ -32,10 +32,10 @@ QUARTERS = CHUNKS[:2]
 
 PAGE_OF = (0, 1, 2, 0, 1, 0, 1, 1)
 
-HEAT_BANKS = 6
+HEAT_BANKS = (0, 1, 2, 3, 4, 5, 3, 5) + (4, 5) * 5
 FLIP_BANKS = (4, 5)
 SECOND_FLIP_BANKS = (6, 7)
-SCORE_BANKS = ((0, 1) + FLIP_BANKS, SECOND_FLIP_BANKS, (2, 3), (0, 1) + FLIP_BANKS)
+SCORE_BANKS = ((0, 1) + FLIP_BANKS, SECOND_FLIP_BANKS + (2, 3)) * 2
 
 SCALAR_WEAVES = (0,)
 KIB = 1024
@@ -134,8 +134,6 @@ def tile_list_buffer_pool_prefetch_kernel(
 
         ident = held.tile([P, P], F32, name="ident")
         make_identity(nc, ident[:])
-        warm = held.tile([P, 1], F32, name="warm")
-        nc.scalar.activation(warm[:], pages[0][:, 0:1], ACT.Sin)
 
         picked_s = placed("picked_s", [P, S], U8)
         nc.vector.tensor_copy(picked_s[:], tab_s[:].indirect(list1[:]))
@@ -227,7 +225,7 @@ def tile_list_buffer_pool_prefetch_kernel(
         pieces_done = []
 
         def square(i, lo, hi, dest, passes=(1, 0)):
-            bank = bank_tile(3 if (i, lo) == (2, 0) else len(pieces_done) % HEAT_BANKS, [P, hi - lo])
+            bank = bank_tile(HEAT_BANKS[len(pieces_done)], [P, hi - lo])
             pieces_done.append((i, lo))
             width = BANK if hi - lo == BANK else P
             for c in range(lo, hi, width):
@@ -430,7 +428,7 @@ def tile_list_buffer_pool_prefetch_kernel(
         def quantise_z0(j):
             lo, hi = CHUNKS[j]
             quantise(z_w[0][:, lo:hi], z_planes[0][j], z[0][:, lo:hi, :])
-            if j < 3:
+            if j < 2:
                 score_first(j)
 
         def score_first(j):
@@ -520,14 +518,15 @@ def tile_list_buffer_pool_prefetch_kernel(
         product(2)
         finish(1)
         sine(3)
-        weave_last(2)
         store(0)
+        score_first(2)
+        weave_last(2)
         product(3)
         finish(2)
-        store(1)
-        weave_last(3)
         quantise_z0(3)
+        store(1)
         score_first(3)
+        weave_last(3)
         finish(3)
         store(2)
         store(3)

@@ -32,12 +32,12 @@ QUARTERS = CHUNKS[:2]
 
 PAGE_OF = (0, 1, 2, 0, 1, 0, 1, 1)
 
-HEAT_BANKS = (0, 1, 2, 3, 4, 5, 3, 5) + (4, 5) * 5
 FLIP_BANKS = (4, 5)
 SECOND_FLIP_BANKS = (6, 7)
-SCORE_BANKS = ((0, 1) + FLIP_BANKS, SECOND_FLIP_BANKS + (2, 3)) * 2
+HEAT_BANKS = (0, 1, 2, 3, 4, 5) + (3, 5) + FLIP_BANKS * (TILES - 3)
+SCORE_BANKS = ((0, 1) + FLIP_BANKS, SECOND_FLIP_BANKS + (2, 3))
+SCALAR_WEAVES = 2
 
-SCALAR_WEAVES = (0,)
 KIB = 1024
 AT = {
     "cos0": 0,
@@ -64,7 +64,7 @@ AT = {
     "works3": 72 * KIB,
     "wo_bf0": 84 * KIB,
     "picked_s": 95 * KIB + 512,
-    "first_weight0_front": 96 * KIB,
+    "weight0_front": 96 * KIB,
     "w4_w1": 96 * KIB,
     "scale_rows": 100 * KIB,
     "weights1": 100 * KIB,
@@ -72,11 +72,11 @@ AT = {
     "wo_bf1": 128 * KIB,
     "wo_s0": 100 * KIB,
     "tab_w0": 124 * KIB,
-    "first_weight1": 126 * KIB,
-    "first_weight0_back": 123 * KIB,
+    "weight1": 126 * KIB,
+    "weight0_back": 123 * KIB,
     "w4_w_raw1": 130 * KIB,
     "wo_raw": 108 * KIB,
-    "whole5": 136 * KIB,
+    "whole4": 136 * KIB,
     "z0": 108 * KIB,
     "works2": 116 * KIB,
     "z0_s0": 116 * KIB,
@@ -147,8 +147,10 @@ def tile_list_buffer_pool_prefetch_kernel(
             picked_s[96:128, :].bitcast(I32).rearrange("p (b c) -> p b c", b=2),
         )
 
+        quads = (0, 2, 1, 3)
+
         def move_scales(half):
-            for quad in (0, 2, 1, 3):
+            for quad in quads:
                 nc.sync.dma_start(
                     planes[half][32 * quad : 32 * quad + 4, :].bitcast(I32).rearrange("p (a c) -> p a c", a=2),
                     scale_rows[96 + 8 * quad : 96 + 8 * quad + 8, S // 4 * half : S // 4 * (half + 1)],
@@ -159,12 +161,12 @@ def tile_list_buffer_pool_prefetch_kernel(
         wgs_rows = wgs.rearrange("(q t e) j -> t q e j", t=4, e=4)
 
         def load_weight(dest, t, lo=0, hi=S):
-            for quad in (0, 2, 1, 3):
+            for quad in quads:
                 nc.sync.dma_start(dest[32 * quad : 32 * quad + 32, :], wgs_rows[t][:, :, lo:hi])
 
-        weight0_front = placed("first_weight0_front", [P, BANK], F32)
-        weight0_back = placed("first_weight0_back", [P, BANK], F32)
-        weight1 = placed("first_weight1", [P, S], F32)
+        weight0_front = placed("weight0_front", [P, BANK], F32)
+        weight0_back = placed("weight0_back", [P, BANK], F32)
+        weight1 = placed("weight1", [P, S], F32)
         load_weight(weight0_front, 0, 0, BANK)
         weights = [placed("weights%d" % j, [P, 2, S], F32) for j in range(2)]
         weight = [weights[t // 2][:, t % 2, :] for t in range(4)]
@@ -215,7 +217,7 @@ def tile_list_buffer_pool_prefetch_kernel(
         ]
         early = held.tile([P, 2 * S], F32, name="early")
         heat0, heat1_back, heat1_front = early[:, 0:S], early[:, S : S + BANK], early[:, S + BANK : 2 * S]
-        heat = {2: fetched[0], 3: placed("heat3", [P, S], F32)[:]}
+        heat = {2: held.tile([P, S], F32, name="heat2")[:], 3: placed("heat3", [P, S], F32)[:]}
         for i in range(4, TILES):
             heat[i] = z_pairs[0][:, S * (i - 4) : S * (i - 3)]
         weighed = {2: heat0, 3: lane[0][:, 0:S]}
@@ -262,15 +264,20 @@ def tile_list_buffer_pool_prefetch_kernel(
         square(0, BANK, S, heat0[:, BANK:S])
         square(1, BANK, S, heat1_back)
         halve(early[:, BANK : S + BANK], early[:, BANK : S + BANK])
-        for i in range(2, TILES):
-            if i == 4:
-                for lo, hi in QUARTERS:
-                    put_fused(0, lo, hi, heat0[:, lo:hi], weight0_front[:, lo:hi])
-                put_fused(1, 0, BANK, heat1_front, weight1[:, 0:BANK])
-                sort_w4(1)
+
+        def make_heat(i):
             for lo, hi in HALVES:
                 square(i, lo, hi, heat[i][:, lo:hi])
             halve(heat[i], heat[i])
+
+        for i in range(2, TILES // 2):
+            make_heat(i)
+        for lo, hi in QUARTERS:
+            put_fused(0, lo, hi, heat0[:, lo:hi], weight0_front[:, lo:hi])
+        put_fused(1, 0, BANK, heat1_front, weight1[:, 0:BANK])
+        sort_w4(1)
+        for i in range(TILES // 2, TILES):
+            make_heat(i)
 
         wo_raw = placed("wo_raw", [P, 2, 4, N], F32)
         for b in range(2):
@@ -291,7 +298,7 @@ def tile_list_buffer_pool_prefetch_kernel(
 
         turns = held.tile([P, M], F32, name="turns")
         whole = placed("whole", [P, M], U32)
-        whole5 = placed("whole5", [P, M], U32)
+        whole4 = placed("whole4", [P, M], U32)
         cos = [placed("cos0", [P, 2, M], F32), held.tile([P, 2, M], F32, name="cos1")]
         works = [placed("works%d" % j, [P, 2, M], F32) for j in range(4)]
 
@@ -395,7 +402,7 @@ def tile_list_buffer_pool_prefetch_kernel(
         flipped_next = fetch(4, SECOND_FLIP_BANKS)
         weigh_pair(1)
         cosine(3, flipped, FLIP_BANKS, whole)
-        cosine(4, flipped_next, SECOND_FLIP_BANKS, whole5)
+        cosine(4, flipped_next, SECOND_FLIP_BANKS, whole4)
         put(5)
         quantise_wo(0, 0, N)
 
@@ -413,9 +420,10 @@ def tile_list_buffer_pool_prefetch_kernel(
         cosine(6, flipped, SCORE_BANKS[0], whole)
         put(LAST)
 
-        middle = placed_mx("z0_s12", [P, BANK], U8)
+        z0_s12 = placed_mx("z0_s12", [P, 2 * CHUNK], U8)
+        z0_s0, z0_s3 = placed_mx("z0_s0", [P, CHUNK], U8), placed_mx("z0_s3", [P, CHUNK], U8)
         z_planes = [
-            [placed_mx("z0_s0", [P, CHUNK], U8)[:], middle[:, 0:CHUNK], middle[:, CHUNK:BANK], placed_mx("z0_s3", [P, CHUNK], U8)[:]],
+            [z0_s0[:], z0_s12[:, 0:CHUNK], z0_s12[:, CHUNK : 2 * CHUNK], z0_s3[:]],
             [z1_s[:, lo:hi] for lo, hi in CHUNKS],
         ]
         x_last = placed("x_last", [P, BANK], F32)
@@ -428,12 +436,9 @@ def tile_list_buffer_pool_prefetch_kernel(
         def quantise_z0(j):
             lo, hi = CHUNKS[j]
             quantise(z_w[0][:, lo:hi], z_planes[0][j], z[0][:, lo:hi, :])
-            if j < 2:
-                score_first(j)
 
-        def score_first(j):
-            sides = N // P // len(SCORE_BANKS[j])
-            sums[j] = [bank_tile(bank, [P, sides, CHUNK]) for bank in SCORE_BANKS[j]]
+        def open_scores(j):
+            sums[j] = [bank_tile(bank, [P, CHUNK]) for bank in SCORE_BANKS[j % 2]]
             score(j, 0)
 
         def fetch_last(j):
@@ -452,17 +457,16 @@ def tile_list_buffer_pool_prefetch_kernel(
 
         def score(j, b):
             lo, hi = CHUNKS[j]
-            sides = N // P // len(sums[j])
-            for n_tile in range(N // P):
-                col, side = P * n_tile, n_tile % sides
+            for n_tile, bank in enumerate(sums[j]):
+                col = P * n_tile
                 nc.tensor.matmul_mx(
-                    out=sums[j][n_tile // sides][:, side, :],
+                    out=bank[:],
                     lhsT=wo_w[:, N * b + col : N * b + col + P].bitcast(E4M3),
                     lhsT_scale=wo_s[b][:, col : col + P],
                     rhs=z_w[b][:, lo:hi].bitcast(E4M3),
                     rhs_scale=z_planes[b][j],
-                    start=(b == 0 and side == 0),
-                    stop=(b == 1 and side == sides - 1),
+                    start=(b == 0),
+                    stop=(b == 1),
                 )
 
         def finish(j):
@@ -470,32 +474,31 @@ def tile_list_buffer_pool_prefetch_kernel(
             quantise(z_w[1][:, lo:hi], z_planes[1][j], z[1][:, lo:hi, :])
             score(j, 1)
 
-        out_rows = out.rearrange("(s p) m -> p s m", p=P)
-
         def store(j):
             lo, hi = CHUNKS[j]
-            sides = N // P // len(sums[j])
-            for place, bank in enumerate(sums[j]):
-                staged = held.tile([P, sides, CHUNK], F32, name="staged%d_%d" % (lo, place))
-                if place % 2 == 0 or lo < M // 2:
+            for n_tile, bank in enumerate(sums[j]):
+                staged = held.tile([P, CHUNK], F32, name="staged%d_%d" % (j, n_tile))
+                if n_tile % 2 == 0 or lo < M // 2:
                     nc.scalar.copy(staged[:], bank[:])
                 else:
                     nc.vector.tensor_copy(staged[:], bank[:])
-                nc.sync.dma_start(out_rows[:, sides * place : sides * (place + 1), lo:hi], staged[:])
+                nc.sync.dma_start(out[P * n_tile : P * (n_tile + 1), lo:hi], staged[:])
 
         def product(j):
             multiply(nc.vector, LAST // 2, *CHUNKS[j])
 
         def weave_last(j):
-            if j in SCALAR_WEAVES:
+            if j < SCALAR_WEAVES:
                 weave(1, *CHUNKS[j], U32, nc.scalar.copy)
             else:
                 weave(1, *CHUNKS[j], I32, nc.vector.tensor_copy)
 
         quantise_z0(0)
+        open_scores(0)
         fetch_last(0)
         fetch_last(1)
         quantise_z0(1)
+        open_scores(1)
         quantise_z0(2)
         split_last(0)
         subtract_turns(0)
@@ -513,19 +516,19 @@ def tile_list_buffer_pool_prefetch_kernel(
         finish(0)
         split_last(3)
         sine(2)
-        subtract_turns(3)
         weave_last(1)
+        subtract_turns(3)
         product(2)
         finish(1)
         sine(3)
         store(0)
-        score_first(2)
+        open_scores(2)
         weave_last(2)
         product(3)
         finish(2)
         quantise_z0(3)
         store(1)
-        score_first(3)
+        open_scores(3)
         weave_last(3)
         finish(3)
         store(2)

@@ -30,65 +30,75 @@ HALVES = [(0, BANK), (BANK, 2 * BANK)]
 CHUNKS = [(lo, lo + CHUNK) for lo in range(0, M, CHUNK)]
 QUARTERS = CHUNKS[:2]
 
-PAGE_OF = (0, 1, 2, 0, 1, 0, 1, 1)
-
-FLIP_BANKS = (4, 5)
+EARLY = S - CHUNK
+FLIP_BANKS = (0, 1)
 SECOND_FLIP_BANKS = (6, 7)
-HEAT_BANKS = (0, 1, 2, 3, 4, 5) + (3, 5) + FLIP_BANKS * (TILES - 3)
-SCORE_BANKS = ((0, 1) + FLIP_BANKS, SECOND_FLIP_BANKS + (2, 3))
+HEAT_BANKS = (0, 1, 2, 3, 4, 5) + SECOND_FLIP_BANKS + FLIP_BANKS * (TILES - 3)
+SLOT_BANKS = ((2, 3), (4, 5), FLIP_BANKS, SECOND_FLIP_BANKS)
+SCORE_BANKS = ((0, 1, 4, 5), SECOND_FLIP_BANKS + (2, 3))
 SCALAR_WEAVES = 2
 
 KIB = 1024
 AT = {
-    "cos0": 0,
-    "tab_w1": 12 * KIB,
-    "page1": 8 * KIB,
-    "page2": 16 * KIB,
-    "z_pairs0": 24 * KIB,
-    "w4_s_raw": 44 * KIB,
-    "v_w0": 44 * KIB,
-    "v_w1": 48 * KIB,
-    "w4_w0": 52 * KIB,
-    "tab_s": 56 * KIB,
-    "w4_w_raw0": 58 * KIB,
-    "planes0": 56 * KIB,
-    "planes1": 58 * KIB,
-    "works0": 44 * KIB,
-    "works1": 52 * KIB + 512,
-    "lane2": 40 * KIB + 512,
-    "z_pairs1": 52 * KIB,
+    "early": 0,
+    "z0": 0,
+    "x0": 8 * KIB,
+    "weights": 13 * KIB,
+    "z1": 13 * KIB,
+    "works3": 21 * KIB,
+    "tab_w1": 144 * KIB,
+    "wo_raw": 144 * KIB,
+    "lane0": 37 * KIB + 512,
+    "weighed5": 48 * KIB + 512,
+    "heat7": 49 * KIB,
+    "late7": 52 * KIB + 512,
+    "wo_s2": 52 * KIB + 512,
+    "x6": 53 * KIB,
+    "heat6": 57 * KIB,
+    "late6": 60 * KIB,
     "wo_s1": 60 * KIB,
-    "page0": 64 * KIB,
-    "heat3": 72 * KIB,
-    "lane1": 72 * KIB,
-    "works3": 72 * KIB,
-    "wo_bf0": 84 * KIB,
-    "picked_s": 95 * KIB + 512,
-    "weight0_front": 96 * KIB,
-    "w4_w1": 96 * KIB,
-    "scale_rows": 100 * KIB,
-    "weights1": 100 * KIB,
-    "weights0": 128 * KIB,
-    "wo_bf1": 128 * KIB,
-    "wo_s0": 100 * KIB,
-    "tab_w0": 124 * KIB,
-    "weight1": 126 * KIB,
-    "weight0_back": 123 * KIB,
-    "w4_w_raw1": 130 * KIB,
-    "wo_raw": 108 * KIB,
-    "whole4": 136 * KIB,
-    "z0": 108 * KIB,
-    "works2": 116 * KIB,
-    "z0_s0": 116 * KIB,
-    "x_last": 120 * KIB,
-    "whole": 124 * KIB,
-    "parts0": 124 * KIB + 256,
-    "parts1": 126 * KIB + 256,
-    "parts2": 128 * KIB + 256,
-    "parts3": 130 * KIB + 256,
-    "x_end": 124 * KIB + 256,
-    "z0_s12": 123 * KIB + 768,
-    "z0_s3": 128 * KIB + 256,
+    "x5": 60 * KIB + 512,
+    "heat5": 65 * KIB,
+    "wo_s0": 65 * KIB,
+    "x4": 65 * KIB + 512,
+    "weighed4": 70 * KIB,
+    "x2": 74 * KIB,
+    "heat4": 76 * KIB,
+    "x3": 78 * KIB,
+    "heat2": 87 * KIB,
+    "w4_sorted": 87 * KIB + 512,
+    "squared": 90 * KIB,
+    "first": 91 * KIB,
+    "heat3": 93 * KIB,
+    "x1": 94 * KIB,
+    "tab_w0": 31 * KIB,
+    "weight": 100 * KIB,
+    "w4_back": 37 * KIB,
+    "weighed3": 83 * KIB + 512,
+    "lane1": 100 * KIB,
+    "tab_s": 108 * KIB,
+    "planes0": 108 * KIB,
+    "picked_s": 100 * KIB,
+    "page1": 29 * KIB,
+    "w4_s_raw": 128 * KIB,
+    "page2": 128 * KIB,
+    "v_w0": 111 * KIB,
+    "v_w1": 115 * KIB,
+    "works2": 111 * KIB,
+    "z0_s0": 111 * KIB,
+    "x_last": 115 * KIB,
+    "z0_s12": 118 * KIB + 768,
+    "whole": 119 * KIB,
+    "turns": 123 * KIB,
+    "parts0": 119 * KIB + 256,
+    "parts1": 121 * KIB + 256,
+    "parts2": 123 * KIB + 256,
+    "parts3": 125 * KIB + 256,
+    "x_end": 119 * KIB + 256,
+    "z0_s3": 123 * KIB + 256,
+    "turns0": 144 * KIB,
+    "staged": 144 * KIB,
+    "scale_rows": 13 * KIB,
 }
 
 
@@ -113,41 +123,41 @@ def tile_list_buffer_pool_prefetch_kernel(
         list1 = held.tile([P, S // 16], U16, name="list1")
         list2 = held.tile([P, S // 16], U16, name="list2")
         list3 = held.tile([P, M // 16], U16, name="list3")
-        nc.sync.dma_start(list1[:], offs)
         tab_s = placed_mx("tab_s", [P, T], U8)
+        nc.vector.memset(tab_s[0:96, :].bitcast(I32), 0)
+        nc.sync.dma_start(list1[:], offs)
         nc.sync.dma_start(tab_s[96:128, :].bitcast(I32), tab_scales.bitcast(I32).rearrange("a g t -> g a t"))
         w4_s_raw = placed("w4_s_raw", [P, H // 4], I32)
         nc.sync.dma_start(w4_s_raw[96:128, :], w4_scales.bitcast(I32).rearrange("a g c -> g a c"))
+        tab_w = [placed("tab_w%d" % a, [P, T], I32) for a in range(2)]
+        w4_halves = w4_words.bitcast(I32).rearrange("a p (b c) -> b p a c", b=2)
+        w4_front = held.tile([P, 2 * H], U8, name="w4_front", align_bytes=64)
+        nc.sync.dma_start(tab_w[0][:], tab_words[0].rearrange("p t i -> p (t i)").bitcast(I32))
+        quads = (0, 2, 1, 3)
+        nc.sync.dma_start(w4_front[:].bitcast(I32).rearrange("p (a c) -> p a c", a=2), w4_halves[0])
+        nc.sync.dma_start(tab_w[1][:], tab_words[1].rearrange("p t i -> p (t i)").bitcast(I32))
         nc.sync.dma_start(list2[:], offs2)
         nc.sync.dma_start(list3[:], offs3)
-        tab_w = [placed("tab_w%d" % a, [P, T], I32) for a in range(2)]
-        w4_w_raw = [placed("w4_w_raw%d" % b, [P, 2, H // 4], I32) for b in range(2)]
-        w4_halves = w4_words.bitcast(I32).rearrange("a p (b c) -> b p a c", b=2)
-        nc.sync.dma_start(tab_w[0][:], tab_words[0].rearrange("p t i -> p (t i)").bitcast(I32))
-        nc.sync.dma_start(w4_w_raw[0][:], w4_halves[0])
-        nc.sync.dma_start(tab_w[1][:], tab_words[1].rearrange("p t i -> p (t i)").bitcast(I32))
-        nc.vector.memset(tab_s[0:96, :].bitcast(I32), 0)
 
-        pages = [placed("page%d" % j, [P, T2], F32) for j in range(3)]
+        pages = [held.tile([P, T2], F32, name="page0")] + [placed("page%d" % j, [P, T2], F32) for j in (1, 2)]
         nc.vector.memset(pages[0][:], 0.0)
-        planes = [placed_mx("planes%d" % half, [P, S + H], U8) for half in range(2)]
-
         ident = held.tile([P, P], F32, name="ident")
         make_identity(nc, ident[:])
+        planes = [placed_mx("planes0", [P, S + H], U8), held.tile([P, S + H], U8, name="planes1", align_bytes=64)]
+        nc.gpsimd.memset(planes[1][:].bitcast(I32), 0)
 
         picked_s = placed("picked_s", [P, S], U8)
         nc.vector.tensor_copy(picked_s[:], tab_s[:].indirect(list1[:]))
         scale_rows = placed("scale_rows", [P, (S + H) // 4], I32)
+        rows = scale_rows[96:128, :].rearrange("p (b s c) -> p b s c", b=2, s=2)
+        nc.vector.tensor_copy(rows[:, 0, 1, :], w4_s_raw[96:128, 0 : H // 8])
         nc.vector.tensor_copy(
-            scale_rows[96:128, :].rearrange("p (b s t q) -> p b s t q", b=2, s=2, t=4)[:, :, 1],
-            w4_s_raw[96:128, :].rearrange("p (b q t) -> p b t q", b=2, t=4),
+            rows[:, 1, 1, :].rearrange("p (t q) -> p t q", t=4),
+            w4_s_raw[96:128, H // 8 : H // 4].rearrange("p (q t) -> p t q", t=4),
         )
-        nc.vector.tensor_copy(
-            scale_rows[96:128, :].rearrange("p (b s c) -> p b s c", b=2, s=2)[:, :, 0],
-            picked_s[96:128, :].bitcast(I32).rearrange("p (b c) -> p b c", b=2),
-        )
-
-        quads = (0, 2, 1, 3)
+        nc.vector.tensor_copy(rows[:, :, 0, :], picked_s[96:128, :].bitcast(I32).rearrange("p (b c) -> p b c", b=2))
+        for j in (1, 2):
+            nc.gpsimd.memset(pages[j][:], 0.0)
 
         def move_scales(half):
             for quad in quads:
@@ -157,73 +167,31 @@ def tile_list_buffer_pool_prefetch_kernel(
                 )
 
         move_scales(0)
-
-        wgs_rows = wgs.rearrange("(q t e) j -> t q e j", t=4, e=4)
-
-        def load_weight(dest, t, lo=0, hi=S):
-            for quad in quads:
-                nc.sync.dma_start(dest[32 * quad : 32 * quad + 32, :], wgs_rows[t][:, :, lo:hi])
-
-        weight0_front = placed("weight0_front", [P, BANK], F32)
-        weight0_back = placed("weight0_back", [P, BANK], F32)
-        weight1 = placed("weight1", [P, S], F32)
-        load_weight(weight0_front, 0, 0, BANK)
-        weights = [placed("weights%d" % j, [P, 2, S], F32) for j in range(2)]
-        weight = [weights[t // 2][:, t % 2, :] for t in range(4)]
-
         v_w = [placed_mx("v_w%d" % a, [P, S], U32) for a in range(2)]
         nc.vector.tensor_copy(v_w[0][:], tab_w[0][:].bitcast(U32).indirect(list1[:]))
-
-        load_weight(weight1, 1)
+        weight = placed("weight", [P, S], F32)
+        nc.sync.dma_start(weight[:, 0:BANK], wgs[:, 0:BANK])
         move_scales(1)
-        load_weight(weight0_back, 0, BANK, S)
-        nc.sync.dma_start(w4_w_raw[1][:], w4_halves[1])
-
-        w4_w = [placed_mx("w4_w%d" % b, [P, 2 * H], U8) for b in range(2)]
-
-        def sort_w4(b):
-            nc.vector.tensor_copy(
-                w4_w[b][:].bitcast(I32).rearrange("p (a t q w) -> p a t q w", a=2, t=4, w=2),
-                w4_w_raw[b][:].rearrange("p a (q t w) -> p a t q w", t=4, w=2),
-            )
-
-        sort_w4(0)
-
+        nc.sync.dma_start(weight[:, BANK:S], wgs[:, BANK:S])
+        w4_back = placed("w4_back", [P, 2, H // 4], I32)
+        nc.sync.dma_start(w4_back[:], w4_halves[1])
         for lo, hi in QUARTERS + HALVES[1:]:
             nc.vector.tensor_copy(
                 v_w[1][:, lo:hi], tab_w[1][:].bitcast(U32).indirect(list1[:, lo // 16 : hi // 16])
             )
 
-        for j in (1, 2):
-            nc.gpsimd.memset(pages[j][:], 0.0)
+        wo_raw = placed("wo_raw", [P, 2, 4, N], F32)
+        nc.sync.dma_start(wo_raw[:, 0, :, :], wo[0:512, :].rearrange("(p t) n -> p t n", t=4))
+        wo_rows = wo[512:1024, :].rearrange("(q t e) n -> t q e n", t=4, e=4)
+        for t in range(4):
+            nc.sync.dma_start(wo_raw[:, 1, t, :], wo_rows[t])
+        weights = placed("weights", [P, 4, S], F32)
+        wgs_rows = wgs.rearrange("(q t e) j -> t q e j", t=4, e=4)
+        for t in (0, 2, 3, 1):
+            for quad in quads:
+                nc.sync.dma_start(weights[32 * quad : 32 * quad + 32, t, :], wgs_rows[t])
 
-        for t in (2, 3):
-            load_weight(weight[t], t)
-
-        lane = [
-            held.tile([P, 2 * S - P], F32, name="lane0"),
-            placed("lane1", [P, 3 * S - P], F32),
-            placed("lane2", [P, 3 * S - P], F32),
-        ]
-        z_pairs = [placed("z_pairs0", [P, 4 * S], F32), placed("z_pairs1", [P, 2 * M], F32)]
-        fetched = [
-            lane[0][:, S - P : 2 * S - P],
-            lane[1][:, 2 * S - P : 3 * S - P],
-            z_pairs[0][:, M - P : 2 * M - P],
-            lane[2][:, S - P : 2 * S - P],
-            lane[2][:, 2 * S - P : 3 * S - P],
-            z_pairs[0][:, 2 * M - P : 3 * M - P],
-            z_pairs[1][:, M - P : 2 * M - P],
-        ]
-        early = held.tile([P, 2 * S], F32, name="early")
-        heat0, heat1_back, heat1_front = early[:, 0:S], early[:, S : S + BANK], early[:, S + BANK : 2 * S]
-        heat = {2: held.tile([P, S], F32, name="heat2")[:], 3: placed("heat3", [P, S], F32)[:]}
-        for i in range(4, TILES):
-            heat[i] = z_pairs[0][:, S * (i - 4) : S * (i - 3)]
-        weighed = {2: heat0, 3: lane[0][:, 0:S]}
-        for i in range(4, TILES):
-            weighed[i] = lane[i // 2 - 1][:, S * (i % 2) : S * (i % 2 + 1)]
-
+        w4_sorted = placed_mx("w4_sorted", [P, 2 * H], U8)
         pieces_done = []
 
         def square(i, lo, hi, dest, passes=(1, 0)):
@@ -235,7 +203,7 @@ def tile_list_buffer_pool_prefetch_kernel(
                     col, plane = H // 2 * a + P * (i % 4), 2 * BANK * a
                     nc.tensor.matmul_mx(
                         out=bank[:, c - lo : c - lo + width],
-                        lhsT=w4_w[i // 4][:, 2 * col : 2 * (col + P)].bitcast(E2M1),
+                        lhsT=(w4_front, w4_sorted)[i // 4][:, 2 * col : 2 * (col + P)].bitcast(E2M1),
                         lhsT_scale=planes[i // 4][:, plane + BANK + P * (i % 4) : plane + BANK + P * (i % 4 + 1)],
                         rhs=v_w[a][:, c : c + width].bitcast(E4M3),
                         rhs_scale=planes[lo // BANK][:, plane + c % BANK : plane + c % BANK + width],
@@ -247,69 +215,93 @@ def tile_list_buffer_pool_prefetch_kernel(
         def halve(dest, values):
             nc.scalar.activation(dest, values, ACT.Identity, bias=-0.5, scale=0.5)
 
-        def put_fused(i, lo, hi, values, factors):
+        def put_fused(i, lo, hi, values):
             nc.vector.tensor_tensor(
-                pages[PAGE_OF[i]][:].indirect(list2[:, lo // 16 : hi // 16]), values, factors, ALU.mult
+                pages[i % 3][:].indirect(list2[:, lo // 16 : hi // 16]), values, weight[:, lo:hi], ALU.mult
             )
 
-        squared = [heat1_front[:, 0:P], heat1_front[:, P:CHUNK]]
+        def put(i, values, lo=0, hi=S):
+            nc.vector.tensor_copy(pages[i % 3][:].indirect(list2[:, lo // 16 : hi // 16]), values)
+
+        early = placed("early", [P, 2 * S], F32)
+        piece = [early[:, CHUNK * j : CHUNK * (j + 1)] for j in range(8)]
+        first = placed("first", [P, CHUNK], F32)
+        squared = placed("squared", [P, S], F32)
         for j in range(2):
-            square(0, P * j, P * (j + 1), squared[j], passes=(0, 1))
+            square(0, P * j, P * (j + 1), first[:, P * j : P * (j + 1)], passes=(0, 1))
         for j in range(2):
-            halve(heat0[:, P * j : P * (j + 1)], squared[j])
-        square(0, CHUNK, BANK, heat1_front[:, 0:CHUNK])
-        halve(heat0[:, CHUNK:BANK], heat1_front[:, 0:CHUNK])
-        square(1, 0, BANK, heat1_front)
-        halve(heat1_front, heat1_front)
-        square(0, BANK, S, heat0[:, BANK:S])
-        square(1, BANK, S, heat1_back)
-        halve(early[:, BANK : S + BANK], early[:, BANK : S + BANK])
+            halve(piece[0][:, P * j : P * (j + 1)], first[:, P * j : P * (j + 1)])
+        square(1, 0, BANK, squared[:, 0:BANK])
+        square(0, CHUNK, BANK, squared[:, BANK : BANK + CHUNK])
+        halve(piece[1], squared[:, 0:CHUNK])
+        halve(piece[2], squared[:, BANK : BANK + CHUNK])
+        halve(piece[3], squared[:, CHUNK:BANK])
+        square(0, BANK, S, squared[:, 0:BANK])
+        square(1, BANK, S, squared[:, BANK:S])
+        halve(early[:, S : 2 * S], squared[:])
+
+        heat = {i: placed("heat%d" % i, [P, S if i < 6 else EARLY], F32) for i in range(2, TILES)}
+        late = {i: placed("late%d" % i, [P, CHUNK], F32) for i in (6, 7)}
+        spare = held.tile([P, BANK], F32, name="spare")
 
         def make_heat(i):
-            for lo, hi in HALVES:
-                square(i, lo, hi, heat[i][:, lo:hi])
-            halve(heat[i], heat[i])
+            square(i, 0, BANK, heat[i][:, 0:BANK])
+            if i < 6:
+                square(i, BANK, S, heat[i][:, BANK:S])
+                halve(heat[i][:], heat[i][:])
+            else:
+                square(i, BANK, S, spare[:])
+                halve(heat[i][:, 0:BANK], heat[i][:, 0:BANK])
+                halve(heat[i][:, BANK:EARLY], spare[:, 0:CHUNK])
+                halve(late[i][:], spare[:, CHUNK:BANK])
 
-        for i in range(2, TILES // 2):
+        for i in (2, 3):
             make_heat(i)
-        for lo, hi in QUARTERS:
-            put_fused(0, lo, hi, heat0[:, lo:hi], weight0_front[:, lo:hi])
-        put_fused(1, 0, BANK, heat1_front, weight1[:, 0:BANK])
-        sort_w4(1)
-        for i in range(TILES // 2, TILES):
-            make_heat(i)
+        put_fused(0, 0, CHUNK, piece[0])
+        put_fused(1, 0, CHUNK, piece[1])
+        put_fused(0, CHUNK, BANK, piece[2])
+        put_fused(1, CHUNK, BANK, piece[3])
+        put_fused(0, BANK, S, early[:, S : S + BANK])
+        put_fused(1, EARLY, S, piece[7])
 
-        wo_raw = placed("wo_raw", [P, 2, 4, N], F32)
-        for b in range(2):
-            wo_rows = wo[512 * b : 512 * b + 512, :].rearrange("(q t e) n -> t q e n", t=4, e=4)
-            for t in range(4):
-                nc.sync.dma_start(wo_raw[:, b, t, :], wo_rows[t])
+        lane = [placed("lane%d" % j, [P, EARLY + 2 * M], F32) for j in range(2)]
+        weighed = {2: early[:, EARLY : EARLY + S], 6: lane[0][:, 0:S], 7: lane[1][:, 0:S]}
+        for i in (3, 4, 5):
+            weighed[i] = placed("weighed%d" % i, [P, S], F32)[:]
 
-        def put(i):
-            nc.vector.tensor_copy(pages[PAGE_OF[i]][:].indirect(list2[:]), weighed[i])
+        def weigh(i, values, lo=0, hi=S):
+            factors = weight[:, lo:hi] if i < 4 else weights[:, i % 4, lo:hi]
+            nc.gpsimd.tensor_tensor(weighed[i][:, lo:hi], values, factors, ALU.mult)
 
-        def weigh_pair(j):
-            nc.gpsimd.tensor_tensor(
-                lane[j + 1][:, 0 : 2 * S],
-                z_pairs[0][:, 2 * S * j : 2 * S * (j + 1)],
-                weights[j][:].rearrange("p t j -> p (t j)"),
-                ALU.mult,
-            )
+        nc.gpsimd.tensor_tensor(piece[7], piece[6], weight[:, BANK:EARLY], ALU.mult)
+        weigh(2, heat[2][:])
+        nc.gpsimd.tensor_copy(
+            w4_sorted[:].bitcast(I32).rearrange("p (a t q w) -> p a t q w", a=2, t=4, w=2),
+            w4_back[:].rearrange("p a (q t w) -> p a t q w", t=4, w=2),
+        )
+        weigh(3, heat[3][:])
 
-        turns = held.tile([P, M], F32, name="turns")
+        fetched = [placed("x%d" % i, [P, M], F32) for i in range(LAST)]
+        dealt = placed("turns0", [P, 8 * M], F32)
+        turns0 = dealt[:, 0 : 4 * M].rearrange("p (k t r) -> p k t r", t=4, r=P)
+        whole0 = dealt[:, 4 * M : 8 * M].bitcast(U32).rearrange("p (k t r) -> p k t r", t=4, r=P)
+        turns = placed("turns", [P, M], F32)
         whole = placed("whole", [P, M], U32)
-        whole4 = placed("whole4", [P, M], U32)
-        cos = [placed("cos0", [P, 2, M], F32), held.tile([P, 2, M], F32, name="cos1")]
-        works = [placed("works%d" % j, [P, 2, M], F32) for j in range(4)]
+        cos = [held.tile([P, 2, M], F32, name="cos%d" % j) for j in range(2)]
+        works = [lane[j][:, EARLY : EARLY + 2 * M].rearrange("p (t m) -> p t m", t=2) for j in range(2)]
+        works.extend(placed("works%d" % j, [P, 2, M], F32)[:] for j in (2, 3))
 
         def load_works(pair):
-            for side in range(2):
-                b, t = divmod(2 * pair + side, 4)
-                rows = work[512 * b : 512 * b + 512, :].rearrange("(q t e) m -> t q e m", t=4, e=4)
-                nc.sync.dma_start(works[pair][:, side, :], rows[t])
+            if pair < 2:
+                rows = work[0:512, :].rearrange("(p t) m -> p t m", t=4)
+                nc.sync.dma_start(works[pair], rows[:, 2 * pair : 2 * pair + 2, :])
+            else:
+                rows = work[512:1024, :].rearrange("(q t e) m -> t q e m", t=4, e=4)
+                for side in range(2):
+                    nc.sync.dma_start(works[pair][:, side, :], rows[2 * pair - 4 + side])
 
         def fetch(i, banks):
-            nc.vector.tensor_copy(fetched[i], pages[PAGE_OF[i]][:].indirect(list3[:]))
+            nc.vector.tensor_copy(fetched[i][:], pages[i % 3][:].indirect(list3[:]))
             flipped = []
             for (lo, hi), j in zip(HALVES, banks):
                 bank = bank_tile(j, [P, BANK])
@@ -322,24 +314,39 @@ def tile_list_buffer_pool_prefetch_kernel(
             nc.scalar.activation(count, x, ACT.Relu, bias=0.25, scale=-1.0 / TURN)
             nc.scalar.activation(u, x, ACT.Relu, bias=CAP / TURN, scale=-1.0 / TURN)
 
-        def cosine(i, flipped, banks, counts):
-            for (lo, hi), bank in zip(HALVES, flipped):
-                split(turns[:, lo:hi], counts[:, lo:hi], bank[:])
-                nc.scalar.activation(counts[:, lo:hi].bitcast(F32), counts[:, lo:hi], ACT.Copy, scale=-1.0)
+        def negate(count):
+            nc.scalar.activation(count.bitcast(F32), count, ACT.Copy, scale=-1.0)
+
+        def deal(i, flipped):
+            for half, bank in enumerate(flipped):
+                count = whole0[:, 4 * half : 4 * half + 4, :, 32 * i : 32 * i + 32]
+                u = turns0[:, 4 * half : 4 * half + 4, :, 32 * i : 32 * i + 32]
+                split(u, count, bank[:].rearrange("p (k q t) -> p k t q", k=4, t=4))
+                negate(count)
+
+        def turn_back(dest, blocks, banks):
             width = M // len(banks)
             rest = [bank_tile(j, [P, width]) for j in banks]
             for lo, hi in HALVES:
-                for first, part in ((True, turns[:]), (False, counts[:].bitcast(F32))):
+                for part in range(2):
                     for c in range(lo, hi, P):
                         nc.tensor.matmul(
-                            rest[c // width][:, c % width : c % width + P], part[:, c : c + P], ident[:],
-                            start=(first and c % width == 0), stop=(not first and c % width == width - P),
+                            rest[c // width][:, c % width : c % width + P], blocks(c)[part], ident[:],
+                            start=(part == 0 and c % width == 0), stop=(part == 1 and c % width == width - P),
                             is_transpose=True,
                         )
             for j, bank in enumerate(rest):
-                nc.scalar.activation(
-                    cos[i // 2 % 2][:, i % 2, width * j : width * (j + 1)], bank[:], ACT.Sin, bias=PHASE, scale=TURN
-                )
+                nc.scalar.activation(dest[:, width * j : width * (j + 1)], bank[:], ACT.Sin, bias=PHASE, scale=TURN)
+
+        def cosine(i, flipped, banks):
+            for (lo, hi), bank in zip(HALVES, flipped):
+                split(turns[:, lo:hi], whole[:, lo:hi], bank[:])
+                negate(whole[:, lo:hi])
+            turn_back(
+                cos[i // 2 % 2][:, i % 2, :], lambda c: (turns[:, c : c + P], whole[:, c : c + P].bitcast(F32)), banks
+            )
+
+        z_pairs = [held.tile([P, 2 * M], F32, name="z_pairs%d" % b, align_bytes=64) for b in range(2)]
 
         def multiply(engine, pair, lo, hi):
             both = z_pairs[pair // 2][:, M * (pair % 2) : M * (pair % 2 + 1)].bitcast(BF16)
@@ -350,12 +357,20 @@ def tile_list_buffer_pool_prefetch_kernel(
                 ALU.mult,
             )
 
-        z = [placed_mx("z0", [P, M, 4], BF16), held.tile([P, M, 4], BF16, name="z1", align_bytes=64)]
+        z = [placed_mx("z%d" % b, [P, M, 4], BF16) for b in range(2)]
         z_w = [held.tile([P, M], U32, name="z_w%d" % b, align_bytes=64) for b in range(2)]
         z1_s = held.tile([P, M], U8, name="z1_s", align_bytes=64)
-        wo_bf = [placed_mx("wo_bf%d" % b, [P, N, 4], BF16) for b in range(2)]
+        wo_parts = [(0, 0, N), (1, 0, N // 2), (1, N // 2, N)]
+        wo_bf = [
+            z_pairs[j // 2][:, M * (j % 2) : M * (j % 2) + 2 * (hi - lo)].bitcast(BF16).rearrange("p (n t) -> p n t", t=4)
+            for j, (b, lo, hi) in enumerate(wo_parts)
+        ]
         wo_w = held.tile([P, 2 * N], U32, name="wo_w", align_bytes=64)
-        wo_s = [placed_mx("wo_s%d" % b, [P, N], U8) for b in range(2)]
+        wo_s = [placed_mx("wo_s%d" % j, [P, hi - lo], U8) for j, (b, lo, hi) in enumerate(wo_parts)]
+
+        def wo_plane(b, col):
+            j = b + b * col // (N // 2)
+            return wo_s[j][:, col - wo_parts[j][1] : col - wo_parts[j][1] + P]
 
         def weave(b, lo, hi, word, copy):
             copy(
@@ -366,59 +381,48 @@ def tile_list_buffer_pool_prefetch_kernel(
         def quantise(codes, scales, values):
             nc.vector.quantize_mx(out=codes.bitcast(E4M3), scales=scales, in_=values.rearrange("p c t -> p (c t)"))
 
-        def quantise_wo(b, lo, hi):
-            quantise(wo_w[:, N * b + lo : N * b + hi], wo_s[b][:, lo:hi], wo_bf[b][:, lo:hi, :])
+        def quantise_wo(j):
+            b, lo, hi = wo_parts[j]
+            quantise(wo_w[:, N * b + lo : N * b + hi], wo_s[j][:], wo_bf[j])
 
-        for t in range(2):
-            load_weight(weight[t], t)
-        load_works(0)
-        load_works(1)
+        deal(0, fetch(0, FLIP_BANKS))
+        put(1, piece[7], BANK, EARLY)
+        put(2, weighed[2])
+        for j, (b, lo, hi) in enumerate(wo_parts):
+            for c in range(lo, hi, P):
+                nc.scalar.copy(wo_bf[j][:, c - lo : c - lo + P, :], wo_raw[:, b, :, c : c + P].rearrange("p t n -> p n t"))
+        for i in range(4, TILES):
+            make_heat(i)
+        weigh(4, heat[4][:])
+        weigh(6, heat[6][:], 0, EARLY)
+        weigh(7, heat[7][:], 0, EARLY)
+        weigh(5, heat[5][:])
+        for pair in range(3):
+            load_works(pair)
 
-        nc.vector.tensor_tensor(heat1_back, heat1_back, weight1[:, BANK:S], ALU.mult)
-        put_fused(0, BANK, S, heat0[:, BANK:S], weight0_back[:])
-        nc.vector.tensor_copy(pages[PAGE_OF[1]][:].indirect(list2[:, BANK // 16 : S // 16]), heat1_back)
-        nc.gpsimd.tensor_tensor(weighed[2], heat[2], weight[2], ALU.mult)
+        deal(1, fetch(1, FLIP_BANKS))
+        put(3, weighed[3])
+        deal(2, fetch(2, FLIP_BANKS))
+        deal(3, fetch(3, FLIP_BANKS))
+        for t in range(4):
+            turn_back(
+                cos[t // 2][:, t % 2, :],
+                lambda c: (turns0[:, c // P, t, :], whole0[:, c // P, t, :].bitcast(F32)),
+                SLOT_BANKS[t],
+            )
+        put(4, weighed[4])
 
-        flipped = fetch(0, FLIP_BANKS)
-        nc.gpsimd.tensor_tensor(weighed[3], heat[3], weight[3], ALU.mult)
-        cosine(0, flipped, FLIP_BANKS, whole)
-        put(2)
-
-        flipped = fetch(1, FLIP_BANKS)
-        weigh_pair(0)
-        cosine(1, flipped, FLIP_BANKS, whole)
-        for b in range(2):
-            for lo in range(0, N, P):
-                nc.scalar.copy(wo_bf[b][:, lo : lo + P, :], wo_raw[:, b, :, lo : lo + P].rearrange("p t n -> p n t"))
-        put(3)
-
-        flipped = fetch(2, FLIP_BANKS)
-        multiply(nc.gpsimd, 0, 0, M)
-        cosine(2, flipped, FLIP_BANKS + SECOND_FLIP_BANKS, whole)
-        load_works(2)
-        put(4)
-
-        flipped = fetch(3, FLIP_BANKS)
-        flipped_next = fetch(4, SECOND_FLIP_BANKS)
-        weigh_pair(1)
-        cosine(3, flipped, FLIP_BANKS, whole)
-        cosine(4, flipped_next, SECOND_FLIP_BANKS, whole4)
-        put(5)
-        quantise_wo(0, 0, N)
-
-        flipped = fetch(5, SECOND_FLIP_BANKS)
-        load_works(3)
-        multiply(nc.gpsimd, 1, 0, M)
-        cosine(5, flipped, SECOND_FLIP_BANKS, whole)
-        weave(0, 0, M, U32, nc.scalar.copy)
-        put(6)
-
-        quantise_wo(1, 0, N // 2)
-        flipped = fetch(6, SECOND_FLIP_BANKS)
-        quantise_wo(1, N // 2, N)
-        multiply(nc.gpsimd, 2, 0, M)
-        cosine(6, flipped, SCORE_BANKS[0], whole)
-        put(LAST)
+        for i in (4, 5, 6):
+            quantise_wo(i - 4)
+            flipped = fetch(i, SECOND_FLIP_BANKS)
+            multiply(nc.gpsimd, i - 4, 0, M)
+            if i < 6:
+                weigh(i + 2, late[i + 2][:], EARLY, S)
+            cosine(i, flipped, SECOND_FLIP_BANKS if i < 6 else SCORE_BANKS[0])
+            if i == 5:
+                load_works(3)
+                weave(0, 0, M, U32, nc.scalar.copy)
+            put(i + 1, weighed[i + 1])
 
         z0_s12 = placed_mx("z0_s12", [P, 2 * CHUNK], U8)
         z0_s0, z0_s3 = placed_mx("z0_s0", [P, CHUNK], U8), placed_mx("z0_s3", [P, CHUNK], U8)
@@ -432,6 +436,7 @@ def tile_list_buffer_pool_prefetch_kernel(
         n_last = [parts[j][:, 1, :] for j in range(4)]
         x_chunk = [x_last[:, 0:CHUNK], x_last[:, CHUNK:BANK], x_last[:, 0:CHUNK], placed("x_end", [P, CHUNK], F32)[:]]
         sums = {}
+        staged_all = placed("staged", [P, 16 * CHUNK], F32)
 
         def quantise_z0(j):
             lo, hi = CHUNKS[j]
@@ -443,7 +448,7 @@ def tile_list_buffer_pool_prefetch_kernel(
 
         def fetch_last(j):
             lo, hi = CHUNKS[j]
-            nc.vector.tensor_copy(x_chunk[j], pages[PAGE_OF[LAST]][:].indirect(list3[:, lo // 16 : hi // 16]))
+            nc.vector.tensor_copy(x_chunk[j], pages[LAST % 3][:].indirect(list3[:, lo // 16 : hi // 16]))
 
         def split_last(j):
             split(u_last[j], n_last[j].bitcast(U32), x_chunk[j])
@@ -462,7 +467,7 @@ def tile_list_buffer_pool_prefetch_kernel(
                 nc.tensor.matmul_mx(
                     out=bank[:],
                     lhsT=wo_w[:, N * b + col : N * b + col + P].bitcast(E4M3),
-                    lhsT_scale=wo_s[b][:, col : col + P],
+                    lhsT_scale=wo_plane(b, col),
                     rhs=z_w[b][:, lo:hi].bitcast(E4M3),
                     rhs_scale=z_planes[b][j],
                     start=(b == 0),
@@ -477,12 +482,12 @@ def tile_list_buffer_pool_prefetch_kernel(
         def store(j):
             lo, hi = CHUNKS[j]
             for n_tile, bank in enumerate(sums[j]):
-                staged = held.tile([P, CHUNK], F32, name="staged%d_%d" % (j, n_tile))
+                staged = staged_all[:, CHUNK * (4 * j + n_tile) : CHUNK * (4 * j + n_tile + 1)]
                 if n_tile % 2 == 0 or lo < M // 2:
-                    nc.scalar.copy(staged[:], bank[:])
+                    nc.scalar.copy(staged, bank[:])
                 else:
-                    nc.vector.tensor_copy(staged[:], bank[:])
-                nc.sync.dma_start(out[P * n_tile : P * (n_tile + 1), lo:hi], staged[:])
+                    nc.vector.tensor_copy(staged, bank[:])
+                nc.sync.dma_start(out[P * n_tile : P * (n_tile + 1), lo:hi], staged)
 
         def product(j):
             multiply(nc.vector, LAST // 2, *CHUNKS[j])

@@ -72,16 +72,19 @@ AT = {
     "heat3": 93 * KIB,
     "x1": 94 * KIB,
     "tab_w0": 31 * KIB,
+    "w4_next": 104 * KIB,
+    "planes1": 31 * KIB,
+    "ident": 135 * KIB + 512,
     "weight": 100 * KIB,
     "w4_back": 37 * KIB,
     "weighed3": 83 * KIB + 512,
     "lane1": 100 * KIB,
     "tab_s": 108 * KIB,
     "planes0": 108 * KIB,
-    "picked_s": 100 * KIB,
-    "page1": 29 * KIB,
-    "w4_s_raw": 128 * KIB,
-    "page2": 128 * KIB,
+    "picked_s": 103 * KIB + 512,
+    "page1": 136 * KIB,
+    "w4_s_raw": 135 * KIB + 256,
+    "page2": 127 * KIB + 512,
     "v_w0": 111 * KIB,
     "v_w1": 115 * KIB,
     "works2": 111 * KIB,
@@ -124,27 +127,24 @@ def tile_list_buffer_pool_prefetch_kernel(
         list2 = held.tile([P, S // 16], U16, name="list2")
         list3 = held.tile([P, M // 16], U16, name="list3")
         tab_s = placed_mx("tab_s", [P, T], U8)
-        nc.vector.memset(tab_s[0:96, :].bitcast(I32), 0)
+        nc.gpsimd.memset(tab_s[0:96, :].bitcast(I32), 0)
         nc.sync.dma_start(list1[:], offs)
         nc.sync.dma_start(tab_s[96:128, :].bitcast(I32), tab_scales.bitcast(I32).rearrange("a g t -> g a t"))
         w4_s_raw = placed("w4_s_raw", [P, H // 4], I32)
         nc.sync.dma_start(w4_s_raw[96:128, :], w4_scales.bitcast(I32).rearrange("a g c -> g a c"))
         tab_w = [placed("tab_w%d" % a, [P, T], I32) for a in range(2)]
         w4_halves = w4_words.bitcast(I32).rearrange("a p (b c) -> b p a c", b=2)
-        w4_front = held.tile([P, 2 * H], U8, name="w4_front", align_bytes=64)
+        w4_first = held.tile([P, 8 * P], U8, name="w4_first", align_bytes=64)
         nc.sync.dma_start(tab_w[0][:], tab_words[0].rearrange("p t i -> p (t i)").bitcast(I32))
         quads = (0, 2, 1, 3)
-        nc.sync.dma_start(w4_front[:].bitcast(I32).rearrange("p (a c) -> p a c", a=2), w4_halves[0])
+        nc.sync.dma_start(w4_first[:].bitcast(I32).rearrange("p (a c) -> p a c", a=2), w4_halves[0][:, :, 0:P])
         nc.sync.dma_start(tab_w[1][:], tab_words[1].rearrange("p t i -> p (t i)").bitcast(I32))
         nc.sync.dma_start(list2[:], offs2)
         nc.sync.dma_start(list3[:], offs3)
 
         pages = [held.tile([P, T2], F32, name="page0")] + [placed("page%d" % j, [P, T2], F32) for j in (1, 2)]
-        nc.vector.memset(pages[0][:], 0.0)
-        ident = held.tile([P, P], F32, name="ident")
-        make_identity(nc, ident[:])
-        planes = [placed_mx("planes0", [P, S + H], U8), held.tile([P, S + H], U8, name="planes1", align_bytes=64)]
-        nc.gpsimd.memset(planes[1][:].bitcast(I32), 0)
+        nc.gpsimd.memset(pages[0][:], 0.0)
+        planes = [placed_mx("planes%d" % half, [P, S + H], U8) for half in range(2)]
 
         picked_s = placed("picked_s", [P, S], U8)
         nc.vector.tensor_copy(picked_s[:], tab_s[:].indirect(list1[:]))
@@ -156,6 +156,8 @@ def tile_list_buffer_pool_prefetch_kernel(
             w4_s_raw[96:128, H // 8 : H // 4].rearrange("p (q t) -> p t q", t=4),
         )
         nc.vector.tensor_copy(rows[:, :, 0, :], picked_s[96:128, :].bitcast(I32).rearrange("p (b c) -> p b c", b=2))
+        ident = placed("ident", [P, P], F32)
+        make_identity(nc, ident[:])
         for j in (1, 2):
             nc.gpsimd.memset(pages[j][:], 0.0)
 
@@ -167,12 +169,15 @@ def tile_list_buffer_pool_prefetch_kernel(
                 )
 
         move_scales(0)
+
         v_w = [placed_mx("v_w%d" % a, [P, S], U32) for a in range(2)]
         nc.vector.tensor_copy(v_w[0][:], tab_w[0][:].bitcast(U32).indirect(list1[:]))
         weight = placed("weight", [P, S], F32)
         nc.sync.dma_start(weight[:, 0:BANK], wgs[:, 0:BANK])
         move_scales(1)
         nc.sync.dma_start(weight[:, BANK:S], wgs[:, BANK:S])
+        w4_next = placed_mx("w4_next", [P, 8 * P], U8)
+        nc.sync.dma_start(w4_next[:].bitcast(I32).rearrange("p (a c) -> p a c", a=2), w4_halves[0][:, :, P:])
         w4_back = placed("w4_back", [P, 2, H // 4], I32)
         nc.sync.dma_start(w4_back[:], w4_halves[1])
         for lo, hi in QUARTERS + HALVES[1:]:
@@ -194,16 +199,21 @@ def tile_list_buffer_pool_prefetch_kernel(
         w4_sorted = placed_mx("w4_sorted", [P, 2 * H], U8)
         pieces_done = []
 
+        def w4_tile(i, a):
+            holder, first_tile, tiles = (w4_first, 0, 2) if i < 2 else (w4_next, 2, 2) if i < 4 else (w4_sorted, 4, 4)
+            col = P * (tiles * a + i - first_tile)
+            return holder[:, 2 * col : 2 * (col + P)]
+
         def square(i, lo, hi, dest, passes=(1, 0)):
             bank = bank_tile(HEAT_BANKS[len(pieces_done)], [P, hi - lo])
             pieces_done.append((i, lo))
             width = BANK if hi - lo == BANK else P
             for c in range(lo, hi, width):
                 for a in passes:
-                    col, plane = H // 2 * a + P * (i % 4), 2 * BANK * a
+                    plane = 2 * BANK * a
                     nc.tensor.matmul_mx(
                         out=bank[:, c - lo : c - lo + width],
-                        lhsT=(w4_front, w4_sorted)[i // 4][:, 2 * col : 2 * (col + P)].bitcast(E2M1),
+                        lhsT=w4_tile(i, a).bitcast(E2M1),
                         lhsT_scale=planes[i // 4][:, plane + BANK + P * (i % 4) : plane + BANK + P * (i % 4 + 1)],
                         rhs=v_w[a][:, c : c + width].bitcast(E4M3),
                         rhs_scale=planes[lo // BANK][:, plane + c % BANK : plane + c % BANK + width],
@@ -234,8 +244,7 @@ def tile_list_buffer_pool_prefetch_kernel(
         square(1, 0, BANK, squared[:, 0:BANK])
         square(0, CHUNK, BANK, squared[:, BANK : BANK + CHUNK])
         halve(piece[1], squared[:, 0:CHUNK])
-        halve(piece[2], squared[:, BANK : BANK + CHUNK])
-        halve(piece[3], squared[:, CHUNK:BANK])
+        halve(early[:, BANK:S], squared[:, CHUNK : BANK + CHUNK])
         square(0, BANK, S, squared[:, 0:BANK])
         square(1, BANK, S, squared[:, BANK:S])
         halve(early[:, S : 2 * S], squared[:])
@@ -259,8 +268,8 @@ def tile_list_buffer_pool_prefetch_kernel(
             make_heat(i)
         put_fused(0, 0, CHUNK, piece[0])
         put_fused(1, 0, CHUNK, piece[1])
-        put_fused(0, CHUNK, BANK, piece[2])
-        put_fused(1, CHUNK, BANK, piece[3])
+        put_fused(0, CHUNK, BANK, piece[3])
+        put_fused(1, CHUNK, BANK, piece[2])
         put_fused(0, BANK, S, early[:, S : S + BANK])
         put_fused(1, EARLY, S, piece[7])
 

@@ -30,10 +30,13 @@ HALVES = [(0, BANK), (BANK, 2 * BANK)]
 CHUNKS = [(lo, lo + CHUNK) for lo in range(0, M, CHUNK)]
 QUARTERS = CHUNKS[:2]
 
-EARLY = S - CHUNK
+LATE = 64
+EARLY = S - LATE
+PAGES = 3
+
 FLIP_BANKS = (0, 1)
 SECOND_FLIP_BANKS = (6, 7)
-HEAT_BANKS = (0, 1, 2, 3, 4, 5) + SECOND_FLIP_BANKS + FLIP_BANKS * (TILES - 3)
+HEAT_BANKS = (0, 1, 2, 3, 4, 5, 6) + (7, 2) + FLIP_BANKS * (TILES - 3)
 SLOT_BANKS = ((2, 3), (4, 5), FLIP_BANKS, SECOND_FLIP_BANKS)
 SCORE_BANKS = ((0, 1, 4, 5), SECOND_FLIP_BANKS + (2, 3))
 SCALAR_WEAVES = 2
@@ -42,66 +45,67 @@ KIB = 1024
 AT = {
     "early": 0,
     "z0": 0,
-    "x0": 8 * KIB,
-    "weights": 13 * KIB,
-    "z1": 13 * KIB,
-    "works3": 21 * KIB,
-    "tab_w1": 144 * KIB,
-    "wo_raw": 144 * KIB,
-    "lane0": 37 * KIB + 512,
-    "weighed5": 48 * KIB + 512,
-    "heat7": 49 * KIB,
-    "late7": 52 * KIB + 512,
-    "wo_s2": 52 * KIB + 512,
-    "x6": 53 * KIB,
-    "heat6": 57 * KIB,
-    "late6": 60 * KIB,
-    "wo_s1": 60 * KIB,
-    "x5": 60 * KIB + 512,
-    "heat5": 65 * KIB,
-    "wo_s0": 65 * KIB,
-    "x4": 65 * KIB + 512,
-    "weighed4": 70 * KIB,
-    "x2": 74 * KIB,
-    "heat4": 76 * KIB,
-    "x3": 78 * KIB,
-    "heat2": 87 * KIB,
-    "w4_sorted": 87 * KIB + 512,
-    "squared": 90 * KIB,
-    "first": 91 * KIB,
-    "heat3": 93 * KIB,
-    "x1": 94 * KIB,
-    "tab_w0": 31 * KIB,
-    "w4_next": 104 * KIB,
-    "planes1": 31 * KIB,
-    "ident": 135 * KIB + 512,
-    "weight": 100 * KIB,
-    "w4_back": 37 * KIB,
-    "weighed3": 83 * KIB + 512,
-    "lane1": 100 * KIB,
-    "tab_s": 108 * KIB,
-    "planes0": 108 * KIB,
-    "picked_s": 103 * KIB + 512,
-    "page1": 136 * KIB,
-    "w4_s_raw": 135 * KIB + 256,
-    "page2": 127 * KIB + 512,
+    "scale_rows": 8 * KIB,
+    "weights": 8 * KIB,
+    "z1": 8 * KIB,
+    "works3": 16 * KIB,
+    "tab_s": 24 * KIB,
+    "planes0": 24 * KIB,
+    "tab_w0": 26 * KIB,
+    "planes1": 26 * KIB,
+    "w4_back": 32 * KIB,
+    "late_weight6": 32 * KIB,
+    "late_weight7": 32 * KIB + 256,
+    "wo_s1": 32 * KIB,
+    "wo_s2": 32 * KIB + 256,
+    "spare6": 43 * KIB,
+    "lane0": 33 * KIB,
+    "weighed4": 44 * KIB + 768,
+    "heat7": 49 * KIB + 256,
+    "weighed5": 49 * KIB,
+    "heat5": 53 * KIB,
+    "wo_s0": 53 * KIB,
+    "x4": 53 * KIB + 512,
+    "back": 65 * KIB,
+    "third": 65 * KIB + 512,
+    "page2": 57 * KIB + 512,
+    "second": 67 * KIB,
+    "front": 66 * KIB + 512,
+    "first": 81 * KIB,
+    "squared": 80 * KIB + 512,
+    "heat2": 77 * KIB,
+    "heat3": 83 * KIB,
+    "w4_sorted": 78 * KIB,
+    "weighed3": 74 * KIB,
+    "x1": 80 * KIB + 512,
+    "heat4": 87 * KIB,
+    "x2": 84 * KIB + 512,
+    "picked_s": 94 * KIB + 512,
+    "weight": 91 * KIB,
+    "w4_next": 95 * KIB,
+    "w4_s_raw": 98 * KIB,
+    "lane1": 90 * KIB,
+    "heat6": 102 * KIB,
+    "spare7": 106 * KIB,
     "v_w0": 111 * KIB,
     "v_w1": 115 * KIB,
     "works2": 111 * KIB,
     "z0_s0": 111 * KIB,
     "x_last": 115 * KIB,
-    "z0_s12": 118 * KIB + 768,
     "whole": 119 * KIB,
     "turns": 123 * KIB,
+    "z0_s12": 118 * KIB + 768,
     "parts0": 119 * KIB + 256,
     "parts1": 121 * KIB + 256,
     "parts2": 123 * KIB + 256,
     "parts3": 125 * KIB + 256,
     "x_end": 119 * KIB + 256,
     "z0_s3": 123 * KIB + 256,
-    "turns0": 144 * KIB,
-    "staged": 144 * KIB,
-    "scale_rows": 13 * KIB,
+    "tab_w1": 132 * KIB,
+    "page1": 128 * KIB,
+    "wo_raw": 136 * KIB,
+    "dealt": 136 * KIB,
+    "staged": 136 * KIB,
 }
 
 
@@ -127,7 +131,7 @@ def tile_list_buffer_pool_prefetch_kernel(
         list2 = held.tile([P, S // 16], U16, name="list2")
         list3 = held.tile([P, M // 16], U16, name="list3")
         tab_s = placed_mx("tab_s", [P, T], U8)
-        nc.gpsimd.memset(tab_s[0:96, :].bitcast(I32), 0)
+        nc.vector.memset(tab_s[0:96, :].bitcast(I32), 0)
         nc.sync.dma_start(list1[:], offs)
         nc.sync.dma_start(tab_s[96:128, :].bitcast(I32), tab_scales.bitcast(I32).rearrange("a g t -> g a t"))
         w4_s_raw = placed("w4_s_raw", [P, H // 4], I32)
@@ -136,30 +140,29 @@ def tile_list_buffer_pool_prefetch_kernel(
         w4_halves = w4_words.bitcast(I32).rearrange("a p (b c) -> b p a c", b=2)
         w4_first = held.tile([P, 8 * P], U8, name="w4_first", align_bytes=64)
         nc.sync.dma_start(tab_w[0][:], tab_words[0].rearrange("p t i -> p (t i)").bitcast(I32))
-        quads = (0, 2, 1, 3)
         nc.sync.dma_start(w4_first[:].bitcast(I32).rearrange("p (a c) -> p a c", a=2), w4_halves[0][:, :, 0:P])
         nc.sync.dma_start(tab_w[1][:], tab_words[1].rearrange("p t i -> p (t i)").bitcast(I32))
         nc.sync.dma_start(list2[:], offs2)
         nc.sync.dma_start(list3[:], offs3)
 
-        pages = [held.tile([P, T2], F32, name="page0")] + [placed("page%d" % j, [P, T2], F32) for j in (1, 2)]
-        nc.gpsimd.memset(pages[0][:], 0.0)
+        pages = [held.tile([P, T2], F32, name="page0")] + [placed("page%d" % j, [P, T2], F32) for j in range(1, PAGES)]
+        nc.vector.memset(pages[0][:], 0.0)
+        ident = held.tile([P, P], F32, name="ident")
+        make_identity(nc, ident[:])
         planes = [placed_mx("planes%d" % half, [P, S + H], U8) for half in range(2)]
 
         picked_s = placed("picked_s", [P, S], U8)
         nc.vector.tensor_copy(picked_s[:], tab_s[:].indirect(list1[:]))
         scale_rows = placed("scale_rows", [P, (S + H) // 4], I32)
-        rows = scale_rows[96:128, :].rearrange("p (b s c) -> p b s c", b=2, s=2)
-        nc.vector.tensor_copy(rows[:, 0, 1, :], w4_s_raw[96:128, 0 : H // 8])
+        sides = scale_rows[96:128, :].rearrange("p (b s c) -> p b s c", b=2, s=2)
+        nc.vector.tensor_copy(sides[:, 0, 1, :], w4_s_raw[96:128, 0 : H // 8])
         nc.vector.tensor_copy(
-            rows[:, 1, 1, :].rearrange("p (t q) -> p t q", t=4),
+            sides[:, 1, 1, :].rearrange("p (t q) -> p t q", t=4),
             w4_s_raw[96:128, H // 8 : H // 4].rearrange("p (q t) -> p t q", t=4),
         )
-        nc.vector.tensor_copy(rows[:, :, 0, :], picked_s[96:128, :].bitcast(I32).rearrange("p (b c) -> p b c", b=2))
-        ident = placed("ident", [P, P], F32)
-        make_identity(nc, ident[:])
-        for j in (1, 2):
-            nc.gpsimd.memset(pages[j][:], 0.0)
+        nc.vector.tensor_copy(sides[:, :, 0, :], picked_s[96:128, :].bitcast(I32).rearrange("p (b c) -> p b c", b=2))
+
+        quads = (0, 2, 1, 3)
 
         def move_scales(half):
             for quad in quads:
@@ -184,6 +187,7 @@ def tile_list_buffer_pool_prefetch_kernel(
             nc.vector.tensor_copy(
                 v_w[1][:, lo:hi], tab_w[1][:].bitcast(U32).indirect(list1[:, lo // 16 : hi // 16])
             )
+        nc.gpsimd.memset(pages[1][:], 0.0)
 
         wo_raw = placed("wo_raw", [P, 2, 4, N], F32)
         nc.sync.dma_start(wo_raw[:, 0, :, :], wo[0:512, :].rearrange("(p t) n -> p t n", t=4))
@@ -192,9 +196,20 @@ def tile_list_buffer_pool_prefetch_kernel(
             nc.sync.dma_start(wo_raw[:, 1, t, :], wo_rows[t])
         weights = placed("weights", [P, 4, S], F32)
         wgs_rows = wgs.rearrange("(q t e) j -> t q e j", t=4, e=4)
-        for t in (0, 2, 3, 1):
+        z_pairs = [
+            held.tile([P, width], F32, name="z_pairs%d" % b, align_bytes=64)
+            for b, width in enumerate((3 * M - P, 2 * M))
+        ]
+        late = {6: z_pairs[0][:, 2 * M : 2 * M + LATE], 7: z_pairs[1][:, M : M + LATE]}
+        late_weight = {i: placed("late_weight%d" % i, [P, LATE], F32) for i in late}
+
+        def load_weight(dest, t, lo, hi):
             for quad in quads:
-                nc.sync.dma_start(weights[32 * quad : 32 * quad + 32, t, :], wgs_rows[t])
+                nc.sync.dma_start(dest[32 * quad : 32 * quad + 32, :], wgs_rows[t][:, :, lo:hi])
+
+        for t in (0, 2, 3, 1):
+            width = EARLY if 4 + t in late else S
+            load_weight(weights[:, t, 0:width], t, 0, width)
 
         w4_sorted = placed_mx("w4_sorted", [P, 2 * H], U8)
         pieces_done = []
@@ -227,71 +242,76 @@ def tile_list_buffer_pool_prefetch_kernel(
 
         def put_fused(i, lo, hi, values):
             nc.vector.tensor_tensor(
-                pages[i % 3][:].indirect(list2[:, lo // 16 : hi // 16]), values, weight[:, lo:hi], ALU.mult
+                pages[i % PAGES][:].indirect(list2[:, lo // 16 : hi // 16]), values, weight[:, lo:hi], ALU.mult
             )
 
         def put(i, values, lo=0, hi=S):
-            nc.vector.tensor_copy(pages[i % 3][:].indirect(list2[:, lo // 16 : hi // 16]), values)
+            nc.vector.tensor_copy(pages[i % PAGES][:].indirect(list2[:, lo // 16 : hi // 16]), values)
 
-        early = placed("early", [P, 2 * S], F32)
-        piece = [early[:, CHUNK * j : CHUNK * (j + 1)] for j in range(8)]
+        early = placed("early", [P, 3 * CHUNK + S], F32)
+        piece = [early[:, CHUNK * j : CHUNK * (j + 1)] for j in range(3)]
+        back0, back1 = [early[:, 3 * CHUNK + lo : 3 * CHUNK + hi] for lo, hi in HALVES]
         first = placed("first", [P, CHUNK], F32)
-        squared = placed("squared", [P, S], F32)
+        squared = placed("squared", [P, BANK + CHUNK], F32)
         for j in range(2):
             square(0, P * j, P * (j + 1), first[:, P * j : P * (j + 1)], passes=(0, 1))
         for j in range(2):
             halve(piece[0][:, P * j : P * (j + 1)], first[:, P * j : P * (j + 1)])
-        square(1, 0, BANK, squared[:, 0:BANK])
-        square(0, CHUNK, BANK, squared[:, BANK : BANK + CHUNK])
-        halve(piece[1], squared[:, 0:CHUNK])
-        halve(early[:, BANK:S], squared[:, CHUNK : BANK + CHUNK])
-        square(0, BANK, S, squared[:, 0:BANK])
-        square(1, BANK, S, squared[:, BANK:S])
-        halve(early[:, S : 2 * S], squared[:])
+        square(0, CHUNK, BANK, squared[:, 0:CHUNK])
+        for lo, hi in QUARTERS:
+            square(1, lo, hi, squared[:, CHUNK + lo : CHUNK + hi])
+        halve(early[:, CHUNK : 3 * CHUNK], squared[:, 0:BANK])
+        second = placed("second", [P, CHUNK], F32)
+        halve(second[:], squared[:, BANK : BANK + CHUNK])
+        back = placed("back", [P, BANK], F32)
+        square(0, BANK, S, back[:])
+        halve(back0, back[:])
+        square(1, BANK, S, squared[:, 0:BANK])
+        halve(back1, squared[:, 0:BANK])
 
-        heat = {i: placed("heat%d" % i, [P, S if i < 6 else EARLY], F32) for i in range(2, TILES)}
-        late = {i: placed("late%d" % i, [P, CHUNK], F32) for i in (6, 7)}
-        spare = held.tile([P, BANK], F32, name="spare")
+        heat = {i: placed("heat%d" % i, [P, EARLY if i in late else S], F32) for i in range(2, TILES)}
+        spare = {i: placed("spare%d" % i, [P, BANK], F32) for i in late}
 
         def make_heat(i):
             square(i, 0, BANK, heat[i][:, 0:BANK])
-            if i < 6:
+            if i not in late:
                 square(i, BANK, S, heat[i][:, BANK:S])
                 halve(heat[i][:], heat[i][:])
             else:
-                square(i, BANK, S, spare[:])
+                square(i, BANK, S, spare[i][:])
+                halve(heat[i][:, BANK:EARLY], spare[i][:, 0 : BANK - LATE])
+                halve(late[i], spare[i][:, BANK - LATE : BANK])
                 halve(heat[i][:, 0:BANK], heat[i][:, 0:BANK])
-                halve(heat[i][:, BANK:EARLY], spare[:, 0:CHUNK])
-                halve(late[i][:], spare[:, CHUNK:BANK])
 
         for i in (2, 3):
             make_heat(i)
         put_fused(0, 0, CHUNK, piece[0])
-        put_fused(1, 0, CHUNK, piece[1])
-        put_fused(0, CHUNK, BANK, piece[3])
-        put_fused(1, CHUNK, BANK, piece[2])
-        put_fused(0, BANK, S, early[:, S : S + BANK])
-        put_fused(1, EARLY, S, piece[7])
+        third = placed("third", [P, CHUNK], F32)
+        nc.vector.tensor_tensor(piece[2], piece[2], weight[:, 0:CHUNK], ALU.mult)
+        put_fused(0, CHUNK, BANK, piece[1])
+        put(1, piece[2], 0, CHUNK)
+        nc.gpsimd.tensor_tensor(third[:], second[:], weight[:, CHUNK:BANK], ALU.mult)
+        nc.gpsimd.memset(pages[2][:], 0.0)
+        put_fused(0, BANK, S, back0)
+        put(1, third[:], CHUNK, BANK)
+        nc.gpsimd.tensor_tensor(back0, back1, weight[:, BANK:S], ALU.mult)
 
         lane = [placed("lane%d" % j, [P, EARLY + 2 * M], F32) for j in range(2)]
-        weighed = {2: early[:, EARLY : EARLY + S], 6: lane[0][:, 0:S], 7: lane[1][:, 0:S]}
+        front = placed("front", [P, 2 * S - P], F32)
+        weighed = {2: front[:, 0:S], 6: lane[0][:, 0:S], 7: lane[1][:, 0:S]}
         for i in (3, 4, 5):
             weighed[i] = placed("weighed%d" % i, [P, S], F32)[:]
 
         def weigh(i, values, lo=0, hi=S):
-            factors = weight[:, lo:hi] if i < 4 else weights[:, i % 4, lo:hi]
+            factors = weight[:, lo:hi] if i < 4 else late_weight[i][:] if lo == EARLY else weights[:, i % 4, lo:hi]
             nc.gpsimd.tensor_tensor(weighed[i][:, lo:hi], values, factors, ALU.mult)
 
-        nc.gpsimd.tensor_tensor(piece[7], piece[6], weight[:, BANK:EARLY], ALU.mult)
-        weigh(2, heat[2][:])
-        nc.gpsimd.tensor_copy(
-            w4_sorted[:].bitcast(I32).rearrange("p (a t q w) -> p a t q w", a=2, t=4, w=2),
-            w4_back[:].rearrange("p a (q t w) -> p a t q w", t=4, w=2),
-        )
-        weigh(3, heat[3][:])
-
-        fetched = [placed("x%d" % i, [P, M], F32) for i in range(LAST)]
-        dealt = placed("turns0", [P, 8 * M], F32)
+        fetched = {i: placed("x%d" % i, [P, M], F32)[:] for i in (1, 2, 4)}
+        fetched[0] = front[:, S - P : 2 * S - P]
+        fetched[3] = lane[1][:, EARLY - P : EARLY - P + M]
+        fetched[5] = z_pairs[0][:, 2 * M - P : 3 * M - P]
+        fetched[6] = z_pairs[1][:, M - P : 2 * M - P]
+        dealt = placed("dealt", [P, 8 * M], F32)
         turns0 = dealt[:, 0 : 4 * M].rearrange("p (k t r) -> p k t r", t=4, r=P)
         whole0 = dealt[:, 4 * M : 8 * M].bitcast(U32).rearrange("p (k t r) -> p k t r", t=4, r=P)
         turns = placed("turns", [P, M], F32)
@@ -309,8 +329,9 @@ def tile_list_buffer_pool_prefetch_kernel(
                 for side in range(2):
                     nc.sync.dma_start(works[pair][:, side, :], rows[2 * pair - 4 + side])
 
-        def fetch(i, banks):
-            nc.vector.tensor_copy(fetched[i][:], pages[i % 3][:].indirect(list3[:]))
+        def fetch(i, banks, cuts=((0, M),)):
+            for lo, hi in cuts:
+                nc.vector.tensor_copy(fetched[i][:, lo:hi], pages[i % PAGES][:].indirect(list3[:, lo // 16 : hi // 16]))
             flipped = []
             for (lo, hi), j in zip(HALVES, banks):
                 bank = bank_tile(j, [P, BANK])
@@ -355,8 +376,6 @@ def tile_list_buffer_pool_prefetch_kernel(
                 cos[i // 2 % 2][:, i % 2, :], lambda c: (turns[:, c : c + P], whole[:, c : c + P].bitcast(F32)), banks
             )
 
-        z_pairs = [held.tile([P, 2 * M], F32, name="z_pairs%d" % b, align_bytes=64) for b in range(2)]
-
         def multiply(engine, pair, lo, hi):
             both = z_pairs[pair // 2][:, M * (pair % 2) : M * (pair % 2 + 1)].bitcast(BF16)
             engine.tensor_tensor(
@@ -371,7 +390,9 @@ def tile_list_buffer_pool_prefetch_kernel(
         z1_s = held.tile([P, M], U8, name="z1_s", align_bytes=64)
         wo_parts = [(0, 0, N), (1, 0, N // 2), (1, N // 2, N)]
         wo_bf = [
-            z_pairs[j // 2][:, M * (j % 2) : M * (j % 2) + 2 * (hi - lo)].bitcast(BF16).rearrange("p (n t) -> p n t", t=4)
+            z_pairs[j // 2][:, M * (j % 2) : M * (j % 2) + 2 * (hi - lo)]
+            .bitcast(BF16)
+            .rearrange("p (n t) -> p n t", t=4)
             for j, (b, lo, hi) in enumerate(wo_parts)
         ]
         wo_w = held.tile([P, 2 * N], U32, name="wo_w", align_bytes=64)
@@ -394,25 +415,37 @@ def tile_list_buffer_pool_prefetch_kernel(
             b, lo, hi = wo_parts[j]
             quantise(wo_w[:, N * b + lo : N * b + hi], wo_s[j][:], wo_bf[j])
 
-        deal(0, fetch(0, FLIP_BANKS))
-        put(1, piece[7], BANK, EARLY)
+        flipped = fetch(0, FLIP_BANKS, HALVES)
+        put(1, back0, BANK, S)
+        weigh(2, heat[2][:])
+        nc.gpsimd.tensor_copy(
+            w4_sorted[:].bitcast(I32).rearrange("p (a t q w) -> p a t q w", a=2, t=4, w=2),
+            w4_back[:].rearrange("p a (q t w) -> p a t q w", t=4, w=2),
+        )
+        weigh(3, heat[3][:])
+        deal(0, flipped)
         put(2, weighed[2])
         for j, (b, lo, hi) in enumerate(wo_parts):
             for c in range(lo, hi, P):
-                nc.scalar.copy(wo_bf[j][:, c - lo : c - lo + P, :], wo_raw[:, b, :, c : c + P].rearrange("p t n -> p n t"))
+                nc.scalar.copy(
+                    wo_bf[j][:, c - lo : c - lo + P, :], wo_raw[:, b, :, c : c + P].rearrange("p t n -> p n t")
+                )
         for i in range(4, TILES):
             make_heat(i)
         weigh(4, heat[4][:])
         weigh(6, heat[6][:], 0, EARLY)
-        weigh(7, heat[7][:], 0, EARLY)
-        weigh(5, heat[5][:])
-        for pair in range(3):
+        for i in late_weight:
+            load_weight(late_weight[i], i % 4, EARLY, S)
+        for pair in (0, 2):
             load_works(pair)
 
         deal(1, fetch(1, FLIP_BANKS))
         put(3, weighed[3])
         deal(2, fetch(2, FLIP_BANKS))
         deal(3, fetch(3, FLIP_BANKS))
+        weigh(7, heat[7][:], 0, EARLY)
+        weigh(5, heat[5][:])
+        load_works(1)
         for t in range(4):
             turn_back(
                 cos[t // 2][:, t % 2, :],
@@ -421,14 +454,14 @@ def tile_list_buffer_pool_prefetch_kernel(
             )
         put(4, weighed[4])
 
-        for i in (4, 5, 6):
+        for i in range(4, LAST):
             quantise_wo(i - 4)
             flipped = fetch(i, SECOND_FLIP_BANKS)
             multiply(nc.gpsimd, i - 4, 0, M)
-            if i < 6:
-                weigh(i + 2, late[i + 2][:], EARLY, S)
-            cosine(i, flipped, SECOND_FLIP_BANKS if i < 6 else SCORE_BANKS[0])
-            if i == 5:
+            if i + 2 in late:
+                weigh(i + 2, late[i + 2], EARLY, S)
+            cosine(i, flipped, SECOND_FLIP_BANKS if i + 1 < LAST else SCORE_BANKS[0])
+            if i - 4 == 1:
                 load_works(3)
                 weave(0, 0, M, U32, nc.scalar.copy)
             put(i + 1, weighed[i + 1])
@@ -445,7 +478,7 @@ def tile_list_buffer_pool_prefetch_kernel(
         n_last = [parts[j][:, 1, :] for j in range(4)]
         x_chunk = [x_last[:, 0:CHUNK], x_last[:, CHUNK:BANK], x_last[:, 0:CHUNK], placed("x_end", [P, CHUNK], F32)[:]]
         sums = {}
-        staged_all = placed("staged", [P, 16 * CHUNK], F32)
+        staged_all = placed("staged", [P, N // P * M], F32)
 
         def quantise_z0(j):
             lo, hi = CHUNKS[j]
@@ -457,7 +490,7 @@ def tile_list_buffer_pool_prefetch_kernel(
 
         def fetch_last(j):
             lo, hi = CHUNKS[j]
-            nc.vector.tensor_copy(x_chunk[j], pages[LAST % 3][:].indirect(list3[:, lo // 16 : hi // 16]))
+            nc.vector.tensor_copy(x_chunk[j], pages[LAST % PAGES][:].indirect(list3[:, lo // 16 : hi // 16]))
 
         def split_last(j):
             split(u_last[j], n_last[j].bitcast(U32), x_chunk[j])

@@ -22,90 +22,30 @@ P = 128
 TILES = H // P
 LAST = TILES - 1
 BANK = 512
+Q = 256
 CAP = 2.5
 TURN = 2.0 * math.pi
 PHASE = math.pi / 2 - CAP
-CHUNK = 256
-HALVES = [(0, BANK), (BANK, 2 * BANK)]
-CHUNKS = [(lo, lo + CHUNK) for lo in range(0, M, CHUNK)]
-QUARTERS = CHUNKS[:2]
-
-LATE = 64
-EARLY = S - LATE
-PAGES = 3
-
-FLIP_BANKS = (0, 1)
-SECOND_FLIP_BANKS = (6, 7)
-HEAT_BANKS = (0, 1, 2, 3, 4, 5, 6) + (7, 2) + FLIP_BANKS * (TILES - 3)
-SLOT_BANKS = ((2, 3), (4, 5), FLIP_BANKS, SECOND_FLIP_BANKS)
-SCORE_BANKS = ((0, 1, 4, 5), SECOND_FLIP_BANKS + (2, 3))
-SCALAR_WEAVES = 2
-
+FLIP_BANKS = ((4, 5), (4, 5), (4, 5), (4, 2), (1, 6), (7, 7), (4, 5, 4, 5))
+BACK_BANKS = {4: (6, 7), 5: (4, 5), 6: (6, 7, 6, 7)}
+SCORE_BANKS = ((6, 7), (4, 5), (0, 1), (2, 3))
+SCALAR_WEAVES = 1
 KIB = 1024
 AT = {
-    "early": 0,
-    "z0": 0,
-    "scale_rows": 8 * KIB,
-    "weights": 8 * KIB,
-    "z1": 8 * KIB,
-    "works3": 16 * KIB,
-    "tab_s": 24 * KIB,
-    "planes0": 24 * KIB,
-    "tab_w0": 26 * KIB,
-    "planes1": 26 * KIB,
-    "w4_back": 32 * KIB,
-    "late_weight6": 32 * KIB,
-    "late_weight7": 32 * KIB + 256,
-    "wo_s1": 32 * KIB,
-    "wo_s2": 32 * KIB + 256,
-    "spare6": 43 * KIB,
-    "lane0": 33 * KIB,
-    "weighed4": 44 * KIB + 768,
-    "heat7": 49 * KIB + 256,
-    "weighed5": 49 * KIB,
-    "heat5": 53 * KIB,
-    "wo_s0": 53 * KIB,
-    "x4": 53 * KIB + 512,
-    "back": 65 * KIB,
-    "third": 65 * KIB + 512,
-    "page2": 57 * KIB + 512,
-    "second": 67 * KIB,
-    "front": 66 * KIB + 512,
-    "first": 81 * KIB,
-    "squared": 80 * KIB + 512,
-    "heat2": 77 * KIB,
-    "heat3": 83 * KIB,
-    "w4_sorted": 78 * KIB,
-    "weighed3": 74 * KIB,
-    "x1": 80 * KIB + 512,
-    "heat4": 87 * KIB,
-    "x2": 84 * KIB + 512,
-    "picked_s": 94 * KIB + 512,
-    "weight": 91 * KIB,
-    "w4_next": 95 * KIB,
-    "w4_s_raw": 98 * KIB,
-    "lane1": 90 * KIB,
-    "heat6": 102 * KIB,
-    "spare7": 106 * KIB,
-    "v_w0": 111 * KIB,
-    "v_w1": 115 * KIB,
-    "works2": 111 * KIB,
-    "z0_s0": 111 * KIB,
-    "x_last": 115 * KIB,
-    "whole": 119 * KIB,
-    "turns": 123 * KIB,
-    "z0_s12": 118 * KIB + 768,
-    "parts0": 119 * KIB + 256,
-    "parts1": 121 * KIB + 256,
-    "parts2": 123 * KIB + 256,
-    "parts3": 125 * KIB + 256,
-    "x_end": 119 * KIB + 256,
-    "z0_s3": 123 * KIB + 256,
-    "tab_w1": 132 * KIB,
-    "page1": 128 * KIB,
-    "wo_raw": 136 * KIB,
-    "dealt": 136 * KIB,
-    "staged": 136 * KIB,
+    "tab_w0": 0, "planes1": 0, "x0": 2, "w4_back": 6, "w4_sorted": 3,
+    "tab_w1": 8, "wo_raw": 8, "cos45": 8, "cos67": 16,
+    "tab_s": 24, "planes0": 24,
+    "scale_rows": 29, "weights0": 26, "weights1": 30, "weights2": 34, "weights3": 38, "wo_w": 26,
+    "weight": 42, "picked_s": 45.5, "w4_next": 46, "w4_first": 47,
+    "ident": 48, "w4_s_raw": 48.25, "page1": 49, "page0": 57,
+    "v_w0": 65, "v_w1": 69, "turns0": 65, "whole0": 67, "whole1": 69, "turns1": 71,
+    "dealt": 73, "x_ring0": 65, "z0_s0": 66, "x_ring1": 66.25, "parts0": 67.25, "z0_s1": 69.25,
+    "parts1": 69.5, "parts2": 71.5, "parts3": 73.5, "z0_s2": 67.25,
+    "z_pairs": 83, "z1": 91, "z_w1": 99, "z1_s": 103,
+    "work0": 105, "heat0": 105, "works2": 121, "works3": 129, "ab": 128,
+    "lane2": 137, "lane6": 137, "lane4": 145, "lane5": 153, "lane3": 161, "lane7": 161, "wo_s": 165,
+    "rest7": 175, "head7": 178,
+    "wo_bf": 175, "cos0": 183, "z0": 191, "z_w0": 199, "staged": 105,
 }
 
 
@@ -118,11 +58,9 @@ def tile_list_buffer_pool_prefetch_kernel(
         shared = ctx.enter_context(tc.tile_pool(name="shared", bufs=1))
         psum = ctx.enter_context(tc.psum_pool(name="psum", bufs=1))
 
-        def placed(name, shape, dtype):
-            return shared.tile(shape, dtype, name=name, offset=AT[name])
-
-        def placed_mx(name, shape, dtype):
-            return shared.tile(shape, dtype, name=name, align_bytes=64, offset=AT[name])
+        def placed(name, shape, dtype, at=None):
+            where = AT[name] if at is None else at
+            return shared.tile(shape, dtype, name=name, align_bytes=64, offset=int(where * KIB))
 
         def bank_tile(j, shape):
             return psum.tile(shape, F32, name="bank%d" % j, tag="bank%d" % j)
@@ -130,39 +68,39 @@ def tile_list_buffer_pool_prefetch_kernel(
         list1 = held.tile([P, S // 16], U16, name="list1")
         list2 = held.tile([P, S // 16], U16, name="list2")
         list3 = held.tile([P, M // 16], U16, name="list3")
-        tab_s = placed_mx("tab_s", [P, T], U8)
-        nc.vector.memset(tab_s[0:96, :].bitcast(I32), 0)
+        tab_s = placed("tab_s", [P, T], U8)
+        nc.gpsimd.memset(tab_s[0:96, :].bitcast(I32), 0)
         nc.sync.dma_start(list1[:], offs)
         nc.sync.dma_start(tab_s[96:128, :].bitcast(I32), tab_scales.bitcast(I32).rearrange("a g t -> g a t"))
         w4_s_raw = placed("w4_s_raw", [P, H // 4], I32)
         nc.sync.dma_start(w4_s_raw[96:128, :], w4_scales.bitcast(I32).rearrange("a g c -> g a c"))
         tab_w = [placed("tab_w%d" % a, [P, T], I32) for a in range(2)]
         w4_halves = w4_words.bitcast(I32).rearrange("a p (b c) -> b p a c", b=2)
-        w4_first = held.tile([P, 8 * P], U8, name="w4_first", align_bytes=64)
+        w4_first = placed("w4_first", [P, 8 * P], U8)
         nc.sync.dma_start(tab_w[0][:], tab_words[0].rearrange("p t i -> p (t i)").bitcast(I32))
+        quads = (0, 2, 1, 3)
         nc.sync.dma_start(w4_first[:].bitcast(I32).rearrange("p (a c) -> p a c", a=2), w4_halves[0][:, :, 0:P])
         nc.sync.dma_start(tab_w[1][:], tab_words[1].rearrange("p t i -> p (t i)").bitcast(I32))
         nc.sync.dma_start(list2[:], offs2)
         nc.sync.dma_start(list3[:], offs3)
 
-        pages = [held.tile([P, T2], F32, name="page0")] + [placed("page%d" % j, [P, T2], F32) for j in range(1, PAGES)]
-        nc.vector.memset(pages[0][:], 0.0)
-        ident = held.tile([P, P], F32, name="ident")
-        make_identity(nc, ident[:])
-        planes = [placed_mx("planes%d" % half, [P, S + H], U8) for half in range(2)]
+        pages = [placed("page%d" % j, [P, T2], F32) for j in range(2)]
+        nc.gpsimd.memset(pages[0][:], 0.0)
+        planes = [placed("planes%d" % half, [P, S + H], U8) for half in range(2)]
 
         picked_s = placed("picked_s", [P, S], U8)
         nc.vector.tensor_copy(picked_s[:], tab_s[:].indirect(list1[:]))
         scale_rows = placed("scale_rows", [P, (S + H) // 4], I32)
-        sides = scale_rows[96:128, :].rearrange("p (b s c) -> p b s c", b=2, s=2)
-        nc.vector.tensor_copy(sides[:, 0, 1, :], w4_s_raw[96:128, 0 : H // 8])
+        rows = scale_rows[96:128, :].rearrange("p (b s c) -> p b s c", b=2, s=2)
+        nc.vector.tensor_copy(rows[:, 0, 1, :], w4_s_raw[96:128, 0 : H // 8])
         nc.vector.tensor_copy(
-            sides[:, 1, 1, :].rearrange("p (t q) -> p t q", t=4),
+            rows[:, 1, 1, :].rearrange("p (t q) -> p t q", t=4),
             w4_s_raw[96:128, H // 8 : H // 4].rearrange("p (q t) -> p t q", t=4),
         )
-        nc.vector.tensor_copy(sides[:, :, 0, :], picked_s[96:128, :].bitcast(I32).rearrange("p (b c) -> p b c", b=2))
-
-        quads = (0, 2, 1, 3)
+        nc.vector.tensor_copy(rows[:, :, 0, :], picked_s[96:128, :].bitcast(I32).rearrange("p (b c) -> p b c", b=2))
+        ident = placed("ident", [P, P], F32)
+        make_identity(nc, ident[:])
+        nc.gpsimd.memset(pages[1][:], 0.0)
 
         def move_scales(half):
             for quad in quads:
@@ -172,69 +110,50 @@ def tile_list_buffer_pool_prefetch_kernel(
                 )
 
         move_scales(0)
-
-        v_w = [placed_mx("v_w%d" % a, [P, S], U32) for a in range(2)]
+        v_w = [placed("v_w%d" % a, [P, S], U32) for a in range(2)]
         nc.vector.tensor_copy(v_w[0][:], tab_w[0][:].bitcast(U32).indirect(list1[:]))
         weight = placed("weight", [P, S], F32)
         nc.sync.dma_start(weight[:, 0:BANK], wgs[:, 0:BANK])
         move_scales(1)
         nc.sync.dma_start(weight[:, BANK:S], wgs[:, BANK:S])
-        w4_next = placed_mx("w4_next", [P, 8 * P], U8)
+        w4_next = placed("w4_next", [P, 8 * P], U8)
         nc.sync.dma_start(w4_next[:].bitcast(I32).rearrange("p (a c) -> p a c", a=2), w4_halves[0][:, :, P:])
         w4_back = placed("w4_back", [P, 2, H // 4], I32)
         nc.sync.dma_start(w4_back[:], w4_halves[1])
-        for lo, hi in QUARTERS + HALVES[1:]:
-            nc.vector.tensor_copy(
-                v_w[1][:, lo:hi], tab_w[1][:].bitcast(U32).indirect(list1[:, lo // 16 : hi // 16])
-            )
-        nc.gpsimd.memset(pages[1][:], 0.0)
+        for lo, hi in ((0, Q), (Q, BANK), (BANK, S)):
+            nc.vector.tensor_copy(v_w[1][:, lo:hi], tab_w[1][:].bitcast(U32).indirect(list1[:, lo // 16 : hi // 16]))
 
         wo_raw = placed("wo_raw", [P, 2, 4, N], F32)
         nc.sync.dma_start(wo_raw[:, 0, :, :], wo[0:512, :].rearrange("(p t) n -> p t n", t=4))
         wo_rows = wo[512:1024, :].rearrange("(q t e) n -> t q e n", t=4, e=4)
         for t in range(4):
             nc.sync.dma_start(wo_raw[:, 1, t, :], wo_rows[t])
-        weights = placed("weights", [P, 4, S], F32)
+        weights = [placed("weights%d" % t, [P, S], F32) for t in range(4)]
         wgs_rows = wgs.rearrange("(q t e) j -> t q e j", t=4, e=4)
-        z_pairs = [
-            held.tile([P, width], F32, name="z_pairs%d" % b, align_bytes=64)
-            for b, width in enumerate((3 * M - P, 2 * M))
-        ]
-        late = {6: z_pairs[0][:, 2 * M : 2 * M + LATE], 7: z_pairs[1][:, M : M + LATE]}
-        late_weight = {i: placed("late_weight%d" % i, [P, LATE], F32) for i in late}
-
-        def load_weight(dest, t, lo, hi):
+        for t in range(4):
             for quad in quads:
-                nc.sync.dma_start(dest[32 * quad : 32 * quad + 32, :], wgs_rows[t][:, :, lo:hi])
+                nc.sync.dma_start(weights[t][32 * quad : 32 * quad + 32, :], wgs_rows[t])
 
-        for t in (0, 2, 3, 1):
-            width = EARLY if 4 + t in late else S
-            load_weight(weights[:, t, 0:width], t, 0, width)
-
-        w4_sorted = placed_mx("w4_sorted", [P, 2 * H], U8)
-        pieces_done = []
+        w4_sorted = placed("w4_sorted", [P, 2 * H], U8)
 
         def w4_tile(i, a):
             holder, first_tile, tiles = (w4_first, 0, 2) if i < 2 else (w4_next, 2, 2) if i < 4 else (w4_sorted, 4, 4)
             col = P * (tiles * a + i - first_tile)
             return holder[:, 2 * col : 2 * (col + P)]
 
-        def square(i, lo, hi, dest, passes=(1, 0)):
-            bank = bank_tile(HEAT_BANKS[len(pieces_done)], [P, hi - lo])
-            pieces_done.append((i, lo))
-            width = BANK if hi - lo == BANK else P
-            for c in range(lo, hi, width):
-                for a in passes:
-                    plane = 2 * BANK * a
-                    nc.tensor.matmul_mx(
-                        out=bank[:, c - lo : c - lo + width],
-                        lhsT=w4_tile(i, a).bitcast(E2M1),
-                        lhsT_scale=planes[i // 4][:, plane + BANK + P * (i % 4) : plane + BANK + P * (i % 4 + 1)],
-                        rhs=v_w[a][:, c : c + width].bitcast(E4M3),
-                        rhs_scale=planes[lo // BANK][:, plane + c % BANK : plane + c % BANK + width],
-                        start=(a == passes[0]),
-                        stop=(a == passes[1]),
-                    )
+        def square(i, lo, hi, dest, j, passes=(1, 0)):
+            bank = bank_tile(j, [P, hi - lo])
+            for a in passes:
+                plane = 2 * BANK * a
+                nc.tensor.matmul_mx(
+                    out=bank[:],
+                    lhsT=w4_tile(i, a).bitcast(E2M1),
+                    lhsT_scale=planes[i // 4][:, plane + BANK + P * (i % 4) : plane + BANK + P * (i % 4 + 1)],
+                    rhs=v_w[a][:, lo:hi].bitcast(E4M3),
+                    rhs_scale=planes[lo // BANK][:, plane + lo % BANK : plane + lo % BANK + hi - lo],
+                    start=(a == passes[0]),
+                    stop=(a == passes[1]),
+                )
             nc.scalar.activation(dest, bank[:], ACT.Square, bias=1.0)
 
         def halve(dest, values):
@@ -242,103 +161,83 @@ def tile_list_buffer_pool_prefetch_kernel(
 
         def put_fused(i, lo, hi, values):
             nc.vector.tensor_tensor(
-                pages[i % PAGES][:].indirect(list2[:, lo // 16 : hi // 16]), values, weight[:, lo:hi], ALU.mult
+                pages[i % 2][:].indirect(list2[:, lo // 16 : hi // 16]), values, weight[:, lo:hi], ALU.mult
             )
 
-        def put(i, values, lo=0, hi=S):
-            nc.vector.tensor_copy(pages[i % PAGES][:].indirect(list2[:, lo // 16 : hi // 16]), values)
+        def put(i, lo, hi, values):
+            nc.vector.tensor_copy(pages[i % 2][:].indirect(list2[:, lo // 16 : hi // 16]), values)
 
-        early = placed("early", [P, 3 * CHUNK + S], F32)
-        piece = [early[:, CHUNK * j : CHUNK * (j + 1)] for j in range(3)]
-        back0, back1 = [early[:, 3 * CHUNK + lo : 3 * CHUNK + hi] for lo, hi in HALVES]
-        first = placed("first", [P, CHUNK], F32)
-        squared = placed("squared", [P, BANK + CHUNK], F32)
-        for j in range(2):
-            square(0, P * j, P * (j + 1), first[:, P * j : P * (j + 1)], passes=(0, 1))
-        for j in range(2):
-            halve(piece[0][:, P * j : P * (j + 1)], first[:, P * j : P * (j + 1)])
-        square(0, CHUNK, BANK, squared[:, 0:CHUNK])
-        for lo, hi in QUARTERS:
-            square(1, lo, hi, squared[:, CHUNK + lo : CHUNK + hi])
-        halve(early[:, CHUNK : 3 * CHUNK], squared[:, 0:BANK])
-        second = placed("second", [P, CHUNK], F32)
-        halve(second[:], squared[:, BANK : BANK + CHUNK])
-        back = placed("back", [P, BANK], F32)
-        square(0, BANK, S, back[:])
-        halve(back0, back[:])
-        square(1, BANK, S, squared[:, 0:BANK])
-        halve(back1, squared[:, 0:BANK])
+        def fetch(i, lo, hi, dest):
+            nc.vector.tensor_copy(dest, pages[i % 2][:].indirect(list3[:, lo // 16 : hi // 16]))
 
-        heat = {i: placed("heat%d" % i, [P, EARLY if i in late else S], F32) for i in range(2, TILES)}
-        spare = {i: placed("spare%d" % i, [P, BANK], F32) for i in late}
+        lane = {i: placed("lane%d" % i, [P, 2 * S if i < LAST else S], F32) for i in range(2, TILES)}
+        head7 = placed("head7", [P, Q], F32)
+        rest7 = placed("rest7", [P, S - Q], F32)
+
+        heat0 = placed("heat0", [P, S + Q], F32)
+        ab = placed("ab", [P, BANK], F32)
+        spill = heat0[:, S : S + Q]
+        for j in range(2):
+            square(0, P * j, P * (j + 1), heat0[:, P * j : P * (j + 1)], j, passes=(0, 1))
+        for j in range(2):
+            halve(heat0[:, P * j : P * (j + 1)], heat0[:, P * j : P * (j + 1)])
+        square(1, 0, Q, ab[:, 0:Q], 2)
+        halve(ab[:, 0:Q], ab[:, 0:Q])
+        square(0, Q, BANK, heat0[:, Q:BANK], 3)
+        square(1, Q, BANK, ab[:, Q:BANK], 4)
+        halve(heat0[:, Q:BANK], heat0[:, Q:BANK])
+        halve(ab[:, Q:BANK], ab[:, Q:BANK])
+        square(0, BANK, S, heat0[:, BANK:S], 5)
+        square(1, BANK, BANK + Q, spill, 6)
+        square(1, BANK + Q, S, lane[2][:, 0:Q], 7)
+        halve(heat0[:, BANK : S + Q], heat0[:, BANK : S + Q])
+        halve(lane[2][:, 0:Q], lane[2][:, 0:Q])
+
+        def heat_of(i):
+            return lane[i][:, S : 2 * S] if i < LAST else lane[i][:]
 
         def make_heat(i):
-            square(i, 0, BANK, heat[i][:, 0:BANK])
-            if i not in late:
-                square(i, BANK, S, heat[i][:, BANK:S])
-                halve(heat[i][:], heat[i][:])
+            for half in range(2):
+                lo, hi = BANK * half, BANK * (half + 1)
+                square(i, lo, hi, heat_of(i)[:, lo:hi], 2 * (i % 2) + half)
+            for half in range(2):
+                lo, hi = BANK * half, BANK * (half + 1)
+                halve(heat_of(i)[:, lo:hi], heat_of(i)[:, lo:hi])
+
+        def weigh(i, lo, hi, dest, values):
+            factors = weight[:, lo:hi] if i < 4 else weights[i % 4][:, lo:hi]
+            nc.gpsimd.tensor_tensor(dest, values, factors, ALU.mult)
+
+        def weigh_tile(i):
+            if i < LAST:
+                weigh(i, 0, S, lane[i][:, 0:S], heat_of(i))
             else:
-                square(i, BANK, S, spare[i][:])
-                halve(heat[i][:, BANK:EARLY], spare[i][:, 0 : BANK - LATE])
-                halve(late[i], spare[i][:, BANK - LATE : BANK])
-                halve(heat[i][:, 0:BANK], heat[i][:, 0:BANK])
+                weigh(i, Q, S, rest7[:], lane[i][:, Q:S])
+                weigh(i, 0, Q, head7[:], lane[i][:, 0:Q])
 
-        for i in (2, 3):
-            make_heat(i)
-        put_fused(0, 0, CHUNK, piece[0])
-        third = placed("third", [P, CHUNK], F32)
-        nc.vector.tensor_tensor(piece[2], piece[2], weight[:, 0:CHUNK], ALU.mult)
-        put_fused(0, CHUNK, BANK, piece[1])
-        put(1, piece[2], 0, CHUNK)
-        nc.gpsimd.tensor_tensor(third[:], second[:], weight[:, CHUNK:BANK], ALU.mult)
-        nc.gpsimd.memset(pages[2][:], 0.0)
-        put_fused(0, BANK, S, back0)
-        put(1, third[:], CHUNK, BANK)
-        nc.gpsimd.tensor_tensor(back0, back1, weight[:, BANK:S], ALU.mult)
-
-        lane = [placed("lane%d" % j, [P, EARLY + 2 * M], F32) for j in range(2)]
-        front = placed("front", [P, 2 * S - P], F32)
-        weighed = {2: front[:, 0:S], 6: lane[0][:, 0:S], 7: lane[1][:, 0:S]}
-        for i in (3, 4, 5):
-            weighed[i] = placed("weighed%d" % i, [P, S], F32)[:]
-
-        def weigh(i, values, lo=0, hi=S):
-            factors = weight[:, lo:hi] if i < 4 else late_weight[i][:] if lo == EARLY else weights[:, i % 4, lo:hi]
-            nc.gpsimd.tensor_tensor(weighed[i][:, lo:hi], values, factors, ALU.mult)
-
-        fetched = {i: placed("x%d" % i, [P, M], F32)[:] for i in (1, 2, 4)}
-        fetched[0] = front[:, S - P : 2 * S - P]
-        fetched[3] = lane[1][:, EARLY - P : EARLY - P + M]
-        fetched[5] = z_pairs[0][:, 2 * M - P : 3 * M - P]
-        fetched[6] = z_pairs[1][:, M - P : 2 * M - P]
         dealt = placed("dealt", [P, 8 * M], F32)
         turns0 = dealt[:, 0 : 4 * M].rearrange("p (k t r) -> p k t r", t=4, r=P)
         whole0 = dealt[:, 4 * M : 8 * M].bitcast(U32).rearrange("p (k t r) -> p k t r", t=4, r=P)
-        turns = placed("turns", [P, M], F32)
-        whole = placed("whole", [P, M], U32)
-        cos = [held.tile([P, 2, M], F32, name="cos%d" % j) for j in range(2)]
-        works = [lane[j][:, EARLY : EARLY + 2 * M].rearrange("p (t m) -> p t m", t=2) for j in range(2)]
-        works.extend(placed("works%d" % j, [P, 2, M], F32)[:] for j in (2, 3))
+        turns = [placed("turns%d" % half, [P, BANK], F32) for half in range(2)]
+        whole = [placed("whole%d" % half, [P, BANK], U32) for half in range(2)]
+        cos0 = placed("cos0", [P, 4, BANK], F32)
+        cos45 = placed("cos45", [P, 2, M], F32)
+        cos67 = placed("cos67", [P, M], F32)
+        work0 = placed("work0", [P, 4, M], F32)
+        works = [placed("works%d" % j, [P, 2, M], F32) for j in (2, 3)]
+        z = [placed("z%d" % b, [P, M, 4], BF16) for b in range(2)]
+        z_w = [placed("z_w%d" % b, [P, M], U32) for b in range(2)]
+        z_pairs = placed("z_pairs", [P, 2 * M], F32)
+        pair_view = z_pairs[:].bitcast(BF16).rearrange("p (w m t) -> p w m t", w=2, t=2)
+        wo_bf = placed("wo_bf", [P, 2, N, 4], BF16)
+        wo_w = placed("wo_w", [P, 2 * N], U32)
+        wo_s = placed("wo_s", [P, 2 * N], U8)
 
-        def load_works(pair):
-            if pair < 2:
-                rows = work[0:512, :].rearrange("(p t) m -> p t m", t=4)
-                nc.sync.dma_start(works[pair], rows[:, 2 * pair : 2 * pair + 2, :])
-            else:
-                rows = work[512:1024, :].rearrange("(q t e) m -> t q e m", t=4, e=4)
-                for side in range(2):
-                    nc.sync.dma_start(works[pair][:, side, :], rows[2 * pair - 4 + side])
-
-        def fetch(i, banks, cuts=((0, M),)):
-            for lo, hi in cuts:
-                nc.vector.tensor_copy(fetched[i][:, lo:hi], pages[i % PAGES][:].indirect(list3[:, lo // 16 : hi // 16]))
-            flipped = []
-            for (lo, hi), j in zip(HALVES, banks):
-                bank = bank_tile(j, [P, BANK])
-                for c in range(lo, hi, P):
-                    nc.tensor.transpose(bank[:, c - lo : c - lo + P], fetched[i][:, c : c + P], ident[:])
-                flipped.append(bank)
-            return flipped
+        def flip(j, x):
+            bank = bank_tile(j, [P, x.shape[1]])
+            for c in range(0, x.shape[1], P):
+                nc.tensor.transpose(bank[:, c : c + P], x[:, c : c + P], ident[:])
+            return bank
 
         def split(u, count, x):
             nc.scalar.activation(count, x, ACT.Relu, bias=0.25, scale=-1.0 / TURN)
@@ -347,206 +246,216 @@ def tile_list_buffer_pool_prefetch_kernel(
         def negate(count):
             nc.scalar.activation(count.bitcast(F32), count, ACT.Copy, scale=-1.0)
 
-        def deal(i, flipped):
-            for half, bank in enumerate(flipped):
+        def turn_back(dest, blocks, j):
+            bank = bank_tile(j, [P, P * len(blocks)])
+            for part in range(2):
+                for c, pair in enumerate(blocks):
+                    nc.tensor.matmul(
+                        bank[:, P * c : P * (c + 1)], pair[part], ident[:],
+                        start=(part == 0 and c == 0), stop=(part == 1 and c == len(blocks) - 1), is_transpose=True,
+                    )
+            nc.scalar.activation(dest, bank[:], ACT.Sin, bias=PHASE, scale=TURN)
+
+        def after_fetch(i, step, x):
+            width = x.shape[1]
+            half, lo = divmod(step * width, BANK)
+            bank = flip(FLIP_BANKS[i][step], x)
+            if i < 4:
                 count = whole0[:, 4 * half : 4 * half + 4, :, 32 * i : 32 * i + 32]
                 u = turns0[:, 4 * half : 4 * half + 4, :, 32 * i : 32 * i + 32]
                 split(u, count, bank[:].rearrange("p (k q t) -> p k t q", k=4, t=4))
                 negate(count)
+            else:
+                split(turns[half][:, lo : lo + width], whole[half][:, lo : lo + width], bank[:])
+                negate(whole[half][:, lo : lo + width])
 
-        def turn_back(dest, blocks, banks):
-            width = M // len(banks)
-            rest = [bank_tile(j, [P, width]) for j in banks]
-            for lo, hi in HALVES:
-                for part in range(2):
-                    for c in range(lo, hi, P):
-                        nc.tensor.matmul(
-                            rest[c // width][:, c % width : c % width + P], blocks(c)[part], ident[:],
-                            start=(part == 0 and c % width == 0), stop=(part == 1 and c % width == width - P),
-                            is_transpose=True,
-                        )
-            for j, bank in enumerate(rest):
-                nc.scalar.activation(dest[:, width * j : width * (j + 1)], bank[:], ACT.Sin, bias=PHASE, scale=TURN)
+        def cosine(i, step, width=BANK):
+            half, lo = divmod(step * width, BANK)
+            row = cos45[:, i - 4, :] if i < 6 else cos67[:]
+            blocks = [
+                (turns[half][:, c : c + P], whole[half][:, c : c + P].bitcast(F32)) for c in range(lo, lo + width, P)
+            ]
+            turn_back(row[:, step * width : (step + 1) * width], blocks, BACK_BANKS[i][step])
 
-        def cosine(i, flipped, banks):
-            for (lo, hi), bank in zip(HALVES, flipped):
-                split(turns[:, lo:hi], whole[:, lo:hi], bank[:])
-                negate(whole[:, lo:hi])
-            turn_back(
-                cos[i // 2 % 2][:, i % 2, :], lambda c: (turns[:, c : c + P], whole[:, c : c + P].bitcast(F32)), banks
-            )
-
-        def multiply(engine, pair, lo, hi):
-            both = z_pairs[pair // 2][:, M * (pair % 2) : M * (pair % 2 + 1)].bitcast(BF16)
-            engine.tensor_tensor(
-                both.rearrange("p (m t) -> p m t", t=2)[:, lo:hi, :].rearrange("p (c f) t -> p c t f", f=4),
-                cos[pair % 2][:, :, lo:hi].rearrange("p t (c f) -> p c t f", f=4),
-                works[pair][:, :, lo:hi].rearrange("p t (c f) -> p c t f", f=4),
+        def block0(k):
+            ring = cos0[:, k % 4, :]
+            turn_back(ring, [(turns0[:, k, t, :], whole0[:, k, t, :].bitcast(F32)) for t in range(4)], k % 4)
+            nc.gpsimd.tensor_tensor(
+                z[0][:, P * k : P * (k + 1), :].rearrange("p (c f) t -> p c t f", f=4),
+                ring.rearrange("p (t c f) -> p c t f", t=4, f=4),
+                work0[:, :, P * k : P * (k + 1)].rearrange("p t (c f) -> p c t f", f=4),
                 ALU.mult,
             )
 
-        z = [placed_mx("z%d" % b, [P, M, 4], BF16) for b in range(2)]
-        z_w = [held.tile([P, M], U32, name="z_w%d" % b, align_bytes=64) for b in range(2)]
-        z1_s = held.tile([P, M], U8, name="z1_s", align_bytes=64)
-        wo_parts = [(0, 0, N), (1, 0, N // 2), (1, N // 2, N)]
-        wo_bf = [
-            z_pairs[j // 2][:, M * (j % 2) : M * (j % 2) + 2 * (hi - lo)]
-            .bitcast(BF16)
-            .rearrange("p (n t) -> p n t", t=4)
-            for j, (b, lo, hi) in enumerate(wo_parts)
-        ]
-        wo_w = held.tile([P, 2 * N], U32, name="wo_w", align_bytes=64)
-        wo_s = [placed_mx("wo_s%d" % j, [P, hi - lo], U8) for j, (b, lo, hi) in enumerate(wo_parts)]
-
-        def wo_plane(b, col):
-            j = b + b * col // (N // 2)
-            return wo_s[j][:, col - wo_parts[j][1] : col - wo_parts[j][1] + P]
-
-        def weave(b, lo, hi, word, copy):
-            copy(
-                z[b][:, lo:hi, :].rearrange("p m t -> p (m t)").bitcast(word).rearrange("p (m w) -> p m w", w=2),
-                z_pairs[b][:, 0 : 2 * M].bitcast(word).rearrange("p (w m) -> p m w", w=2)[:, lo:hi, :],
+        def pair45(half):
+            lo, hi = BANK * half, BANK * (half + 1)
+            nc.gpsimd.tensor_tensor(
+                pair_view[:, 0, lo:hi, :].rearrange("p (c f) t -> p c t f", f=4),
+                cos45[:, :, lo:hi].rearrange("p t (c f) -> p c t f", f=4),
+                works[0][:, :, lo:hi].rearrange("p t (c f) -> p c t f", f=4),
+                ALU.mult,
             )
+
+        def single(engine, side, lo, hi):
+            engine.tensor_tensor(pair_view[:, 1, lo:hi, side], cos67[:, lo:hi], works[1][:, side, lo:hi], ALU.mult)
 
         def quantise(codes, scales, values):
             nc.vector.quantize_mx(out=codes.bitcast(E4M3), scales=scales, in_=values.rearrange("p c t -> p (c t)"))
 
-        def quantise_wo(j):
-            b, lo, hi = wo_parts[j]
-            quantise(wo_w[:, N * b + lo : N * b + hi], wo_s[j][:], wo_bf[j])
+        def round_wo(b):
+            for c in range(0, N, P):
+                nc.scalar.copy(wo_bf[:, b, c : c + P, :], wo_raw[:, b, :, c : c + P].rearrange("p t n -> p n t"))
 
-        flipped = fetch(0, FLIP_BANKS, HALVES)
-        put(1, back0, BANK, S)
-        weigh(2, heat[2][:])
+        def period(i, after_a, after_c):
+            first, second, third = lane[i][:, 0:BANK], lane[i][:, BANK:S], lane[i][:, S : S + BANK]
+            put(i, 0, Q, first[:, 0:Q])
+            fetch(i - 1, 0, BANK, third)
+            after_fetch(i - 1, 0, third)
+            after_a()
+            put(i, Q, BANK, first[:, Q:BANK])
+            fetch(i - 1, BANK, BANK + Q, first[:, 0:Q])
+            put(i, BANK, BANK + Q, second[:, 0:Q])
+            fetch(i - 1, BANK + Q, M, first[:, Q:BANK])
+            put(i, BANK + Q, S, second[:, Q:BANK])
+            after_fetch(i - 1, 1, first)
+            after_c()
+
+        make_heat(2)
+        make_heat(3)
+        round_wo(0)
+        x0 = placed("x0", [P, M], F32)
+        put_fused(0, 0, Q, heat0[:, 0:Q])
+        put_fused(1, 0, Q, ab[:, 0:Q])
+        put_fused(0, Q, BANK, heat0[:, Q:BANK])
+        put_fused(1, Q, BANK, ab[:, Q:BANK])
+        put_fused(0, BANK, S, heat0[:, BANK:S])
+        put_fused(1, BANK, BANK + Q, spill)
+        for half in range(2):
+            fetch(0, BANK * half, BANK * (half + 1), x0[:, BANK * half : BANK * (half + 1)])
+        weigh(1, S - Q, S, spill, lane[2][:, 0:Q])
+        put(1, S - Q, S, spill)
+        weigh_tile(2)
+        for half in range(2):
+            after_fetch(0, half, x0[:, BANK * half : BANK * (half + 1)])
         nc.gpsimd.tensor_copy(
             w4_sorted[:].bitcast(I32).rearrange("p (a t q w) -> p a t q w", a=2, t=4, w=2),
             w4_back[:].rearrange("p a (q t w) -> p a t q w", t=4, w=2),
         )
-        weigh(3, heat[3][:])
-        deal(0, flipped)
-        put(2, weighed[2])
-        for j, (b, lo, hi) in enumerate(wo_parts):
-            for c in range(lo, hi, P):
-                nc.scalar.copy(
-                    wo_bf[j][:, c - lo : c - lo + P, :], wo_raw[:, b, :, c : c + P].rearrange("p t n -> p n t")
-                )
-        for i in range(4, TILES):
-            make_heat(i)
-        weigh(4, heat[4][:])
-        weigh(6, heat[6][:], 0, EARLY)
-        for i in late_weight:
-            load_weight(late_weight[i], i % 4, EARLY, S)
-        for pair in (0, 2):
-            load_works(pair)
-
-        deal(1, fetch(1, FLIP_BANKS))
-        put(3, weighed[3])
-        deal(2, fetch(2, FLIP_BANKS))
-        deal(3, fetch(3, FLIP_BANKS))
-        weigh(7, heat[7][:], 0, EARLY)
-        weigh(5, heat[5][:])
-        load_works(1)
+        weigh_tile(3)
+        nc.sync.dma_start(work0[:], work[0:512, :].rearrange("(p t) m -> p t m", t=4))
+        work_rows = work[512:1024, :].rearrange("(q t e) m -> t q e m", t=4, e=4)
         for t in range(4):
-            turn_back(
-                cos[t // 2][:, t % 2, :],
-                lambda c: (turns0[:, c // P, t, :], whole0[:, c // P, t, :].bitcast(F32)),
-                SLOT_BANKS[t],
-            )
-        put(4, weighed[4])
+            nc.sync.dma_start(works[t // 2][:, t % 2, :], work_rows[t])
 
-        for i in range(4, LAST):
-            quantise_wo(i - 4)
-            flipped = fetch(i, SECOND_FLIP_BANKS)
-            multiply(nc.gpsimd, i - 4, 0, M)
-            if i + 2 in late:
-                weigh(i + 2, late[i + 2], EARLY, S)
-            cosine(i, flipped, SECOND_FLIP_BANKS if i + 1 < LAST else SCORE_BANKS[0])
-            if i - 4 == 1:
-                load_works(3)
-                weave(0, 0, M, U32, nc.scalar.copy)
-            put(i + 1, weighed[i + 1])
+        def heat_and_weigh(i):
+            make_heat(i)
+            weigh_tile(i)
 
-        z0_s12 = placed_mx("z0_s12", [P, 2 * CHUNK], U8)
-        z0_s0, z0_s3 = placed_mx("z0_s0", [P, CHUNK], U8), placed_mx("z0_s3", [P, CHUNK], U8)
-        z_planes = [
-            [z0_s0[:], z0_s12[:, 0:CHUNK], z0_s12[:, CHUNK : 2 * CHUNK], z0_s3[:]],
-            [z1_s[:, lo:hi] for lo, hi in CHUNKS],
-        ]
-        x_last = placed("x_last", [P, BANK], F32)
-        parts = [placed("parts%d" % j, [P, 2, CHUNK], F32) for j in range(4)]
-        u_last = [parts[j][:, 0, :] for j in range(4)]
-        n_last = [parts[j][:, 1, :] for j in range(4)]
-        x_chunk = [x_last[:, 0:CHUNK], x_last[:, CHUNK:BANK], x_last[:, 0:CHUNK], placed("x_end", [P, CHUNK], F32)[:]]
+        def quantise_wo():
+            quantise(wo_w[:], wo_s[:], wo_bf[:].rearrange("p b n t -> p (b n) t"))
+
+        def blocks0(ks):
+            for k in ks:
+                block0(k)
+
+        round_wo(1)
+        period(2, lambda: heat_and_weigh(4), lambda: heat_and_weigh(5))
+        period(3, lambda: heat_and_weigh(6), lambda: make_heat(7))
+        period(4, lambda: (quantise_wo(), weigh_tile(7), blocks0(range(0, 4))), lambda: blocks0(range(4, 6)))
+        period(5, lambda: (blocks0(range(6, 8)), cosine(4, 0)), lambda: cosine(4, 1))
+
+        put(6, 0, Q, lane[6][:, 0:Q])
+        for lo in (0, BANK):
+            fetch(5, lo, lo + BANK, lane[6][:, S + lo : S + lo + BANK])
+        put(6, Q, S, lane[6][:, Q:S])
+        for half in range(2):
+            after_fetch(5, half, lane[6][:, S + BANK * half : S + BANK * (half + 1)])
+        for half in range(2):
+            cosine(5, half)
+            pair45(half)
+        put(LAST, 0, Q, head7[:])
+        for lo in range(0, M, Q):
+            fetch(6, lo, lo + Q, lane[LAST][:, lo : lo + Q])
+        put(LAST, Q, S, rest7[:])
+        for step in range(5):
+            if step < 4:
+                after_fetch(6, step, lane[LAST][:, Q * step : Q * (step + 1)])
+            if step > 0:
+                cosine(6, step - 1, Q)
+                single(nc.gpsimd, 0, Q * (step - 1), Q * step)
+
+        chunks = [(lo, lo + Q) for lo in range(0, M, Q)]
+        z0_s = [placed("z0_s%d" % j, [P, Q if j < 2 else BANK], U8) for j in range(3)]
+        z0_planes = [z0_s[0][:], z0_s[1][:], z0_s[2][:, 0:Q], z0_s[2][:, Q:BANK]]
+        z1_s = placed("z1_s", [P, M], U8)
+        x_ring = [placed("x_ring%d" % j, [P, Q], F32) for j in range(2)]
+        parts = [placed("parts%d" % j, [P, 2, Q], F32) for j in range(4)]
+        staged = placed("staged", [P, 8, BANK], F32)
         sums = {}
-        staged_all = placed("staged", [P, N // P * M], F32)
 
-        def quantise_z0(j):
-            lo, hi = CHUNKS[j]
-            quantise(z_w[0][:, lo:hi], z_planes[0][j], z[0][:, lo:hi, :])
-
-        def open_scores(j):
-            sums[j] = [bank_tile(bank, [P, CHUNK]) for bank in SCORE_BANKS[j % 2]]
-            score(j, 0)
-
-        def fetch_last(j):
-            lo, hi = CHUNKS[j]
-            nc.vector.tensor_copy(x_chunk[j], pages[LAST % PAGES][:].indirect(list3[:, lo // 16 : hi // 16]))
-
-        def split_last(j):
-            split(u_last[j], n_last[j].bitcast(U32), x_chunk[j])
-
-        def subtract_turns(j):
-            nc.vector.tensor_tensor(u_last[j], u_last[j], n_last[j].bitcast(I32), ALU.subtract)
-
-        def sine(j):
-            lo, hi = CHUNKS[j]
-            nc.scalar.activation(cos[LAST // 2 % 2][:, LAST % 2, lo:hi], u_last[j], ACT.Sin, bias=PHASE, scale=TURN)
+        def plane(b, lo, hi):
+            return z0_planes[lo // Q] if b == 0 else z1_s[:, lo:hi]
 
         def score(j, b):
-            lo, hi = CHUNKS[j]
-            for n_tile, bank in enumerate(sums[j]):
-                col = P * n_tile
+            lo, hi = chunks[j]
+            if b == 0:
+                sums[j] = [bank_tile(k, [P, 2, Q]) for k in SCORE_BANKS[j]]
+            for n_tile in range(4):
+                col = N * b + P * n_tile
                 nc.tensor.matmul_mx(
-                    out=bank[:],
-                    lhsT=wo_w[:, N * b + col : N * b + col + P].bitcast(E4M3),
-                    lhsT_scale=wo_plane(b, col),
+                    out=sums[j][n_tile // 2][:, n_tile % 2, :],
+                    lhsT=wo_w[:, col : col + P].bitcast(E4M3),
+                    lhsT_scale=wo_s[:, col : col + P],
                     rhs=z_w[b][:, lo:hi].bitcast(E4M3),
-                    rhs_scale=z_planes[b][j],
-                    start=(b == 0),
-                    stop=(b == 1),
+                    rhs_scale=plane(b, lo, hi),
+                    start=(b == 0 and n_tile % 2 == 0),
+                    stop=(b == 1 and n_tile % 2 == 1),
                 )
 
-        def finish(j):
-            lo, hi = CHUNKS[j]
-            quantise(z_w[1][:, lo:hi], z_planes[1][j], z[1][:, lo:hi, :])
-            score(j, 1)
+        def finish(j, b):
+            lo, hi = chunks[j]
+            quantise(z_w[b][:, lo:hi], plane(b, lo, hi), z[b][:, lo:hi, :])
+            score(j, b)
 
-        def store(j):
-            lo, hi = CHUNKS[j]
-            for n_tile, bank in enumerate(sums[j]):
-                staged = staged_all[:, CHUNK * (4 * j + n_tile) : CHUNK * (4 * j + n_tile + 1)]
-                if n_tile % 2 == 0 or lo < M // 2:
-                    nc.scalar.copy(staged, bank[:])
-                else:
-                    nc.vector.tensor_copy(staged, bank[:])
-                nc.sync.dma_start(out[P * n_tile : P * (n_tile + 1), lo:hi], staged)
+        def fetch_last(j):
+            fetch(LAST, chunks[j][0], chunks[j][1], x_ring[j % 2][:])
+
+        def split_last(j):
+            split(parts[j][:, 0, :], parts[j][:, 1, :].bitcast(U32), x_ring[j % 2][:])
+
+        def subtract_turns(j):
+            nc.vector.tensor_tensor(parts[j][:, 0, :], parts[j][:, 0, :], parts[j][:, 1, :].bitcast(I32), ALU.subtract)
+
+        def sine(j):
+            lo, hi = chunks[j]
+            nc.scalar.activation(cos67[:, lo:hi], parts[j][:, 0, :], ACT.Sin, bias=PHASE, scale=TURN)
 
         def product(j):
-            multiply(nc.vector, LAST // 2, *CHUNKS[j])
+            single(nc.vector, 1, *chunks[j])
 
-        def weave_last(j):
-            if j < SCALAR_WEAVES:
-                weave(1, *CHUNKS[j], U32, nc.scalar.copy)
-            else:
-                weave(1, *CHUNKS[j], I32, nc.vector.tensor_copy)
+        def weave(j):
+            lo, hi = chunks[j]
+            word, copy = (U32, nc.scalar.copy) if j < SCALAR_WEAVES else (I32, nc.vector.tensor_copy)
+            copy(
+                z[1][:, lo:hi, :].rearrange("p m t -> p (m t)").bitcast(word).rearrange("p (m w) -> p m w", w=2),
+                z_pairs[:].bitcast(word).rearrange("p (w m) -> p m w", w=2)[:, lo:hi, :],
+            )
 
-        quantise_z0(0)
-        open_scores(0)
+        def store(j):
+            lo, hi = chunks[j]
+            for k, bank in enumerate(sums[j]):
+                dest = staged[:, 2 * j + k, :]
+                copy = nc.vector.tensor_copy if (j == 3 and k == 1) else nc.scalar.copy
+                copy(dest, bank[:].rearrange("p a c -> p (a c)"))
+                nc.sync.dma_start(
+                    out[2 * P * k : 2 * P * (k + 1), lo:hi].rearrange("(a p) c -> p a c", a=2),
+                    dest.rearrange("p (a c) -> p a c", a=2),
+                )
+
+        finish(0, 0)
         fetch_last(0)
         fetch_last(1)
-        quantise_z0(1)
-        open_scores(1)
-        quantise_z0(2)
+        finish(1, 0)
         split_last(0)
         subtract_turns(0)
         split_last(1)
@@ -554,29 +463,28 @@ def tile_list_buffer_pool_prefetch_kernel(
         fetch_last(2)
         subtract_turns(1)
         product(0)
-        weave_last(0)
+        weave(0)
         fetch_last(3)
         split_last(2)
         sine(1)
         subtract_turns(2)
         product(1)
-        finish(0)
+        finish(0, 1)
         split_last(3)
         sine(2)
-        weave_last(1)
+        weave(1)
+        finish(2, 0)
         subtract_turns(3)
         product(2)
-        finish(1)
+        finish(1, 1)
         sine(3)
         store(0)
-        open_scores(2)
-        weave_last(2)
+        weave(2)
         product(3)
-        finish(2)
-        quantise_z0(3)
+        finish(2, 1)
+        finish(3, 0)
         store(1)
-        open_scores(3)
-        weave_last(3)
-        finish(3)
+        weave(3)
+        finish(3, 1)
         store(2)
         store(3)

@@ -26,24 +26,27 @@ Q = 256
 CAP = 2.5
 TURN = 2.0 * math.pi
 PHASE = math.pi / 2 - CAP
-FLIP_BANKS = ((4, 5), (4, 5), (4, 5), (4, 2), (1, 6), (7, 7), (4, 5, 4, 5))
+FLIP_BANKS = ((0, 1), (0, 1), (0, 1), (0, 1), (1, 1), (7, 7), (4, 5, 4, 5))
 BACK_BANKS = {4: (6, 7), 5: (4, 5), 6: (6, 7, 6, 7)}
-SCORE_BANKS = ((6, 7), (4, 5), (0, 1), (2, 3))
-SCALAR_WEAVES = 1
+SCORE_BANKS = ((6,), (4, 5), (0, 1), (2, 3), (7, 6))
+EDGES = (0, 128, 384, 640, 896, 1024)
+PLANE_EDGES = (0, 128, 384, 640, 1024)
+SCALAR_WEAVES = ()
+VECTOR_STORES = ((3, 1), (4, 1))
 KIB = 1024
 AT = {
     "tab_w0": 0, "planes1": 0, "x0": 2, "w4_back": 6, "w4_sorted": 3,
     "tab_w1": 8, "wo_raw": 8, "cos45": 8, "cos67": 16,
     "tab_s": 24, "planes0": 24,
-    "scale_rows": 29, "weights0": 26, "weights1": 30, "weights2": 34, "weights3": 38, "wo_w": 26,
+    "scale_rows": 29, "weights0": 26, "weights1": 30, "wo_w": 26,
     "weight": 42, "picked_s": 45.5, "w4_next": 46, "w4_first": 47,
     "ident": 48, "w4_s_raw": 48.25, "page1": 49, "page0": 57,
     "v_w0": 65, "v_w1": 69, "turns0": 65, "whole0": 67, "whole1": 69, "turns1": 71,
-    "dealt": 73, "x_ring0": 65, "z0_s0": 66, "x_ring1": 66.25, "parts0": 67.25, "z0_s1": 69.25,
-    "parts1": 69.5, "parts2": 71.5, "parts3": 73.5, "z0_s2": 67.25,
+    "dealt": 73, "x_a": 65, "z0_s0": 66, "x_b": 66.25, "parts0": 68.25, "z0_s1": 69.25,
+    "parts1": 69.5, "parts2": 71.5, "parts3": 73.5, "parts4": 75.5, "z0_s2": 66.25, "z0_s3": 71.5, "x_e": 69.5,
     "z_pairs": 83, "z1": 91, "z_w1": 99, "z1_s": 103,
     "work0": 105, "heat0": 105, "works2": 121, "works3": 129, "ab": 128,
-    "lane2": 137, "lane6": 137, "lane4": 145, "lane5": 153, "lane3": 161, "lane7": 161, "wo_s": 165,
+    "lane2": 137, "lane6": 137, "lane4": 145, "lane5": 153, "lane3": 161, "lane7": 161, "wo_s": 203,
     "rest7": 175, "head7": 178,
     "wo_bf": 175, "cos0": 183, "z0": 191, "z_w0": 199, "staged": 105,
 }
@@ -128,7 +131,8 @@ def tile_list_buffer_pool_prefetch_kernel(
         wo_rows = wo[512:1024, :].rearrange("(q t e) n -> t q e n", t=4, e=4)
         for t in range(4):
             nc.sync.dma_start(wo_raw[:, 1, t, :], wo_rows[t])
-        weights = [placed("weights%d" % t, [P, S], F32) for t in range(4)]
+        weights1 = placed("weights1", [P, 3, S], F32)
+        weights = [placed("weights0", [P, S], F32)[:]] + [weights1[:, t, :] for t in range(3)]
         wgs_rows = wgs.rearrange("(q t e) j -> t q e j", t=4, e=4)
         for t in range(4):
             for quad in quads:
@@ -177,19 +181,20 @@ def tile_list_buffer_pool_prefetch_kernel(
         heat0 = placed("heat0", [P, S + Q], F32)
         ab = placed("ab", [P, BANK], F32)
         spill = heat0[:, S : S + Q]
+        first = [ab[:, 0:P], heat0[:, Q : Q + P]]
         for j in range(2):
-            square(0, P * j, P * (j + 1), heat0[:, P * j : P * (j + 1)], j, passes=(0, 1))
+            square(0, P * j, P * (j + 1), first[j], j, passes=(0, 1))
         for j in range(2):
-            halve(heat0[:, P * j : P * (j + 1)], heat0[:, P * j : P * (j + 1)])
-        square(1, 0, Q, ab[:, 0:Q], 2)
+            halve(heat0[:, P * j : P * (j + 1)], first[j])
+        square(1, 0, Q, ab[:, 0:Q], 0)
         halve(ab[:, 0:Q], ab[:, 0:Q])
-        square(0, Q, BANK, heat0[:, Q:BANK], 3)
-        square(1, Q, BANK, ab[:, Q:BANK], 4)
+        square(0, Q, BANK, heat0[:, Q:BANK], 1)
+        square(1, Q, BANK, ab[:, Q:BANK], 0)
         halve(heat0[:, Q:BANK], heat0[:, Q:BANK])
         halve(ab[:, Q:BANK], ab[:, Q:BANK])
-        square(0, BANK, S, heat0[:, BANK:S], 5)
-        square(1, BANK, BANK + Q, spill, 6)
-        square(1, BANK + Q, S, lane[2][:, 0:Q], 7)
+        square(0, BANK, S, heat0[:, BANK:S], 1)
+        square(1, BANK, BANK + Q, spill, 0)
+        square(1, BANK + Q, S, lane[2][:, 0:Q], 1)
         halve(heat0[:, BANK : S + Q], heat0[:, BANK : S + Q])
         halve(lane[2][:, 0:Q], lane[2][:, 0:Q])
 
@@ -199,7 +204,7 @@ def tile_list_buffer_pool_prefetch_kernel(
         def make_heat(i):
             for half in range(2):
                 lo, hi = BANK * half, BANK * (half + 1)
-                square(i, lo, hi, heat_of(i)[:, lo:hi], 2 * (i % 2) + half)
+                square(i, lo, hi, heat_of(i)[:, lo:hi], half)
             for half in range(2):
                 lo, hi = BANK * half, BANK * (half + 1)
                 halve(heat_of(i)[:, lo:hi], heat_of(i)[:, lo:hi])
@@ -287,17 +292,9 @@ def tile_list_buffer_pool_prefetch_kernel(
                 ALU.mult,
             )
 
-        def pair45(half):
-            lo, hi = BANK * half, BANK * (half + 1)
-            nc.gpsimd.tensor_tensor(
-                pair_view[:, 0, lo:hi, :].rearrange("p (c f) t -> p c t f", f=4),
-                cos45[:, :, lo:hi].rearrange("p t (c f) -> p c t f", f=4),
-                works[0][:, :, lo:hi].rearrange("p t (c f) -> p c t f", f=4),
-                ALU.mult,
-            )
-
-        def single(engine, side, lo, hi):
-            engine.tensor_tensor(pair_view[:, 1, lo:hi, side], cos67[:, lo:hi], works[1][:, side, lo:hi], ALU.mult)
+        def single(engine, i, lo, hi):
+            row = cos45[:, i - 4, lo:hi] if i < 6 else cos67[:, lo:hi]
+            engine.tensor_tensor(pair_view[:, i // 2 - 2, lo:hi, i % 2], row, works[i // 2 - 2][:, i % 2, lo:hi], ALU.mult)
 
         def quantise(codes, scales, values):
             nc.vector.quantize_mx(out=codes.bitcast(E4M3), scales=scales, in_=values.rearrange("p c t -> p (c t)"))
@@ -307,17 +304,15 @@ def tile_list_buffer_pool_prefetch_kernel(
                 nc.scalar.copy(wo_bf[:, b, c : c + P, :], wo_raw[:, b, :, c : c + P].rearrange("p t n -> p n t"))
 
         def period(i, after_a, after_c):
-            first, second, third = lane[i][:, 0:BANK], lane[i][:, BANK:S], lane[i][:, S : S + BANK]
-            put(i, 0, Q, first[:, 0:Q])
-            fetch(i - 1, 0, BANK, third)
-            after_fetch(i - 1, 0, third)
+            x = lane[i][:, S : 2 * S]
+            put(i, 0, Q, lane[i][:, 0:Q])
+            fetch(i - 1, 0, M, x)
+            if i == 4:
+                quantise_wo()
+            put(i, Q, S, lane[i][:, Q:S])
+            after_fetch(i - 1, 0, x[:, 0:BANK])
             after_a()
-            put(i, Q, BANK, first[:, Q:BANK])
-            fetch(i - 1, BANK, BANK + Q, first[:, 0:Q])
-            put(i, BANK, BANK + Q, second[:, 0:Q])
-            fetch(i - 1, BANK + Q, M, first[:, Q:BANK])
-            put(i, BANK + Q, S, second[:, Q:BANK])
-            after_fetch(i - 1, 1, first)
+            after_fetch(i - 1, 1, x[:, BANK:M])
             after_c()
 
         make_heat(2)
@@ -330,8 +325,7 @@ def tile_list_buffer_pool_prefetch_kernel(
         put_fused(1, Q, BANK, ab[:, Q:BANK])
         put_fused(0, BANK, S, heat0[:, BANK:S])
         put_fused(1, BANK, BANK + Q, spill)
-        for half in range(2):
-            fetch(0, BANK * half, BANK * (half + 1), x0[:, BANK * half : BANK * (half + 1)])
+        fetch(0, 0, M, x0[:])
         weigh(1, S - Q, S, spill, lane[2][:, 0:Q])
         put(1, S - Q, S, spill)
         weigh_tile(2)
@@ -361,67 +355,88 @@ def tile_list_buffer_pool_prefetch_kernel(
         round_wo(1)
         period(2, lambda: heat_and_weigh(4), lambda: heat_and_weigh(5))
         period(3, lambda: heat_and_weigh(6), lambda: make_heat(7))
-        period(4, lambda: (quantise_wo(), weigh_tile(7), blocks0(range(0, 4))), lambda: blocks0(range(4, 6)))
-        period(5, lambda: (blocks0(range(6, 8)), cosine(4, 0)), lambda: cosine(4, 1))
+        period(4, lambda: (weigh_tile(7), blocks0(range(0, 2))), lambda: blocks0(range(2, 6)))
+        period(5, lambda: blocks0(range(6, 8)), lambda: None)
+        for half in range(2):
+            cosine(4, half)
+            single(nc.gpsimd, 4, BANK * half, BANK * (half + 1))
 
         put(6, 0, Q, lane[6][:, 0:Q])
-        for lo in (0, BANK):
-            fetch(5, lo, lo + BANK, lane[6][:, S + lo : S + lo + BANK])
+        fetch(5, 0, M, lane[6][:, S : 2 * S])
         put(6, Q, S, lane[6][:, Q:S])
         for half in range(2):
             after_fetch(5, half, lane[6][:, S + BANK * half : S + BANK * (half + 1)])
         for half in range(2):
             cosine(5, half)
-            pair45(half)
+            single(nc.gpsimd, 5, BANK * half, BANK * (half + 1))
         put(LAST, 0, Q, head7[:])
-        for lo in range(0, M, Q):
-            fetch(6, lo, lo + Q, lane[LAST][:, lo : lo + Q])
+        for lo in (0, BANK):
+            fetch(6, lo, lo + BANK, lane[LAST][:, lo : lo + BANK])
         put(LAST, Q, S, rest7[:])
         for step in range(5):
             if step < 4:
                 after_fetch(6, step, lane[LAST][:, Q * step : Q * (step + 1)])
             if step > 0:
                 cosine(6, step - 1, Q)
-                single(nc.gpsimd, 0, Q * (step - 1), Q * step)
+                single(nc.gpsimd, 6, Q * (step - 1), Q * step)
 
-        chunks = [(lo, lo + Q) for lo in range(0, M, Q)]
-        z0_s = [placed("z0_s%d" % j, [P, Q if j < 2 else BANK], U8) for j in range(3)]
-        z0_planes = [z0_s[0][:], z0_s[1][:], z0_s[2][:, 0:Q], z0_s[2][:, Q:BANK]]
+        chunks = list(zip(EDGES[:-1], EDGES[1:]))
+        plane_parts = list(zip(PLANE_EDGES[:-1], PLANE_EDGES[1:]))
+        z0_s = [placed("z0_s%d" % j, [P, hi - lo], U8) for j, (lo, hi) in enumerate(plane_parts)]
         z1_s = placed("z1_s", [P, M], U8)
-        x_ring = [placed("x_ring%d" % j, [P, Q], F32) for j in range(2)]
-        parts = [placed("parts%d" % j, [P, 2, Q], F32) for j in range(4)]
-        staged = placed("staged", [P, 8, BANK], F32)
+        parts = [placed("parts%d" % j, [P, 2, hi - lo], F32) for j, (lo, hi) in enumerate(chunks)]
+        x_a = placed("x_a", [P, Q], F32)
+        x_last = [
+            x_a[:, 0:P],
+            placed("x_b", [P, Q], F32)[:],
+            x_a[:],
+            parts[0][:].rearrange("p a c -> p (a c)"),
+            placed("x_e", [P, P], F32)[:],
+        ]
+        staged = placed("staged", [P, 4 * M], F32)
         sums = {}
 
-        def plane(b, lo, hi):
-            return z0_planes[lo // Q] if b == 0 else z1_s[:, lo:hi]
+        def plane(j, b):
+            lo, hi = chunks[j]
+            if b == 1:
+                return z1_s[:, lo:hi]
+            k = min(j, len(plane_parts) - 1)
+            return z0_s[k][:, lo - plane_parts[k][0] : hi - plane_parts[k][0]]
 
         def score(j, b):
             lo, hi = chunks[j]
+            share = 4 // len(SCORE_BANKS[j])
             if b == 0:
-                sums[j] = [bank_tile(k, [P, 2, Q]) for k in SCORE_BANKS[j]]
+                sums[j] = [bank_tile(k, [P, share, hi - lo]) for k in SCORE_BANKS[j]]
             for n_tile in range(4):
                 col = N * b + P * n_tile
                 nc.tensor.matmul_mx(
-                    out=sums[j][n_tile // 2][:, n_tile % 2, :],
+                    out=sums[j][n_tile // share][:, n_tile % share, :],
                     lhsT=wo_w[:, col : col + P].bitcast(E4M3),
                     lhsT_scale=wo_s[:, col : col + P],
                     rhs=z_w[b][:, lo:hi].bitcast(E4M3),
-                    rhs_scale=plane(b, lo, hi),
-                    start=(b == 0 and n_tile % 2 == 0),
-                    stop=(b == 1 and n_tile % 2 == 1),
+                    rhs_scale=plane(j, b),
+                    start=(b == 0 and n_tile % share == 0),
+                    stop=(b == 1 and n_tile % share == share - 1),
                 )
 
-        def finish(j, b):
+        def late(k):
+            lo, hi = plane_parts[k]
+            quantise(z_w[0][:, lo:hi], z0_s[k][:], z[0][:, lo:hi, :])
+
+        def open_scores(j):
+            score(j, 0)
+
+        def finish(j):
             lo, hi = chunks[j]
-            quantise(z_w[b][:, lo:hi], plane(b, lo, hi), z[b][:, lo:hi, :])
-            score(j, b)
+            quantise(z_w[1][:, lo:hi], plane(j, 1), z[1][:, lo:hi, :])
+            score(j, 1)
 
         def fetch_last(j):
-            fetch(LAST, chunks[j][0], chunks[j][1], x_ring[j % 2][:])
+            fetch(LAST, chunks[j][0], chunks[j][1], x_last[j])
 
         def split_last(j):
-            split(parts[j][:, 0, :], parts[j][:, 1, :].bitcast(U32), x_ring[j % 2][:])
+            split(parts[j][:, 0, :], parts[j][:, 1, :].bitcast(U32), x_last[j])
 
         def subtract_turns(j):
             nc.vector.tensor_tensor(parts[j][:, 0, :], parts[j][:, 0, :], parts[j][:, 1, :].bitcast(I32), ALU.subtract)
@@ -431,11 +446,11 @@ def tile_list_buffer_pool_prefetch_kernel(
             nc.scalar.activation(cos67[:, lo:hi], parts[j][:, 0, :], ACT.Sin, bias=PHASE, scale=TURN)
 
         def product(j):
-            single(nc.vector, 1, *chunks[j])
+            single(nc.vector, LAST, *chunks[j])
 
         def weave(j):
             lo, hi = chunks[j]
-            word, copy = (U32, nc.scalar.copy) if j < SCALAR_WEAVES else (I32, nc.vector.tensor_copy)
+            word, copy = (U32, nc.scalar.copy) if j in SCALAR_WEAVES else (I32, nc.vector.tensor_copy)
             copy(
                 z[1][:, lo:hi, :].rearrange("p m t -> p (m t)").bitcast(word).rearrange("p (m w) -> p m w", w=2),
                 z_pairs[:].bitcast(word).rearrange("p (w m) -> p m w", w=2)[:, lo:hi, :],
@@ -443,48 +458,63 @@ def tile_list_buffer_pool_prefetch_kernel(
 
         def store(j):
             lo, hi = chunks[j]
+            share = 4 // len(sums[j])
             for k, bank in enumerate(sums[j]):
-                dest = staged[:, 2 * j + k, :]
-                copy = nc.vector.tensor_copy if (j == 3 and k == 1) else nc.scalar.copy
+                at = 4 * lo + k * share * (hi - lo)
+                dest = staged[:, at : at + share * (hi - lo)]
+                copy = nc.vector.tensor_copy if (j, k) in VECTOR_STORES else nc.scalar.copy
                 copy(dest, bank[:].rearrange("p a c -> p (a c)"))
                 nc.sync.dma_start(
-                    out[2 * P * k : 2 * P * (k + 1), lo:hi].rearrange("(a p) c -> p a c", a=2),
-                    dest.rearrange("p (a c) -> p a c", a=2),
+                    out[share * P * k : share * P * (k + 1), lo:hi].rearrange("(a p) c -> p a c", a=share),
+                    dest.rearrange("p (a c) -> p a c", a=share),
                 )
 
-        finish(0, 0)
+        late(0)
         fetch_last(0)
         fetch_last(1)
-        finish(1, 0)
+        open_scores(0)
+        late(1)
         split_last(0)
         subtract_turns(0)
-        split_last(1)
         sine(0)
         fetch_last(2)
+        split_last(1)
+        open_scores(1)
         subtract_turns(1)
         product(0)
-        weave(0)
-        fetch_last(3)
-        split_last(2)
         sine(1)
-        subtract_turns(2)
+        fetch_last(3)
+        weave(0)
+        split_last(2)
         product(1)
-        finish(0, 1)
-        split_last(3)
+        finish(0)
+        store(0)
+        subtract_turns(2)
         sine(2)
         weave(1)
-        finish(2, 0)
-        subtract_turns(3)
-        product(2)
-        finish(1, 1)
-        sine(3)
-        store(0)
-        weave(2)
-        product(3)
-        finish(2, 1)
-        finish(3, 0)
+        split_last(3)
+        fetch_last(4)
+        finish(1)
         store(1)
-        weave(3)
-        finish(3, 1)
+        late(2)
+        open_scores(2)
+        product(2)
+        subtract_turns(3)
+        sine(3)
+        split_last(4)
+        weave(2)
+        subtract_turns(4)
+        finish(2)
         store(2)
+        sine(4)
+        product(3)
+        late(3)
+        open_scores(3)
+        open_scores(4)
+        weave(3)
+        product(4)
+        finish(3)
+        weave(4)
+        finish(4)
         store(3)
+        store(4)

@@ -30,6 +30,7 @@ FLIP_BANKS = ((0, 1), (0, 1), (0, 1), (0, 1), (1, 1), (7, 7), (4, 5, 4, 5))
 BACK_BANKS = {4: (6, 7), 5: (4, 5), 6: (6, 7, 6, 7)}
 SCORE_BANKS = ((6,), (4, 5), (0, 1), (2, 3), (7, 6))
 EDGES = (0, 128, 384, 640, 896, 1024)
+PAIRED = EDGES[3]
 PLANE_EDGES = (0, 128, 384, 640, 1024)
 SCALAR_WEAVES = ()
 VECTOR_STORES = ((3, 1), (4, 1))
@@ -47,7 +48,7 @@ AT = {
     "z_pairs": 83, "z1": 91, "z_w1": 99, "z1_s": 103,
     "work0": 105, "heat0": 105, "works2": 121, "works3": 129, "ab": 128,
     "lane2": 137, "lane6": 137, "lane4": 145, "lane5": 153, "lane3": 161, "lane7": 161, "wo_s": 203,
-    "rest7": 175, "head7": 178,
+    "rest7": 175, "head7": 178, "weighed6": 179,
     "wo_bf": 175, "cos0": 183, "z0": 191, "z_w0": 199, "staged": 105,
 }
 
@@ -175,6 +176,7 @@ def tile_list_buffer_pool_prefetch_kernel(
             nc.vector.tensor_copy(dest, pages[i % 2][:].indirect(list3[:, lo // 16 : hi // 16]))
 
         lane = {i: placed("lane%d" % i, [P, 2 * S if i < LAST else S], F32) for i in range(2, TILES)}
+        weighed6 = placed("weighed6", [P, S], F32)
         head7 = placed("head7", [P, Q], F32)
         rest7 = placed("rest7", [P, S - Q], F32)
 
@@ -215,7 +217,7 @@ def tile_list_buffer_pool_prefetch_kernel(
 
         def weigh_tile(i):
             if i < LAST:
-                weigh(i, 0, S, lane[i][:, 0:S], heat_of(i))
+                weigh(i, 0, S, lane[i][:, 0:S] if i < 6 else weighed6[:], heat_of(i))
             else:
                 weigh(i, Q, S, rest7[:], lane[i][:, Q:S])
                 weigh(i, 0, Q, head7[:], lane[i][:, 0:Q])
@@ -227,7 +229,7 @@ def tile_list_buffer_pool_prefetch_kernel(
         whole = [placed("whole%d" % half, [P, BANK], U32) for half in range(2)]
         cos0 = placed("cos0", [P, 4, BANK], F32)
         cos45 = placed("cos45", [P, 2, M], F32)
-        cos67 = placed("cos67", [P, M], F32)
+        cos67 = placed("cos67", [P, M + M - PAIRED], F32)
         work0 = placed("work0", [P, 4, M], F32)
         works = [placed("works%d" % j, [P, 2, M], F32) for j in (2, 3)]
         z = [placed("z%d" % b, [P, M, 4], BF16) for b in range(2)]
@@ -276,7 +278,7 @@ def tile_list_buffer_pool_prefetch_kernel(
 
         def cosine(i, step, width=BANK):
             half, lo = divmod(step * width, BANK)
-            row = cos45[:, i - 4, :] if i < 6 else cos67[:]
+            row = cos45[:, i - 4, :] if i < 6 else cos67[:, 0:M]
             blocks = [
                 (turns[half][:, c : c + P], whole[half][:, c : c + P].bitcast(F32)) for c in range(lo, lo + width, P)
             ]
@@ -354,16 +356,16 @@ def tile_list_buffer_pool_prefetch_kernel(
 
         round_wo(1)
         period(2, lambda: heat_and_weigh(4), lambda: heat_and_weigh(5))
-        period(3, lambda: heat_and_weigh(6), lambda: make_heat(7))
-        period(4, lambda: (weigh_tile(7), blocks0(range(0, 2))), lambda: blocks0(range(2, 6)))
+        period(3, lambda: make_heat(6), lambda: make_heat(7))
+        period(4, lambda: (weigh_tile(6), weigh_tile(7), blocks0(range(0, 2))), lambda: blocks0(range(2, 6)))
         period(5, lambda: blocks0(range(6, 8)), lambda: None)
         for half in range(2):
             cosine(4, half)
             single(nc.gpsimd, 4, BANK * half, BANK * (half + 1))
 
-        put(6, 0, Q, lane[6][:, 0:Q])
+        put(6, 0, Q, weighed6[:, 0:Q])
         fetch(5, 0, M, lane[6][:, S : 2 * S])
-        put(6, Q, S, lane[6][:, Q:S])
+        put(6, Q, S, weighed6[:, Q:S])
         for half in range(2):
             after_fetch(5, half, lane[6][:, S + BANK * half : S + BANK * (half + 1)])
         for half in range(2):
@@ -378,7 +380,8 @@ def tile_list_buffer_pool_prefetch_kernel(
                 after_fetch(6, step, lane[LAST][:, Q * step : Q * (step + 1)])
             if step > 0:
                 cosine(6, step - 1, Q)
-                single(nc.gpsimd, 6, Q * (step - 1), Q * step)
+                if Q * (step - 1) < PAIRED:
+                    single(nc.gpsimd, 6, Q * (step - 1), min(Q * step, PAIRED))
 
         chunks = list(zip(EDGES[:-1], EDGES[1:]))
         plane_parts = list(zip(PLANE_EDGES[:-1], PLANE_EDGES[1:]))
@@ -443,10 +446,21 @@ def tile_list_buffer_pool_prefetch_kernel(
 
         def sine(j):
             lo, hi = chunks[j]
-            nc.scalar.activation(cos67[:, lo:hi], parts[j][:, 0, :], ACT.Sin, bias=PHASE, scale=TURN)
+            shift = M - PAIRED if lo >= PAIRED else 0
+            nc.scalar.activation(cos67[:, lo + shift : hi + shift], parts[j][:, 0, :], ACT.Sin, bias=PHASE, scale=TURN)
 
         def product(j):
-            single(nc.vector, LAST, *chunks[j])
+            lo, hi = chunks[j]
+            if lo < PAIRED:
+                single(nc.vector, LAST, lo, hi)
+            else:
+                both = cos67[:, PAIRED:].rearrange("p (t m) -> p t m", t=2)
+                nc.vector.tensor_tensor(
+                    pair_view[:, 1, lo:hi, :].rearrange("p (c f) t -> p c t f", f=4),
+                    both[:, :, lo - PAIRED : hi - PAIRED].rearrange("p t (c f) -> p c t f", f=4),
+                    works[1][:, :, lo:hi].rearrange("p t (c f) -> p c t f", f=4),
+                    ALU.mult,
+                )
 
         def weave(j):
             lo, hi = chunks[j]

@@ -23,33 +23,42 @@ TILES = H // P
 LAST = TILES - 1
 BANK = 512
 Q = 256
+CHUNKS = M // Q
 CAP = 2.5
 TURN = 2.0 * math.pi
-PHASE = math.pi / 2 - CAP
+QUADS = (0, 2, 1, 3)
+
 FLIP_BANKS = ((0, 1), (0, 1), (0, 1), (0, 1), (1, 1), (7, 7), (4, 5, 4, 5))
 BACK_BANKS = {4: (6, 7), 5: (4, 5), 6: (6, 7, 6, 7)}
-SCORE_BANKS = ((6,), (4, 5), (0, 1), (2, 3), (7, 6))
-EDGES = (0, 128, 384, 640, 896, 1024)
-PAIRED = EDGES[3]
-PLANE_EDGES = (0, 128, 384, 640, 1024)
-SCALAR_WEAVES = ()
-VECTOR_STORES = ((3, 1), (4, 1))
+SCORE_BANKS = ((6, 7), (4, 5), (0, 1), (2, 3, 6, 7))
+Z0_EDGES = (0, Q, 3 * Q, M)
+SCALAR_WEAVES = 2
+
 KIB = 1024
 AT = {
-    "tab_w0": 0, "planes1": 0, "x0": 2, "w4_back": 6, "w4_sorted": 3,
+    "tab_w0": 0, "planes1": 0, "x0": 2, "w4_sorted": 3, "w4_back": 6,
     "tab_w1": 8, "wo_raw": 8, "cos45": 8, "cos67": 16,
     "tab_s": 24, "planes0": 24,
-    "scale_rows": 29, "weights0": 26, "weights1": 30, "wo_w": 26,
-    "weight": 42, "picked_s": 45.5, "w4_next": 46, "w4_first": 47,
-    "ident": 48, "w4_s_raw": 48.25, "page1": 49, "page0": 57,
+    "weights0": 26, "wo_w": 26, "scale_rows": 29, "weights1": 30,
+    "weight": 42, "picked_s": 45.5, "w4_next": 46,
+    "w4_first": 47,
+    "ident": 48, "w4_s_raw": 48.25, "page1": 49,
+    "page0": 57,
     "v_w0": 65, "v_w1": 69, "turns0": 65, "whole0": 67, "whole1": 69, "turns1": 71,
-    "dealt": 73, "x_a": 65, "z0_s0": 66, "x_b": 66.25, "parts0": 68.25, "z0_s1": 69.25,
-    "parts1": 69.5, "parts2": 71.5, "parts3": 73.5, "parts4": 75.5, "z0_s2": 66.25, "z0_s3": 71.5, "x_e": 69.5,
-    "z_pairs": 83, "z1": 91, "z_w1": 99, "z1_s": 103,
-    "work0": 105, "heat0": 105, "works2": 121, "works3": 129, "ab": 128,
-    "lane2": 137, "lane6": 137, "lane4": 145, "lane5": 153, "lane3": 161, "lane7": 161, "wo_s": 203,
-    "rest7": 175, "head7": 178, "weighed6": 179,
-    "wo_bf": 175, "cos0": 183, "z0": 191, "z_w0": 199, "staged": 105,
+    "x_a": 65, "z0_s0": 66, "x_b": 66.25, "parts0": 67.25, "z0_s1": 69.25, "parts1": 69.75, "parts2": 71.75,
+    "dealt": 73, "parts3": 73.75, "z0_s2": 73.75, "z_pairs": 83, "z1": 91, "z_w1": 99, "z1_s": 103,
+    "heat0": 105, "work0": 105, "staged": 105,
+    "works0": 121, "heat1": 128, "works1": 129,
+    "lane2": 137, "heat6": 141,
+    "lane4": 145,
+    "lane5": 153,
+    "lane3": 161, "heat7": 161,
+    "wo_bf": 175, "rest7": 175, "head7": 178, "weighed6": 179,
+    "cos0": 183,
+    "z0": 191,
+    "z_w0": 199,
+    "wo_s": 203,
+    "per_turn": 204,
 }
 
 
@@ -62,9 +71,8 @@ def tile_list_buffer_pool_prefetch_kernel(
         shared = ctx.enter_context(tc.tile_pool(name="shared", bufs=1))
         psum = ctx.enter_context(tc.psum_pool(name="psum", bufs=1))
 
-        def placed(name, shape, dtype, at=None):
-            where = AT[name] if at is None else at
-            return shared.tile(shape, dtype, name=name, align_bytes=64, offset=int(where * KIB))
+        def placed(name, shape, dtype):
+            return shared.tile(shape, dtype, name=name, align_bytes=64, offset=int(AT[name] * KIB))
 
         def bank_tile(j, shape):
             return psum.tile(shape, F32, name="bank%d" % j, tag="bank%d" % j)
@@ -74,15 +82,14 @@ def tile_list_buffer_pool_prefetch_kernel(
         list3 = held.tile([P, M // 16], U16, name="list3")
         tab_s = placed("tab_s", [P, T], U8)
         nc.gpsimd.memset(tab_s[0:96, :].bitcast(I32), 0)
-        nc.sync.dma_start(list1[:], offs)
         nc.sync.dma_start(tab_s[96:128, :].bitcast(I32), tab_scales.bitcast(I32).rearrange("a g t -> g a t"))
+        nc.sync.dma_start(list1[:], offs)
         w4_s_raw = placed("w4_s_raw", [P, H // 4], I32)
         nc.sync.dma_start(w4_s_raw[96:128, :], w4_scales.bitcast(I32).rearrange("a g c -> g a c"))
         tab_w = [placed("tab_w%d" % a, [P, T], I32) for a in range(2)]
         w4_halves = w4_words.bitcast(I32).rearrange("a p (b c) -> b p a c", b=2)
         w4_first = placed("w4_first", [P, 8 * P], U8)
         nc.sync.dma_start(tab_w[0][:], tab_words[0].rearrange("p t i -> p (t i)").bitcast(I32))
-        quads = (0, 2, 1, 3)
         nc.sync.dma_start(w4_first[:].bitcast(I32).rearrange("p (a c) -> p a c", a=2), w4_halves[0][:, :, 0:P])
         nc.sync.dma_start(tab_w[1][:], tab_words[1].rearrange("p t i -> p (t i)").bitcast(I32))
         nc.sync.dma_start(list2[:], offs2)
@@ -90,8 +97,8 @@ def tile_list_buffer_pool_prefetch_kernel(
 
         pages = [placed("page%d" % j, [P, T2], F32) for j in range(2)]
         nc.gpsimd.memset(pages[0][:], 0.0)
-        planes = [placed("planes%d" % half, [P, S + H], U8) for half in range(2)]
 
+        planes = [placed("planes%d" % b, [P, S + H], U8) for b in range(2)]
         picked_s = placed("picked_s", [P, S], U8)
         nc.vector.tensor_copy(picked_s[:], tab_s[:].indirect(list1[:]))
         scale_rows = placed("scale_rows", [P, (S + H) // 4], I32)
@@ -106,16 +113,19 @@ def tile_list_buffer_pool_prefetch_kernel(
         make_identity(nc, ident[:])
         nc.gpsimd.memset(pages[1][:], 0.0)
 
-        def move_scales(half):
-            for quad in quads:
+        def move_scales(b):
+            for quad in QUADS:
                 nc.sync.dma_start(
-                    planes[half][32 * quad : 32 * quad + 4, :].bitcast(I32).rearrange("p (a c) -> p a c", a=2),
-                    scale_rows[96 + 8 * quad : 96 + 8 * quad + 8, S // 4 * half : S // 4 * (half + 1)],
+                    planes[b][32 * quad : 32 * quad + 4, :].bitcast(I32).rearrange("p (a c) -> p a c", a=2),
+                    scale_rows[96 + 8 * quad : 96 + 8 * quad + 8, S // 4 * b : S // 4 * (b + 1)],
                 )
+
+        def pick_words(a, lo, hi):
+            nc.vector.tensor_copy(v_w[a][:, lo:hi], tab_w[a][:].bitcast(U32).indirect(list1[:, lo // 16 : hi // 16]))
 
         move_scales(0)
         v_w = [placed("v_w%d" % a, [P, S], U32) for a in range(2)]
-        nc.vector.tensor_copy(v_w[0][:], tab_w[0][:].bitcast(U32).indirect(list1[:]))
+        pick_words(0, 0, S)
         weight = placed("weight", [P, S], F32)
         nc.sync.dma_start(weight[:, 0:BANK], wgs[:, 0:BANK])
         move_scales(1)
@@ -125,7 +135,7 @@ def tile_list_buffer_pool_prefetch_kernel(
         w4_back = placed("w4_back", [P, 2, H // 4], I32)
         nc.sync.dma_start(w4_back[:], w4_halves[1])
         for lo, hi in ((0, Q), (Q, BANK), (BANK, S)):
-            nc.vector.tensor_copy(v_w[1][:, lo:hi], tab_w[1][:].bitcast(U32).indirect(list1[:, lo // 16 : hi // 16]))
+            pick_words(1, lo, hi)
 
         wo_raw = placed("wo_raw", [P, 2, 4, N], F32)
         nc.sync.dma_start(wo_raw[:, 0, :, :], wo[0:512, :].rearrange("(p t) n -> p t n", t=4))
@@ -136,7 +146,7 @@ def tile_list_buffer_pool_prefetch_kernel(
         weights = [placed("weights0", [P, S], F32)[:]] + [weights1[:, t, :] for t in range(3)]
         wgs_rows = wgs.rearrange("(q t e) j -> t q e j", t=4, e=4)
         for t in range(4):
-            for quad in quads:
+            for quad in QUADS:
                 nc.sync.dma_start(weights[t][32 * quad : 32 * quad + 32, :], wgs_rows[t])
 
         w4_sorted = placed("w4_sorted", [P, 2 * H], U8)
@@ -149,13 +159,13 @@ def tile_list_buffer_pool_prefetch_kernel(
         def square(i, lo, hi, dest, j, passes=(1, 0)):
             bank = bank_tile(j, [P, hi - lo])
             for a in passes:
-                plane = 2 * BANK * a
+                base = 2 * BANK * a
                 nc.tensor.matmul_mx(
                     out=bank[:],
                     lhsT=w4_tile(i, a).bitcast(E2M1),
-                    lhsT_scale=planes[i // 4][:, plane + BANK + P * (i % 4) : plane + BANK + P * (i % 4 + 1)],
+                    lhsT_scale=planes[i // 4][:, base + BANK + P * (i % 4) : base + BANK + P * (i % 4 + 1)],
                     rhs=v_w[a][:, lo:hi].bitcast(E4M3),
-                    rhs_scale=planes[lo // BANK][:, plane + lo % BANK : plane + lo % BANK + hi - lo],
+                    rhs_scale=planes[lo // BANK][:, base + lo % BANK : base + lo % BANK + hi - lo],
                     start=(a == passes[0]),
                     stop=(a == passes[1]),
                 )
@@ -175,64 +185,63 @@ def tile_list_buffer_pool_prefetch_kernel(
         def fetch(i, lo, hi, dest):
             nc.vector.tensor_copy(dest, pages[i % 2][:].indirect(list3[:, lo // 16 : hi // 16]))
 
-        lane = {i: placed("lane%d" % i, [P, 2 * S if i < LAST else S], F32) for i in range(2, TILES)}
-        weighed6 = placed("weighed6", [P, S], F32)
+        lane = {i: placed("lane%d" % i, [P, 2 * S], F32) for i in range(2, 6)}
+        heat = {i: lane[i][:, S : 2 * S] for i in range(2, 6)}
+        heat[6] = placed("heat6", [P, S], F32)[:]
+        heat[LAST] = placed("heat7", [P, S], F32)[:]
+        weighed = {i: lane[i][:, 0:S] for i in range(2, 6)}
+        weighed[6] = placed("weighed6", [P, S], F32)[:]
         head7 = placed("head7", [P, Q], F32)
         rest7 = placed("rest7", [P, S - Q], F32)
 
         heat0 = placed("heat0", [P, S + Q], F32)
-        ab = placed("ab", [P, BANK], F32)
-        spill = heat0[:, S : S + Q]
-        first = [ab[:, 0:P], heat0[:, Q : Q + P]]
+        heat1 = placed("heat1", [P, BANK], F32)
+        third1 = heat0[:, S : S + Q]
+        last1 = lane[2][:, P : P + Q]
+        first = [heat1[:, 0:P], heat0[:, Q : Q + P]]
         for j in range(2):
             square(0, P * j, P * (j + 1), first[j], j, passes=(0, 1))
         for j in range(2):
             halve(heat0[:, P * j : P * (j + 1)], first[j])
-        square(1, 0, Q, ab[:, 0:Q], 0)
-        halve(ab[:, 0:Q], ab[:, 0:Q])
+        square(1, 0, Q, heat1[:, 0:Q], 0)
+        halve(heat1[:, 0:Q], heat1[:, 0:Q])
         square(0, Q, BANK, heat0[:, Q:BANK], 1)
-        square(1, Q, BANK, ab[:, Q:BANK], 0)
+        square(1, Q, BANK, heat1[:, Q:BANK], 0)
         halve(heat0[:, Q:BANK], heat0[:, Q:BANK])
-        halve(ab[:, Q:BANK], ab[:, Q:BANK])
+        halve(heat1[:, Q:BANK], heat1[:, Q:BANK])
         square(0, BANK, S, heat0[:, BANK:S], 1)
-        square(1, BANK, BANK + Q, spill, 0)
-        square(1, BANK + Q, S, lane[2][:, 0:Q], 1)
+        square(1, BANK, BANK + Q, third1, 0)
+        square(1, BANK + Q, S, last1, 1)
         halve(heat0[:, BANK : S + Q], heat0[:, BANK : S + Q])
-        halve(lane[2][:, 0:Q], lane[2][:, 0:Q])
-
-        def heat_of(i):
-            return lane[i][:, S : 2 * S] if i < LAST else lane[i][:]
+        halve(last1, last1)
 
         def make_heat(i):
             for half in range(2):
                 lo, hi = BANK * half, BANK * (half + 1)
-                square(i, lo, hi, heat_of(i)[:, lo:hi], half)
+                square(i, lo, hi, heat[i][:, lo:hi], half)
             for half in range(2):
                 lo, hi = BANK * half, BANK * (half + 1)
-                halve(heat_of(i)[:, lo:hi], heat_of(i)[:, lo:hi])
+                halve(heat[i][:, lo:hi], heat[i][:, lo:hi])
 
         def weigh(i, lo, hi, dest, values):
             factors = weight[:, lo:hi] if i < 4 else weights[i % 4][:, lo:hi]
             nc.gpsimd.tensor_tensor(dest, values, factors, ALU.mult)
 
         def weigh_tile(i):
-            if i < LAST:
-                weigh(i, 0, S, lane[i][:, 0:S] if i < 6 else weighed6[:], heat_of(i))
-            else:
-                weigh(i, Q, S, rest7[:], lane[i][:, Q:S])
-                weigh(i, 0, Q, head7[:], lane[i][:, 0:Q])
+            weigh(i, 0, S, weighed[i], heat[i])
 
         dealt = placed("dealt", [P, 8 * M], F32)
-        turns0 = dealt[:, 0 : 4 * M].rearrange("p (k t r) -> p k t r", t=4, r=P)
-        whole0 = dealt[:, 4 * M : 8 * M].bitcast(U32).rearrange("p (k t r) -> p k t r", t=4, r=P)
+        dealt_turns = dealt[:, 0 : 4 * M].rearrange("p (k t r) -> p k t r", t=4, r=P)
+        dealt_whole = dealt[:, 4 * M : 8 * M].bitcast(U32).rearrange("p (k t r) -> p k t r", t=4, r=P)
         turns = [placed("turns%d" % half, [P, BANK], F32) for half in range(2)]
         whole = [placed("whole%d" % half, [P, BANK], U32) for half in range(2)]
         cos0 = placed("cos0", [P, 4, BANK], F32)
         cos45 = placed("cos45", [P, 2, M], F32)
-        cos67 = placed("cos67", [P, M + M - PAIRED], F32)
+        cos67 = placed("cos67", [P, 2, M], F32)
         work0 = placed("work0", [P, 4, M], F32)
-        works = [placed("works%d" % j, [P, 2, M], F32) for j in (2, 3)]
-        z = [placed("z%d" % b, [P, M, 4], BF16) for b in range(2)]
+        works = [placed("works%d" % j, [P, 2, M], F32) for j in range(2)]
+        z0 = placed("z0", [P, M, 4], BF16)
+        z1 = placed("z1", [P, M, 4], BF16)
         z_w = [placed("z_w%d" % b, [P, M], U32) for b in range(2)]
         z_pairs = placed("z_pairs", [P, 2 * M], F32)
         pair_view = z_pairs[:].bitcast(BF16).rearrange("p (w m t) -> p w m t", w=2, t=2)
@@ -249,8 +258,6 @@ def tile_list_buffer_pool_prefetch_kernel(
         def split(u, count, x):
             nc.scalar.activation(count, x, ACT.Relu, bias=0.25, scale=-1.0 / TURN)
             nc.scalar.activation(u, x, ACT.Relu, bias=CAP / TURN, scale=-1.0 / TURN)
-
-        def negate(count):
             nc.scalar.activation(count.bitcast(F32), count, ACT.Copy, scale=-1.0)
 
         def turn_back(dest, blocks, j):
@@ -261,42 +268,46 @@ def tile_list_buffer_pool_prefetch_kernel(
                         bank[:, P * c : P * (c + 1)], pair[part], ident[:],
                         start=(part == 0 and c == 0), stop=(part == 1 and c == len(blocks) - 1), is_transpose=True,
                     )
-            nc.scalar.activation(dest, bank[:], ACT.Sin, bias=PHASE, scale=TURN)
+            nc.scalar.activation(dest, bank[:], ACT.Sin, bias=math.pi / 2 - CAP, scale=TURN)
 
         def after_fetch(i, step, x):
             width = x.shape[1]
             half, lo = divmod(step * width, BANK)
             bank = flip(FLIP_BANKS[i][step], x)
             if i < 4:
-                count = whole0[:, 4 * half : 4 * half + 4, :, 32 * i : 32 * i + 32]
-                u = turns0[:, 4 * half : 4 * half + 4, :, 32 * i : 32 * i + 32]
+                count = dealt_whole[:, 4 * half : 4 * half + 4, :, 32 * i : 32 * i + 32]
+                u = dealt_turns[:, 4 * half : 4 * half + 4, :, 32 * i : 32 * i + 32]
                 split(u, count, bank[:].rearrange("p (k q t) -> p k t q", k=4, t=4))
-                negate(count)
             else:
                 split(turns[half][:, lo : lo + width], whole[half][:, lo : lo + width], bank[:])
-                negate(whole[half][:, lo : lo + width])
 
-        def cosine(i, step, width=BANK):
+        def cosine(i, step, width):
             half, lo = divmod(step * width, BANK)
-            row = cos45[:, i - 4, :] if i < 6 else cos67[:, 0:M]
+            row = cos45[:, i - 4, :] if i < 6 else cos67[:, 0, :]
             blocks = [
                 (turns[half][:, c : c + P], whole[half][:, c : c + P].bitcast(F32)) for c in range(lo, lo + width, P)
             ]
             turn_back(row[:, step * width : (step + 1) * width], blocks, BACK_BANKS[i][step])
 
-        def block0(k):
-            ring = cos0[:, k % 4, :]
-            turn_back(ring, [(turns0[:, k, t, :], whole0[:, k, t, :].bitcast(F32)) for t in range(4)], k % 4)
-            nc.gpsimd.tensor_tensor(
-                z[0][:, P * k : P * (k + 1), :].rearrange("p (c f) t -> p c t f", f=4),
-                ring.rearrange("p (t c f) -> p c t f", t=4, f=4),
-                work0[:, :, P * k : P * (k + 1)].rearrange("p t (c f) -> p c t f", f=4),
-                ALU.mult,
-            )
+        def z0_blocks(lo, hi):
+            for k in range(lo, hi):
+                ring = cos0[:, k % 4, :]
+                codes = [(dealt_turns[:, k, t, :], dealt_whole[:, k, t, :].bitcast(F32)) for t in range(4)]
+                turn_back(ring, codes, k % 4)
+                nc.gpsimd.tensor_tensor(
+                    z0[:, P * k : P * (k + 1), :].rearrange("p (c f) t -> p c t f", f=4),
+                    ring.rearrange("p (t c f) -> p c t f", t=4, f=4),
+                    work0[:, :, P * k : P * (k + 1)].rearrange("p t (c f) -> p c t f", f=4),
+                    ALU.mult,
+                )
 
-        def single(engine, i, lo, hi):
-            row = cos45[:, i - 4, lo:hi] if i < 6 else cos67[:, lo:hi]
-            engine.tensor_tensor(pair_view[:, i // 2 - 2, lo:hi, i % 2], row, works[i // 2 - 2][:, i % 2, lo:hi], ALU.mult)
+        def z1_halves(i):
+            for half in range(2):
+                lo, hi = BANK * half, BANK * (half + 1)
+                cosine(i, half, BANK)
+                nc.gpsimd.tensor_tensor(
+                    pair_view[:, 0, lo:hi, i - 4], cos45[:, i - 4, lo:hi], works[0][:, i - 4, lo:hi], ALU.mult
+                )
 
         def quantise(codes, scales, values):
             nc.vector.quantize_mx(out=codes.bitcast(E4M3), scales=scales, in_=values.rearrange("p c t -> p (c t)"))
@@ -305,230 +316,196 @@ def tile_list_buffer_pool_prefetch_kernel(
             for c in range(0, N, P):
                 nc.scalar.copy(wo_bf[:, b, c : c + P, :], wo_raw[:, b, :, c : c + P].rearrange("p t n -> p n t"))
 
-        def period(i, after_a, after_c):
-            x = lane[i][:, S : 2 * S]
-            put(i, 0, Q, lane[i][:, 0:Q])
-            fetch(i - 1, 0, M, x)
-            if i == 4:
-                quantise_wo()
-            put(i, Q, S, lane[i][:, Q:S])
-            after_fetch(i - 1, 0, x[:, 0:BANK])
-            after_a()
-            after_fetch(i - 1, 1, x[:, BANK:M])
-            after_c()
-
+        per_turn = placed("per_turn", [P, Q], F32)
+        nc.gpsimd.memset(per_turn[:], 1.0)
         make_heat(2)
         make_heat(3)
         round_wo(0)
         x0 = placed("x0", [P, M], F32)
         put_fused(0, 0, Q, heat0[:, 0:Q])
-        put_fused(1, 0, Q, ab[:, 0:Q])
+        put_fused(1, 0, Q, heat1[:, 0:Q])
         put_fused(0, Q, BANK, heat0[:, Q:BANK])
-        put_fused(1, Q, BANK, ab[:, Q:BANK])
+        put_fused(1, Q, BANK, heat1[:, Q:BANK])
         put_fused(0, BANK, S, heat0[:, BANK:S])
-        put_fused(1, BANK, BANK + Q, spill)
+        put_fused(1, BANK, BANK + Q, third1)
         fetch(0, 0, M, x0[:])
-        weigh(1, S - Q, S, spill, lane[2][:, 0:Q])
-        put(1, S - Q, S, spill)
-        weigh_tile(2)
+        weigh(1, S - Q, S, third1, last1)
+        put(1, S - Q, S, third1)
+        for lo, hi in ((0, Q), (Q, S)):
+            weigh(2, lo, hi, weighed[2][:, lo:hi], heat[2][:, lo:hi])
         for half in range(2):
             after_fetch(0, half, x0[:, BANK * half : BANK * (half + 1)])
+        weigh_tile(3)
         nc.gpsimd.tensor_copy(
             w4_sorted[:].bitcast(I32).rearrange("p (a t q w) -> p a t q w", a=2, t=4, w=2),
             w4_back[:].rearrange("p a (q t w) -> p a t q w", t=4, w=2),
         )
-        weigh_tile(3)
         nc.sync.dma_start(work0[:], work[0:512, :].rearrange("(p t) m -> p t m", t=4))
         work_rows = work[512:1024, :].rearrange("(q t e) m -> t q e m", t=4, e=4)
         for t in range(4):
             nc.sync.dma_start(works[t // 2][:, t % 2, :], work_rows[t])
-
-        def heat_and_weigh(i):
-            make_heat(i)
-            weigh_tile(i)
-
-        def quantise_wo():
-            quantise(wo_w[:], wo_s[:], wo_bf[:].rearrange("p b n t -> p (b n) t"))
-
-        def blocks0(ks):
-            for k in ks:
-                block0(k)
-
         round_wo(1)
-        period(2, lambda: heat_and_weigh(4), lambda: heat_and_weigh(5))
-        period(3, lambda: make_heat(6), lambda: make_heat(7))
-        period(4, lambda: (weigh_tile(6), weigh_tile(7), blocks0(range(0, 2))), lambda: blocks0(range(2, 6)))
-        period(5, lambda: blocks0(range(6, 8)), lambda: None)
-        for half in range(2):
-            cosine(4, half)
-            single(nc.gpsimd, 4, BANK * half, BANK * (half + 1))
+        nc.scalar.activation(per_turn[:], per_turn[:], ACT.Copy, scale=-1.0 / TURN)
 
-        put(6, 0, Q, weighed6[:, 0:Q])
-        fetch(5, 0, M, lane[6][:, S : 2 * S])
-        put(6, Q, S, weighed6[:, Q:S])
+        def put_first(i):
+            put(i, 0, Q, weighed[i][:, 0:Q])
+            fetch(i - 1, 0, M, heat[i])
+
+        def put_rest(i):
+            put(i, Q, S, weighed[i][:, Q:S])
+
+        def x_half(i, half):
+            after_fetch(i, half, heat[i + 1][:, BANK * half : BANK * (half + 1)])
+
+        put_first(2)
+        put_rest(2)
         for half in range(2):
-            after_fetch(5, half, lane[6][:, S + BANK * half : S + BANK * (half + 1)])
+            x_half(1, half)
+            make_heat(4 + half)
+            weigh_tile(4 + half)
+
+        put_first(3)
+        put_rest(3)
         for half in range(2):
-            cosine(5, half)
-            single(nc.gpsimd, 5, BANK * half, BANK * (half + 1))
+            x_half(2, half)
+            make_heat(6 + half)
+
+        put_first(4)
+        quantise(wo_w[:], wo_s[:], wo_bf[:].rearrange("p b n t -> p (b n) t"))
+        put_rest(4)
+        x_half(3, 0)
+        weigh_tile(6)
+        weigh(LAST, Q, S, rest7[:], heat[LAST][:, Q:S])
+        weigh(LAST, 0, Q, head7[:], heat[LAST][:, 0:Q])
+        z0_blocks(0, 2)
+        x_half(3, 1)
+        z0_blocks(2, 6)
+
+        put_first(5)
+        put_rest(5)
+        x_half(4, 0)
+        z0_blocks(6, 8)
+        x_half(4, 1)
+        z1_halves(4)
+
+        put_first(6)
+        put_rest(6)
+        for half in range(2):
+            x_half(5, half)
+        z1_halves(5)
+
         put(LAST, 0, Q, head7[:])
         for lo in (0, BANK):
-            fetch(6, lo, lo + BANK, lane[LAST][:, lo : lo + BANK])
+            fetch(6, lo, lo + BANK, heat[LAST][:, lo : lo + BANK])
         put(LAST, Q, S, rest7[:])
-        for step in range(5):
-            if step < 4:
-                after_fetch(6, step, lane[LAST][:, Q * step : Q * (step + 1)])
+        for step in range(CHUNKS + 1):
+            if step < CHUNKS:
+                after_fetch(6, step, heat[LAST][:, Q * step : Q * (step + 1)])
             if step > 0:
                 cosine(6, step - 1, Q)
-                if Q * (step - 1) < PAIRED:
-                    single(nc.gpsimd, 6, Q * (step - 1), min(Q * step, PAIRED))
 
-        chunks = list(zip(EDGES[:-1], EDGES[1:]))
-        plane_parts = list(zip(PLANE_EDGES[:-1], PLANE_EDGES[1:]))
-        z0_s = [placed("z0_s%d" % j, [P, hi - lo], U8) for j, (lo, hi) in enumerate(plane_parts)]
+        z0_parts = list(zip(Z0_EDGES[:-1], Z0_EDGES[1:]))
+        z0_s = [placed("z0_s%d" % k, [P, hi - lo], U8) for k, (lo, hi) in enumerate(z0_parts)]
         z1_s = placed("z1_s", [P, M], U8)
-        parts = [placed("parts%d" % j, [P, 2, hi - lo], F32) for j, (lo, hi) in enumerate(chunks)]
+        parts = [placed("parts%d" % j, [P, 2, Q], F32) for j in range(CHUNKS)]
         x_a = placed("x_a", [P, Q], F32)
-        x_last = [
-            x_a[:, 0:P],
-            placed("x_b", [P, Q], F32)[:],
-            x_a[:],
-            parts[0][:].rearrange("p a c -> p (a c)"),
-            placed("x_e", [P, P], F32)[:],
-        ]
+        x_last = [x_a[:], placed("x_b", [P, Q], F32)[:], x_a[:], parts[0][:, 0, :]]
         staged = placed("staged", [P, 4 * M], F32)
         sums = {}
 
-        def plane(j, b):
-            lo, hi = chunks[j]
-            if b == 1:
-                return z1_s[:, lo:hi]
-            k = min(j, len(plane_parts) - 1)
-            return z0_s[k][:, lo - plane_parts[k][0] : hi - plane_parts[k][0]]
-
-        def score(j, b):
-            lo, hi = chunks[j]
+        def score(j, b, scales):
             share = 4 // len(SCORE_BANKS[j])
-            if b == 0:
-                sums[j] = [bank_tile(k, [P, share, hi - lo]) for k in SCORE_BANKS[j]]
             for n_tile in range(4):
                 col = N * b + P * n_tile
                 nc.tensor.matmul_mx(
                     out=sums[j][n_tile // share][:, n_tile % share, :],
                     lhsT=wo_w[:, col : col + P].bitcast(E4M3),
                     lhsT_scale=wo_s[:, col : col + P],
-                    rhs=z_w[b][:, lo:hi].bitcast(E4M3),
-                    rhs_scale=plane(j, b),
+                    rhs=z_w[b][:, Q * j : Q * (j + 1)].bitcast(E4M3),
+                    rhs_scale=scales,
                     start=(b == 0 and n_tile % share == 0),
                     stop=(b == 1 and n_tile % share == share - 1),
                 )
 
-        def late(k):
-            lo, hi = plane_parts[k]
-            quantise(z_w[0][:, lo:hi], z0_s[k][:], z[0][:, lo:hi, :])
+        def quantise_z0(k):
+            lo, hi = z0_parts[k]
+            quantise(z_w[0][:, lo:hi], z0_s[k][:], z0[:, lo:hi, :])
 
-        def open_scores(j):
-            score(j, 0)
-
-        def finish(j):
-            lo, hi = chunks[j]
-            quantise(z_w[1][:, lo:hi], plane(j, 1), z[1][:, lo:hi, :])
-            score(j, 1)
+        def first_pass(j, k):
+            sums[j] = [bank_tile(bank, [P, 4 // len(SCORE_BANKS[j]), Q]) for bank in SCORE_BANKS[j]]
+            at = Q * j - z0_parts[k][0]
+            score(j, 0, z0_s[k][:, at : at + Q])
 
         def fetch_last(j):
-            fetch(LAST, chunks[j][0], chunks[j][1], x_last[j])
+            window = pages[LAST % 2][:].indirect(list3[:, Q // 16 * j : Q // 16 * (j + 1)])
+            nc.vector.tensor_tensor(x_last[j], window, per_turn[:], ALU.mult)
 
-        def split_last(j):
-            split(parts[j][:, 0, :], parts[j][:, 1, :].bitcast(U32), x_last[j])
+        def count_turns(j):
+            nc.scalar.activation(parts[j][:, 1, :].bitcast(U32), x_last[j], ACT.Relu, bias=0.25)
 
-        def subtract_turns(j):
-            nc.vector.tensor_tensor(parts[j][:, 0, :], parts[j][:, 0, :], parts[j][:, 1, :].bitcast(I32), ALU.subtract)
+        def reduce_turns(j):
+            nc.vector.scalar_tensor_tensor(
+                parts[j][:, 0, :], x_last[j], -CAP / TURN, parts[j][:, 1, :].bitcast(I32), ALU.max, ALU.subtract
+            )
 
         def sine(j):
-            lo, hi = chunks[j]
-            shift = M - PAIRED if lo >= PAIRED else 0
-            nc.scalar.activation(cos67[:, lo + shift : hi + shift], parts[j][:, 0, :], ACT.Sin, bias=PHASE, scale=TURN)
+            dest = cos67[:, 1, Q * j : Q * (j + 1)]
+            nc.scalar.activation(dest, parts[j][:, 0, :], ACT.Sin, bias=math.pi / 2, scale=TURN)
 
-        def product(j):
-            lo, hi = chunks[j]
-            if lo < PAIRED:
-                single(nc.vector, LAST, lo, hi)
-            else:
-                both = cos67[:, PAIRED:].rearrange("p (t m) -> p t m", t=2)
-                nc.vector.tensor_tensor(
-                    pair_view[:, 1, lo:hi, :].rearrange("p (c f) t -> p c t f", f=4),
-                    both[:, :, lo - PAIRED : hi - PAIRED].rearrange("p t (c f) -> p c t f", f=4),
-                    works[1][:, :, lo:hi].rearrange("p t (c f) -> p c t f", f=4),
-                    ALU.mult,
-                )
+        def multiply(j):
+            lo, hi = Q * j, Q * (j + 1)
+            nc.vector.tensor_tensor(
+                pair_view[:, 1, lo:hi, :].rearrange("p (c f) t -> p c t f", f=4),
+                cos67[:, :, lo:hi].rearrange("p t (c f) -> p c t f", f=4),
+                works[1][:, :, lo:hi].rearrange("p t (c f) -> p c t f", f=4),
+                ALU.mult,
+            )
 
         def weave(j):
-            lo, hi = chunks[j]
-            word, copy = (U32, nc.scalar.copy) if j in SCALAR_WEAVES else (I32, nc.vector.tensor_copy)
+            lo, hi = Q * j, Q * (j + 1)
+            word, copy = (U32, nc.scalar.copy) if j < SCALAR_WEAVES else (I32, nc.vector.tensor_copy)
             copy(
-                z[1][:, lo:hi, :].rearrange("p m t -> p (m t)").bitcast(word).rearrange("p (m w) -> p m w", w=2),
+                z1[:, lo:hi, :].rearrange("p m t -> p (m t)").bitcast(word).rearrange("p (m w) -> p m w", w=2),
                 z_pairs[:].bitcast(word).rearrange("p (w m) -> p m w", w=2)[:, lo:hi, :],
             )
 
+        def second_pass(j):
+            lo, hi = Q * j, Q * (j + 1)
+            quantise(z_w[1][:, lo:hi], z1_s[:, lo:hi], z1[:, lo:hi, :])
+            score(j, 1, z1_s[:, lo:hi])
+
         def store(j):
-            lo, hi = chunks[j]
             share = 4 // len(sums[j])
             for k, bank in enumerate(sums[j]):
-                at = 4 * lo + k * share * (hi - lo)
-                dest = staged[:, at : at + share * (hi - lo)]
-                copy = nc.vector.tensor_copy if (j, k) in VECTOR_STORES else nc.scalar.copy
+                at = Q * (4 * j + k * share)
+                dest = staged[:, at : at + share * Q]
+                copy = nc.vector.tensor_copy if (j == CHUNKS - 1 and k % 2 == 1) else nc.scalar.copy
                 copy(dest, bank[:].rearrange("p a c -> p (a c)"))
                 nc.sync.dma_start(
-                    out[share * P * k : share * P * (k + 1), lo:hi].rearrange("(a p) c -> p a c", a=share),
+                    out[share * P * k : share * P * (k + 1), Q * j : Q * (j + 1)].rearrange("(a p) c -> p a c", a=share),
                     dest.rearrange("p (a c) -> p a c", a=share),
                 )
 
-        late(0)
-        fetch_last(0)
-        fetch_last(1)
-        open_scores(0)
-        late(1)
-        split_last(0)
-        subtract_turns(0)
-        sine(0)
-        fetch_last(2)
-        split_last(1)
-        open_scores(1)
-        subtract_turns(1)
-        product(0)
-        sine(1)
-        fetch_last(3)
-        weave(0)
-        split_last(2)
-        product(1)
-        finish(0)
-        store(0)
-        subtract_turns(2)
-        sine(2)
-        weave(1)
-        split_last(3)
-        fetch_last(4)
-        finish(1)
-        store(1)
-        late(2)
-        open_scores(2)
-        product(2)
-        subtract_turns(3)
-        sine(3)
-        split_last(4)
-        weave(2)
-        subtract_turns(4)
-        finish(2)
-        store(2)
-        sine(4)
-        product(3)
-        late(3)
-        open_scores(3)
-        open_scores(4)
-        weave(3)
-        product(4)
-        finish(3)
-        weave(4)
-        finish(4)
-        store(3)
-        store(4)
+        def stage(work_on, j):
+            if 0 <= j < CHUNKS:
+                work_on(j)
+
+        quantise_z0(0)
+        first_pass(0, 0)
+        for step in range(CHUNKS + 4):
+            stage(fetch_last, step)
+            if step == 1:
+                quantise_z0(1)
+                first_pass(1, 1)
+                first_pass(2, 1)
+            stage(reduce_turns, step - 1)
+            stage(weave, step - 3)
+            if step == CHUNKS + 1:
+                quantise_z0(2)
+            stage(count_turns, step)
+            stage(sine, step - 1)
+            stage(second_pass, step - 3)
+            stage(multiply, step - 2)
+            stage(store, step - 4)
+            if step == CHUNKS + 1:
+                first_pass(CHUNKS - 1, 2)

import math
from contextlib import ExitStack

import concourse.mybir as mybir
from concourse.masks import make_identity

K, H, N, T, S, T2, M = 1024, 1024, 512, 2048, 1024, 2048, 1024
FLOPS = 2 * K * H * S + 2 * H * N * M

F32 = mybir.dt.float32
BF16 = mybir.dt.bfloat16
I32 = mybir.dt.int32
U32 = mybir.dt.uint32
U16 = mybir.dt.uint16
U8 = mybir.dt.uint8
E4M3 = mybir.dt.float8_e4m3fn_x4
E2M1 = mybir.dt.float4_e2m1fn_x4
ACT = mybir.ActivationFunctionType
ALU = mybir.AluOpType

P = 128
TILES = H // P
LAST = TILES - 1
BANK = 512
Q = 256
CHUNKS = M // Q
CAP = 2.5
TURN = 2.0 * math.pi
QUADS = (0, 2, 1, 3)

FLIP_BANKS = ((0, 1), (0, 1), (0, 1), (0, 1), (1, 1), (7, 7), (4, 5, 4, 5))
BACK_BANKS = {4: (6, 7), 5: (4, 5), 6: (6, 7, 6, 7)}
SCORE_BANKS = ((6, 7), (4, 5), (0, 1), (2, 3, 6, 7))
Z0_EDGES = (0, Q, 3 * Q, M)
SCALAR_WEAVES = 2

KIB = 1024
AT = {
    "tab_w0": 0, "planes1": 0, "x0": 2, "w4_sorted": 3, "w4_back": 6,
    "tab_w1": 8, "wo_raw": 8, "cos45": 8, "cos67": 16,
    "tab_s": 24, "planes0": 24,
    "weights0": 26, "wo_w": 26, "scale_rows": 29, "weights1": 30,
    "weight": 42, "picked_s": 45.5, "w4_next": 46,
    "w4_first": 47,
    "ident": 48, "w4_s_raw": 48.25, "page1": 49,
    "page0": 57,
    "v_w0": 65, "v_w1": 69, "turns0": 65, "whole0": 67, "whole1": 69, "turns1": 71,
    "x_a": 65, "z0_s0": 66, "x_b": 66.25, "parts0": 67.25, "z0_s1": 69.25, "parts1": 69.75, "parts2": 71.75,
    "dealt": 73, "parts3": 73.75, "z0_s2": 73.75, "z_pairs": 83, "z1": 91, "z_w1": 99, "z1_s": 103,
    "heat0": 105, "work0": 105, "staged": 105,
    "works0": 121, "heat1": 128, "works1": 129,
    "lane2": 137, "heat6": 141,
    "lane4": 145,
    "lane5": 153,
    "lane3": 161, "heat7": 161,
    "wo_bf": 175, "rest7": 175, "head7": 178, "weighed6": 179,
    "cos0": 183,
    "z0": 191,
    "z_w0": 199,
    "wo_s": 203,
    "per_turn": 204,
}


def tile_list_buffer_pool_prefetch_kernel(
    tc, tab_words, tab_scales, offs, w4_words, w4_scales, wgs, offs2, offs3, work, wo, out
):
    nc = tc.nc
    with ExitStack() as ctx:
        held = ctx.enter_context(tc.tile_pool(name="held", bufs=1))
        shared = ctx.enter_context(tc.tile_pool(name="shared", bufs=1))
        psum = ctx.enter_context(tc.psum_pool(name="psum", bufs=1))

        def placed(name, shape, dtype):
            return shared.tile(shape, dtype, name=name, align_bytes=64, offset=int(AT[name] * KIB))

        def bank_tile(j, shape):
            return psum.tile(shape, F32, name="bank%d" % j, tag="bank%d" % j)

        list1 = held.tile([P, S // 16], U16, name="list1")
        list2 = held.tile([P, S // 16], U16, name="list2")
        list3 = held.tile([P, M // 16], U16, name="list3")
        tab_s = placed("tab_s", [P, T], U8)
        nc.gpsimd.memset(tab_s[0:96, :].bitcast(I32), 0)
        nc.sync.dma_start(tab_s[96:128, :].bitcast(I32), tab_scales.bitcast(I32).rearrange("a g t -> g a t"))
        nc.sync.dma_start(list1[:], offs)
        w4_s_raw = placed("w4_s_raw", [P, H // 4], I32)
        nc.sync.dma_start(w4_s_raw[96:128, :], w4_scales.bitcast(I32).rearrange("a g c -> g a c"))
        tab_w = [placed("tab_w%d" % a, [P, T], I32) for a in range(2)]
        w4_halves = w4_words.bitcast(I32).rearrange("a p (b c) -> b p a c", b=2)
        w4_first = placed("w4_first", [P, 8 * P], U8)
        nc.sync.dma_start(tab_w[0][:], tab_words[0].rearrange("p t i -> p (t i)").bitcast(I32))
        nc.sync.dma_start(w4_first[:].bitcast(I32).rearrange("p (a c) -> p a c", a=2), w4_halves[0][:, :, 0:P])
        nc.sync.dma_start(tab_w[1][:], tab_words[1].rearrange("p t i -> p (t i)").bitcast(I32))
        nc.sync.dma_start(list2[:], offs2)
        nc.sync.dma_start(list3[:], offs3)

        pages = [placed("page%d" % j, [P, T2], F32) for j in range(2)]
        nc.gpsimd.memset(pages[0][:], 0.0)

        planes = [placed("planes%d" % b, [P, S + H], U8) for b in range(2)]
        picked_s = placed("picked_s", [P, S], U8)
        nc.vector.tensor_copy(picked_s[:], tab_s[:].indirect(list1[:]))
        scale_rows = placed("scale_rows", [P, (S + H) // 4], I32)
        rows = scale_rows[96:128, :].rearrange("p (b s c) -> p b s c", b=2, s=2)
        nc.vector.tensor_copy(rows[:, 0, 1, :], w4_s_raw[96:128, 0 : H // 8])
        nc.vector.tensor_copy(
            rows[:, 1, 1, :].rearrange("p (t q) -> p t q", t=4),
            w4_s_raw[96:128, H // 8 : H // 4].rearrange("p (q t) -> p t q", t=4),
        )
        nc.vector.tensor_copy(rows[:, :, 0, :], picked_s[96:128, :].bitcast(I32).rearrange("p (b c) -> p b c", b=2))
        ident = placed("ident", [P, P], F32)
        make_identity(nc, ident[:])
        nc.gpsimd.memset(pages[1][:], 0.0)

        def move_scales(b):
            for quad in QUADS:
                nc.sync.dma_start(
                    planes[b][32 * quad : 32 * quad + 4, :].bitcast(I32).rearrange("p (a c) -> p a c", a=2),
                    scale_rows[96 + 8 * quad : 96 + 8 * quad + 8, S // 4 * b : S // 4 * (b + 1)],
                )

        def pick_words(a, lo, hi):
            nc.vector.tensor_copy(v_w[a][:, lo:hi], tab_w[a][:].bitcast(U32).indirect(list1[:, lo // 16 : hi // 16]))

        move_scales(0)
        v_w = [placed("v_w%d" % a, [P, S], U32) for a in range(2)]
        pick_words(0, 0, S)
        weight = placed("weight", [P, S], F32)
        nc.sync.dma_start(weight[:, 0:BANK], wgs[:, 0:BANK])
        move_scales(1)
        nc.sync.dma_start(weight[:, BANK:S], wgs[:, BANK:S])
        w4_next = placed("w4_next", [P, 8 * P], U8)
        nc.sync.dma_start(w4_next[:].bitcast(I32).rearrange("p (a c) -> p a c", a=2), w4_halves[0][:, :, P:])
        w4_back = placed("w4_back", [P, 2, H // 4], I32)
        nc.sync.dma_start(w4_back[:], w4_halves[1])
        for lo, hi in ((0, Q), (Q, BANK), (BANK, S)):
            pick_words(1, lo, hi)

        wo_raw = placed("wo_raw", [P, 2, 4, N], F32)
        nc.sync.dma_start(wo_raw[:, 0, :, :], wo[0:512, :].rearrange("(p t) n -> p t n", t=4))
        wo_rows = wo[512:1024, :].rearrange("(q t e) n -> t q e n", t=4, e=4)
        for t in range(4):
            nc.sync.dma_start(wo_raw[:, 1, t, :], wo_rows[t])
        weights1 = placed("weights1", [P, 3, S], F32)
        weights = [placed("weights0", [P, S], F32)[:]] + [weights1[:, t, :] for t in range(3)]
        wgs_rows = wgs.rearrange("(q t e) j -> t q e j", t=4, e=4)
        for t in range(4):
            for quad in QUADS:
                nc.sync.dma_start(weights[t][32 * quad : 32 * quad + 32, :], wgs_rows[t])

        w4_sorted = placed("w4_sorted", [P, 2 * H], U8)

        def w4_tile(i, a):
            holder, first_tile, tiles = (w4_first, 0, 2) if i < 2 else (w4_next, 2, 2) if i < 4 else (w4_sorted, 4, 4)
            col = P * (tiles * a + i - first_tile)
            return holder[:, 2 * col : 2 * (col + P)]

        def square(i, lo, hi, dest, j, passes=(1, 0)):
            bank = bank_tile(j, [P, hi - lo])
            for a in passes:
                base = 2 * BANK * a
                nc.tensor.matmul_mx(
                    out=bank[:],
                    lhsT=w4_tile(i, a).bitcast(E2M1),
                    lhsT_scale=planes[i // 4][:, base + BANK + P * (i % 4) : base + BANK + P * (i % 4 + 1)],
                    rhs=v_w[a][:, lo:hi].bitcast(E4M3),
                    rhs_scale=planes[lo // BANK][:, base + lo % BANK : base + lo % BANK + hi - lo],
                    start=(a == passes[0]),
                    stop=(a == passes[1]),
                )
            nc.scalar.activation(dest, bank[:], ACT.Square, bias=1.0)

        def halve(dest, values):
            nc.scalar.activation(dest, values, ACT.Identity, bias=-0.5, scale=0.5)

        def put_fused(i, lo, hi, values):
            nc.vector.tensor_tensor(
                pages[i % 2][:].indirect(list2[:, lo // 16 : hi // 16]), values, weight[:, lo:hi], ALU.mult
            )

        def put(i, lo, hi, values):
            nc.vector.tensor_copy(pages[i % 2][:].indirect(list2[:, lo // 16 : hi // 16]), values)

        def fetch(i, lo, hi, dest):
            nc.vector.tensor_copy(dest, pages[i % 2][:].indirect(list3[:, lo // 16 : hi // 16]))

        lane = {i: placed("lane%d" % i, [P, 2 * S], F32) for i in range(2, 6)}
        heat = {i: lane[i][:, S : 2 * S] for i in range(2, 6)}
        heat[6] = placed("heat6", [P, S], F32)[:]
        heat[LAST] = placed("heat7", [P, S], F32)[:]
        weighed = {i: lane[i][:, 0:S] for i in range(2, 6)}
        weighed[6] = placed("weighed6", [P, S], F32)[:]
        head7 = placed("head7", [P, Q], F32)
        rest7 = placed("rest7", [P, S - Q], F32)

        heat0 = placed("heat0", [P, S + Q], F32)
        heat1 = placed("heat1", [P, BANK], F32)
        third1 = heat0[:, S : S + Q]
        last1 = lane[2][:, P : P + Q]
        first = [heat1[:, 0:P], heat0[:, Q : Q + P]]
        for j in range(2):
            square(0, P * j, P * (j + 1), first[j], j, passes=(0, 1))
        for j in range(2):
            halve(heat0[:, P * j : P * (j + 1)], first[j])
        square(1, 0, Q, heat1[:, 0:Q], 0)
        halve(heat1[:, 0:Q], heat1[:, 0:Q])
        square(0, Q, BANK, heat0[:, Q:BANK], 1)
        square(1, Q, BANK, heat1[:, Q:BANK], 0)
        halve(heat0[:, Q:BANK], heat0[:, Q:BANK])
        halve(heat1[:, Q:BANK], heat1[:, Q:BANK])
        square(0, BANK, S, heat0[:, BANK:S], 1)
        square(1, BANK, BANK + Q, third1, 0)
        square(1, BANK + Q, S, last1, 1)
        halve(heat0[:, BANK : S + Q], heat0[:, BANK : S + Q])
        halve(last1, last1)

        def make_heat(i):
            for half in range(2):
                lo, hi = BANK * half, BANK * (half + 1)
                square(i, lo, hi, heat[i][:, lo:hi], half)
            for half in range(2):
                lo, hi = BANK * half, BANK * (half + 1)
                halve(heat[i][:, lo:hi], heat[i][:, lo:hi])

        def weigh(i, lo, hi, dest, values):
            factors = weight[:, lo:hi] if i < 4 else weights[i % 4][:, lo:hi]
            nc.gpsimd.tensor_tensor(dest, values, factors, ALU.mult)

        def weigh_tile(i):
            weigh(i, 0, S, weighed[i], heat[i])

        dealt = placed("dealt", [P, 8 * M], F32)
        dealt_turns = dealt[:, 0 : 4 * M].rearrange("p (k t r) -> p k t r", t=4, r=P)
        dealt_whole = dealt[:, 4 * M : 8 * M].bitcast(U32).rearrange("p (k t r) -> p k t r", t=4, r=P)
        turns = [placed("turns%d" % half, [P, BANK], F32) for half in range(2)]
        whole = [placed("whole%d" % half, [P, BANK], U32) for half in range(2)]
        cos0 = placed("cos0", [P, 4, BANK], F32)
        cos45 = placed("cos45", [P, 2, M], F32)
        cos67 = placed("cos67", [P, 2, M], F32)
        work0 = placed("work0", [P, 4, M], F32)
        works = [placed("works%d" % j, [P, 2, M], F32) for j in range(2)]
        z0 = placed("z0", [P, M, 4], BF16)
        z1 = placed("z1", [P, M, 4], BF16)
        z_w = [placed("z_w%d" % b, [P, M], U32) for b in range(2)]
        z_pairs = placed("z_pairs", [P, 2 * M], F32)
        pair_view = z_pairs[:].bitcast(BF16).rearrange("p (w m t) -> p w m t", w=2, t=2)
        wo_bf = placed("wo_bf", [P, 2, N, 4], BF16)
        wo_w = placed("wo_w", [P, 2 * N], U32)
        wo_s = placed("wo_s", [P, 2 * N], U8)

        def flip(j, x):
            bank = bank_tile(j, [P, x.shape[1]])
            for c in range(0, x.shape[1], P):
                nc.tensor.transpose(bank[:, c : c + P], x[:, c : c + P], ident[:])
            return bank

        def split(u, count, x):
            nc.scalar.activation(count, x, ACT.Relu, bias=0.25, scale=-1.0 / TURN)
            nc.scalar.activation(u, x, ACT.Relu, bias=CAP / TURN, scale=-1.0 / TURN)
            nc.scalar.activation(count.bitcast(F32), count, ACT.Copy, scale=-1.0)

        def turn_back(dest, blocks, j):
            bank = bank_tile(j, [P, P * len(blocks)])
            for part in range(2):
                for c, pair in enumerate(blocks):
                    nc.tensor.matmul(
                        bank[:, P * c : P * (c + 1)], pair[part], ident[:],
                        start=(part == 0 and c == 0), stop=(part == 1 and c == len(blocks) - 1), is_transpose=True,
                    )
            nc.scalar.activation(dest, bank[:], ACT.Sin, bias=math.pi / 2 - CAP, scale=TURN)

        def after_fetch(i, step, x):
            width = x.shape[1]
            half, lo = divmod(step * width, BANK)
            bank = flip(FLIP_BANKS[i][step], x)
            if i < 4:
                count = dealt_whole[:, 4 * half : 4 * half + 4, :, 32 * i : 32 * i + 32]
                u = dealt_turns[:, 4 * half : 4 * half + 4, :, 32 * i : 32 * i + 32]
                split(u, count, bank[:].rearrange("p (k q t) -> p k t q", k=4, t=4))
            else:
                split(turns[half][:, lo : lo + width], whole[half][:, lo : lo + width], bank[:])

        def cosine(i, step, width):
            half, lo = divmod(step * width, BANK)
            row = cos45[:, i - 4, :] if i < 6 else cos67[:, 0, :]
            blocks = [
                (turns[half][:, c : c + P], whole[half][:, c : c + P].bitcast(F32)) for c in range(lo, lo + width, P)
            ]
            turn_back(row[:, step * width : (step + 1) * width], blocks, BACK_BANKS[i][step])

        def z0_blocks(lo, hi):
            for k in range(lo, hi):
                ring = cos0[:, k % 4, :]
                codes = [(dealt_turns[:, k, t, :], dealt_whole[:, k, t, :].bitcast(F32)) for t in range(4)]
                turn_back(ring, codes, k % 4)
                nc.gpsimd.tensor_tensor(
                    z0[:, P * k : P * (k + 1), :].rearrange("p (c f) t -> p c t f", f=4),
                    ring.rearrange("p (t c f) -> p c t f", t=4, f=4),
                    work0[:, :, P * k : P * (k + 1)].rearrange("p t (c f) -> p c t f", f=4),
                    ALU.mult,
                )

        def z1_halves(i):
            for half in range(2):
                lo, hi = BANK * half, BANK * (half + 1)
                cosine(i, half, BANK)
                nc.gpsimd.tensor_tensor(
                    pair_view[:, 0, lo:hi, i - 4], cos45[:, i - 4, lo:hi], works[0][:, i - 4, lo:hi], ALU.mult
                )

        def quantise(codes, scales, values):
            nc.vector.quantize_mx(out=codes.bitcast(E4M3), scales=scales, in_=values.rearrange("p c t -> p (c t)"))

        def round_wo(b):
            for c in range(0, N, P):
                nc.scalar.copy(wo_bf[:, b, c : c + P, :], wo_raw[:, b, :, c : c + P].rearrange("p t n -> p n t"))

        per_turn = placed("per_turn", [P, Q], F32)
        nc.gpsimd.memset(per_turn[:], 1.0)
        make_heat(2)
        make_heat(3)
        round_wo(0)
        x0 = placed("x0", [P, M], F32)
        put_fused(0, 0, Q, heat0[:, 0:Q])
        put_fused(1, 0, Q, heat1[:, 0:Q])
        put_fused(0, Q, BANK, heat0[:, Q:BANK])
        put_fused(1, Q, BANK, heat1[:, Q:BANK])
        put_fused(0, BANK, S, heat0[:, BANK:S])
        put_fused(1, BANK, BANK + Q, third1)
        fetch(0, 0, M, x0[:])
        weigh(1, S - Q, S, third1, last1)
        put(1, S - Q, S, third1)
        for lo, hi in ((0, Q), (Q, S)):
            weigh(2, lo, hi, weighed[2][:, lo:hi], heat[2][:, lo:hi])
        for half in range(2):
            after_fetch(0, half, x0[:, BANK * half : BANK * (half + 1)])
        weigh_tile(3)
        nc.gpsimd.tensor_copy(
            w4_sorted[:].bitcast(I32).rearrange("p (a t q w) -> p a t q w", a=2, t=4, w=2),
            w4_back[:].rearrange("p a (q t w) -> p a t q w", t=4, w=2),
        )
        nc.sync.dma_start(work0[:], work[0:512, :].rearrange("(p t) m -> p t m", t=4))
        work_rows = work[512:1024, :].rearrange("(q t e) m -> t q e m", t=4, e=4)
        for t in range(4):
            nc.sync.dma_start(works[t // 2][:, t % 2, :], work_rows[t])
        round_wo(1)
        nc.scalar.activation(per_turn[:], per_turn[:], ACT.Copy, scale=-1.0 / TURN)

        def put_first(i):
            put(i, 0, Q, weighed[i][:, 0:Q])
            fetch(i - 1, 0, M, heat[i])

        def put_rest(i):
            put(i, Q, S, weighed[i][:, Q:S])

        def x_half(i, half):
            after_fetch(i, half, heat[i + 1][:, BANK * half : BANK * (half + 1)])

        put_first(2)
        put_rest(2)
        for half in range(2):
            x_half(1, half)
            make_heat(4 + half)
            weigh_tile(4 + half)

        put_first(3)
        put_rest(3)
        for half in range(2):
            x_half(2, half)
            make_heat(6 + half)

        put_first(4)
        quantise(wo_w[:], wo_s[:], wo_bf[:].rearrange("p b n t -> p (b n) t"))
        put_rest(4)
        x_half(3, 0)
        weigh_tile(6)
        weigh(LAST, Q, S, rest7[:], heat[LAST][:, Q:S])
        weigh(LAST, 0, Q, head7[:], heat[LAST][:, 0:Q])
        z0_blocks(0, 2)
        x_half(3, 1)
        z0_blocks(2, 6)

        put_first(5)
        put_rest(5)
        x_half(4, 0)
        z0_blocks(6, 8)
        x_half(4, 1)
        z1_halves(4)

        put_first(6)
        put_rest(6)
        for half in range(2):
            x_half(5, half)
        z1_halves(5)

        put(LAST, 0, Q, head7[:])
        for lo in (0, BANK):
            fetch(6, lo, lo + BANK, heat[LAST][:, lo : lo + BANK])
        put(LAST, Q, S, rest7[:])
        for step in range(CHUNKS + 1):
            if step < CHUNKS:
                after_fetch(6, step, heat[LAST][:, Q * step : Q * (step + 1)])
            if step > 0:
                cosine(6, step - 1, Q)

        z0_parts = list(zip(Z0_EDGES[:-1], Z0_EDGES[1:]))
        z0_s = [placed("z0_s%d" % k, [P, hi - lo], U8) for k, (lo, hi) in enumerate(z0_parts)]
        z1_s = placed("z1_s", [P, M], U8)
        parts = [placed("parts%d" % j, [P, 2, Q], F32) for j in range(CHUNKS)]
        x_a = placed("x_a", [P, Q], F32)
        x_last = [x_a[:], placed("x_b", [P, Q], F32)[:], x_a[:], parts[0][:, 0, :]]
        staged = placed("staged", [P, 4 * M], F32)
        sums = {}

        def score(j, b, scales):
            share = 4 // len(SCORE_BANKS[j])
            for n_tile in range(4):
                col = N * b + P * n_tile
                nc.tensor.matmul_mx(
                    out=sums[j][n_tile // share][:, n_tile % share, :],
                    lhsT=wo_w[:, col : col + P].bitcast(E4M3),
                    lhsT_scale=wo_s[:, col : col + P],
                    rhs=z_w[b][:, Q * j : Q * (j + 1)].bitcast(E4M3),
                    rhs_scale=scales,
                    start=(b == 0 and n_tile % share == 0),
                    stop=(b == 1 and n_tile % share == share - 1),
                )

        def quantise_z0(k):
            lo, hi = z0_parts[k]
            quantise(z_w[0][:, lo:hi], z0_s[k][:], z0[:, lo:hi, :])

        def first_pass(j, k):
            sums[j] = [bank_tile(bank, [P, 4 // len(SCORE_BANKS[j]), Q]) for bank in SCORE_BANKS[j]]
            at = Q * j - z0_parts[k][0]
            score(j, 0, z0_s[k][:, at : at + Q])

        def fetch_last(j):
            window = pages[LAST % 2][:].indirect(list3[:, Q // 16 * j : Q // 16 * (j + 1)])
            nc.vector.tensor_tensor(x_last[j], window, per_turn[:], ALU.mult)

        def count_turns(j):
            nc.scalar.activation(parts[j][:, 1, :].bitcast(U32), x_last[j], ACT.Relu, bias=0.25)

        def reduce_turns(j):
            nc.vector.scalar_tensor_tensor(
                parts[j][:, 0, :], x_last[j], -CAP / TURN, parts[j][:, 1, :].bitcast(I32), ALU.max, ALU.subtract
            )

        def sine(j):
            dest = cos67[:, 1, Q * j : Q * (j + 1)]
            nc.scalar.activation(dest, parts[j][:, 0, :], ACT.Sin, bias=math.pi / 2, scale=TURN)

        def multiply(j):
            lo, hi = Q * j, Q * (j + 1)
            nc.vector.tensor_tensor(
                pair_view[:, 1, lo:hi, :].rearrange("p (c f) t -> p c t f", f=4),
                cos67[:, :, lo:hi].rearrange("p t (c f) -> p c t f", f=4),
                works[1][:, :, lo:hi].rearrange("p t (c f) -> p c t f", f=4),
                ALU.mult,
            )

        def weave(j):
            lo, hi = Q * j, Q * (j + 1)
            word, copy = (U32, nc.scalar.copy) if j < SCALAR_WEAVES else (I32, nc.vector.tensor_copy)
            copy(
                z1[:, lo:hi, :].rearrange("p m t -> p (m t)").bitcast(word).rearrange("p (m w) -> p m w", w=2),
                z_pairs[:].bitcast(word).rearrange("p (w m) -> p m w", w=2)[:, lo:hi, :],
            )

        def second_pass(j):
            lo, hi = Q * j, Q * (j + 1)
            quantise(z_w[1][:, lo:hi], z1_s[:, lo:hi], z1[:, lo:hi, :])
            score(j, 1, z1_s[:, lo:hi])

        def store(j):
            share = 4 // len(sums[j])
            for k, bank in enumerate(sums[j]):
                at = Q * (4 * j + k * share)
                dest = staged[:, at : at + share * Q]
                copy = nc.vector.tensor_copy if (j == CHUNKS - 1 and k % 2 == 1) else nc.scalar.copy
                copy(dest, bank[:].rearrange("p a c -> p (a c)"))
                nc.sync.dma_start(
                    out[share * P * k : share * P * (k + 1), Q * j : Q * (j + 1)].rearrange("(a p) c -> p a c", a=share),
                    dest.rearrange("p (a c) -> p a c", a=share),
                )

        def stage(work_on, j):
            if 0 <= j < CHUNKS:
                work_on(j)

        quantise_z0(0)
        first_pass(0, 0)
        for step in range(CHUNKS + 4):
            stage(fetch_last, step)
            if step == 1:
                quantise_z0(1)
                first_pass(1, 1)
                first_pass(2, 1)
            stage(reduce_turns, step - 1)
            stage(weave, step - 3)
            if step == CHUNKS + 1:
                quantise_z0(2)
            stage(count_turns, step)
            stage(sine, step - 1)
            stage(second_pass, step - 3)
            stage(multiply, step - 2)
            stage(store, step - 4)
            if step == CHUNKS + 1:
                first_pass(CHUNKS - 1, 2)
